import numpy as np, ml_dtypes
CORES = [48,51,52,55]
N = 4
import mx_ref
BF = ml_dtypes.bfloat16
def gentries(a):
    return np.ascontiguousarray(a.reshape(8, 16, -1).transpose(0, 2, 1)).reshape(8, -1)
def gtable(e):
    e = np.asarray(e); return np.ascontiguousarray(e.reshape(8, -1, 16).transpose(0, 2, 1)).reshape(128, -1).astype(np.int32)
def gcols(t, e):
    v = np.concatenate([t.reshape(8, 16, -1, 4), np.zeros((8, 16, 1, 4), BF)], axis=2)
    return np.ascontiguousarray(np.stack([v[g][:, e[g]] for g in range(8)])).reshape(128, -1)
def tile(rs):
    return np.stack(rs, axis=2).reshape(128, -1).astype(BF)
def pick(q, e):
    c = np.concatenate([q[0].reshape(128, -1, 4), np.zeros((128, 1, 4), np.uint8)], axis=1); s = np.concatenate([q[1], np.ones((16, 1), np.uint8)], axis=1)
    return (np.ascontiguousarray(c[:, e].reshape(128, -1)), np.ascontiguousarray(s[:, e]))
def join(*qs):
    return (np.concatenate([q[0] for q in qs], axis=1), np.concatenate([q[1] for q in qs], axis=1))
def put(q, e, v):
    c, s = q[0].reshape(128, -1, 4).copy(), q[1].copy(); c[:, e] = v[0].reshape(128, -1, 4); s[:, e] = v[1]
    return (c.reshape(128, -1), s)
def pk(c, s):
    return (np.ascontiguousarray(c), mx_ref.live(s))
def emit(q):
    return q[0], q[1]
def packed(v, rng):
    q = [mx_ref.quantize(np.ascontiguousarray(v[r])) for r in range(N)]
    return np.stack([a for a, b in q]), np.stack([mx_ref.plane(b, rng) for a, b in q])
def values_of_codes():
    e, c = np.zeros((128, 128, 4), np.float32), np.zeros((128, 2, 4), np.uint8)
    e[np.arange(128), np.arange(128), 0] = 1
    c[:127, :, 0] = np.arange(256).reshape(2, 128).T[:127]
    return mx_ref.matmul(mx_ref.quantize(e.reshape(128, 512).astype(BF)), (c.reshape(128, 8), np.full((16, 2), 127, np.uint8))).T.reshape(-1).astype(np.float64)
CODE_VALUE, SCALE_VALUE = values_of_codes(), 2.0 ** (np.arange(256) - 127.0)
def decode(q):
    return (CODE_VALUE[q[0]].reshape(16, 8, -1, 4) * SCALE_VALUE[q[1]][:, None, :, None] + 0.0).reshape(128, -1).astype(np.float32)
def f(rng, *shape):
    return mx_ref.flush((rng.standard_normal(shape, dtype=np.float32) * np.exp2(rng.integers(-2, 3, shape[:-1] + (1,)))).astype(BF))
def wide(rng, *shape, cols=0):
    v = rng.standard_normal(shape, dtype=np.float32) * np.exp2(rng.integers(-12, 13, shape)).astype(np.float32)
    if cols: v *= np.repeat(np.exp2(rng.integers(-cols, cols + 1, shape[:-2] + (1, shape[-1] // 4))) * (rng.random(shape[:-2] + (1, shape[-1] // 4)) > 0.0625), 4, axis=-1).astype(np.float32)
    return mx_ref.flush(v.astype(BF))
C, GW, R, SWEEPS = 384, 96, 3, 6
JUMP = [0, 1, 4]
def big(v):
    v = v.astype(np.float32)
    v[np.abs(v) < np.float32(2.0 ** -16)] = 0
    return v.astype(BF)
def numbers_of(rng):
    return {"x": big(f(rng, N, 128, 4 * C)), "u": np.array(f(rng, N, 128, 512)), "v": np.array(f(rng, N, 128, 512))}
def weights(rng, still=[]):
    w = big(f(rng, N, 128, 2048)).reshape(N, 8, 16, 4, 8, 16, 4)
    for i in still:
        w[:, :, i] = 0
        w[:, :, :, :, :, i] = 0
    c, p = packed(w.reshape(N, 128, 2048), rng)
    return {"wc": c, "ws": p}
def ltable(a):
    return gtable(a.transpose(1, 0, 2).reshape(8, 3 * C))
def drawn(rng):
    a = np.zeros((3, 8, C), np.int64)
    for g in range(8):
        o = rng.permutation(C)
        a[0, g, o[::2]] = o[1::2]
        a[0, g, o[1::2]] = o[::2]
        for k in (1, 2):
            if g & JUMP[k] == 0:
                o = rng.permutation(C)
                a[k, g] = o
                a[k, g ^ JUMP[k], o] = np.arange(C)
    return a
def links(rng):
    return np.stack([ltable(drawn(rng)) for r in range(N)])
def setup_inputs(rng):
    return {**numbers_of(rng), "lk": links(rng), **weights(rng)}
def setup_inputs_ties(rng):
    d = numbers_of(rng)
    x = d["x"].reshape(N, 8, 16, C, 4)
    x[:, :, 0] = 0
    x[:, :, 0, :, 0] = rng.integers(0, 4, (N, 8, C)).astype(np.float32).astype(BF)
    u = d["u"].reshape(N, 128, 128, 4)
    u[:, :, ::16] = 0
    o = rng.permutation(N)
    for r in range(N):
        for h in range(0, 128, 16): u[r, h, h, 0] = 0.0 if r == o[0] else -1.0 if r == o[1] else 1.0
    return {"x": x.reshape(N, 128, 4 * C), "u": u.reshape(N, 128, 512), "v": d["v"], "lk": links(rng), **weights(rng, [0])}
def setup_inputs_near(rng):
    d = numbers_of(rng)
    x = d["x"].astype(np.float32).reshape(N, 8, 16, C, 4)
    x[:, :, 0] = 0
    x[:, :, 8:] = 0
    x[:, :, 0, :, 0] = 1
    s = rng.integers(0, 16, (N, 8, C))
    x[:, :, 8] = ((s[:, :, :, None] >> np.arange(4)) & 1) * np.exp2(np.arange(4) - 21.0)
    x[:, :, 11, :, 0] = 2.0 ** -10
    u = d["u"].reshape(N, 128, 128, 4)
    u[:, :, ::16] = 0
    o = rng.permutation(N) % 4
    for r in range(N):
        far = rng.permutation(8)
        if o[r] == 0: x[r, :, 0, :, 0] = 7
        if o[r] == 1: x[r, :, 0, :, 0] = -1
        if o[r] < 2:
            for i in range(4): x[r, far[i], 0, rng.integers(C), 0] = (-1.5 if i == 0 else 1.5) * 2.0 ** 29
        if o[r] == 3:
            x[r, :, 8:] = 0
            x[r, :, 10, :, 0] = (8 + rng.integers(0, 8, (8, C))) * 2.0 ** -33
        k = 1.0 if o[r] == 0 else 2.0 ** -30
        for g in range(8):
            h = 16 * g
            if o[r] < 2:
                u[r, h, h, 0] = k
                u[r, h + 11, h, 0] = k
            if o[r] == 2 and g == far[0]: u[r, h, h, 0] = 1.0
            if o[r] == 2 and g == far[1]: u[r, h, h, 0] = -1.0
            if o[r] < 3: u[r, h + 8, h] = k
            else: u[r, h + 10, h, 0] = k * 1.125 if g >= 4 else k
    return {"x": x.reshape(N, 128, 4 * C).astype(BF), "u": u.reshape(N, 128, 512), "v": d["v"], "lk": links(rng), **weights(rng, [0, 8, 9, 10, 11, 12, 13, 14, 15])}
def setup_inputs_cubes(rng):
    d = numbers_of(rng)
    x = d["x"].reshape(N, 8, 16, C, 4)
    x[:, :, 0] = 0
    low = (1.125 + 0.25 * rng.integers(0, 4, (N, 8, 8, C, 4))) * np.exp2(10.0 - rng.integers(8, 15, (N, 8, 8, C, 4)))
    x[:, :, 8:] = (low * rng.choice([-1.0, 1.0], (N, 8, 8, C, 4))).astype(np.float32).astype(BF)
    x[:, :, 8, :, 0] = 2016.0
    u = d["u"].reshape(N, 128, 128, 4)
    u[:, :, ::16] = 0
    p, e = [], rng.permutation(N)
    for r in range(N):
        o = rng.permutation(C) if e[r] % 2 else np.arange(C)
        k = np.zeros(C, np.float32)
        k[o] = np.repeat(rng.integers(-7, 8, C // 2), 2)
        x[r, :, 0, :, 0] = k.astype(BF)
        a = np.tile(np.arange(C), (3, 8, 1))
        a[0][:, o] = o[np.arange(C) ^ 1]
        p.append(ltable(a))
        for h in range(0, 128, 16): u[r, h, h, 0] = -1.0 if e[r] == 0 else 1.0
    w = big(f(rng, N, 128, 2048)).reshape(N, 8, 16, 4, 8, 16, 4)
    w[:, :, 0] = 0
    w[:, :, 8, :, :, :, 0] = 0
    w[:, :, :, :, :, 0] = 0
    w[:, :, :, :, :, 8:] = 0
    for g in range(8): w[:, g, 8, 0, g, 8, 0] = -1.0
    c, s = packed(w.reshape(N, 128, 2048), rng)
    return {"x": x.reshape(N, 128, 4 * C), "u": u.reshape(N, 128, 512), "v": d["v"], "lk": np.stack(p), "wc": c, "ws": s}
def setup_inputs_ends(rng):
    d = numbers_of(rng)
    o = rng.permutation(N) % 4
    a, b = np.flatnonzero(o < 2)[:2]
    o[[a + 1, b]] = o[[b, a + 1]]
    sg = rng.choice([-1.0, 1.0], N)
    x = np.ones((N, 8, 16, C, 4))
    u = d["u"].astype(np.float32).reshape(N, 8, 16, 8, 16, 4)
    u[:, :, :, :, 0] = 0
    v = rng.choice([-1.0, 1.0], (N, 128, 512))
    w = np.zeros((N, 128, 4, 128, 4), np.float32)
    i, p = np.arange(128), []
    for r in range(N):
        large = o[r] < 2
        size = 2.0 ** 30 if large else 2.0 ** -30
        h = rng.permutation(8)
        x[r, h[4:]] = rng.choice([1.0, 0.875, 0.75] if large else [1.0, 1.125, 1.25], (4, 1, C, 1))
        x[r] *= sg[r] * size
        v[r] *= size
        k = size * sg[r] * (1.0 if o[r] % 2 == 0 else -1.0)
        for g in range(8):
            for c in (h[:4] if g in h[:4] else h): u[r, c, :, g, 0] = k
        for b in range(4): w[r, i, b, i, b] = sg[r] * sg[r - 1] * (-2.0 if large else 2.0)
        a = drawn(rng)
        if large:
            a[:2] = C - 1 - np.arange(C)
            a[2] = np.arange(C)
        p.append(ltable(a))
    c, s = packed(w.reshape(N, 128, 2048).astype(BF), rng)
    return {"x": x.reshape(N, 128, 4 * C).astype(np.float32).astype(BF), "u": u.reshape(N, 128, 512).astype(BF), "v": v.astype(np.float32).astype(BF), "lk": np.stack(p), "wc": c, "ws": s}
def setup_inputs_spread(rng):
    d = setup_inputs(rng)
    d["x"] = big(wide(rng, N, 128, 4 * C, cols=6))
    return d
def check_inputs(d):
    b = []
    for k in ("x", "u", "v"):
        a = np.abs(d[k].astype(np.float32))
        if not (np.isfinite(a).all() and ((a == 0) | (a >= 2.0 ** -30) & (a <= 2.0 ** 30)).all()): b.append("a value of " + k)
    none, least, most = [emit(mx_ref.quantize(np.full((128, 16), k, np.float32).astype(BF)))[1][0, 0] for k in (0.0, 2.0 ** -16, 2.0 ** 5)]
    for r in range(N):
        e = gentries(d["lk"][r])
        if not ((e >= 0) & (e < C)).all(): b.append("an entry of lk")
        else:
            n = other_ends(d["lk"][r])
            if (np.take_along_axis(n, n, axis=1) != np.arange(8 * C)).any(): b.append("a link of lk isn't the same from both ends")
            if (n == np.arange(8 * C)).any(): b.append("a link of lk from a node to itself")
        if ((d["wc"][r] == 0x7F) | (d["wc"][r] == 0xFF)).any(): b.append("wc: a code that is no number")
        s = mx_ref.live(d["ws"][r])
        if ((s != none) & ((s < least) | (s > most))).any(): b.append("ws: a scale out of range")
    return b
def other_ends(a):
    e = gentries(a).reshape(8, 3, C).astype(np.int64)
    return np.stack([(e[:, k] + C * (np.arange(8) ^ JUMP[k])[:, None]).reshape(-1) for k in range(3)])
def parts(t):
    return t.reshape(8, 16, -1, 4).transpose(0, 2, 1, 3).reshape(-1, 16, 4)
def whole(p):
    return np.ascontiguousarray(p.reshape(8, -1, 16, 4).transpose(0, 2, 1, 3)).reshape(128, -1)
def reference(x, u, v, lk, wc, ws):
    qu = [mx_ref.quantize(u[r]) for r in range(N)]
    lay = [pk(wc[r], ws[r]) for r in range(N)]
    ends = [other_ends(lk[r]) for r in range(N)]
    now = [x[r] for r in range(N)]
    node = np.arange(8 * C)
    away, mark = [None] * N, [np.zeros((3, 8 * C), bool) for r in range(N)]
    route = [None] * N
    for t in range(R):
        sent, blend, gate = [], [], []
        for r in range(N):
            q, n = mx_ref.quantize(now[r]), ends[r]
            s = mx_ref.matmul(qu[r], q)[::16] + np.float32(0.0)
            l = np.argsort(s, axis=1, kind="stable")[:, :GW]
            slot = np.full((8, C), -1)
            np.put_along_axis(slot, l, np.tile(np.arange(GW), (8, 1)), axis=1)
            slot, s = slot.reshape(-1), s.reshape(-1)
            a, m = away[r], mark[r]
            if t == 0: a = (s[n] < s) | (s[n] == s) & (n < node)
            for i in range(SWEEPS):
                sink = ~a.any(axis=0) & (slot < 0)
                turn = sink & (~m | m.all(axis=0))
                came = np.take_along_axis(turn, n, axis=1)
                a = (a | turn) & ~came
                m = (m & ~sink) | came
            away[r], mark[r] = a, m
            k = np.argmin(np.where(a, s[n], np.float32(np.inf)), axis=0)
            to = np.where((slot < 0) & a.any(axis=0), n[k, node], node)
            e = to[to]
            e = e[e]
            own = decode(q)
            p = parts(own)
            blend.append(((p[to] + p[e]) * np.float32(0.5)).astype(BF))
            sent.append(mx_ref.quantize(gcols(own.astype(BF), l)))
            gate.append(slot)
            route[r] = e
        for r in range(N):
            h = parts(tile([mx_ref.matmul(pick(lay[r], np.arange(128 * b, 128 * b + 128)), sent[r - 1]) * np.float32(0.015625) for b in range(4)]))
            z, e, k = blend[r], route[r], gate[r][route[r]]
            w = k >= 0
            z[w] = (z[w].astype(np.float32) + h[GW * (e[w] // C) + k[w]].astype(np.float32)).astype(BF)
            now[r] = whole(z)
    y, nd = np.zeros((N, 128, C), np.float32), np.zeros((N, 8, 2 * C), np.float32)
    oc, osc = np.zeros((N, 128, 4 * C), np.uint8), np.zeros((N, 16, C), np.uint8)
    for r in range(N):
        q = mx_ref.quantize(now[r])
        y[r] = mx_ref.matmul(mx_ref.quantize(v[r]), q)
        nd[r, :, :C] = route[r].reshape(8, C)
        a, m = away[r].astype(np.int64), mark[r].astype(np.int64)
        nd[r, :, C:] = (a[0] + 2 * a[1] + 4 * a[2] + 8 * m[0] + 16 * m[1] + 32 * m[2]).reshape(8, C)
        oc[r], osc[r] = emit(q)
    return {"y": y, "nd": nd, "oc": oc, "osc": osc}

@@ -1,0 +1,727 @@
+import math
+from concourse.bass import DstId, RemoteDMATransfer
+from concourse.mybir import dt, AluOpType, AxisListType, ActivationFunctionType
+
+OP = AluOpType
+COPY, IDENT = ActivationFunctionType.Copy, ActivationFunctionType.Identity
+C, GW, R, SWEEPS = 384, 96, 3, 6
+JUMP = [0, 1, 4]
+
+TILES = ["gone", "qsel", "qneg", "q3", "q1_0", "q1_1", "q1_2", "st0", "st1", "st2", "sto", "came0", "came1", "came2",
+         "own0", "own1", "own2", "hop0", "hop1", "hop2", "cls0", "cls1", "cls2", "cls3", "hopf0", "ct0", "ct1", "ct2", "ct3", "ge", "gm", "gb"]
+TI = {n: i for i, n in enumerate(TILES)}
+NT = len(TILES)
+VSWEEP = [0, 448, 352, 320, 224, 512]
+VHOP = 512
+SLOTS = [4, 4, 4, 4, 4, 4, 4]
+FSHARE = [6, 4, 3, 3, 0, 0]
+FFIRST = 2
+SSHARE = 3
+ENGINES = 8
+
+F32, BF, I32, U16, X4, U8 = "float32", "bfloat16", "int32", "uint16", "float8_e4m3fn_x4", "uint8"
+SCRATCH = {}
+WIDE = {"KF": "JM MD ND IJF CMr RM J0 J1 J2 D0 D1 D2", "KI": "PC UL WL", "XI": "EI EP",
+        "XF": "SB1 ST SB2 ST2 SB3 ST3 t0 t1 t2 ua ub PE la lb lc qa qb qd qm ea eb ec ba bb",
+        "XB": "G3 G9 MA MB MC TU R0 R1 R2 va0 va1 va2 mx0 mx1 mx2 pk0 pk1 pk2 self SJ PP OC0 OC1 OC2 JC EQ LT LE ML"}
+HOME = {n: w for w in WIDE for n in WIDE[w].split()}
+PLACE, LEN = {}, {}
+
+
+def sb(name, n, d):
+    w = HOME.get(name, name)
+    a = SCRATCH[w][1][1] if w in SCRATCH else 0
+    PLACE[name], LEN[name] = (w, a), n
+    SCRATCH[w] = ("sbuf", [128, a + (n if w == name else (n + 15) // 16 * 16)], d)
+
+
+def mx(name, n):
+    sb(name + "c", n, X4)
+    sb(name + "s", n, U8)
+
+
+for _n, _w, _d in [
+        ("X0", 1536, BF), ("U", 512, BF), ("VV", 512, BF),
+        ("LKT", 72, I32), ("LKS", 72, I32), ("OFT", 72, U16), ("OFJ", 72, U16), ("OFS", 72, U16),
+        ("UL", 24, I32), ("ULo", 24, U16), ("WL", 128, I32), ("WLo", 128, U16),
+        ("PC", 16, I32), ("PF", 48, F32), ("WT", 1024, BF), ("CB", 512 * NT, BF), ("FB", 4 * 516, BF),
+        ("GC", 96, BF), ("GCt", 96, BF), ("GD", 128, BF), ("GDt", 128, BF), ("GH", 96, BF), ("KM", 32, BF), ("GOt", 512, BF),
+        ("JM", C, F32), ("MD", C, F32), ("ND", C, F32), ("MX", C, F32), ("NX", C, F32), ("NS", 24, F32), ("TM", 2 * C, BF), ("IJF", C, F32),
+        ("CMr", 96, F32), ("RM", 96, F32), ("J0", 96, F32), ("J1", 96, F32), ("J2", 96, F32), ("qm", C, F32),
+        ("TS", 3 * C, F32), ("SB1", C, F32), ("ST", C, F32), ("EQ", C, BF), ("ET", 4 * C, BF),
+        ("GT", 512, BF), ("G3", 96, BF), ("G9", 96, BF), ("PLo", 24, U16), ("LW", C, F32), ("SB2", C, F32),
+        ("ST2", C, F32), ("SB3", GW, F32), ("ST3", GW, F32), ("ELo", 6, U16),
+        ("FT", 16 * C, BF), ("HT", 16 * C, BF), ("SL", 4 * C, F32), ("FD", 4 * C, BF), ("Z", 4 * C, BF), ("WA", 4 * C, BF),
+        ("LT", C, BF), ("LE", C, BF), ("ML", C, BF), ("AW", 1280, BF), ("RF", 1280, BF), ("NB", 2 * C, F32),
+        ("MA", 96, BF), ("MB", 96, BF), ("MC", 96, BF), ("IN", 512, BF), ("TU", 96, BF), ("W", 512, BF), ("GA", 1280, BF),
+        ("R0", 96, BF), ("R1", 96, BF), ("R2", 96, BF), ("va0", 96, BF), ("va1", 96, BF), ("va2", 96, BF),
+        ("mx0", 96, BF), ("mx1", 96, BF), ("mx2", 96, BF), ("pk0", 96, BF), ("pk1", 96, BF), ("pk2", 96, BF),
+        ("self", 96, BF), ("SJ", 96, BF), ("t0", 96, F32), ("t1", 96, F32), ("t2", 96, F32),
+        ("ua", 96, F32), ("ub", 96, F32), ("PP", 96, BF), ("PE", 96, F32),
+        ("la", 96, F32), ("lb", 48, F32), ("lc", 24, F32), ("DL", 24, U16), ("EL", 24, U16), ("HL", 24, U16),
+        ("D0", C, F32), ("D1", C, F32), ("D2", C, F32), ("CTF", C, F32),
+        ("qa", C, F32), ("qb", 192, F32), ("qd", 96, F32), ("OC0", 96, BF), ("OC1", 96, BF), ("OC2", 96, BF), ("JC", 96, BF),
+        ("ea", 96, F32), ("eb", 96, F32), ("ec", 96, F32), ("EI", 96, I32), ("EP", 288, I32), ("ba", 96, F32), ("bb", 96, F32),
+        ("C0", 4 * C, BF), ("C1", 4 * C, BF), ("C2", 4 * C, BF), ("E0", 512, BF), ("E1", 512, BF), ("E2", 512, BF)]:
+    sb(_n, _w, _d)
+for _n, _w in [("QX", C), ("QU", 128), ("QUP", C), ("QV", 128), ("WC", 512), ("WP", 2048), ("QK", 128 * NT), ("QF", 2048),
+               ("QT", 7 * C), ("QG", 128), ("QAW", 320), ("QRF", 320), ("QIN", 128), ("QGA", 320), ("QW", 128),
+               ("QE", 3 * 128), ("LD", 320), ("QND", C)]:
+    mx(_n, _w)
+PS = ["PV0", "PV1", "PV2", "PV3", "PA", "PB", "PCC", "PD"]
+for _n in PS:
+    SCRATCH[_n] = ("psum", [128, 512], F32)
+    PLACE[_n], LEN[_n] = (_n, 0), 512
+SEMAPHORES = ["sv", "ss", "st", "sg", "lcl", "arr0", "arr1", "arr2"] + ["d%d" % i for i in range(10)]
+
+
+def rank_program(g, core, T, topo):
+    rank = T.rank_of(core)
+    if rank is None:
+        return
+    nxt = T.cores[(rank + 1) % len(T.cores)]
+    Q = {"V": g.vector, "S": g.scalar, "T": g.tensor, "G": g, "Y": g.sync}
+    SEM = {"V": "sv", "S": "ss", "T": "st", "G": "sg"}
+    cnt = {s: 0 for s in SEMAPHORES}
+    known = {q: {} for q in Q}
+    clk, wrs, rds, bank = {}, {}, {}, {}
+
+    def overlap(a, b):
+        if a[1] <= b[0] or b[1] <= a[0]: return False
+        d = math.gcd(a[2], b[2])
+        return not (d > 1 and (a[0] - b[0]) % d)
+
+    def await_(q, deps):
+        best = {}
+        for s, c in deps:
+            best[s] = max(best.get(s, 0), c)
+        for s, c in sorted(best.items(), key=lambda t: -t[1]):
+            if known[q].get(s, 0) >= c: continue
+            Q[q].wait_ge(T.sem[s], c)
+            known[q][s] = c
+            for s2, c2 in clk[(s, c)].items():
+                if known[q].get(s2, 0) < c2: known[q][s2] = c2
+
+    def deps_of(q, rd, wr):
+        deps = []
+        for n, lo, hi, st in rd:
+            if n in PS: continue
+            for e in wrs.get(n, []):
+                if overlap(e[0], (lo, hi, st)): deps.append(e[1])
+        for n, lo, hi, st in wr:
+            if n in PS: continue
+            for e in wrs.get(n, []):
+                if overlap(e[0], (lo, hi, st)): deps.append(e[1])
+            for e in rds.get(n, []):
+                if overlap(e[0], (lo, hi, st)): deps.append(e[1])
+        for n in set(x[0] for x in list(rd) + list(wr) if x[0] in PS):
+            for q2, m in bank.get(n, {}).items():
+                if q2 != q: deps.append(m)
+        return deps
+
+    def record(q, m, rd, wr):
+        for n, lo, hi, st in wr:
+            if n in PS: continue
+            for tab in (wrs, rds):
+                tab[n] = [e for e in tab.get(n, []) if not (e[0][0] >= lo and e[0][1] <= hi and (st == 1 or (e[0][2] == st and e[0][0] == lo)))]
+            wrs[n].append(((lo, hi, st), m, q))
+        for n, lo, hi, st in rd:
+            if n in PS: continue
+            rds[n] = [e for e in rds.get(n, []) if not (e[2] == q and q != "D" and e[0] == (lo, hi, st))] + [((lo, hi, st), m, q)]
+        for n in set(x[0] for x in list(rd) + list(wr) if x[0] in PS):
+            b = bank.get(n, {})
+            b = {q2: m2 for q2, m2 in b.items() if q2 == q or known[q].get(m2[0], 0) < m2[1]}
+            b[q] = m
+            bank[n] = b
+
+    def do(q, fn, rd, wr):
+        await_(q, deps_of(q, rd, wr))
+        s = SEM[q]
+        cnt[s] += 1
+        m = (s, cnt[s])
+        fn(Q[q]).then_inc(T.sem[s], 1)
+        c = dict(known[q])
+        c[s] = cnt[s]
+        clk[m] = c
+        record(q, m, rd, wr)
+
+    def dma(q, s, pairs, rd=(), wr=()):
+        await_(q, deps_of("D", rd, wr))
+        for o, i in pairs:
+            Q[q].dma_start(o, i).then_inc(T.sem[s], 16)
+            cnt[s] += 16
+        m = (s, cnt[s])
+        c = dict(known[q])
+        c[s] = cnt[s]
+        clk[m] = c
+        record("D", m, rd, wr)
+
+    def r(n, lo=0, hi=None, st=1):
+        w, a = PLACE[n]
+        return (w, a + lo, a + (LEN[n] if hi is None else hi), st)
+
+    def ap(x):
+        n, lo, hi, st = x
+        return T[n][:, lo:hi] if st == 1 else T[n][:, lo:hi:st]
+
+    isr = lambda x: isinstance(x, tuple)
+    val = lambda x: ap(x) if isr(x) else x
+
+    def ts(o, i, s1, op0, s2=None, op1=None):
+        rd = [i] + [s for s in (s1, s2) if isr(s)]
+        if op1 is None: do("V", lambda e: e.tensor_scalar(ap(o), ap(i), val(s1), None, op0), rd, [o])
+        else: do("V", lambda e: e.tensor_scalar(ap(o), ap(i), val(s1), val(s2), op0, op1), rd, [o])
+
+    def tt(o, a, b, op, off=None):
+        if off is None: do("V", lambda e: e.tensor_tensor(ap(o), ap(a), ap(b), op), [a, b], [o])
+        else: do("V", lambda e: e.tensor_tensor(ap(o), ap(a).indirect(ap(off)), ap(b), op), [a, b, off], [o])
+
+    def tc(o, a, off=None):
+        if off is None: do("V", lambda e: e.tensor_copy(ap(o), ap(a)), [a], [o])
+        else: do("V", lambda e: e.tensor_copy(ap(o), ap(a).indirect(ap(off))), [a, off], [o])
+
+    def act(o, a, bias=0.0, scale=1.0, off=None, fn=COPY):
+        rd = [a] + [x for x in (scale, bias, off) if isr(x)]
+        if off is None: do("S", lambda e: e.activation(ap(o), ap(a), fn, bias=val(bias), scale=val(scale)), rd, [o])
+        else: do("S", lambda e: e.activation(ap(o), ap(a).indirect(ap(off)), fn, bias=val(bias), scale=val(scale)), rd, [o])
+
+    def scan(o, a, b, op0=OP.mult, op1=OP.add):
+        do("V", lambda e: e.tensor_tensor_scan(ap(o), ap(a), ap(b), 0.0, op0, op1), [a, b], [o])
+
+    def fill(o, c):
+        do("V", lambda e: e.memset(ap(o), c), [], [o])
+
+    def quant(n, a, b, src):
+        q, s = r(n + "c", a, b), r(n + "s", a, b)
+        do("V", lambda e: e.quantize_mx(ap(q), ap(s), ap(src)), [src], [q, s])
+
+    def pick(n, src, k, off):
+        m, w = 16 * (off[2] - off[1]), LEN[src + "c"]
+        do("V", lambda e: e.tensor_copy(T[n + "c"][:, 0:m].bitcast(dt.uint32), T[src + "c"][:, 0:w].bitcast(dt.uint32).indirect(ap(off))), [r(src + "c"), off], [r(n + "c")])
+        do("S", lambda e: e.activation(T[n + "s"][:, 0:m], T[src + "s"][:, 0:w].indirect(ap(off)), COPY), [r(src + "s"), off], [r(n + "s")])
+
+    def mm(bk, st, mv, n, start=True, stop=True):
+        l, ls = r(st[0] + "c", st[1], st[1] + 128), r(st[0] + "s", st[1], st[1] + 128)
+        m, ms = r(mv[0] + "c", mv[1], mv[1] + n), r(mv[0] + "s", mv[1], mv[1] + n)
+        o = r(bk, 0, n)
+        do("T", lambda e: e.matmul_mx(ap(o), ap(l), ap(ls), ap(m), ap(ms), start, stop), [l, ls, m, ms], [o])
+
+    def iota(o, pat, base, cm):
+        fl = SCRATCH[o[0]][2] != I32
+        if fl: do("G", lambda e: e.iota(ap(o), pat, base, cm, allow_small_or_imprecise_dtypes=True), [], [o])
+        else: do("G", lambda e: e.iota(ap(o), pat, base, cm), [], [o])
+
+    def sel(o, i, pat, op, fl, base, cm):
+        do("G", lambda e: e.affine_select(ap(o), ap(i), pat, op, fl, base, cm), [i], [o])
+
+    K = lambda n: ("QK", 128 * TI[n])
+    tile0 = lambda n: 512 * TI[n]
+    tile = lambda n, a=0, st=1: r("CB", tile0(n) + a, tile0(n) + 512, st)
+
+    dma("Y", "d0", [(T.X0[:], T.x[:])], wr=[r("X0")])
+    dma("S", "d1", [(T.U[:], T.u[:])], wr=[r("U")])
+    dma("Y", "d2", [(T.LKT[:], T.lk[:])], wr=[r("LKT")])
+    pr = [(T.LKS[:, 0:24], T.lk[:, 0:24])]
+    for h in range(8):
+        a = h ^ JUMP[1]
+        pr.append((T.LKS[16 * h:16 * h + 16, 24:48], T.lk[16 * a:16 * a + 16, 24:48]))
+    for h in range(0, 8, 4):
+        a = h ^ JUMP[2]
+        pr.append((T.LKS[16 * h:16 * h + 64, 48:72], T.lk[16 * a:16 * a + 64, 48:72]))
+    dma("Y", "d3", pr, wr=[r("LKS")])
+    dma("Y", "d4", [(T.WCc[:].bitcast(dt.uint8), T.wc[:]), (T.WCs[:], T.ws[:])], wr=[r("WCc"), r("WCs")])
+    dma("Y", "d5", [(T.VV[:], T.v[:])], wr=[r("VV")])
+
+    GRP = {0: ([[16, 8]], 0), 1: ([[32, 4], [-16, 2]], 16), 4: ([[-64, 2], [16, 4]], 64)}
+    CLS = lambda A: 16 * (A & 1) + 64 * (A >> 1)
+    neg = lambda pat: [[-a, b] for a, b in pat]
+    for k in range(3):
+        iota(r("UL", 8 * k, 8 * k + 8), GRP[JUMP[k]][0], GRP[JUMP[k]][1], 0)
+    iota(r("PC", 0, 1), [[0, 1]], 0, 1)
+    iota(r("JM"), [[0, 24], [1, 16]], 0, 0)
+    fill(r("WT", 0, 512), 1.0)
+    for j, w in enumerate([-6.0, -2.0, 3.0, -1.0]):
+        fill(r("WT", 512 + 128 * j, 640 + 128 * j), w)
+    WCOL = {1.0: 0, -6.0: 512, -2.0: 640, 3.0: 768, -1.0: 896}
+    tc(r("ULo"), r("UL"))
+    for a in (0, 1024): act(r("FB", a, a + 1024), r("WT", 0, 1024), scale=0.0)
+    act(r("FB", 2048), r("WT", 0, 16), scale=0.0)
+    PFC = {}
+
+    def pcol(name):
+        PFC[name] = len(PFC)
+        return r("PF", PFC[name], PFC[name] + 1)
+
+    P = lambda name: r("PF", PFC[name], PFC[name] + 1)
+
+    def scol(name, a, scale=1.0, bias=0.0):
+        act(pcol(name), P(a), bias=bias, scale=scale, fn=IDENT if isr(bias) else COPY)
+
+    p = r("PC", 0, 1)
+    for j, (n, sh, an) in enumerate([("i", 0, 15), ("s", 0, 3), ("kk", 2, 3), ("g0", 4, 1), ("g1", 5, 1), ("g2", 6, 1)]):
+        o = r("PC", j + 1, j + 2)
+        ts(o, p, sh, OP.arith_shift_right, an, OP.bitwise_and)
+        tc(pcol(n), o)
+    ts(r("MD"), r("JM"), P("i"), OP.is_equal)
+    act(r("MX"), r("MD"), scale=2e29, bias=-1e29)
+    act(r("ND"), r("MD"), scale=-1.0, bias=1.0)
+    act(r("NX"), r("MD"), scale=-2e29)
+    for A in range(4):
+        for h in range(2):
+            a = 516 * A + 3 + 256 * h
+            sel(r("FB", a, a + 253, 4), r("WT", 0, 64), [[-32, 2], [0, 2], [-1, 16]], OP.is_equal, 0.0, -CLS(A), 1)
+    for k in range(3):
+        gp, gb = GRP[JUMP[k]]
+        sel(r("GCt", 32 * k, 32 * k + 32), r("WT", 0, 32), neg(gp) + [[0, 4]], OP.is_ge, 0.0, -gb, 1)
+        sel(r("GC", 32 * k, 32 * k + 32), r("GCt", 32 * k, 32 * k + 32), gp + [[0, 4]], OP.is_ge, 0.0, gb + 15, -1)
+    sel(r("NX"), r("NX"), [[0, 24], [1, 16]], OP.not_equal, -2e29, 0, 0)
+    sel(r("GOt"), r("WT", 0, 512), [[-16, 8], [0, 64]], OP.is_ge, 0.0, 0, 1)
+    sel(tile("gone"), r("GOt"), [[16, 8], [0, 64]], OP.is_ge, 0.0, 15, -1)
+
+    def zeros(a, b):
+        while a < b:
+            n = min(1024, b - a)
+            act(r("CB", a, a + n), r("WT", 0, n), scale=0.0)
+            a += n
+
+    z0, zc = tile0("qsel"), tile0("came0")
+    quant("QU", 0, 128, r("U"))
+    zeros(zc, zc + 2048)
+    pick("QUP", "QU", 3, r("ULo"))
+    quant("QX", 0, C, r("X0"))
+
+    def scores():
+        mm("PA", ("QUP", 0), ("QX", 0), C)
+        mm("PB", ("QUP", 0), ("QX", 0), C)
+        mm("PCC", ("QUP", 128), ("QX", 0), C)
+        mm("PD", ("QUP", 256), ("QX", 0), C)
+        act(r("TS", 0, C), r("PB", 0, C))
+        act(r("TS", C, 2 * C), r("PCC", 0, C))
+        act(r("TS", 2 * C, 3 * C), r("PD", 0, C))
+
+    scores()
+    act(r("NB", 0, C), r("PB", 0, C))
+    for k, n in ((1, "g0"), (2, "g2")): scol("sg%d" % k, n, -2.0, 1.0)
+    act(r("NB", C, 2 * C), r("PB", 0, C), scale=P("sg1"))
+    act(r("SB2"), r("PB", 0, C), scale=P("sg2"))
+    act(r("SL", 0, C), r("PCC", 0, C), scale=P("sg1"))
+    act(r("SL", C, 2 * C), r("PD", 0, C), scale=P("sg2"))
+    act(r("RF", C, 512), r("WT", 0, 512 - C), scale=0.0)
+
+    def setup_first():
+        quant("QK", 0, 128, tile("gone"))
+        for A in range(4):
+            for b in range(4):
+                quant("QF", 512 * A + 128 * b, 512 * A + 128 * b + 128, r("FB", 516 * A + 3 - b, 516 * A + 515 - b))
+
+    fill(r("CB", z0, zc), 0.0)
+    for n, a in (("GT", C), ("W", C), ("GA", 1152), ("AW", 1152), ("RF", 1152)):
+        fill(r(n, a), 0.0)
+    for t in range(R):
+        fill(r("E%d" % t, 4 * GW, 512), 0.0)
+
+    def setup_zeros():
+        zeros(zc + 2048, tile0("hop0"))
+        for a in (0, 768): act(r("ET", a, a + 768), r("WT", 0, 768), scale=0.0)
+        act(r("IN"), r("WT", 0, 512), scale=0.0)
+        act(r("GA", 640, 1152), r("WT", 0, 512), scale=0.0)
+
+    iota(r("IJF"), [[1, C]], 0, 0)
+    for n, w in (("qsel", 1.0), ("qneg", -1.0), ("q3", 3.0)):
+        for s in range(4):
+            sel(tile(n, 5 * s, 16), r("WT", WCOL[w], WCOL[w] + 32), [[-16, 8], [-4, 4]], OP.is_equal, 0.0, -s, 1)
+    for k in range(3):
+        for s in range(4):
+            sel(tile("q1_%d" % k, 16 * k + 5 * s, 64), r("WT", 0, 8), [[-16, 8]], OP.is_equal, 0.0, -4 * k - s, 1)
+    for k in range(3):
+        for e in (0, 1 + k): sel(tile("st%d" % k, e, 4), r("WT", WCOL[3.0], WCOL[3.0] + 128), [[-1, 128]], OP.is_equal, 0.0, 0, 1)
+    sel(tile("sto", 0, 4), r("WT", 0, 128), [[-1, 128]], OP.is_equal, 0.0, 0, 1)
+    for k in range(3):
+        for s in range(4): sel(tile("sto", 16 * k + 4 * s + 1 + k, 64), r("WT", 0, 8), [[-16, 8]], OP.is_equal, 0.0, -4 * k - s, 1)
+    for A in range(4):
+        a = 32 * A
+        sel(r("GDt", a, a + 32), r("WT", 0, 32), [[0, 2], [-32, 2], [0, 8]], OP.is_ge, 0.0, -CLS(A), 1)
+        sel(r("GD", a, a + 32), r("GDt", a, a + 32), [[0, 2], [32, 2], [0, 8]], OP.is_ge, 0.0, CLS(A) + 15, -1)
+    iota(r("CMr"), [[0, 24], [1, 4]], 0, 0)
+    iota(r("D0"), [[0, 48], [1, 8]], 0, 0)
+    iota(r("D1"), [[0, 6], [8, 8], [0, 8]], 0, 0)
+    iota(r("D2"), [[64, 6], [0, 64]], 0, 0)
+    iota(r("J0"), [[0, 48], [4, 2]], 0, 0)
+    iota(r("J1"), [[0, 6], [8, 8], [0, 2]], 0, 0)
+    iota(r("J2"), [[64, 6], [0, 16]], 0, 0)
+    iota(r("CB", tile0("hop0"), tile0("cls0")), [[0, 1536]], 0, 0)
+    iota(r("CB", tile0("hopf0"), tile0("gb") + 512), [[0, 512 * (TI["gb"] + 1 - TI["hopf0"])]], 0, 0)
+    for b in range(4):
+        for A in range(4):
+            a = 32 * b + 8 * A
+            iota(r("WL", a, a + 8), [[0, 2], [32, 2], [0, 2]], 128 * b + CLS(A), 0)
+    iota(r("HT"), [[0, 16 * C]], 0, 0)
+
+    def quant_tiles(a, b):
+        a, b = TI[a], TI[b] + 1
+        while a < b:
+            n = min(4, b - a)
+            quant("QK", 128 * a, 128 * (a + n), r("CB", 512 * a, 512 * (a + n)))
+            a += n
+
+    tc(r("OFT", 0, 24), r("LKT", 0, 24))
+    for k in (1, 2): ts(r("OFT", 24 * k, 24 * k + 24), r("LKT", 24 * k, 24 * k + 24), float(C * k), OP.add)
+    tc(r("OFJ"), r("LKT"))
+    tc(r("OFS"), r("LKS"))
+    for s in range(4): ts(pcol("ms%d" % s), P("s"), float(s), OP.is_equal)
+    for k in range(4): ts(pcol("mr%d" % k), P("kk"), float(k), OP.is_equal)
+
+    def setup_columns():
+        for k in range(3):
+            scol("mc%d" % k, "mr%d" % k, -6.0)
+            scol("mw%d" % k, "mr%d" % k, -2.0)
+        scol("A2", "g2", 2.0, P("g0"))
+        scol("A384", "A2", 384.0)
+        scol("a3s", "A384", P("mr3"))
+        for k, n, f in ((1, "g0", 384.0), (2, "g2", 768.0)):
+            scol("x%d" % k, n, -2.0 * f, f)
+            scol("y%d" % k, "x%d" % k, 1.0, P("A384"))
+            scol("z%d" % k, "y%d" % k, P("mr3"))
+        scol("h768", "g1", 768.0)
+        scol("b1", "mr1", 2.0, P("mr0"))
+        scol("bit", "mr2", 4.0, P("b1"))
+        scol("bit8", "bit", 8.0)
+        for s in range(4): scol("mo%d" % s, "ms%d" % s, P("mr0"))
+
+    def setup_moves():
+        for k in range(3):
+            for s in range(4):
+                act(tile("came%d" % k, 5 * s, 16), r("GC", 32 * k, 32 * k + 32), scale=P("mc%d" % k))
+                act(tile("own%d" % k, 16 * k + 5 * s, 64), r("GC", 32 * k + k, 32 * k + 32, 4), scale=P("mw%d" % k))
+
+    def setup_classes():
+        for A in range(4):
+            for h in range(4):
+                o, src = tile0("cls%d" % A) + 128 * h, tile0("gone") + 64 * ((A & 1) + 2 * (h & 1) + 4 * (A >> 1))
+                for g0 in range(2): act(r("CB", o + 64 * g0, o + 64 * g0 + 64), r("CB", src, src + 64))
+
+    def setup_hops(k):
+        if k == 0: ts(r("KM"), r("CMr", 0, 32), P("kk"), OP.is_equal)
+        h = r("GH", 32 * k, 32 * k + 32)
+        tt(h, r("GC", 32 * k, 32 * k + 32), r("KM"), OP.mult)
+        for s in range(4): act(tile("hop%d" % k, 5 * s, 16), h)
+
+    def setup_tables():
+        for s in range(4): act(tile("hopf0", 5 * s, 16), r("GC", 0, 32))
+        for A in range(4):
+            d = r("GD", 32 * A, 32 * A + 32)
+            tt(d, d, r("KM"), OP.mult)
+            for s in range(4): act(tile("ct%d" % A, 5 * s, 16), d)
+        for e, n in ((0, "ge"), (1, "ge"), (2, "gm"), (3, "gb")):
+            act(tile(n, e, 4), tile("gone", e, 4))
+
+    def setup_routes():
+        ts(r("RM"), r("CMr"), P("kk"), OP.is_equal)
+        for d in range(3): act(r("D%d" % d), r("D%d" % d), scale=P("mr%d" % d))
+        tt(r("qa"), r("D0"), r("D1"), OP.add)
+        tt(r("CTF"), r("qa"), r("D2"), OP.add)
+        ts(r("t0"), r("J0"), P("s"), OP.add, P("mr0"), OP.mult)
+        ts(r("t1"), r("J1"), P("mr1"), OP.mult, P("a3s"), OP.add)
+        ts(r("t2"), r("J2"), P("mr2"), OP.mult)
+        tt(r("ua"), r("t0"), r("t1"), OP.add)
+        tt(r("JC"), r("ua"), r("t2"), OP.add)
+
+    def setup_ends_s(k):
+        act(r("qa"), r("CTF"), off=r("OFJ", 24 * k, 24 * k + 24))
+        for s in range(4): act(r("qm", 96 * s, 96 * s + 96), r("qa", s, C, 4), scale=P("ms%d" % s))
+
+    def setup_ends(k):
+        tt(r("qb"), r("qm", 0, 192), r("qm", 192, C), OP.add)
+        tt(r("qd"), r("qb", 0, 96), r("qb", 96, 192), OP.add)
+        ts(r("OC%d" % k), r("qd"), P("a3s") if k == 0 else P("z%d" % k), OP.add)
+
+    def setup_layer():
+        ts(r("WLo"), r("WL"), P("i"), OP.add)
+        pick("WP", "WC", 16, r("WLo"))
+
+    def masked(src):
+        for s in range(4):
+            o = r("W", s, C, 4)
+            if s < 2: ts(o, src, P("ms%d" % s), OP.mult)
+            else: act(o, src, scale=P("ms%d" % s))
+
+    def gather_w(n):
+        v = n // 16
+        win = r("W", 0, C)
+        act(r("GA", n, 1152), win, off=r("OFS", v, 72))
+        if n: tc(r("GA", 0, n), win, off=r("OFS", 0, v))
+
+    def to_list(src, o):
+        tt(r("la"), src, r("RM"), OP.mult)
+        tt(r("lb"), r("la", 0, 96, 2), r("la", 1, 96, 2), OP.add)
+        tt(r("lc"), r("lb", 0, 48, 2), r("lb", 1, 48, 2), OP.add)
+        tc(o, r("lc"))
+
+    def send(t):
+        m = topo.engines(core, nxt)[:ENGINES]
+        mask = sum(1 << e for e in m)
+        rid, pid, _ = topo.addr(nxt)
+        n = 128 if t == 0 else GW
+        a = 0 if t == 0 else 32 + GW * t
+        c, s = r("QEc", 128 * t, 128 * t + n), r("QEs", 128 * t, 128 * t + n)
+        await_("G", deps_of("D", [c, s], []))
+        sem = T.sem["arr%d" % t]
+        g.remote_dma(T.LDc[:, a:a + n].bitcast(dt.uint8), T.QEc[:, 128 * t:128 * t + n].bitcast(dt.uint8), sem, T.sem.lcl, pid, rid, mask)
+        g.remote_dma(T.LDs[:, a:a + n], T.QEs[:, 128 * t:128 * t + n], sem, T.sem.lcl, pid, rid, mask)
+        cnt["lcl"] += 2 * len(m)
+        pe = len(topo.engines(T.cores[(rank - 1) % len(T.cores)], core)[:ENGINES])
+        cnt["arr%d" % t] = 2 * pe
+        clk[("arr%d" % t, 2 * pe)] = {}
+        record("D", ("arr%d" % t, 2 * pe), [], [r("LDc", a, a + n), r("LDs", a, a + n)])
+
+    def state():
+        for k in range(3): act(r("IN", 1 + k, 4 * 96, 4), r("PV%d" % k, 0, 96), scale=1.0 / 3.0)
+
+    def inject(stop):
+        for k in range(3): mm("PV%d" % k, K("st%d" % k), ("QIN", 0), 128, True, stop)
+        mm("PV3", K("sto"), ("QIN", 0), 128, True, stop)
+
+    def number_parts():
+        ts(r("ea"), r("PE"), 768.0, OP.is_ge, 768.0, OP.mult)
+        tt(r("eb"), r("PE"), r("ea"), OP.add)
+        ts(r("ec"), r("eb"), P("h768"), OP.add)
+        tc(r("EI"), r("ec"))
+        for e, m in enumerate((15, 240, 3840)): ts(r("EP", 96 * e, 96 * e + 96), r("EI"), m, OP.bitwise_and)
+        tc(r("qa", 0, 288), r("EP"))
+        tt(r("ea"), r("ba"), r("bb"), OP.add)
+        for s in range(4):
+            for e in range(3): act(r("ET", 4 * s + e, 4 * C, 16), r("qa", 96 * e, 96 * e + 96), scale=P("mo%d" % s))
+            act(r("ET", 4 * s + 3, 4 * C, 16), r("ea"), scale=P("ms%d" % s))
+
+    rot = [0]
+    for t in range(R):
+        if t: scores()
+        tt(r("SB1"), r("PA", 0, C), r("MX"), OP.min)
+        scan(r("ST"), r("NX"), r("SB1"), OP.add, OP.max)
+        ts(r("NS"), r("ST", 15, C, 16), -1.0, OP.mult)
+        if t == 0: setup_first()
+        fq = [(A, b) for A in range(4) for b in range(4)]
+        for j in range(6):
+            if t == 0 and j < 3: (setup_zeros, setup_columns, setup_moves)[j]()
+            for _ in range(FSHARE[j]):
+                if fq:
+                    A, b = fq.pop(0)
+                    bk = ("PCC", "PD")[rot[0] % 2]
+                    rot[0] += 1
+                    mm(bk, ("QF", 512 * A + 128 * b), ("QX", 0), C)
+                    act(r("FT", 1536 * b + C * A, 1536 * b + C * A + C), r(bk, 0, C), scale=0.5)
+            for a in range(24 - SSHARE, 24) if t and j == FFIRST else ():
+                m = 16 * a + 16
+                x = r("TM", C * (a % 2), C * (a % 2) + m)
+                act(x, r("TS", 0, m), bias=r("NS", a, a + 1), fn=ActivationFunctionType.Relu)
+                act(r("C2", a % 4, 4 * m, 4), x, fn=ActivationFunctionType.Sign)
+            n = "C2" if j == 5 else "C%d" % (j % 2)
+            for e in range(4):
+                a = 4 * j + e
+                m = 16 * a + 16
+                col = r("ST", m - 1, m)
+                if t == 0 or a < 24 - SSHARE: ts(r(n, e, 4 * m, 4), r("TS", 0, m), col, OP.is_gt)
+                if m < C: ts(r(n, 4 * m + e, 4 * C, 4), r("TS", m, C), col, OP.is_ge)
+            quant("QT", C * j, C * j + C, r(n))
+            mm("PB", K("gone"), ("QT", C * j), C, j == 0, j == 5)
+            if j == 4:
+                tt(r("ET", 0, 4 * C, 4), r("PA", 0, C), r("ST"), OP.is_equal)
+                quant("QT", 6 * C, 7 * C, r("ET"))
+                mm("PB", K("gone"), ("QT", 6 * C), C, False, False)
+            if t and j == 1:
+                quant("QIN", 0, 128, r("IN"))
+                inject(True)
+        if t == 0:
+            quant_tiles("qsel", "own2")
+            quant("QGA", 192, 320, r("GA", 768, 1280))
+        ts(r("GT", 0, C), r("PB", 0, C), float(GW + 1), OP.is_lt)
+        quant("QG", 0, 128, r("GT"))
+        mm("PA", K("qsel"), ("QG", 0), 128)
+        if t == 0:
+            act(r("LW"), r("IJF"))
+            tt(r("AW", 0, C), r("TS", 0, C), r("NB", 0, C), OP.is_lt, off=r("OFJ", 0, 24))
+            for k, own in ((1, r("NB", C, 2 * C)), (2, r("SB2"))):
+                x = r(("LT", "EQ")[k - 1])
+                tt(x, r("SL", C * k - C, C * k), own, OP.is_lt, off=r("OFJ", 24 * k, 24 * k + 24))
+                act(r("AW", C * k, C * k + C), x, bias=P("g%d" % (2 * k - 2)), scale=P("sg%d" % k), fn=IDENT)
+            tt(r("LE"), r("TS", 0, C), r("NB", 0, C), OP.is_equal, off=r("OFJ", 0, 24))
+            tt(r("ML"), r("IJF"), r("LW"), OP.is_lt, off=r("OFJ", 0, 24))
+            tt(r("RF", 0, C), r("LE"), r("ML"), OP.mult)
+            quant("QRF", 0, 128, r("RF", 0, 512))
+            quant("QAW", 0, 320, r("AW"))
+            for k in range(3):
+                mm("PV%d" % k, K("q3"), ("QAW", 96 * k), 128, True, k > 0)
+                mm("PV3", K("q1_%d" % k), ("QAW", 96 * k), 128, k == 0, False)
+            mm("PV0", K("q3"), ("QRF", 0), 128, False, True)
+            mm("PV3", K("q1_0"), ("QRF", 0), 128, False, True)
+        ts(r("G3"), r("PA", 0, 96), 6.0, OP.mult, -3.0, OP.add)
+        ts(r("G9"), r("PA", 0, 96), 9.0, OP.mult, 0.5, OP.add)
+
+        def list1():
+            tt(r("SB2"), r("PB", 0, C), r("MD"), OP.mult)
+            scan(r("ST2"), r("ND"), r("SB2"))
+            ts(r("PLo"), r("ST2", 15, C, 16), -1.0, OP.add)
+            o = r("PLo")
+            do("V", lambda e: e.tensor_copy(T.LW[:, 0:C].indirect(ap(o)), ap(r("IJF"))), [r("IJF"), o], [r("LW")])
+
+        def list2():
+            tt(r("SB3"), r("LW", 0, GW), r("MD", 0, GW), OP.mult)
+            scan(r("ST3"), r("ND", 0, GW), r("SB3"))
+            ts(r("ELo"), r("ST3", 15, GW, 16), P("A384"), OP.add)
+
+        def gates():
+            for b in range(4):
+                act(r("E%d" % t, b, 4 * GW, 4), r("FT", 1536 * b, 1536 * b + 1536), scale=2.0, off=r("ELo"))
+
+        def pass_on():
+            quant("QE", 128 * t, 128 * t + 128, r("E%d" % t))
+            send(t)
+
+        def scores_at(k):
+            return lambda: act(r("NB", C * k, C * k + C), r("TS"), off=r("OFT", 24 * k, 24 * k + 24))
+
+        def order(j):
+            a, b = ((0, 1), (0, 2), (1, 2))[j]
+            return lambda: tt(r("RF", C * j, C * j + C), r("TS"), r("NB", C * a, C * a + C), OP.is_lt, off=r("OFT", 24 * b, 24 * b + 24))
+
+        def orders():
+            order(2)()
+            quant("QRF", 0, 320, r("RF"))
+            for j, (bk, a, ka, b, kb) in enumerate((("PA", 0, "qneg", 1, "qneg"), ("PB", 0, "qsel", 2, "qneg"))):
+                mm(bk, K(ka), ("QRF", 96 * a), 128, True, False)
+                mm(bk, K(kb), ("QRF", 96 * b), 128, False, True)
+
+        def orders2():
+            for j, bk in enumerate(("PA", "PB")): act(r("R%d" % j), r(bk, 0, 96), bias=3.0 - j)
+            mm("PA", K("qsel"), ("QRF", 96), 128, True, False)
+            mm("PA", K("qsel"), ("QRF", 192), 128, False, True)
+            act(r("R2"), r("PA", 0, 96), bias=1.0)
+
+        sq = [(A, j) for A in range(4) for j in range(7)]
+        pend = []
+
+        def slots(n):
+            for _ in range(n):
+                if not sq: return
+                A, j = sq.pop(0)
+                mm("PCC" if A % 2 == 0 else "PD", K("cls%d" % A), ("QT", C * (6 if j == 0 else j - 1)), C, j == 0, j == 6)
+                if j == 6: pend.append(A)
+
+        def slot_copies():
+            while pend:
+                A = pend.pop(0)
+                act(r("SL", C * A, C * A + C), r("PCC" if A % 2 == 0 else "PD", 0, C), bias=float(C * A - 1))
+
+        onS = [[scores_at(0)], [scores_at(1)], [gates], [], [], [orders2]]
+        onV = [[list1], [list2], [order(0)], [pass_on, order(1)], [orders], []]
+        if t == 0:
+            setup_classes()
+            for k in range(3): onS[k].append(lambda k=k: setup_hops(k))
+            onS[3].append(setup_tables)
+            for k in range(3):
+                onS[1 + k].append(lambda k=k: setup_ends_s(k))
+                onS[2 + k].append(lambda k=k: setup_ends(k))
+            onV[0].append(lambda: quant_tiles("cls0", "cls3"))
+            onV[0].append(setup_routes)
+            onV[3].append(lambda: quant_tiles("hop0", "hop2"))
+            onV[4].append(lambda: quant_tiles("hopf0", "gb"))
+            onV[5].append(setup_layer)
+        for i in range(SWEEPS):
+            tt(r("MA"), r("PV0", 0, 96), r("G3"), OP.max)
+            tt(r("MB"), r("PV1", 0, 96), r("MA"), OP.max)
+            tt(r("MC"), r("PV2", 0, 96), r("MB"), OP.max)
+            tt(r("TU"), r("PV3", 0, 96), r("MC"), OP.is_ge)
+            if t == 0 or i: state()
+            masked(r("TU"))
+            ts(r("IN", 0, 4 * 96, 4), r("MC"), -1.0 / 3.0, OP.mult, 1.0, OP.add)
+            quant("QIN", 0, 128, r("IN"))
+            gather_w(VSWEEP[i])
+            slot_copies()
+            for f in onS[i]: f()
+            inject(False)
+            for f in onV[i]: f()
+            quant("QGA", 0, 288, r("GA", 0, 1152))
+            for k in range(3): mm("PV%d" % k, K("came%d" % k), ("QGA", 96 * k), 128, False, True)
+            for k in range(3): mm("PV3", K("own%d" % k), ("QGA", 96 * k), 128, False, k == 2)
+            slots(SLOTS[i])
+        for k in range(3): tt(r("va%d" % k), r("PV%d" % k, 0, 96), r("R%d" % k), OP.min)
+        if t < R - 1:
+            state()
+            act(r("IN", 0, 4 * 96, 4), r("PV0", 0, 96), scale=0.0)
+        else:
+            ts(r("ba"), r("PV3", 0, 96), 1.0, OP.is_ge, P("bit"), OP.mult)
+            ts(r("bb"), r("PV3", 0, 96), -1.0, OP.is_le, P("bit8"), OP.mult)
+        for k in range(3): tt(r("mx%d" % k), r("va%d" % k), r("G9") if k == 0 else r("mx%d" % (k - 1)), OP.max)
+        for k in range(3): tt(r("pk%d" % k), r("va%d" % k), r("mx2"), OP.is_ge)
+        tt(r("self"), r("mx2"), r("G9"), OP.is_equal)
+        tt(r("SJ"), r("self"), r("JC"), OP.mult)
+        for k in range(3): tt(r("t%d" % k), r("pk%d" % k), r("OC%d" % k), OP.mult)
+        tt(r("ua"), r("t0"), r("SJ"), OP.add)
+        tt(r("ub"), r("t1"), r("t2"), OP.add)
+        tt(r("PP"), r("ua"), r("ub"), OP.add)
+        masked(r("PP"))
+        gather_w(VHOP)
+        slot_copies()
+        quant("QW", 0, 128, r("W"))
+        mm("PV3", K("hopf0"), ("QW", 0), 128)
+        quant("QGA", 0, 288, r("GA", 0, 1152))
+        for k in range(3): mm("PV%d" % k, K("hop%d" % k), ("QGA", 96 * k), 128)
+        slots(SLOTS[SWEEPS])
+        to_list(r("PV3", 0, 96), r("DL"))
+        for k in range(3): tt(r("t%d" % k), r("PV%d" % k, 0, 96), r("pk%d" % k), OP.mult)
+        tt(r("ua"), r("t0"), r("SJ"), OP.add)
+        tt(r("ub"), r("t1"), r("t2"), OP.add)
+        tt(r("PP"), r("ua"), r("ub"), OP.add)
+        masked(r("PP"))
+        quant("QW", 0, 128, r("W"))
+        mm("PV2", K("ct2"), ("QW", 0), 128)
+        mm("PV0", K("ct0"), ("QW", 0), 128)
+        mm("PA", K("hopf0"), ("QW", 0), 128)
+        mm("PV1", K("ct1"), ("QW", 0), 128)
+        mm("PV3", K("ct3"), ("QW", 0), 128)
+        slot_copies()
+        for A in (2, 3, 0, 1):
+            for s in range(4):
+                o, x = r("WA", C * A + s, C * A + C, 4), r("PV%d" % A, 0, 96)
+                if A < 2: ts(o, x, P("ms%d" % s), OP.mult)
+                else: act(o, x, scale=P("ms%d" % s))
+        to_list(r("PA", 0, 96), r("EL"))
+        act(r("GA", 192, C), r("WA"), off=r("EL", 12, 24))
+        tc(r("GA", 0, 192), r("WA"), off=r("EL", 0, 12))
+        for b in range(4):
+            act(r("FD", C * b, C * b + C), r("FT", 1536 * b, 1536 * b + 1536), off=r("DL"))
+        quant("QG", 0, 128, r("GA", 0, 512))
+        mm("PB", K("hopf0"), ("QG", 0), 128)
+        a, o = (0, 0) if t == 0 else (GW * t, 32)
+        for j in range(8):
+            two = [("PV0", "PV1", "PV2", "PV3")[2 * (j % 2) + i] for i in range(2)]
+            for i in range(2): mm(two[i], ("WP", 256 * j + 128 * i), ("LD", a), 128)
+            for i in range(2):
+                b, A = j // 2, 2 * (j % 2) + i
+                act(r("HT", 1536 * b + C * A, 1536 * b + C * A + GW), r(two[i], o, o + GW), scale=0.015625)
+        to_list(r("PB", 0, 96), r("EL"))
+        if t == R - 1:
+            tc(r("PE"), r("PB", 0, 96))
+            number_parts()
+        tt(r("SB2"), r("SL"), r("MD"), OP.mult, off=r("EL"))
+        scan(r("ST2"), r("ND"), r("SB2"))
+        tc(r("HL"), r("ST2", 15, C, 16))
+        for b in range(4):
+            tt(r("Z", C * b, C * b + C), r("FT", 1536 * b, 1536 * b + 1536), r("FD", C * b, C * b + C), OP.add, off=r("EL"))
+        for b in range(4):
+            tt(r("X0", b, 4 * C, 4), r("HT", 1536 * b, 1536 * b + 1536), r("Z", C * b, C * b + C), OP.add, off=r("HL"))
+        quant("QX", 0, C, r("X0"))
+        if t == 0: quant("QV", 0, 128, r("VV"))
+    mm("PA", ("QV", 0), ("QX", 0), C)
+    act(r("TS", 2 * C, 3 * C), r("PA", 0, C))
+    dma("Y", "d7", [(T.oc[:], T.QXc[:, 0:C].bitcast(dt.uint8))] + [(T.osc[4 * k:4 * k + 4, :], T.QXs[32 * k:32 * k + 4, 0:C]) for k in range(4)], rd=[r("QXc"), r("QXs")])
+    dma("Y", "d8", [(T.y[:], T.TS[:, 2 * C:3 * C])], rd=[r("TS", 2 * C, 3 * C)])
+    quant("QND", 0, C, r("ET"))
+    mm("PB", K("ge"), ("QND", 0), C, True, False)
+    mm("PB", K("gm"), ("QND", 0), C, False, True)
+    mm("PCC", K("gb"), ("QND", 0), C)
+    act(r("TS", 0, C), r("PB", 0, C))
+    act(r("TS", C, 2 * C), r("PCC", 0, C))
+    dma("Y", "d9", [(T.nd[:], T.TS[0:128:16, 0:2 * C])], rd=[r("TS", 0, 2 * C)])
+    for s in SEMAPHORES:
+        if cnt[s]: g.wait_ge(T.sem[s], cnt[s])

@@ -2,28 +2,29 @@ import math
 from concourse.bass import DstId, RemoteDMATransfer
 from concourse.mybir import dt, AluOpType, AxisListType, ActivationFunctionType
 
-OP = AluOpType
-COPY, IDENT = ActivationFunctionType.Copy, ActivationFunctionType.Identity
+OP, FN = AluOpType, ActivationFunctionType
+COPY, IDENT = FN.Copy, FN.Identity
 C, GW, R, SWEEPS = 384, 96, 3, 6
 JUMP = [0, 1, 4]
 
-TILES = ["gone", "qsel", "qneg", "q3", "q1_0", "q1_1", "q1_2", "st0", "st1", "st2", "sto", "came0", "came1", "came2",
-         "own0", "own1", "own2", "hop0", "hop1", "hop2", "cls0", "cls1", "cls2", "cls3", "hopf0", "ct0", "ct1", "ct2", "ct3", "ge", "gm", "gb"]
+T1 = ["ld", "lo", "lc0", "lc1", "lc2", "ad", "ao", "ac0", "ac1", "ac2", "ord", "st"]
+T2 = ["gs", "lg", "lv", "nm", "dl1", "ct0", "ct1", "ct2", "ct3", "dl2"]
+TILES = T1 + T2 + ["gone"]
 TI = {n: i for i, n in enumerate(TILES)}
 NT = len(TILES)
-VSWEEP = [0, 448, 352, 320, 224, 512]
-VHOP = 512
-SLOTS = [4, 4, 4, 4, 4, 4, 4]
-FSHARE = [6, 4, 3, 3, 0, 0]
-FFIRST = 2
-SSHARE = 3
+ELEM = [("gs", "ct3"), ("nm", "ct3"), ("ct0", "dl2"), ("dl1", "dl2")]
+FS = 5 * C
+HOLD, DROP = 8192.0, 1048576.0
+VSWEEP = [512, 512, 512, 512, 512, 512]
+VSTEP = 192
+SOWN = 3
 ENGINES = 8
 
 F32, BF, I32, U16, X4, U8 = "float32", "bfloat16", "int32", "uint16", "float8_e4m3fn_x4", "uint8"
 SCRATCH = {}
-WIDE = {"KF": "JM MD ND IJF CMr RM J0 J1 J2 D0 D1 D2", "KI": "PC UL WL", "XI": "EI EP",
-        "XF": "SB1 ST SB2 ST2 SB3 ST3 t0 t1 t2 ua ub PE la lb lc qa qb qd qm ea eb ec ba bb",
-        "XB": "G3 G9 MA MB MC TU R0 R1 R2 va0 va1 va2 mx0 mx1 mx2 pk0 pk1 pk2 self SJ PP OC0 OC1 OC2 JC EQ LT LE ML"}
+WIDE = {"KF": "JM MD MX NX HD HD4 I4 IJF CONST SLS", "KI": "PC UL X16 XA XB2", "KB": "WT DGR GC0 GCT GCA GDT CF CF2 GW1 GW2 OCL OCH ML Y",
+        "XF": "SB1 ST ST2 ST3 ST4 RS RC PL GF NS", "XB": "CS WW BT BA BN JK TM",
+        "XU": "PLo ELo DL L2 L3 EL HL0 HL1 HL2 HL3", "KU": "ULo OFJ OFS"}
 HOME = {n: w for w in WIDE for n in WIDE[w].split()}
 PLACE, LEN = {}, {}
 
@@ -40,39 +41,35 @@ def mx(name, n):
     sb(name + "s", n, U8)
 
 
+CW = [C, 128, 176, 240, 304, 368]
+CA = [sum(CW[:j]) for j in range(7)]
 for _n, _w, _d in [
-        ("X0", 1536, BF), ("U", 512, BF), ("VV", 512, BF),
-        ("LKT", 72, I32), ("LKS", 72, I32), ("OFT", 72, U16), ("OFJ", 72, U16), ("OFS", 72, U16),
-        ("UL", 24, I32), ("ULo", 24, U16), ("WL", 128, I32), ("WLo", 128, U16),
-        ("PC", 16, I32), ("PF", 48, F32), ("WT", 1024, BF), ("CB", 512 * NT, BF), ("FB", 4 * 516, BF),
-        ("GC", 96, BF), ("GCt", 96, BF), ("GD", 128, BF), ("GDt", 128, BF), ("GH", 96, BF), ("KM", 32, BF), ("GOt", 512, BF),
-        ("JM", C, F32), ("MD", C, F32), ("ND", C, F32), ("MX", C, F32), ("NX", C, F32), ("NS", 24, F32), ("TM", 2 * C, BF), ("IJF", C, F32),
-        ("CMr", 96, F32), ("RM", 96, F32), ("J0", 96, F32), ("J1", 96, F32), ("J2", 96, F32), ("qm", C, F32),
-        ("TS", 3 * C, F32), ("SB1", C, F32), ("ST", C, F32), ("EQ", C, BF), ("ET", 4 * C, BF),
-        ("GT", 512, BF), ("G3", 96, BF), ("G9", 96, BF), ("PLo", 24, U16), ("LW", C, F32), ("SB2", C, F32),
-        ("ST2", C, F32), ("SB3", GW, F32), ("ST3", GW, F32), ("ELo", 6, U16),
-        ("FT", 16 * C, BF), ("HT", 16 * C, BF), ("SL", 4 * C, F32), ("FD", 4 * C, BF), ("Z", 4 * C, BF), ("WA", 4 * C, BF),
-        ("LT", C, BF), ("LE", C, BF), ("ML", C, BF), ("AW", 1280, BF), ("RF", 1280, BF), ("NB", 2 * C, F32),
-        ("MA", 96, BF), ("MB", 96, BF), ("MC", 96, BF), ("IN", 512, BF), ("TU", 96, BF), ("W", 512, BF), ("GA", 1280, BF),
-        ("R0", 96, BF), ("R1", 96, BF), ("R2", 96, BF), ("va0", 96, BF), ("va1", 96, BF), ("va2", 96, BF),
-        ("mx0", 96, BF), ("mx1", 96, BF), ("mx2", 96, BF), ("pk0", 96, BF), ("pk1", 96, BF), ("pk2", 96, BF),
-        ("self", 96, BF), ("SJ", 96, BF), ("t0", 96, F32), ("t1", 96, F32), ("t2", 96, F32),
-        ("ua", 96, F32), ("ub", 96, F32), ("PP", 96, BF), ("PE", 96, F32),
-        ("la", 96, F32), ("lb", 48, F32), ("lc", 24, F32), ("DL", 24, U16), ("EL", 24, U16), ("HL", 24, U16),
-        ("D0", C, F32), ("D1", C, F32), ("D2", C, F32), ("CTF", C, F32),
-        ("qa", C, F32), ("qb", 192, F32), ("qd", 96, F32), ("OC0", 96, BF), ("OC1", 96, BF), ("OC2", 96, BF), ("JC", 96, BF),
-        ("ea", 96, F32), ("eb", 96, F32), ("ec", 96, F32), ("EI", 96, I32), ("EP", 288, I32), ("ba", 96, F32), ("bb", 96, F32),
-        ("C0", 4 * C, BF), ("C1", 4 * C, BF), ("C2", 4 * C, BF), ("E0", 512, BF), ("E1", 512, BF), ("E2", 512, BF)]:
+        ("X0", 1536, BF), ("U", 512, BF), ("VV", 512, BF), ("LKT", 72, I32), ("LKS", 72, I32), ("LK2", 96, I32),
+        ("ULo", 24, U16), ("OFJ", 72, U16), ("OFS", 72, U16), ("UL", 24, I32), ("PC", 16, I32), ("X16", 96, I32), ("XA", 96, I32), ("XB2", 96, I32),
+        ("PF", 96, F32), ("WT", 512, BF), ("ZB", 1024, BF), ("CB", 512 * NT, BF), ("FB", 516, BF), ("GOt", 512, BF),
+        ("DGR", 32, BF), ("GC0", 32, BF), ("GCT", 64, BF), ("GCA", C, BF), ("GDT", 128, BF), ("CF", C, BF), ("CF2", 1280, BF), ("GW1", C, BF), ("GW2", 320, BF),
+        ("OCL", 96, BF), ("OCH", 96, BF), ("ML", C, BF), ("Y", C, BF),
+        ("JM", C, F32), ("MD", C, F32), ("MX", C, F32), ("NX", C, F32), ("HD", C, F32), ("HD4", 96, F32), ("I4", 96, F32), ("IJF", C, F32),
+        ("CONST", 24, F32), ("SLS", 96, F32), ("RST", C, BF), ("NODE", 3 * FS + C, F32),
+        ("TS", C, F32), ("W0", C, F32), ("W1", C, F32), ("W2", C, F32), ("BASE", C, F32), ("A0", C, F32), ("A1", C, F32), ("RF", 512, BF), ("RG", C, BF),
+        ("SB1", C, F32), ("ST", C, F32), ("ST2", C, F32), ("ST3", GW, F32), ("ST4", 96, F32), ("RS", 24, F32), ("RC", 24, F32), ("PL", 24, F32),
+        ("GF", 24, F32), ("NS", 24, F32), ("CS", C, BF), ("WW", 96, BF), ("BT", 96, BF), ("BA", 96, BF), ("BN", 96, BF), ("JK", C, BF), ("TM", 2 * C, BF),
+        ("PLo", 24, U16), ("ELo", 6, U16), ("DL", 24, U16), ("L2", 24, U16), ("L3", 24, U16), ("EL", 24, U16),
+        ("HL0", 24, U16), ("HL1", 24, U16), ("HL2", 24, U16), ("HL3", 24, U16),
+        ("CT", 4 * CA[6], BF), ("G", 512, BF), ("G2", 512, BF), ("W", 512, BF), ("GA", 1280, BF), ("C2", 512, BF), ("IN", 512, BF),
+        ("VT", 512, BF), ("PT", 512, BF), ("GS", 512, BF), ("WA", 3 * FS + C, BF), ("LW", C, F32), ("SG", C, BF),
+        ("F0", FS, BF), ("FT", 4 * FS, BF), ("H0", 512, BF), ("HT", 2048, BF), ("FD", 4 * C, BF), ("Z", 4 * C, BF),
+        ("E", 512, BF), ("ND", 4 * C, BF), ("OUT", 3 * C, F32)]:
     sb(_n, _w, _d)
-for _n, _w in [("QX", C), ("QU", 128), ("QUP", C), ("QV", 128), ("WC", 512), ("WP", 2048), ("QK", 128 * NT), ("QF", 2048),
-               ("QT", 7 * C), ("QG", 128), ("QAW", 320), ("QRF", 320), ("QIN", 128), ("QGA", 320), ("QW", 128),
-               ("QE", 3 * 128), ("LD", 320), ("QND", C)]:
+for _n, _w in [("QX", C), ("QU", 128), ("QUP", C), ("QV", 128), ("WC", 512), ("QK", 128 * NT), ("QF", 512), ("QT", CA[6]),
+               ("QG", 128), ("QG2", 128), ("QRF", 128), ("QW", 128 * SWEEPS), ("QD", 320 * SWEEPS), ("QC2", 128), ("QIN", 128),
+               ("QVT", 128), ("QPT", 128), ("QS", 128), ("QE", 3 * 128), ("LD", 320), ("QND", C)]:
     mx(_n, _w)
-PS = ["PV0", "PV1", "PV2", "PV3", "PA", "PB", "PCC", "PD"]
+PS = ["PA", "PB", "PCC", "PD", "LA", "LB", "AB", "PE"]
 for _n in PS:
     SCRATCH[_n] = ("psum", [128, 512], F32)
     PLACE[_n], LEN[_n] = (_n, 0), 512
-SEMAPHORES = ["sv", "ss", "st", "sg", "lcl", "arr0", "arr1", "arr2"] + ["d%d" % i for i in range(10)]
+SEMAPHORES = ["sv", "ss", "st", "sg", "lcl", "arr0", "arr1", "arr2"] + ["d%d" % i for i in range(20)]
 
 
 def rank_program(g, core, T, topo):
@@ -145,7 +142,11 @@ def rank_program(g, core, T, topo):
         clk[m] = c
         record(q, m, rd, wr)
 
-    def dma(q, s, pairs, rd=(), wr=()):
+    dn = [0]
+
+    def dma(q, pairs, rd=(), wr=()):
+        s = "d%d" % dn[0]
+        dn[0] += 1
         await_(q, deps_of("D", rd, wr))
         for o, i in pairs:
             Q[q].dma_start(o, i).then_inc(T.sem[s], 16)
@@ -180,12 +181,17 @@ def rank_program(g, core, T, topo):
         if off is None: do("V", lambda e: e.tensor_copy(ap(o), ap(a)), [a], [o])
         else: do("V", lambda e: e.tensor_copy(ap(o), ap(a).indirect(ap(off))), [a, off], [o])
 
-    def act(o, a, bias=0.0, scale=1.0, off=None, fn=COPY):
+    def scatter(win, off, a):
+        do("V", lambda e: e.tensor_copy(ap(win).indirect(ap(off)), ap(a)), [a, off], [win])
+
+    def act(o, a, bias=0.0, scale=1.0, off=None, fn=COPY, acc=None):
         rd = [a] + [x for x in (scale, bias, off) if isr(x)]
-        if off is None: do("S", lambda e: e.activation(ap(o), ap(a), fn, bias=val(bias), scale=val(scale)), rd, [o])
+        if isr(bias) and fn == COPY: fn = IDENT
+        if acc is not None: do("S", lambda e: e.activation(ap(o), ap(a), fn, bias=val(bias), scale=val(scale), accum_out=ap(acc)), rd, [o, acc])
+        elif off is None: do("S", lambda e: e.activation(ap(o), ap(a), fn, bias=val(bias), scale=val(scale)), rd, [o])
         else: do("S", lambda e: e.activation(ap(o), ap(a).indirect(ap(off)), fn, bias=val(bias), scale=val(scale)), rd, [o])
 
-    def scan(o, a, b, op0=OP.mult, op1=OP.add):
+    def scan(o, a, b, op0, op1):
         do("V", lambda e: e.tensor_tensor_scan(ap(o), ap(a), ap(b), 0.0, op0, op1), [a, b], [o])
 
     def fill(o, c):
@@ -195,7 +201,7 @@ def rank_program(g, core, T, topo):
         q, s = r(n + "c", a, b), r(n + "s", a, b)
         do("V", lambda e: e.quantize_mx(ap(q), ap(s), ap(src)), [src], [q, s])
 
-    def pick(n, src, k, off):
+    def pick(n, src, off):
         m, w = 16 * (off[2] - off[1]), LEN[src + "c"]
         do("V", lambda e: e.tensor_copy(T[n + "c"][:, 0:m].bitcast(dt.uint32), T[src + "c"][:, 0:w].bitcast(dt.uint32).indirect(ap(off))), [r(src + "c"), off], [r(n + "c")])
         do("S", lambda e: e.activation(T[n + "s"][:, 0:m], T[src + "s"][:, 0:w].indirect(ap(off)), COPY), [r(src + "s"), off], [r(n + "s")])
@@ -206,21 +212,50 @@ def rank_program(g, core, T, topo):
         o = r(bk, 0, n)
         do("T", lambda e: e.matmul_mx(ap(o), ap(l), ap(ls), ap(m), ap(ms), start, stop), [l, ls, m, ms], [o])
 
-    def iota(o, pat, base, cm):
+    def sums(bk, terms, start=True, stop=True):
+        for j, (st, mv) in enumerate(terms): mm(bk, st, mv, 128, start and j == 0, stop and j == len(terms) - 1)
+
+    def iota(o, pat, base, cm=0):
         fl = SCRATCH[o[0]][2] != I32
         if fl: do("G", lambda e: e.iota(ap(o), pat, base, cm, allow_small_or_imprecise_dtypes=True), [], [o])
         else: do("G", lambda e: e.iota(ap(o), pat, base, cm), [], [o])
 
+    def const(o, c):
+        iota(o, [[0, len(range(o[1], o[2], o[3]))]], c)
+
     def sel(o, i, pat, op, fl, base, cm):
         do("G", lambda e: e.affine_select(ap(o), ap(i), pat, op, fl, base, cm), [i], [o])
 
-    K = lambda n: ("QK", 128 * TI[n])
-    tile0 = lambda n: 512 * TI[n]
-    tile = lambda n, a=0, st=1: r("CB", tile0(n) + a, tile0(n) + 512, st)
+    def zero(o):
+        act(o, r("ZB", 0, len(range(o[1], o[2], o[3]))))
 
-    dma("Y", "d0", [(T.X0[:], T.x[:])], wr=[r("X0")])
-    dma("S", "d1", [(T.U[:], T.u[:])], wr=[r("U")])
-    dma("Y", "d2", [(T.LKT[:], T.lk[:])], wr=[r("LKT")])
+    K = lambda n: ("QK", 128 * TI[n])
+    EB = lambda b: ("QF", 128 * b)
+    tile0 = lambda n: 512 * TI[n]
+    col = lambda n, j: r(n, j, j + 1)
+    PFC = {}
+
+    def pcol(name, n=1):
+        PFC[name] = sum(x[1] for x in PFC.values()), n
+        return r("PF", PFC[name][0], PFC[name][0] + n)
+
+    P = lambda name, j=0: col("PF", PFC[name][0] + j)
+    PV = lambda name: r("PF", PFC[name][0], PFC[name][0] + PFC[name][1])
+    GRP = {0: ([[16, 8]], 0), 1: ([[32, 4], [-16, 2]], 16), 4: ([[-64, 2], [16, 4]], 64)}
+    CLS = lambda A: 16 * (A & 1) + 64 * (A >> 1)
+    neg = lambda pat: [[-a, b] for a, b in pat]
+
+    dma("Y", [(T.X0[:], T.x[:])], wr=[r("X0")])
+    dma("S", [(T.U[:], T.u[:])], wr=[r("U")])
+    dma("Y", [(T.LKT[:], T.lk[:])], wr=[r("LKT")])
+    fill(r("ZB"), 0.0)
+    fill(r("WT"), 1.0)
+    for k in range(3):
+        iota(r("UL", 8 * k, 8 * k + 8), GRP[JUMP[k]][0], GRP[JUMP[k]][1])
+    iota(r("PC", 0, 1), [[0, 1]], 0, 1)
+    iota(r("JM"), [[0, 24], [1, 16]], 0)
+    iota(r("I4"), [[0, 24], [1, 4]], 0)
+    iota(r("LK2"), [[4, 4], [16, 24]], 0)
     pr = [(T.LKS[:, 0:24], T.lk[:, 0:24])]
     for h in range(8):
         a = h ^ JUMP[1]
@@ -228,134 +263,93 @@ def rank_program(g, core, T, topo):
     for h in range(0, 8, 4):
         a = h ^ JUMP[2]
         pr.append((T.LKS[16 * h:16 * h + 64, 48:72], T.lk[16 * a:16 * a + 64, 48:72]))
-    dma("Y", "d3", pr, wr=[r("LKS")])
-    dma("Y", "d4", [(T.WCc[:].bitcast(dt.uint8), T.wc[:]), (T.WCs[:], T.ws[:])], wr=[r("WCc"), r("WCs")])
-    dma("Y", "d5", [(T.VV[:], T.v[:])], wr=[r("VV")])
+    dma("Y", pr, wr=[r("LKS")])
+    za, zb = tile0("ad"), tile0("gone")
+    dma("Y", [(T.CB[:, a:min(a + 1024, zb)], T.ZB[:, 0:min(1024, zb - a)]) for a in range(za, zb, 1024)], rd=[r("ZB")], wr=[r("CB", za, zb)])
+    dma("Y", [(T.WCc[:].bitcast(dt.uint8), T.wc[:]), (T.WCs[:], T.ws[:]), (T.VV[:], T.v[:])], wr=[r("WCc"), r("WCs"), r("VV")])
+    dma("Y", [(T.LK2[4 * k + s:128:16, 24 * q:24 * q + 24], T.lk[4 * q + s:128:16, 24 * k:24 * k + 24]) for k in range(3) for q in range(4) for s in range(4)], wr=[r("LK2")])
+    dma("Y", [(T.WA[:, a:a + 1024], T.ZB[:]) for a in range(0, LEN["WA"], 1024)] + [(T.ND[:, 0:1024], T.ZB[:]), (T.ND[:, 1024:1536], T.ZB[:, 0:512])],
+        rd=[r("ZB")], wr=[r("WA"), r("ND")])
 
-    GRP = {0: ([[16, 8]], 0), 1: ([[32, 4], [-16, 2]], 16), 4: ([[-64, 2], [16, 4]], 64)}
-    CLS = lambda A: 16 * (A & 1) + 64 * (A >> 1)
-    neg = lambda pat: [[-a, b] for a, b in pat]
-    for k in range(3):
-        iota(r("UL", 8 * k, 8 * k + 8), GRP[JUMP[k]][0], GRP[JUMP[k]][1], 0)
-    iota(r("PC", 0, 1), [[0, 1]], 0, 1)
-    iota(r("JM"), [[0, 24], [1, 16]], 0, 0)
-    fill(r("WT", 0, 512), 1.0)
-    for j, w in enumerate([-6.0, -2.0, 3.0, -1.0]):
-        fill(r("WT", 512 + 128 * j, 640 + 128 * j), w)
-    WCOL = {1.0: 0, -6.0: 512, -2.0: 640, 3.0: 768, -1.0: 896}
     tc(r("ULo"), r("UL"))
-    for a in (0, 1024): act(r("FB", a, a + 1024), r("WT", 0, 1024), scale=0.0)
-    act(r("FB", 2048), r("WT", 0, 16), scale=0.0)
-    PFC = {}
-
-    def pcol(name):
-        PFC[name] = len(PFC)
-        return r("PF", PFC[name], PFC[name] + 1)
-
-    P = lambda name: r("PF", PFC[name], PFC[name] + 1)
-
-    def scol(name, a, scale=1.0, bias=0.0):
-        act(pcol(name), P(a), bias=bias, scale=scale, fn=IDENT if isr(bias) else COPY)
-
-    p = r("PC", 0, 1)
-    for j, (n, sh, an) in enumerate([("i", 0, 15), ("s", 0, 3), ("kk", 2, 3), ("g0", 4, 1), ("g1", 5, 1), ("g2", 6, 1)]):
-        o = r("PC", j + 1, j + 2)
-        ts(o, p, sh, OP.arith_shift_right, an, OP.bitwise_and)
-        tc(pcol(n), o)
-    ts(r("MD"), r("JM"), P("i"), OP.is_equal)
-    act(r("MX"), r("MD"), scale=2e29, bias=-1e29)
-    act(r("ND"), r("MD"), scale=-1.0, bias=1.0)
-    act(r("NX"), r("MD"), scale=-2e29)
-    for A in range(4):
-        for h in range(2):
-            a = 516 * A + 3 + 256 * h
-            sel(r("FB", a, a + 253, 4), r("WT", 0, 64), [[-32, 2], [0, 2], [-1, 16]], OP.is_equal, 0.0, -CLS(A), 1)
-    for k in range(3):
-        gp, gb = GRP[JUMP[k]]
-        sel(r("GCt", 32 * k, 32 * k + 32), r("WT", 0, 32), neg(gp) + [[0, 4]], OP.is_ge, 0.0, -gb, 1)
-        sel(r("GC", 32 * k, 32 * k + 32), r("GCt", 32 * k, 32 * k + 32), gp + [[0, 4]], OP.is_ge, 0.0, gb + 15, -1)
-    sel(r("NX"), r("NX"), [[0, 24], [1, 16]], OP.not_equal, -2e29, 0, 0)
-    sel(r("GOt"), r("WT", 0, 512), [[-16, 8], [0, 64]], OP.is_ge, 0.0, 0, 1)
-    sel(tile("gone"), r("GOt"), [[16, 8], [0, 64]], OP.is_ge, 0.0, 15, -1)
-
-    def zeros(a, b):
-        while a < b:
-            n = min(1024, b - a)
-            act(r("CB", a, a + n), r("WT", 0, n), scale=0.0)
-            a += n
-
-    z0, zc = tile0("qsel"), tile0("came0")
+    p = col("PC", 0)
+    for j, (sh, an) in enumerate([(0, 15), (0, 3), (2, 3), (4, 1), (5, 1), (6, 1)]):
+        ts(col("PC", j + 1), p, sh, OP.arith_shift_right, an, OP.bitwise_and)
+    tc(pcol("p", 6), r("PC", 1, 7))
+    pi, ps, pk, g0, g1, g2 = [P("p", j) for j in range(6)]
+    ts(r("MD"), r("JM"), pi, OP.is_equal)
+    act(r("MX"), r("MD"), scale=-2e29, bias=1e29)
+    act(r("NX"), r("MD"), scale=2e29)
+    for a in range(0, 1536, 768): zero(r("CT", a, a + 768))
+    zero(r("FB"))
+    sel(r("NX"), r("NX"), [[0, 24], [1, 16]], OP.not_equal, 2e29, 0, 0)
+    sel(r("GOt"), r("WT"), [[-16, 8], [0, 64]], OP.is_ge, 0.0, 0, 1)
+    sel(r("CB", zb, zb + 512), r("GOt"), [[16, 8], [0, 64]], OP.is_ge, 0.0, 15, -1)
+    fill(r("RST"), 1.0)
+    fill(r("RST", 0, C, 16), 0.0)
+    fill(col("RS", 0), 0.0)
+    for j in range(1, 6): fill(r("CT", 4 * CA[j] + 256 * j, 4 * CA[j + 1]), 0.0)
     quant("QU", 0, 128, r("U"))
-    zeros(zc, zc + 2048)
-    pick("QUP", "QU", 3, r("ULo"))
+    pick("QUP", "QU", r("ULo"))
     quant("QX", 0, C, r("X0"))
+    row = lambda j: col("MD", j)
 
-    def scores():
-        mm("PA", ("QUP", 0), ("QX", 0), C)
-        mm("PB", ("QUP", 0), ("QX", 0), C)
-        mm("PCC", ("QUP", 128), ("QX", 0), C)
-        mm("PD", ("QUP", 256), ("QX", 0), C)
-        act(r("TS", 0, C), r("PB", 0, C))
-        act(r("TS", C, 2 * C), r("PCC", 0, C))
-        act(r("TS", 2 * C, 3 * C), r("PD", 0, C))
+    def setup_columns():
+        ts(pcol("ms", 4), r("I4", 0, 4), ps, OP.is_equal)
+        ts(pcol("mr", 4), r("I4", 0, 4), pk, OP.is_equal)
+        act(pcol("n3"), P("mr", 3), scale=-1.0, bias=1.0)
+        act(pcol("mk", 4), PV("ms"), scale=P("n3"))
+        act(pcol("mn", 4), PV("mk"), scale=-1.0)
+        act(pcol("m7", 4), PV("mr"), scale=-7.0)
+        act(pcol("m512", 4), PV("mr"), scale=512.0)
+        act(pcol("m29", 4), PV("mr"), scale=512.0 * 29)
+        act(pcol("k16"), pi, scale=HOLD, bias=-15 * HOLD)
+        act(pcol("k4"), pk, scale=HOLD, bias=-3 * HOLD)
+        act(pcol("kc"), pi, scale=HOLD - 1, bias=-15 * (HOLD - 1))
+        act(r("CONST"), r("CONST"), bias=P("kc"))
+        act(r("HD"), r("MD"), scale=-DROP - HOLD, bias=HOLD)
 
-    scores()
-    act(r("NB", 0, C), r("PB", 0, C))
-    for k, n in ((1, "g0"), (2, "g2")): scol("sg%d" % k, n, -2.0, 1.0)
-    act(r("NB", C, 2 * C), r("PB", 0, C), scale=P("sg1"))
-    act(r("SB2"), r("PB", 0, C), scale=P("sg2"))
-    act(r("SL", 0, C), r("PCC", 0, C), scale=P("sg1"))
-    act(r("SL", C, 2 * C), r("PD", 0, C), scale=P("sg2"))
-    act(r("RF", C, 512), r("WT", 0, 512 - C), scale=0.0)
+    def setup_rows():
+        act(pcol("sg1"), g0, scale=-2.0, bias=1.0)
+        act(pcol("sg2"), g2, scale=-2.0, bias=1.0)
+        act(pcol("p4"), row(4), scale=P("sg1"))
+        act(pcol("p8"), row(8), scale=P("sg2"))
+        ts(pcol("wa"), row(0), row(1), OP.subtract, row(2), OP.subtract)
+        ts(pcol("w0"), P("wa"), row(10), OP.subtract)
+        ts(pcol("w1"), row(6), row(2), OP.subtract, P("p4"), OP.subtract)
+        ts(pcol("w2"), row(6), row(10), OP.add, P("p8"), OP.add)
+        ts(pcol("ba"), row(0), row(1), OP.subtract, P("p4"), OP.add)
+        act(pcol("base"), P("ba"), bias=P("p8"))
+        act(pcol("ys"), row(1), scale=-2.0, bias=row(0))
+        ts(pcol("ya"), row(4), g0, OP.mult, row(1), OP.subtract)
+        ts(pcol("yb"), row(8), g2, OP.mult, P("ya"), OP.add)
+        act(pcol("y"), P("yb"), scale=-1.0, bias=1.0)
+        ts(pcol("da"), row(0), row(1), OP.add, row(4), OP.add)
+        act(pcol("dr"), P("da"), bias=row(8))
 
-    def setup_first():
-        quant("QK", 0, 128, tile("gone"))
-        for A in range(4):
-            for b in range(4):
-                quant("QF", 512 * A + 128 * b, 512 * A + 128 * b + 128, r("FB", 516 * A + 3 - b, 516 * A + 515 - b))
+    iota(r("IJF"), [[1, C]], 0)
+    iota(r("CONST"), [[16, 24]], 0)
+    cf = lambda n: r("CF", 32 * TI[n], 32 * TI[n] + 32)
+    gca = lambda n: r("GCA", 32 * TI[n], 32 * TI[n] + 32)
 
-    fill(r("CB", z0, zc), 0.0)
-    for n, a in (("GT", C), ("W", C), ("GA", 1152), ("AW", 1152), ("RF", 1152)):
-        fill(r(n, a), 0.0)
-    for t in range(R):
-        fill(r("E%d" % t, 4 * GW, 512), 0.0)
+    def group_mask(o, c, n=1):
+        gp, gb = GRP[c]
+        rep = [[0, n]] if n > 1 else []
+        x = r("GOt", 0, 32 * n)
+        sel(x, r("WT", 0, 32 * n), rep + neg(gp) + [[0, 4]], OP.is_ge, 0.0, -gb, 1)
+        sel(o, x, rep + gp + [[0, 4]], OP.is_ge, 0.0, gb + 15, -1)
 
-    def setup_zeros():
-        zeros(zc + 2048, tile0("hop0"))
-        for a in (0, 768): act(r("ET", a, a + 768), r("WT", 0, 768), scale=0.0)
-        act(r("IN"), r("WT", 0, 512), scale=0.0)
-        act(r("GA", 640, 1152), r("WT", 0, 512), scale=0.0)
+    group_mask(r("GCA"), 0, 12)
+    for n in ("lc", "ac"):
+        for k in (1, 2): group_mask(gca("%s%d" % (n, k)), JUMP[k])
+    sel(r("FB", 3, 515, 4), r("WT", 0, 128), [[-1, 128]], OP.is_equal, 0.0, 0, 1)
+    for n in ("G", "W", "RF", "IN", "C2", "G2", "VT", "E", "GS", "PT", "H0"): const(r(n), 0)
+    const(r("GA", 1152, 1280), 0)
 
-    iota(r("IJF"), [[1, C]], 0, 0)
-    for n, w in (("qsel", 1.0), ("qneg", -1.0), ("q3", 3.0)):
-        for s in range(4):
-            sel(tile(n, 5 * s, 16), r("WT", WCOL[w], WCOL[w] + 32), [[-16, 8], [-4, 4]], OP.is_equal, 0.0, -s, 1)
-    for k in range(3):
-        for s in range(4):
-            sel(tile("q1_%d" % k, 16 * k + 5 * s, 64), r("WT", 0, 8), [[-16, 8]], OP.is_equal, 0.0, -4 * k - s, 1)
-    for k in range(3):
-        for e in (0, 1 + k): sel(tile("st%d" % k, e, 4), r("WT", WCOL[3.0], WCOL[3.0] + 128), [[-1, 128]], OP.is_equal, 0.0, 0, 1)
-    sel(tile("sto", 0, 4), r("WT", 0, 128), [[-1, 128]], OP.is_equal, 0.0, 0, 1)
-    for k in range(3):
-        for s in range(4): sel(tile("sto", 16 * k + 4 * s + 1 + k, 64), r("WT", 0, 8), [[-16, 8]], OP.is_equal, 0.0, -4 * k - s, 1)
-    for A in range(4):
-        a = 32 * A
-        sel(r("GDt", a, a + 32), r("WT", 0, 32), [[0, 2], [-32, 2], [0, 8]], OP.is_ge, 0.0, -CLS(A), 1)
-        sel(r("GD", a, a + 32), r("GDt", a, a + 32), [[0, 2], [32, 2], [0, 8]], OP.is_ge, 0.0, CLS(A) + 15, -1)
-    iota(r("CMr"), [[0, 24], [1, 4]], 0, 0)
-    iota(r("D0"), [[0, 48], [1, 8]], 0, 0)
-    iota(r("D1"), [[0, 6], [8, 8], [0, 8]], 0, 0)
-    iota(r("D2"), [[64, 6], [0, 64]], 0, 0)
-    iota(r("J0"), [[0, 48], [4, 2]], 0, 0)
-    iota(r("J1"), [[0, 6], [8, 8], [0, 2]], 0, 0)
-    iota(r("J2"), [[64, 6], [0, 16]], 0, 0)
-    iota(r("CB", tile0("hop0"), tile0("cls0")), [[0, 1536]], 0, 0)
-    iota(r("CB", tile0("hopf0"), tile0("gb") + 512), [[0, 512 * (TI["gb"] + 1 - TI["hopf0"])]], 0, 0)
-    for b in range(4):
-        for A in range(4):
-            a = 32 * b + 8 * A
-            iota(r("WL", a, a + 8), [[0, 2], [32, 2], [0, 2]], 128 * b + CLS(A), 0)
-    iota(r("HT"), [[0, 16 * C]], 0, 0)
+    def lay(a, b):
+        a, b = TI[a], TI[b] + 1
+        tt(r("GW1", 32 * a, 32 * b), r("CF", 32 * a, 32 * b), r("GCA", 32 * a, 32 * b), OP.mult)
+        for s in range(4): act(r("CB", 512 * a + 5 * s, 512 * b, 16), r("GW1", 32 * a, 32 * b))
 
     def quant_tiles(a, b):
         a, b = TI[a], TI[b] + 1
@@ -364,98 +358,93 @@ def rank_program(g, core, T, topo):
             quant("QK", 128 * a, 128 * (a + n), r("CB", 512 * a, 512 * (a + n)))
             a += n
 
-    tc(r("OFT", 0, 24), r("LKT", 0, 24))
-    for k in (1, 2): ts(r("OFT", 24 * k, 24 * k + 24), r("LKT", 24 * k, 24 * k + 24), float(C * k), OP.add)
-    tc(r("OFJ"), r("LKT"))
-    tc(r("OFS"), r("LKS"))
-    for s in range(4): ts(pcol("ms%d" % s), P("s"), float(s), OP.is_equal)
-    for k in range(4): ts(pcol("mr%d" % k), P("kk"), float(k), OP.is_equal)
+    def setup_turns():
+        for a in range(0, za, 512): zero(r("CB", a, a + 512))
+        ts(r("DGR"), r("I4", 0, 32), pk, OP.is_equal)
+        ts(r("GCT", 0, 32), r("DGR"), -2.0, OP.mult, -4.0, OP.add)
+        act(cf("ld"), r("GCT", 0, 32), scale=P("dr"))
+        act(cf("lo"), r("DGR"), scale=-4.0, bias=-1.0)
+        act(r("GCT", 32, 64), r("DGR"), scale=-2.0, bias=3.0)
+        for k in range(3): act(cf("lc%d" % k), r("GCT", 32, 64), scale=P("mr", k))
+        lay("ld", "lc2")
+        a = tile0("gs")
+        for s in range(4): act(r("CB", a + 4 * s, a + 512, 16), gca("ld"), scale=P("ms", s))
 
-    def setup_columns():
-        for k in range(3):
-            scol("mc%d" % k, "mr%d" % k, -6.0)
-            scol("mw%d" % k, "mr%d" % k, -2.0)
-        scol("A2", "g2", 2.0, P("g0"))
-        scol("A384", "A2", 384.0)
-        scol("a3s", "A384", P("mr3"))
-        for k, n, f in ((1, "g0", 384.0), (2, "g2", 768.0)):
-            scol("x%d" % k, n, -2.0 * f, f)
-            scol("y%d" % k, "x%d" % k, 1.0, P("A384"))
-            scol("z%d" % k, "y%d" % k, P("mr3"))
-        scol("h768", "g1", 768.0)
-        scol("b1", "mr1", 2.0, P("mr0"))
-        scol("bit", "mr2", 4.0, P("b1"))
-        scol("bit8", "bit", 8.0)
-        for s in range(4): scol("mo%d" % s, "ms%d" % s, P("mr0"))
+    def setup_aways():
+        act(cf("ad"), r("DGR"), scale=P("dr"))
+        act(cf("ao"), r("DGR"), scale=0.5)
+        act(r("GCT", 0, 32), r("DGR"), scale=-0.5)
+        fill(r("GCT", 3, 32, 4), 1.0)
+        for k in range(3): act(cf("ac%d" % k), r("GCT", 0, 32), scale=P("mr", k))
+        a = 32 * TI["ord"]
+        fill(r("CF", a, a + 32), 0.0)
+        for k, (x, y, op) in enumerate(((2, 10, OP.add), (6, 2, OP.subtract), (6, 10, OP.add))):
+            ts(r("CF", a + k, a + 32, 4), r("WT", 0, 8), row(x), OP.mult, row(y), op)
+        ts(pcol("sa"), P("mr", 2), float(FS), OP.mult, P("mr", 0), OP.add)
+        ts(cf("st"), r("WT", 0, 32), P("sa"), OP.mult, P("mr", 1), OP.add)
+        lay("ad", "st")
 
-    def setup_moves():
-        for k in range(3):
-            for s in range(4):
-                act(tile("came%d" % k, 5 * s, 16), r("GC", 32 * k, 32 * k + 32), scale=P("mc%d" % k))
-                act(tile("own%d" % k, 16 * k + 5 * s, 64), r("GC", 32 * k + k, 32 * k + 32, 4), scale=P("mw%d" % k))
+    c2 = lambda e, n, a=0, st=1: r("CF2", 320 * e + 32 * T2.index(n) + a, 320 * e + 32 * T2.index(n) + 32, st)
 
-    def setup_classes():
+    def setup_factors():
+        const(r("CF2"), 0)
+        const(c2(0, "gs"), 1)
+        const(c2(0, "lg"), -1)
+        const(c2(0, "lg", 3, 4), 1)
+        for e, c in ((0, 1), (1, 1), (3, 2)): const(c2(e, "dl1"), c)
+        for e in (2, 3): const(c2(e, "dl2"), FS)
+        a = 32 * T2.index("ct0")
+        for e in range(3): const(r("CF2", 320 * e + a + e, 320 * e + a + 128, 4), 1)
+        const(r("CF2", 960 + a, 960 + a + 128), 1)
+        group_mask(r("GW2"), 0, 10)
         for A in range(4):
-            for h in range(4):
-                o, src = tile0("cls%d" % A) + 128 * h, tile0("gone") + 64 * ((A & 1) + 2 * (h & 1) + 4 * (A >> 1))
-                for g0 in range(2): act(r("CB", o + 64 * g0, o + 64 * g0 + 64), r("CB", src, src + 64))
+            x = r("GDT", 32 * A, 32 * A + 32)
+            sel(x, r("WT", 0, 32), [[0, 2], [-32, 2], [0, 8]], OP.is_ge, 0.0, -CLS(A), 1)
+            sel(r("GW2", a + 32 * A, a + 32 * A + 32), x, [[0, 2], [32, 2], [0, 8]], OP.is_ge, 0.0, CLS(A) + 15, -1)
+        iota(r("NODE"), [[4 * C, 2], [C, 2], [1, FS]][0:0] + [[1, LEN["NODE"]]], 0)
+        for A in range(1, 4): iota(r("NODE", FS * A, FS * A + C), [[1, C]], C * ((A & 1) + 4 * (A >> 1)))
 
-    def setup_hops(k):
-        if k == 0: ts(r("KM"), r("CMr", 0, 32), P("kk"), OP.is_equal)
-        h = r("GH", 32 * k, 32 * k + 32)
-        tt(h, r("GC", 32 * k, 32 * k + 32), r("KM"), OP.mult)
-        for s in range(4): act(tile("hop%d" % k, 5 * s, 16), h)
+    def setup_short(e):
+        if e == 0:
+            act(c2(0, "lv"), r("DGR"), scale=2048.0, bias=-1024.0)
+            act(c2(0, "nm"), r("DGR"), scale=-2.0)
+            act(pcol("nb"), P("mr", 3), scale=9.5, bias=-9.0)
+            act(c2(1, "nm"), r("DGR"), scale=-4.0, bias=P("nb"))
+        a, b = T2.index(ELEM[e][0]) + (e == 0), T2.index(ELEM[e][1]) + 1
+        x = r("CF2", 320 * e + 32 * a, 320 * e + 32 * b)
+        tt(x, x, r("GW2", 32 * a, 32 * b), OP.mult)
+        o = tile0("gs")
+        for s in range(4): act(r("CB", o + 512 * a + 4 * s + e, o + 512 * b, 16), x, scale=P("ms", s))
 
-    def setup_tables():
-        for s in range(4): act(tile("hopf0", 5 * s, 16), r("GC", 0, 32))
-        for A in range(4):
-            d = r("GD", 32 * A, 32 * A + 32)
-            tt(d, d, r("KM"), OP.mult)
-            for s in range(4): act(tile("ct%d" % A, 5 * s, 16), d)
-        for e, n in ((0, "ge"), (1, "ge"), (2, "gm"), (3, "gb")):
-            act(tile(n, e, 4), tile("gone", e, 4))
+    def setup_ends():
+        ts(pcol("s3"), ps, P("mr", 3), OP.mult, 16.0, OP.add)
+        for q in range(4): ts(r("X16", q, 96, 4), r("LK2", 24 * q, 24 * q + 24), P("s3"), OP.add)
+        ts(r("XA"), r("X16"), 31, OP.bitwise_and)
+        ts(r("XB2"), r("X16"), 992, OP.bitwise_and)
+        ts(r("OCL"), r("XA"), -16.0, OP.add)
+        tc(r("OCH"), r("XB2"))
+        ts(pcol("a1"), g0, P("mr", 1), OP.not_equal)
+        ts(pcol("a2"), g2, P("mr", 2), OP.not_equal, 2.0, OP.mult)
 
     def setup_routes():
-        ts(r("RM"), r("CMr"), P("kk"), OP.is_equal)
-        for d in range(3): act(r("D%d" % d), r("D%d" % d), scale=P("mr%d" % d))
-        tt(r("qa"), r("D0"), r("D1"), OP.add)
-        tt(r("CTF"), r("qa"), r("D2"), OP.add)
-        ts(r("t0"), r("J0"), P("s"), OP.add, P("mr0"), OP.mult)
-        ts(r("t1"), r("J1"), P("mr1"), OP.mult, P("a3s"), OP.add)
-        ts(r("t2"), r("J2"), P("mr2"), OP.mult)
-        tt(r("ua"), r("t0"), r("t1"), OP.add)
-        tt(r("JC"), r("ua"), r("t2"), OP.add)
+        act(pcol("cls"), P("a1"), bias=P("a2"))
+        act(pcol("ws"), P("mr", 2), scale=2.0, bias=-1.0)
+        act(pcol("wsc"), P("ws"), scale=P("n3"))
+        act(pcol("wb"), pk, scale=-1.0, bias=3.0)
+        act(pcol("thr"), P("mr", 3), scale=-18.0, bias=0.5)
+        act(pcol("two"), P("mr", 3), bias=1.0)
+        act(r("HD4"), r("HD4"), scale=-DROP - HOLD, bias=HOLD)
+        act(pcol("b1"), P("mr", 1), scale=2.0, bias=P("mr", 0))
+        act(pcol("bit"), P("mr", 2), scale=4.0, bias=P("b1"))
+        act(pcol("bit8"), P("bit"), scale=8.0)
+        act(pcol("h768"), g1, scale=2.0 * C)
+        for b in range(4): act(pcol("hb%d" % b), P("k16"), scale=4.0, bias=1024.0 + b)
 
-    def setup_ends_s(k):
-        act(r("qa"), r("CTF"), off=r("OFJ", 24 * k, 24 * k + 24))
-        for s in range(4): act(r("qm", 96 * s, 96 * s + 96), r("qa", s, C, 4), scale=P("ms%d" % s))
-
-    def setup_ends(k):
-        tt(r("qb"), r("qm", 0, 192), r("qm", 192, C), OP.add)
-        tt(r("qd"), r("qb", 0, 96), r("qb", 96, 192), OP.add)
-        ts(r("OC%d" % k), r("qd"), P("a3s") if k == 0 else P("z%d" % k), OP.add)
-
-    def setup_layer():
-        ts(r("WLo"), r("WL"), P("i"), OP.add)
-        pick("WP", "WC", 16, r("WLo"))
-
-    def masked(src):
-        for s in range(4):
-            o = r("W", s, C, 4)
-            if s < 2: ts(o, src, P("ms%d" % s), OP.mult)
-            else: act(o, src, scale=P("ms%d" % s))
-
-    def gather_w(n):
-        v = n // 16
-        win = r("W", 0, C)
-        act(r("GA", n, 1152), win, off=r("OFS", v, 72))
-        if n: tc(r("GA", 0, n), win, off=r("OFS", 0, v))
-
-    def to_list(src, o):
-        tt(r("la"), src, r("RM"), OP.mult)
-        tt(r("lb"), r("la", 0, 96, 2), r("la", 1, 96, 2), OP.add)
-        tt(r("lc"), r("lb", 0, 48, 2), r("lb", 1, 48, 2), OP.add)
-        tc(o, r("lc"))
+    def setup_slots():
+        act(pcol("o1"), g2, scale=2.0, bias=g0)
+        act(pcol("o2"), P("o1"), scale=128.0, bias=-256.0)
+        act(pcol("o3"), P("o2"), bias=float(GW))
+        act(r("SLS"), r("IJF", 0, GW), bias=P("o2"))
 
     def send(t):
         m = topo.engines(core, nxt)[:ENGINES]
@@ -474,254 +463,240 @@ def rank_program(g, core, T, topo):
         clk[("arr%d" % t, 2 * pe)] = {}
         record("D", ("arr%d" % t, 2 * pe), [], [r("LDc", a, a + n), r("LDs", a, a + n)])
 
-    def state():
-        for k in range(3): act(r("IN", 1 + k, 4 * 96, 4), r("PV%d" % k, 0, 96), scale=1.0 / 3.0)
+    def spread(dst, src):
+        n = LEN[src]
+        pairs = []
+        for A in range(4):
+            for h in range(8):
+                a = CLS(A) + 16 * (h & 2)
+                pairs.append((T[dst][16 * h:16 * h + 16, n * A:n * A + n], T[src][a:a + 16, 0:n]))
+        dma("Y", pairs, rd=[r(src)], wr=[r(dst)])
 
-    def inject(stop):
-        for k in range(3): mm("PV%d" % k, K("st%d" % k), ("QIN", 0), 128, True, stop)
-        mm("PV3", K("sto"), ("QIN", 0), 128, True, stop)
+    def to_list(bk, o):
+        scan(r("ST4"), r("HD4"), r(bk, 0, 96), OP.add, OP.max)
+        ts(r(o), r("ST4", 3, 96, 4), P("k4"), OP.add)
 
-    def number_parts():
-        ts(r("ea"), r("PE"), 768.0, OP.is_ge, 768.0, OP.mult)
-        tt(r("eb"), r("PE"), r("ea"), OP.add)
-        ts(r("ec"), r("eb"), P("h768"), OP.add)
-        tc(r("EI"), r("ec"))
-        for e, m in enumerate((15, 240, 3840)): ts(r("EP", 96 * e, 96 * e + 96), r("EI"), m, OP.bitwise_and)
-        tc(r("qa", 0, 288), r("EP"))
-        tt(r("ea"), r("ba"), r("bb"), OP.add)
-        for s in range(4):
-            for e in range(3): act(r("ET", 4 * s + e, 4 * C, 16), r("qa", 96 * e, 96 * e + 96), scale=P("mo%d" % s))
-            act(r("ET", 4 * s + 3, 4 * C, 16), r("ea"), scale=P("ms%d" % s))
+    def moved(i, own, came):
+        return [(K(own), ("QW", 128 * i))] + [(K("%s%d" % (came, k)), ("QD", 320 * i + 96 * k)) for k in range(3)]
 
-    rot = [0]
     for t in range(R):
-        if t: scores()
-        tt(r("SB1"), r("PA", 0, C), r("MX"), OP.min)
-        scan(r("ST"), r("NX"), r("SB1"), OP.add, OP.max)
-        ts(r("NS"), r("ST", 15, C, 16), -1.0, OP.mult)
-        if t == 0: setup_first()
-        fq = [(A, b) for A in range(4) for b in range(4)]
-        for j in range(6):
-            if t == 0 and j < 3: (setup_zeros, setup_columns, setup_moves)[j]()
-            for _ in range(FSHARE[j]):
-                if fq:
-                    A, b = fq.pop(0)
-                    bk = ("PCC", "PD")[rot[0] % 2]
-                    rot[0] += 1
-                    mm(bk, ("QF", 512 * A + 128 * b), ("QX", 0), C)
-                    act(r("FT", 1536 * b + C * A, 1536 * b + C * A + C), r(bk, 0, C), scale=0.5)
-            for a in range(24 - SSHARE, 24) if t and j == FFIRST else ():
-                m = 16 * a + 16
-                x = r("TM", C * (a % 2), C * (a % 2) + m)
-                act(x, r("TS", 0, m), bias=r("NS", a, a + 1), fn=ActivationFunctionType.Relu)
-                act(r("C2", a % 4, 4 * m, 4), x, fn=ActivationFunctionType.Sign)
-            n = "C2" if j == 5 else "C%d" % (j % 2)
-            for e in range(4):
-                a = 4 * j + e
-                m = 16 * a + 16
-                col = r("ST", m - 1, m)
-                if t == 0 or a < 24 - SSHARE: ts(r(n, e, 4 * m, 4), r("TS", 0, m), col, OP.is_gt)
-                if m < C: ts(r(n, 4 * m + e, 4 * C, 4), r("TS", m, C), col, OP.is_ge)
-            quant("QT", C * j, C * j + C, r(n))
-            mm("PB", K("gone"), ("QT", C * j), C, j == 0, j == 5)
-            if j == 4:
-                tt(r("ET", 0, 4 * C, 4), r("PA", 0, C), r("ST"), OP.is_equal)
-                quant("QT", 6 * C, 7 * C, r("ET"))
-                mm("PB", K("gone"), ("QT", 6 * C), C, False, False)
-            if t and j == 1:
+        pass
+        mm("PA", ("QUP", 0), ("QX", 0), C)
+        mm("PB", ("QUP", 0), ("QX", 0), C)
+        mm("PCC", ("QUP", 128), ("QX", 0), C)
+        mm("PD", ("QUP", 256), ("QX", 0), C)
+        act(r("TS"), r("PB", 0, C))
+        tt(r("SB1"), r("PA", 0, C), r("MX"), OP.max)
+        scan(r("ST"), r("NX"), r("SB1"), OP.add, OP.min)
+        ts(r("NS", 24 - SOWN, 24), r("ST", 16 * (24 - SOWN) + 15, C, 16), -1.0, OP.mult)
+        node = lambda a: r("CT", 4 * CA[a // 4] + a % 4, 4 * CA[a // 4] + 64 * a, 4)
+        for a in range(24 - SOWN, 24):
+            x = r("TM", C * (a % 2), C * (a % 2) + 16 * a)
+            act(x, r("TS", 0, 16 * a), bias=col("NS", a), fn=FN.Relu)
+            act(node(a), x, fn=FN.Sign, acc=col("RS", a))
+        if t == 0:
+            setup_columns()
+            setup_rows()
+            quant("QK", 128 * TI["gone"], 128 * TI["gone"] + 128, r("CB", zb, zb + 512))
+        for j in (4, 3, 5, 2, 1, 0):
+            for a in range(4 * j + 3, 4 * j - 1, -1):
+                if 0 < a < 24 - SOWN:
+                    ts(node(a), r("TS", 0, 16 * a), col("ST", 16 * a + 15), OP.is_gt)
+                    act(r("JK", 0, 16 * a), node(a), acc=col("RS", a))
+            if j == 0:
+                tt(r("CT", 0, 4 * C, 4), r("PA", 0, C), r("ST"), OP.is_ge)
+            quant("QT", CA[j], CA[j + 1], r("CT", 4 * CA[j], 4 * CA[j + 1]))
+            if j == 3 and t:
                 quant("QIN", 0, 128, r("IN"))
-                inject(True)
+        for j in (0, 4, 3, 5, 2, 1): mm("PE", K("gone"), ("QT", CA[j]), CW[j], j == 0, j == 1)
+        scan(r("CS"), r("RST"), r("CT", 0, 4 * C, 4), OP.mult, OP.add)
+        tt(r("RC"), r("CONST"), r("RS"), OP.subtract)
+        tt(r("RC"), r("RC"), r("CS", 15, C, 16), OP.subtract)
+        act(r("W1"), r("PCC", 0, C), scale=P("w1"))
+        act(r("W2"), r("PD", 0, C), scale=P("w2"))
         if t == 0:
-            quant_tiles("qsel", "own2")
-            quant("QGA", 192, 320, r("GA", 768, 1280))
-        ts(r("GT", 0, C), r("PB", 0, C), float(GW + 1), OP.is_lt)
-        quant("QG", 0, 128, r("GT"))
-        mm("PA", K("qsel"), ("QG", 0), 128)
-        if t == 0:
+            act(r("W0"), r("PB", 0, C), scale=P("w0"))
+            act(r("BASE"), r("PB", 0, C), scale=P("base"))
             act(r("LW"), r("IJF"))
-            tt(r("AW", 0, C), r("TS", 0, C), r("NB", 0, C), OP.is_lt, off=r("OFJ", 0, 24))
-            for k, own in ((1, r("NB", C, 2 * C)), (2, r("SB2"))):
-                x = r(("LT", "EQ")[k - 1])
-                tt(x, r("SL", C * k - C, C * k), own, OP.is_lt, off=r("OFJ", 24 * k, 24 * k + 24))
-                act(r("AW", C * k, C * k + C), x, bias=P("g%d" % (2 * k - 2)), scale=P("sg%d" % k), fn=IDENT)
-            tt(r("LE"), r("TS", 0, C), r("NB", 0, C), OP.is_equal, off=r("OFJ", 0, 24))
+            tc(r("OFJ"), r("LKT"))
+            tc(r("OFS"), r("LKS"))
             tt(r("ML"), r("IJF"), r("LW"), OP.is_lt, off=r("OFJ", 0, 24))
-            tt(r("RF", 0, C), r("LE"), r("ML"), OP.mult)
-            quant("QRF", 0, 128, r("RF", 0, 512))
-            quant("QAW", 0, 320, r("AW"))
-            for k in range(3):
-                mm("PV%d" % k, K("q3"), ("QAW", 96 * k), 128, True, k > 0)
-                mm("PV3", K("q1_%d" % k), ("QAW", 96 * k), 128, k == 0, False)
-            mm("PV0", K("q3"), ("QRF", 0), 128, False, True)
-            mm("PV3", K("q1_0"), ("QRF", 0), 128, False, True)
-        ts(r("G3"), r("PA", 0, 96), 6.0, OP.mult, -3.0, OP.add)
-        ts(r("G9"), r("PA", 0, 96), 9.0, OP.mult, 0.5, OP.add)
+            act(r("Y"), r("ML"), scale=P("ys"), bias=P("y"))
+            setup_turns()
+            tt(r("A0"), r("W0"), r("BASE"), OP.subtract, off=r("OFJ", 0, 24))
+            tt(r("A1"), r("W1"), r("A0"), OP.subtract, off=r("OFJ", 24, 48))
+            tt(r("RG"), r("W2"), r("A1"), OP.is_lt, off=r("OFJ", 48, 72))
+            tt(r("RF", 0, C), r("RG"), r("Y"), OP.is_equal)
+            quant("QRF", 0, 128, r("RF"))
+            quant_tiles("ld", "lc2")
+            quant_tiles("gs", "gs")
+        pass
+        scan(r("ST2"), r("HD"), r("PE", 0, C), OP.add, OP.max)
+        tt(r("PL"), r("ST2", 15, C, 16), r("RC"), OP.add)
+        ts(r("GF"), r("PL"), GW - 0.5, OP.is_lt)
+        for q in range(4):
+            o = r("G", 4 * q, C, 16)
+            if q < 2: ts(o, r("GF"), P("m7", q), OP.mult, P("mr", q), OP.add)
+            else: act(o, r("GF"), scale=P("m7", q), bias=P("mr", q))
+        quant("QG", 0, 128, r("G"))
+        first = [(K("ld"), ("QRF", 0)) if t == 0 else (EB(0), ("QIN", 0)), (K("gs"), ("QG", 0))]
+        sums("LA", first)
 
-        def list1():
-            tt(r("SB2"), r("PB", 0, C), r("MD"), OP.mult)
-            scan(r("ST2"), r("ND"), r("SB2"))
-            ts(r("PLo"), r("ST2", 15, C, 16), -1.0, OP.add)
-            o = r("PLo")
-            do("V", lambda e: e.tensor_copy(T.LW[:, 0:C].indirect(ap(o)), ap(r("IJF"))), [r("IJF"), o], [r("LW")])
+        def unpack(b):
+            bk = ("PCC", "PD")[b % 2]
+            mm(bk, EB(b), ("QX", 0), C)
+            act(r("F0", C * b, C * b + C), r(bk, 0, C), scale=0.5)
 
-        def list2():
-            tt(r("SB3"), r("LW", 0, GW), r("MD", 0, GW), OP.mult)
-            scan(r("ST3"), r("ND", 0, GW), r("SB3"))
-            ts(r("ELo"), r("ST3", 15, GW, 16), P("A384"), OP.add)
+        def in_order():
+            tc(r("PLo"), r("PL"))
+            scatter(r("LW"), r("PLo"), r("IJF"))
+
+        def gate_list():
+            scan(r("ST3"), r("HD", 0, GW), r("LW", 0, GW), OP.add, OP.max)
+            ts(r("ELo"), r("ST3", 15, GW, 16), P("k16"), OP.add)
 
         def gates():
-            for b in range(4):
-                act(r("E%d" % t, b, 4 * GW, 4), r("FT", 1536 * b, 1536 * b + 1536), scale=2.0, off=r("ELo"))
+            for b in range(4): act(r("E", b, 4 * GW, 4), r("F0", C * b, C * b + C), scale=2.0, off=r("ELo"))
+
+        def no_slots():
+            act(r("F0", 4 * C, FS), r("IJF"), scale=0.0, bias=P("o3"))
+
+        def slots():
+            scatter(r("F0", 4 * C, FS), r("ELo"), r("SLS"))
 
         def pass_on():
-            quant("QE", 128 * t, 128 * t + 128, r("E%d" % t))
+            quant("QE", 128 * t, 128 * t + 128, r("E"))
             send(t)
 
-        def scores_at(k):
-            return lambda: act(r("NB", C * k, C * k + C), r("TS"), off=r("OFT", 24 * k, 24 * k + 24))
+        def stay():
+            for q in range(4): act(r("G2", 4 * q, C, 16), r("GF"), scale=P("m29", q), bias=P("m512", q))
 
-        def order(j):
-            a, b = ((0, 1), (0, 2), (1, 2))[j]
-            return lambda: tt(r("RF", C * j, C * j + C), r("TS"), r("NB", C * a, C * a + C), OP.is_lt, off=r("OFT", 24 * b, 24 * b + 24))
+        def order0():
+            act(r("A0"), r("TS"), scale=P("w0"), off=r("OFJ", 0, 24))
 
-        def orders():
-            order(2)()
-            quant("QRF", 0, 320, r("RF"))
-            for j, (bk, a, ka, b, kb) in enumerate((("PA", 0, "qneg", 1, "qneg"), ("PB", 0, "qsel", 2, "qneg"))):
-                mm(bk, K(ka), ("QRF", 96 * a), 128, True, False)
-                mm(bk, K(kb), ("QRF", 96 * b), 128, False, True)
+        def order1():
+            tt(r("A1"), r("W1"), r("A0"), OP.subtract, off=r("OFJ", 24, 48))
 
-        def orders2():
-            for j, bk in enumerate(("PA", "PB")): act(r("R%d" % j), r(bk, 0, 96), bias=3.0 - j)
-            mm("PA", K("qsel"), ("QRF", 96), 128, True, False)
-            mm("PA", K("qsel"), ("QRF", 192), 128, False, True)
-            act(r("R2"), r("PA", 0, 96), bias=1.0)
+        def order2():
+            tt(r("RF", 0, C), r("W2"), r("A1"), OP.is_lt, off=r("OFJ", 48, 72))
+            quant("QRF", 0, 128, r("RF"))
 
-        sq = [(A, j) for A in range(4) for j in range(7)]
-        pend = []
+        def weights():
+            mm("PA", K("ord"), ("QRF", 0), 128)
+            act(r("WW"), r("PA", 0, 96), scale=P("wsc"), bias=P("wb"), fn=FN.Square)
 
-        def slots(n):
-            for _ in range(n):
-                if not sq: return
-                A, j = sq.pop(0)
-                mm("PCC" if A % 2 == 0 else "PD", K("cls%d" % A), ("QT", C * (6 if j == 0 else j - 1)), C, j == 0, j == 6)
-                if j == 6: pend.append(A)
+        def layer():
+            a, o = (0, 0) if t == 0 else (GW * t, 32)
+            for b in range(4):
+                bk = ("PCC", "PD")[b % 2]
+                mm(bk, ("WC", 128 * b), ("LD", a), 128)
+                act(r("H0", b, 4 * GW, 4), r(bk, o, o + GW), scale=0.015625)
+            spread("HT", "H0")
 
-        def slot_copies():
-            while pend:
-                A = pend.pop(0)
-                act(r("SL", C * A, C * A + C), r("PCC" if A % 2 == 0 else "PD", 0, C), bias=float(C * A - 1))
-
-        onS = [[scores_at(0)], [scores_at(1)], [gates], [], [], [orders2]]
-        onV = [[list1], [list2], [order(0)], [pass_on, order(1)], [orders], []]
-        if t == 0:
-            setup_classes()
-            for k in range(3): onS[k].append(lambda k=k: setup_hops(k))
-            onS[3].append(setup_tables)
-            for k in range(3):
-                onS[1 + k].append(lambda k=k: setup_ends_s(k))
-                onS[2 + k].append(lambda k=k: setup_ends(k))
-            onV[0].append(lambda: quant_tiles("cls0", "cls3"))
-            onV[0].append(setup_routes)
-            onV[3].append(lambda: quant_tiles("hop0", "hop2"))
-            onV[4].append(lambda: quant_tiles("hopf0", "gb"))
-            onV[5].append(setup_layer)
-        for i in range(SWEEPS):
-            tt(r("MA"), r("PV0", 0, 96), r("G3"), OP.max)
-            tt(r("MB"), r("PV1", 0, 96), r("MA"), OP.max)
-            tt(r("MC"), r("PV2", 0, 96), r("MB"), OP.max)
-            tt(r("TU"), r("PV3", 0, 96), r("MC"), OP.is_ge)
-            if t == 0 or i: state()
-            masked(r("TU"))
-            ts(r("IN", 0, 4 * 96, 4), r("MC"), -1.0 / 3.0, OP.mult, 1.0, OP.add)
-            quant("QIN", 0, 128, r("IN"))
-            gather_w(VSWEEP[i])
-            slot_copies()
-            for f in onS[i]: f()
-            inject(False)
-            for f in onV[i]: f()
-            quant("QGA", 0, 288, r("GA", 0, 1152))
-            for k in range(3): mm("PV%d" % k, K("came%d" % k), ("QGA", 96 * k), 128, False, True)
-            for k in range(3): mm("PV3", K("own%d" % k), ("QGA", 96 * k), 128, False, k == 2)
-            slots(SLOTS[i])
-        for k in range(3): tt(r("va%d" % k), r("PV%d" % k, 0, 96), r("R%d" % k), OP.min)
-        if t < R - 1:
-            state()
-            act(r("IN", 0, 4 * 96, 4), r("PV0", 0, 96), scale=0.0)
+        un = lambda b: (lambda: unpack(b))
+        onS = [[un(0), un(1), no_slots], [un(2), un(3), lambda: spread("FT", "F0"), gates], [stay], [], [], []]
+        onV = [[in_order], [gate_list, slots], [pass_on], [lambda: quant("QG2", 0, 128, r("G2"))], [], []]
+        if t:
+            onS[2].append(order0)
+            onV[3].append(order1)
+            onV[4].append(order2)
+            onS[5].append(weights)
         else:
-            ts(r("ba"), r("PV3", 0, 96), 1.0, OP.is_ge, P("bit"), OP.mult)
-            ts(r("bb"), r("PV3", 0, 96), -1.0, OP.is_le, P("bit8"), OP.mult)
-        for k in range(3): tt(r("mx%d" % k), r("va%d" % k), r("G9") if k == 0 else r("mx%d" % (k - 1)), OP.max)
-        for k in range(3): tt(r("pk%d" % k), r("va%d" % k), r("mx2"), OP.is_ge)
-        tt(r("self"), r("mx2"), r("G9"), OP.is_equal)
-        tt(r("SJ"), r("self"), r("JC"), OP.mult)
-        for k in range(3): tt(r("t%d" % k), r("pk%d" % k), r("OC%d" % k), OP.mult)
-        tt(r("ua"), r("t0"), r("SJ"), OP.add)
-        tt(r("ub"), r("t1"), r("t2"), OP.add)
-        tt(r("PP"), r("ua"), r("ub"), OP.add)
-        masked(r("PP"))
-        gather_w(VHOP)
-        slot_copies()
-        quant("QW", 0, 128, r("W"))
-        mm("PV3", K("hopf0"), ("QW", 0), 128)
-        quant("QGA", 0, 288, r("GA", 0, 1152))
-        for k in range(3): mm("PV%d" % k, K("hop%d" % k), ("QGA", 96 * k), 128)
-        slots(SLOTS[SWEEPS])
-        to_list(r("PV3", 0, 96), r("DL"))
-        for k in range(3): tt(r("t%d" % k), r("PV%d" % k, 0, 96), r("pk%d" % k), OP.mult)
-        tt(r("ua"), r("t0"), r("SJ"), OP.add)
-        tt(r("ub"), r("t1"), r("t2"), OP.add)
-        tt(r("PP"), r("ua"), r("ub"), OP.add)
-        masked(r("PP"))
-        quant("QW", 0, 128, r("W"))
-        mm("PV2", K("ct2"), ("QW", 0), 128)
-        mm("PV0", K("ct0"), ("QW", 0), 128)
-        mm("PA", K("hopf0"), ("QW", 0), 128)
-        mm("PV1", K("ct1"), ("QW", 0), 128)
-        mm("PV3", K("ct3"), ("QW", 0), 128)
-        slot_copies()
+            for b in range(4): quant("QF", 128 * b, 128 * b + 128, r("FB", 3 - b, 515 - b))
+            setup_factors()
+            onS[0].insert(0, setup_slots)
+            onS[1].append(setup_aways)
+            onV[2].append(lambda: quant_tiles("ad", "st"))
+            onV[2].append(lambda: ts(r("HD4"), r("I4"), pk, OP.is_equal))
+            onV[2].append(setup_ends)
+            onS[3].append(setup_routes)
+            for e in range(4): onS[1 + e].append(lambda e=e: setup_short(e))
+            onV[5].append(lambda: quant_tiles("lg", "dl2"))
+            onS[5].append(weights)
+        done = 0
+        for i in range(SWEEPS):
+            pass
+            bk, nb = ("LA", "LB")[i % 2], ("LB", "LA")[i % 2]
+            past = (first if i < 3 else [(EB(0), ("QC2", 0))]) + [x for j in range(0 if i < 3 else 2, i) for x in moved(j, "lo", "lc")]
+            if i < SWEEPS - 1: sums(nb, past, True, False)
+            for s in range(4): ts(r("W", s, C, 4), r(bk, 0, 96), P("mn", s), OP.max, P("mk", s), OP.min)
+            if i == 2: act(r("C2", 0, C, 4), r(bk, 0, 96))
+            quant("QW", 128 * i, 128 * i + 128, r("W"))
+            n = VSWEEP[i]
+            act(r("GA", n, 1152), r("W", 0, C), off=r("OFS", n // 16, 72))
+            tc(r("GA", 0, n), r("W", 0, C), off=r("OFS", 0, n // 16))
+            n = 320 if t == 0 else 288
+            quant("QD", 320 * i, 320 * i + n, r("GA", 0, 4 * n))
+            if i < SWEEPS - 1: sums(nb, moved(i, "lo", "lc"), False, True)
+            if i == 2: quant("QC2", 0, 128, r("C2"))
+            if t or i >= 3:
+                if done == 0: sums("AB", [(K("ad"), ("QRF", 0)) if t == 0 else (EB(1), ("QIN", 0))], True, False)
+                for j in range(done, i + 1): sums("AB", moved(j, "ao", "ac"), False, j == SWEEPS - 1)
+                done = i + 1
+            for f in onV[i]: f()
+            for f in onS[i]: f()
+        pass
+        tt(r("VT", 0, C, 4), r("AB", 0, 96), r("WW"), OP.mult)
+        quant("QVT", 0, 128, r("VT"))
+        sums("PA", [(K("lg"), ("QG2", 0)), (K("lv"), ("QVT", 0))])
+        ts(r("IN", 1, C, 4), r("AB", 0, 96), P("thr"), OP.is_gt, P("two"), OP.mult)
+        tt(r("PT", 0, C, 4), r("PA", 0, 96), r("OCL"), OP.min)
+        tt(r("PT", 1, C, 4), r("PA", 0, 96), r("OCH"), OP.min)
+        ts(r("PT", 2, C, 4), r("PA", 0, 96), P("cls"), OP.min)
+        ts(r("PT", 3, C, 4), r("PA", 0, 96), -1.0, OP.mult, 0.0, OP.max)
+        quant("QPT", 0, 128, r("PT"))
+        four = ("LA", "LB", "PCC", "PD")
+        for A in (0, 2): mm(four[A], K("ct%d" % A), ("QPT", 0), 128)
+        sums("PA", [(K("dl1"), ("QPT", 0)), (K("dl2"), ("QPT", 0))])
+        for A in (1, 3): mm(four[A], K("ct%d" % A), ("QPT", 0), 128)
+        sums("PB", [(EB(0), ("QC2", 0)), (K("lg"), ("QG", 0))] + [x for j in range(2, SWEEPS) for x in moved(j, "lo", "lc")])
         for A in (2, 3, 0, 1):
             for s in range(4):
-                o, x = r("WA", C * A + s, C * A + C, 4), r("PV%d" % A, 0, 96)
-                if A < 2: ts(o, x, P("ms%d" % s), OP.mult)
-                else: act(o, x, scale=P("ms%d" % s))
-        to_list(r("PA", 0, 96), r("EL"))
-        act(r("GA", 192, C), r("WA"), off=r("EL", 12, 24))
-        tc(r("GA", 0, 192), r("WA"), off=r("EL", 0, 12))
-        for b in range(4):
-            act(r("FD", C * b, C * b + C), r("FT", 1536 * b, 1536 * b + 1536), off=r("DL"))
-        quant("QG", 0, 128, r("GA", 0, 512))
-        mm("PB", K("hopf0"), ("QG", 0), 128)
-        a, o = (0, 0) if t == 0 else (GW * t, 32)
-        for j in range(8):
-            two = [("PV0", "PV1", "PV2", "PV3")[2 * (j % 2) + i] for i in range(2)]
-            for i in range(2): mm(two[i], ("WP", 256 * j + 128 * i), ("LD", a), 128)
-            for i in range(2):
-                b, A = j // 2, 2 * (j % 2) + i
-                act(r("HT", 1536 * b + C * A, 1536 * b + C * A + GW), r(two[i], o, o + GW), scale=0.015625)
-        to_list(r("PB", 0, 96), r("EL"))
+                o, x = r("WA", FS * A + s, FS * A + C, 4), r(four[A], 0, 96)
+                if A < 2: ts(o, x, P("ms", s), OP.mult)
+                else: act(o, x, scale=P("ms", s))
+            if A == 0: to_list("PA", "DL")
+        pass
+        for j, (a, b) in enumerate((("DL", "L2"), ("L2", "L3"), ("L3", "EL"))):
+            act(r("GS", VSTEP, C), r("WA"), off=r(a, VSTEP // 16, 24))
+            tc(r("GS", 0, VSTEP), r("WA"), off=r(a, 0, VSTEP // 16))
+            quant("QS", 0, 128, r("GS"))
+            mm("PA", K("st"), ("QS", 0), 128)
+            act(r("FD", C * j, C * j + C), r("FT", C * j), off=r("DL"))
+            if j == 0:
+                act(r("IN", 0, C, 4), r("PB", 0, 96))
+                layer()
+            to_list("PA", b)
+        pass
+        act(r("SG"), r("FT", 4 * C), off=r("EL"))
+        act(r("FD", 3 * C, 4 * C), r("FT", 3 * C), off=r("DL"))
         if t == R - 1:
-            tc(r("PE"), r("PB", 0, 96))
-            number_parts()
-        tt(r("SB2"), r("SL"), r("MD"), OP.mult, off=r("EL"))
-        scan(r("ST2"), r("ND"), r("SB2"))
-        tc(r("HL"), r("ST2", 15, C, 16))
+            act(r("OUT", 0, C), r("NODE"), bias=P("h768"), off=r("EL"))
+            quant("QIN", 0, 128, r("IN"))
+            mm("PB", K("nm"), ("QIN", 0), 128)
         for b in range(4):
-            tt(r("Z", C * b, C * b + C), r("FT", 1536 * b, 1536 * b + 1536), r("FD", C * b, C * b + C), OP.add, off=r("EL"))
+            tt(r("Z", C * b, C * b + C), r("FT", C * b), r("FD", C * b, C * b + C), OP.add, off=r("EL"))
+            if b == 0:
+                scan(r("ST2"), r("HD"), r("SG"), OP.add, OP.max)
+                for j in range(4): ts(r("HL%d" % j), r("ST2", 15, C, 16), 4.0, OP.mult, P("hb%d" % j), OP.add)
+        if t == R - 1:
+            ts(r("BN"), r("PB", 0, 96), 0.5, OP.is_gt, P("bit8"), OP.mult)
+            act(r("BA"), r("IN", 1, C, 4), scale=P("bit"))
+            for s in range(4):
+                act(r("ND", 4 * s, 4 * C, 16), r("BA"), scale=P("ms", s))
+                act(r("ND", 4 * s + 1, 4 * C, 16), r("BN"), scale=P("ms", s))
         for b in range(4):
-            tt(r("X0", b, 4 * C, 4), r("HT", 1536 * b, 1536 * b + 1536), r("Z", C * b, C * b + C), OP.add, off=r("HL"))
+            tt(r("X0", b, 4 * C, 4), r("HT"), r("Z", C * b, C * b + C), OP.add, off=r("HL%d" % b))
         quant("QX", 0, C, r("X0"))
         if t == 0: quant("QV", 0, 128, r("VV"))
+    pass
     mm("PA", ("QV", 0), ("QX", 0), C)
-    act(r("TS", 2 * C, 3 * C), r("PA", 0, C))
-    dma("Y", "d7", [(T.oc[:], T.QXc[:, 0:C].bitcast(dt.uint8))] + [(T.osc[4 * k:4 * k + 4, :], T.QXs[32 * k:32 * k + 4, 0:C]) for k in range(4)], rd=[r("QXc"), r("QXs")])
-    dma("Y", "d8", [(T.y[:], T.TS[:, 2 * C:3 * C])], rd=[r("TS", 2 * C, 3 * C)])
-    quant("QND", 0, C, r("ET"))
-    mm("PB", K("ge"), ("QND", 0), C, True, False)
-    mm("PB", K("gm"), ("QND", 0), C, False, True)
-    mm("PCC", K("gb"), ("QND", 0), C)
-    act(r("TS", 0, C), r("PB", 0, C))
-    act(r("TS", C, 2 * C), r("PCC", 0, C))
-    dma("Y", "d9", [(T.nd[:], T.TS[0:128:16, 0:2 * C])], rd=[r("TS", 0, 2 * C)])
+    act(r("OUT", 2 * C, 3 * C), r("PA", 0, C))
+    dma("Y", [(T.oc[:], T.QXc[:, 0:C].bitcast(dt.uint8))] + [(T.osc[4 * k:4 * k + 4, :], T.QXs[32 * k:32 * k + 4, 0:C]) for k in range(4)], rd=[r("QXc"), r("QXs")])
+    dma("Y", [(T.y[:], T.OUT[:, 2 * C:3 * C])], rd=[r("OUT", 2 * C, 3 * C)])
+    quant("QND", 0, C, r("ND"))
+    mm("PB", K("gone"), ("QND", 0), C)
+    act(r("OUT", C, 2 * C), r("PB", 0, C))
+    dma("Y", [(T.nd[:], T.OUT[0:128:16, 0:2 * C])], rd=[r("OUT", 0, 2 * C)])
     for s in SEMAPHORES:
         if cnt[s]: g.wait_ge(T.sem[s], cnt[s])

@@ -7,23 +7,28 @@ COPY, IDENT = FN.Copy, FN.Identity
 C, GW, R, SWEEPS = 384, 96, 3, 6
 JUMP = [0, 1, 4]
 
-T1 = ["ld", "lo", "lc0", "lc1", "lc2", "ad", "ao", "ac0", "ac1", "ac2", "ord", "st"]
+T1A, T1B = ["ld", "lo", "lc0", "lc1", "lc2"], ["ad", "ao", "ord", "st", "ac0", "ac1", "ac2"]
 T2 = ["gs", "lg", "lv", "nm", "dl1", "ct0", "ct1", "ct2", "ct3", "dl2"]
-TILES = T1 + T2 + ["gone"]
+TILES = T1A + T1B + T2 + ["gone"]
 TI = {n: i for i, n in enumerate(TILES)}
 NT = len(TILES)
-ELEM = [("gs", "ct3"), ("nm", "ct3"), ("ct0", "dl2"), ("dl1", "dl2")]
+ROOM = {n: 512 * i for l in (T1A, T1B + T2 + ["gone"]) for i, n in enumerate(l)}
+ELEM = [("lg", "ct3"), ("nm", "ct3"), ("ct0", "dl2"), ("dl1", "dl2")]
 FS = 5 * C
 HOLD, DROP = 8192.0, 1048576.0
-VSWEEP = [512, 512, 512, 512, 512, 512]
+FBANK = ["PA", "PB", "AB", "PA"]
+VSWEEP = [0, 448, 320, 320, 512, 512]
+VFIRST = [0, 448, 192, 256, 0, 256]
 VSTEP = 192
-SOWN = 3
+SOWN = [2, 3, 3]
+VSUM = 1
+PAIRED = [3]
 ENGINES = 8
 
 F32, BF, I32, U16, X4, U8 = "float32", "bfloat16", "int32", "uint16", "float8_e4m3fn_x4", "uint8"
 SCRATCH = {}
-WIDE = {"KF": "JM MD MX NX HD HD4 I4 IJF CONST SLS", "KI": "PC UL X16 XA XB2", "KB": "WT DGR GC0 GCT GCA GDT CF CF2 GW1 GW2 OCL OCH ML Y",
-        "XF": "SB1 ST ST2 ST3 ST4 RS RC PL GF NS", "XB": "CS WW BT BA BN JK TM",
+WIDE = {"KF": "JM MD MX NX HD HD4 I4 IJF CONST SLS", "KI": "PC UL X16 XA XB2", "KB": "WT DGR GCT GCA GDT CF CF2 GW1 GW2 OCL OCH ML Y ALT",
+        "XF": "SB1 ST ST2 ST3 ST4 RS RC PL GF NS", "XB": "CS WW BA BN JK TM", "ZT": "G IN C2 G2 VT ND",
         "XU": "PLo ELo DL L2 L3 EL HL0 HL1 HL2 HL3", "KU": "ULo OFJ OFS"}
 HOME = {n: w for w in WIDE for n in WIDE[w].split()}
 PLACE, LEN = {}, {}
@@ -46,20 +51,20 @@ CA = [sum(CW[:j]) for j in range(7)]
 for _n, _w, _d in [
         ("X0", 1536, BF), ("U", 512, BF), ("VV", 512, BF), ("LKT", 72, I32), ("LKS", 72, I32), ("LK2", 96, I32),
         ("ULo", 24, U16), ("OFJ", 72, U16), ("OFS", 72, U16), ("UL", 24, I32), ("PC", 16, I32), ("X16", 96, I32), ("XA", 96, I32), ("XB2", 96, I32),
-        ("PF", 96, F32), ("WT", 512, BF), ("ZB", 1024, BF), ("CB", 512 * NT, BF), ("FB", 516, BF), ("GOt", 512, BF),
-        ("DGR", 32, BF), ("GC0", 32, BF), ("GCT", 64, BF), ("GCA", C, BF), ("GDT", 128, BF), ("CF", C, BF), ("CF2", 1280, BF), ("GW1", C, BF), ("GW2", 320, BF),
-        ("OCL", 96, BF), ("OCH", 96, BF), ("ML", C, BF), ("Y", C, BF),
+        ("PF", 96, F32), ("WT", 512, BF), ("ZB", 512, BF), ("CB", ROOM["gone"] + 512, BF), ("FB", 516, BF), ("GOt", 512, BF),
+        ("DGR", 32, BF), ("GCT", 64, BF), ("GCA", 32, BF), ("GDT", 128, BF), ("CF", C, BF), ("CF2", 1280, BF),
+        ("OCL", 96, BF), ("OCH", 96, BF), ("ML", C, BF), ("Y", C, BF), ("ALT", 2 * C, BF),
         ("JM", C, F32), ("MD", C, F32), ("MX", C, F32), ("NX", C, F32), ("HD", C, F32), ("HD4", 96, F32), ("I4", 96, F32), ("IJF", C, F32),
-        ("CONST", 24, F32), ("SLS", 96, F32), ("RST", C, BF), ("NODE", 3 * FS + C, F32),
+        ("CONST", 24, F32), ("SLS", 96, F32), ("RST", C, BF), ("NODE", 3 * FS + C, F32), ("SLF", C, BF),
         ("TS", C, F32), ("W0", C, F32), ("W1", C, F32), ("W2", C, F32), ("BASE", C, F32), ("A0", C, F32), ("A1", C, F32), ("RF", 512, BF), ("RG", C, BF),
         ("SB1", C, F32), ("ST", C, F32), ("ST2", C, F32), ("ST3", GW, F32), ("ST4", 96, F32), ("RS", 24, F32), ("RC", 24, F32), ("PL", 24, F32),
-        ("GF", 24, F32), ("NS", 24, F32), ("CS", C, BF), ("WW", 96, BF), ("BT", 96, BF), ("BA", 96, BF), ("BN", 96, BF), ("JK", C, BF), ("TM", 2 * C, BF),
+        ("GF", 24, F32), ("NS", 24, F32), ("CS", C, BF), ("WW", 96, BF), ("BA", 96, BF), ("BN", 96, BF), ("JK", C, BF), ("TM", 2 * C, BF),
         ("PLo", 24, U16), ("ELo", 6, U16), ("DL", 24, U16), ("L2", 24, U16), ("L3", 24, U16), ("EL", 24, U16),
         ("HL0", 24, U16), ("HL1", 24, U16), ("HL2", 24, U16), ("HL3", 24, U16),
-        ("CT", 4 * CA[6], BF), ("G", 512, BF), ("G2", 512, BF), ("W", 512, BF), ("GA", 1280, BF), ("C2", 512, BF), ("IN", 512, BF),
-        ("VT", 512, BF), ("PT", 512, BF), ("GS", 512, BF), ("WA", 3 * FS + C, BF), ("LW", C, F32), ("SG", C, BF),
-        ("F0", FS, BF), ("FT", 4 * FS, BF), ("H0", 512, BF), ("HT", 2048, BF), ("FD", 4 * C, BF), ("Z", 4 * C, BF),
-        ("E", 512, BF), ("ND", 4 * C, BF), ("OUT", 3 * C, F32)]:
+        ("CT", 4 * CA[6], BF), ("G", 512, BF), ("IN", 512, BF), ("C2", 512, BF), ("G2", 512, BF), ("VT", 512, BF), ("ND", 4 * C, BF),
+        ("W", 512, BF), ("GA", 1280, BF), ("PT", 512, BF), ("GS", 512, BF), ("WA", 3 * FS + C, BF), ("LW", C, F32), ("SG", C, BF),
+        ("F0", FS, BF), ("FT", 4 * FS, BF), ("H0", 512, BF), ("HT", 2048, BF), ("FD", 8 * C, BF), ("Z", 8 * C, BF),
+        ("E", 512, BF), ("OUT", 3 * C, F32)]:
     sb(_n, _w, _d)
 for _n, _w in [("QX", C), ("QU", 128), ("QUP", C), ("QV", 128), ("WC", 512), ("QK", 128 * NT), ("QF", 512), ("QT", CA[6]),
                ("QG", 128), ("QG2", 128), ("QRF", 128), ("QW", 128 * SWEEPS), ("QD", 320 * SWEEPS), ("QC2", 128), ("QIN", 128),
@@ -69,7 +74,7 @@ PS = ["PA", "PB", "PCC", "PD", "LA", "LB", "AB", "PE"]
 for _n in PS:
     SCRATCH[_n] = ("psum", [128, 512], F32)
     PLACE[_n], LEN[_n] = (_n, 0), 512
-SEMAPHORES = ["sv", "ss", "st", "sg", "lcl", "arr0", "arr1", "arr2"] + ["d%d" % i for i in range(20)]
+SEMAPHORES = ["sv", "ss", "st", "sg", "lcl", "arr0", "arr1", "arr2"] + ["d%d" % i for i in range(30)]
 
 
 def rank_program(g, core, T, topo):
@@ -167,6 +172,7 @@ def rank_program(g, core, T, topo):
 
     isr = lambda x: isinstance(x, tuple)
     val = lambda x: ap(x) if isr(x) else x
+    size = lambda o: len(range(o[1], o[2], o[3]))
 
     def ts(o, i, s1, op0, s2=None, op1=None):
         rd = [i] + [s for s in (s1, s2) if isr(s)]
@@ -183,6 +189,9 @@ def rank_program(g, core, T, topo):
 
     def scatter(win, off, a):
         do("V", lambda e: e.tensor_copy(ap(win).indirect(ap(off)), ap(a)), [a, off], [win])
+
+    def total(o, a):
+        do("V", lambda e: e.tensor_reduce(ap(o), ap(a), AxisListType.X, OP.add), [a], [o])
 
     def act(o, a, bias=0.0, scale=1.0, off=None, fn=COPY, acc=None):
         rd = [a] + [x for x in (scale, bias, off) if isr(x)]
@@ -221,17 +230,17 @@ def rank_program(g, core, T, topo):
         else: do("G", lambda e: e.iota(ap(o), pat, base, cm), [], [o])
 
     def const(o, c):
-        iota(o, [[0, len(range(o[1], o[2], o[3]))]], c)
+        iota(o, [[0, size(o)]], c)
 
     def sel(o, i, pat, op, fl, base, cm):
         do("G", lambda e: e.affine_select(ap(o), ap(i), pat, op, fl, base, cm), [i], [o])
 
-    def zero(o):
-        act(o, r("ZB", 0, len(range(o[1], o[2], o[3]))))
+    def zeros(*xs):
+        pairs = [(T[n][:, a:min(a + 512, hi)], T.ZB[:, 0:min(512, hi - a)]) for n, lo, hi, _ in xs for a in range(lo, hi, 512)]
+        dma("Y", pairs, rd=[r("ZB")], wr=xs)
 
     K = lambda n: ("QK", 128 * TI[n])
     EB = lambda b: ("QF", 128 * b)
-    tile0 = lambda n: 512 * TI[n]
     col = lambda n, j: r(n, j, j + 1)
     PFC = {}
 
@@ -244,18 +253,24 @@ def rank_program(g, core, T, topo):
     GRP = {0: ([[16, 8]], 0), 1: ([[32, 4], [-16, 2]], 16), 4: ([[-64, 2], [16, 4]], 64)}
     CLS = lambda A: 16 * (A & 1) + 64 * (A >> 1)
     neg = lambda pat: [[-a, b] for a, b in pat]
+    row = lambda j: col("MD", j)
+    cf = lambda n: r("CF", 32 * TI[n], 32 * TI[n] + 32)
+    c2 = lambda e, n, a=0, st=1: r("CF2", 320 * e + 32 * T2.index(n) + a, 320 * e + 32 * T2.index(n) + 32, st)
 
-    dma("Y", [(T.X0[:], T.x[:])], wr=[r("X0")])
     dma("S", [(T.U[:], T.u[:])], wr=[r("U")])
+    dma("Y", [(T.X0[:], T.x[:])], wr=[r("X0")])
     dma("Y", [(T.LKT[:], T.lk[:])], wr=[r("LKT")])
     fill(r("ZB"), 0.0)
     fill(r("WT"), 1.0)
+    iota(r("PC", 0, 1), [[0, 1]], 0, 1)
     for k in range(3):
         iota(r("UL", 8 * k, 8 * k + 8), GRP[JUMP[k]][0], GRP[JUMP[k]][1])
-    iota(r("PC", 0, 1), [[0, 1]], 0, 1)
     iota(r("JM"), [[0, 24], [1, 16]], 0)
     iota(r("I4"), [[0, 24], [1, 4]], 0)
     iota(r("LK2"), [[4, 4], [16, 24]], 0)
+    for a in range(0, 4 * C, 512): act(r("CT", a, a + 512), r("ZB"))
+    zeros(*[r("CT", 4 * CA[j] + 256 * j, 4 * CA[j + 1]) for j in range(1, 6)])
+    zeros(r("CB", 0, ROOM["ad"] + 512 * 5), r("CB", ROOM["gs"], ROOM["lg"]), r("G"), r("W", C), r("RF", C), r("GA", 1152), r("FB"))
     pr = [(T.LKS[:, 0:24], T.lk[:, 0:24])]
     for h in range(8):
         a = h ^ JUMP[1]
@@ -264,49 +279,54 @@ def rank_program(g, core, T, topo):
         a = h ^ JUMP[2]
         pr.append((T.LKS[16 * h:16 * h + 64, 48:72], T.lk[16 * a:16 * a + 64, 48:72]))
     dma("Y", pr, wr=[r("LKS")])
-    za, zb = tile0("ad"), tile0("gone")
-    dma("Y", [(T.CB[:, a:min(a + 1024, zb)], T.ZB[:, 0:min(1024, zb - a)]) for a in range(za, zb, 1024)], rd=[r("ZB")], wr=[r("CB", za, zb)])
-    dma("Y", [(T.WCc[:].bitcast(dt.uint8), T.wc[:]), (T.WCs[:], T.ws[:]), (T.VV[:], T.v[:])], wr=[r("WCc"), r("WCs"), r("VV")])
+    zeros(r("CB", 512 * 5, ROOM["gs"]), r("CB", ROOM["lg"], ROOM["gone"]), r("C2"), r("G2"), r("E", C))
     dma("Y", [(T.LK2[4 * k + s:128:16, 24 * q:24 * q + 24], T.lk[4 * q + s:128:16, 24 * k:24 * k + 24]) for k in range(3) for q in range(4) for s in range(4)], wr=[r("LK2")])
-    dma("Y", [(T.WA[:, a:a + 1024], T.ZB[:]) for a in range(0, LEN["WA"], 1024)] + [(T.ND[:, 0:1024], T.ZB[:]), (T.ND[:, 1024:1536], T.ZB[:, 0:512])],
-        rd=[r("ZB")], wr=[r("WA"), r("ND")])
+    zeros(r("VT"), r("IN"), r("PT", C), r("GS", C), r("H0", C), r("ND"))
+    dma("Y", [(T.WCc[:].bitcast(dt.uint8), T.wc[:]), (T.WCs[:], T.ws[:]), (T.VV[:], T.v[:])], wr=[r("WCc"), r("WCs"), r("VV")])
 
-    tc(r("ULo"), r("UL"))
     p = col("PC", 0)
     for j, (sh, an) in enumerate([(0, 15), (0, 3), (2, 3), (4, 1), (5, 1), (6, 1)]):
         ts(col("PC", j + 1), p, sh, OP.arith_shift_right, an, OP.bitwise_and)
     tc(pcol("p", 6), r("PC", 1, 7))
     pi, ps, pk, g0, g1, g2 = [P("p", j) for j in range(6)]
-    ts(r("MD"), r("JM"), pi, OP.is_equal)
-    act(r("MX"), r("MD"), scale=-2e29, bias=1e29)
-    act(r("NX"), r("MD"), scale=2e29)
-    for a in range(0, 1536, 768): zero(r("CT", a, a + 768))
-    zero(r("FB"))
-    sel(r("NX"), r("NX"), [[0, 24], [1, 16]], OP.not_equal, 2e29, 0, 0)
-    sel(r("GOt"), r("WT"), [[-16, 8], [0, 64]], OP.is_ge, 0.0, 0, 1)
-    sel(r("CB", zb, zb + 512), r("GOt"), [[16, 8], [0, 64]], OP.is_ge, 0.0, 15, -1)
+    tc(r("ULo"), r("UL"))
     fill(r("RST"), 1.0)
     fill(r("RST", 0, C, 16), 0.0)
     fill(col("RS", 0), 0.0)
-    for j in range(1, 6): fill(r("CT", 4 * CA[j] + 256 * j, 4 * CA[j + 1]), 0.0)
+    ts(r("MD"), r("JM"), pi, OP.is_equal)
+    act(r("MX"), r("MD"), scale=-2e29, bias=1e29)
+    act(r("NX"), r("MD"), scale=2e29)
+    ts(pcol("ms", 4), r("I4", 0, 4), ps, OP.is_equal)
+    ts(pcol("mr", 4), r("I4", 0, 4), pk, OP.is_equal)
+    ts(r("DGR"), r("I4", 0, 32), pk, OP.is_equal)
     quant("QU", 0, 128, r("U"))
     pick("QUP", "QU", r("ULo"))
-    quant("QX", 0, C, r("X0"))
-    row = lambda j: col("MD", j)
+    fill(r("NX", 0, C, 16), 2e29)
+    a = ROOM["gone"]
+    sel(r("GOt"), r("WT"), [[-16, 8], [0, 64]], OP.is_ge, 0.0, 0, 1)
+    sel(r("CB", a, a + 512), r("GOt"), [[16, 8], [0, 64]], OP.is_ge, 0.0, 15, -1)
+    iota(r("IJF"), [[1, C]], 0)
+    iota(r("LW"), [[1, C]], 0)
+    iota(r("CONST"), [[16, 24]], 0)
+
+    def group_mask(o, c, src=None):
+        gp, gb = GRP[c]
+        n = size(o) // 32
+        rep = [[0, n]] if n > 1 else []
+        x = r("GOt", 0, 32 * n)
+        sel(x, src or o, rep + neg(gp) + [[0, 4]], OP.is_ge, 0.0, -gb, 1)
+        sel(o, x, rep + gp + [[0, 4]], OP.is_ge, 0.0, gb + 15, -1)
+
+    group_mask(r("GCA"), 0, r("WT", 0, 32))
 
     def setup_columns():
-        ts(pcol("ms", 4), r("I4", 0, 4), ps, OP.is_equal)
-        ts(pcol("mr", 4), r("I4", 0, 4), pk, OP.is_equal)
         act(pcol("n3"), P("mr", 3), scale=-1.0, bias=1.0)
         act(pcol("mk", 4), PV("ms"), scale=P("n3"))
         act(pcol("mn", 4), PV("mk"), scale=-1.0)
         act(pcol("m7", 4), PV("mr"), scale=-7.0)
-        act(pcol("m512", 4), PV("mr"), scale=512.0)
-        act(pcol("m29", 4), PV("mr"), scale=512.0 * 29)
         act(pcol("k16"), pi, scale=HOLD, bias=-15 * HOLD)
-        act(pcol("k4"), pk, scale=HOLD, bias=-3 * HOLD)
-        act(pcol("kc"), pi, scale=HOLD - 1, bias=-15 * (HOLD - 1))
-        act(r("CONST"), r("CONST"), bias=P("kc"))
+        act(pcol("kc"), pi, scale=1 - HOLD, bias=15 * (HOLD - 1) + GW - 0.5)
+        act(r("CONST"), r("CONST"), scale=-1.0, bias=P("kc"))
         act(r("HD"), r("MD"), scale=-DROP - HOLD, bias=HOLD)
 
     def setup_rows():
@@ -314,107 +334,85 @@ def rank_program(g, core, T, topo):
         act(pcol("sg2"), g2, scale=-2.0, bias=1.0)
         act(pcol("p4"), row(4), scale=P("sg1"))
         act(pcol("p8"), row(8), scale=P("sg2"))
+        act(pcol("ys"), row(1), scale=-2.0, bias=row(0))
         ts(pcol("wa"), row(0), row(1), OP.subtract, row(2), OP.subtract)
         ts(pcol("w0"), P("wa"), row(10), OP.subtract)
+        ts(pcol("ya"), row(4), g0, OP.mult, row(1), OP.subtract)
+        ts(pcol("yb"), row(8), g2, OP.mult, P("ya"), OP.add)
+        ts(pcol("da"), row(0), row(1), OP.add, row(4), OP.add)
         ts(pcol("w1"), row(6), row(2), OP.subtract, P("p4"), OP.subtract)
         ts(pcol("w2"), row(6), row(10), OP.add, P("p8"), OP.add)
         ts(pcol("ba"), row(0), row(1), OP.subtract, P("p4"), OP.add)
         act(pcol("base"), P("ba"), bias=P("p8"))
-        act(pcol("ys"), row(1), scale=-2.0, bias=row(0))
-        ts(pcol("ya"), row(4), g0, OP.mult, row(1), OP.subtract)
-        ts(pcol("yb"), row(8), g2, OP.mult, P("ya"), OP.add)
         act(pcol("y"), P("yb"), scale=-1.0, bias=1.0)
-        ts(pcol("da"), row(0), row(1), OP.add, row(4), OP.add)
         act(pcol("dr"), P("da"), bias=row(8))
 
-    iota(r("IJF"), [[1, C]], 0)
-    iota(r("CONST"), [[16, 24]], 0)
-    cf = lambda n: r("CF", 32 * TI[n], 32 * TI[n] + 32)
-    gca = lambda n: r("GCA", 32 * TI[n], 32 * TI[n] + 32)
+    def lay(names):
+        a, n = 32 * TI[names[0]], len(names)
+        x = r("CF", a, a + 32 * n)
+        group_mask(r("CF", a, a + 32 * (n - 2)), 0)
+        for k in (1, 2): group_mask(cf(names[k - 3]), JUMP[k])
+        for s in range(4): sel(r("CB", 5 * s, 512 * n, 16), x, [[0, 32 * n]], OP.is_ge, 0.0, 0, 0)
 
-    def group_mask(o, c, n=1):
-        gp, gb = GRP[c]
-        rep = [[0, n]] if n > 1 else []
-        x = r("GOt", 0, 32 * n)
-        sel(x, r("WT", 0, 32 * n), rep + neg(gp) + [[0, 4]], OP.is_ge, 0.0, -gb, 1)
-        sel(o, x, rep + gp + [[0, 4]], OP.is_ge, 0.0, gb + 15, -1)
-
-    group_mask(r("GCA"), 0, 12)
-    for n in ("lc", "ac"):
-        for k in (1, 2): group_mask(gca("%s%d" % (n, k)), JUMP[k])
-    sel(r("FB", 3, 515, 4), r("WT", 0, 128), [[-1, 128]], OP.is_equal, 0.0, 0, 1)
-    for n in ("G", "W", "RF", "IN", "C2", "G2", "VT", "E", "GS", "PT", "H0"): const(r(n), 0)
-    const(r("GA", 1152, 1280), 0)
-
-    def lay(a, b):
-        a, b = TI[a], TI[b] + 1
-        tt(r("GW1", 32 * a, 32 * b), r("CF", 32 * a, 32 * b), r("GCA", 32 * a, 32 * b), OP.mult)
-        for s in range(4): act(r("CB", 512 * a + 5 * s, 512 * b, 16), r("GW1", 32 * a, 32 * b))
-
-    def quant_tiles(a, b):
-        a, b = TI[a], TI[b] + 1
-        while a < b:
-            n = min(4, b - a)
-            quant("QK", 128 * a, 128 * (a + n), r("CB", 512 * a, 512 * (a + n)))
-            a += n
+    def quant_tiles(names):
+        for j in range(0, len(names), 4):
+            a, n = names[j], len(names[j:j + 4])
+            quant("QK", 128 * TI[a], 128 * (TI[a] + n), r("CB", ROOM[a], ROOM[a] + 512 * n))
 
     def setup_turns():
-        for a in range(0, za, 512): zero(r("CB", a, a + 512))
-        ts(r("DGR"), r("I4", 0, 32), pk, OP.is_equal)
-        ts(r("GCT", 0, 32), r("DGR"), -2.0, OP.mult, -4.0, OP.add)
+        act(r("GCT", 0, 32), r("DGR"), scale=-2.0, bias=-4.0)
         act(cf("ld"), r("GCT", 0, 32), scale=P("dr"))
         act(cf("lo"), r("DGR"), scale=-4.0, bias=-1.0)
         act(r("GCT", 32, 64), r("DGR"), scale=-2.0, bias=3.0)
         for k in range(3): act(cf("lc%d" % k), r("GCT", 32, 64), scale=P("mr", k))
-        lay("ld", "lc2")
-        a = tile0("gs")
-        for s in range(4): act(r("CB", a + 4 * s, a + 512, 16), gca("ld"), scale=P("ms", s))
+        a = ROOM["gs"]
+        for s in range(4): act(r("CB", a + 4 * s, a + 512, 16), r("GCA"), scale=P("ms", s))
 
     def setup_aways():
         act(cf("ad"), r("DGR"), scale=P("dr"))
         act(cf("ao"), r("DGR"), scale=0.5)
         act(r("GCT", 0, 32), r("DGR"), scale=-0.5)
-        fill(r("GCT", 3, 32, 4), 1.0)
+        act(r("GCT", 3, 32, 4), r("WT", 0, 8))
         for k in range(3): act(cf("ac%d" % k), r("GCT", 0, 32), scale=P("mr", k))
         a = 32 * TI["ord"]
-        fill(r("CF", a, a + 32), 0.0)
-        for k, (x, y, op) in enumerate(((2, 10, OP.add), (6, 2, OP.subtract), (6, 10, OP.add))):
+        for k, (x, y, op) in enumerate(((2, 10, OP.add), (6, 2, OP.subtract), (6, 10, OP.add), (0, 0, OP.subtract))):
             ts(r("CF", a + k, a + 32, 4), r("WT", 0, 8), row(x), OP.mult, row(y), op)
-        ts(pcol("sa"), P("mr", 2), float(FS), OP.mult, P("mr", 0), OP.add)
-        ts(cf("st"), r("WT", 0, 32), P("sa"), OP.mult, P("mr", 1), OP.add)
-        lay("ad", "st")
-
-    c2 = lambda e, n, a=0, st=1: r("CF2", 320 * e + 32 * T2.index(n) + a, 320 * e + 32 * T2.index(n) + 32, st)
+        act(pcol("sa"), P("mr", 2), scale=float(FS), bias=P("mr", 0))
+        act(cf("st"), r("WT", 0, 32), scale=P("sa"), bias=P("mr", 1))
 
     def setup_factors():
-        const(r("CF2"), 0)
-        const(c2(0, "gs"), 1)
+        sel(r("FB", 3, 515, 4), r("WT", 0, 128), [[-1, 128]], OP.is_equal, 0.0, 0, 1)
+        a = 32 * T2.index("ct0")
+        for A in range(4):
+            x = r("GDT", 32 * A, 32 * A + 32)
+            sel(x, r("WT", 0, 32), [[0, 2], [-32, 2], [0, 8]], OP.is_ge, 0.0, -CLS(A), 1)
+            sel(r("CF2", 960 + a + 32 * A, 960 + a + 32 * A + 32), x, [[0, 2], [32, 2], [0, 8]], OP.is_ge, 0.0, CLS(A) + 15, -1)
         const(c2(0, "lg"), -1)
         const(c2(0, "lg", 3, 4), 1)
         for e, c in ((0, 1), (1, 1), (3, 2)): const(c2(e, "dl1"), c)
         for e in (2, 3): const(c2(e, "dl2"), FS)
-        a = 32 * T2.index("ct0")
-        for e in range(3): const(r("CF2", 320 * e + a + e, 320 * e + a + 128, 4), 1)
-        const(r("CF2", 960 + a, 960 + a + 128), 1)
-        group_mask(r("GW2"), 0, 10)
-        for A in range(4):
-            x = r("GDT", 32 * A, 32 * A + 32)
-            sel(x, r("WT", 0, 32), [[0, 2], [-32, 2], [0, 8]], OP.is_ge, 0.0, -CLS(A), 1)
-            sel(r("GW2", a + 32 * A, a + 32 * A + 32), x, [[0, 2], [32, 2], [0, 8]], OP.is_ge, 0.0, CLS(A) + 15, -1)
-        iota(r("NODE"), [[4 * C, 2], [C, 2], [1, FS]][0:0] + [[1, LEN["NODE"]]], 0)
+        for e in range(3): sel(r("CF2", 320 * e + a, 320 * e + a + 128), r("CF2", 960 + a, 960 + a + 128), [[0, 32], [1, 4]], OP.is_equal, 0.0, -e, 0)
+        for e, x, y in ((0, "lg", "dl1"), (1, "nm", "dl1"), (2, "dl2", "dl2"), (3, "dl1", "dl1"), (3, "dl2", "dl2")):
+            group_mask(r("CF2", 320 * e + 32 * T2.index(x), 320 * e + 32 * T2.index(y) + 32), 0)
+
+    def setup_nodes():
+        iota(r("NODE"), [[1, LEN["NODE"]]], 0)
         for A in range(1, 4): iota(r("NODE", FS * A, FS * A + C), [[1, C]], C * ((A & 1) + 4 * (A >> 1)))
 
-    def setup_short(e):
-        if e == 0:
-            act(c2(0, "lv"), r("DGR"), scale=2048.0, bias=-1024.0)
-            act(c2(0, "nm"), r("DGR"), scale=-2.0)
-            act(pcol("nb"), P("mr", 3), scale=9.5, bias=-9.0)
-            act(c2(1, "nm"), r("DGR"), scale=-4.0, bias=P("nb"))
-        a, b = T2.index(ELEM[e][0]) + (e == 0), T2.index(ELEM[e][1]) + 1
+    def short_factors():
+        act(c2(0, "lv"), r("DGR"), scale=2048.0, bias=-1024.0)
+        act(c2(0, "nm"), r("DGR"), scale=-2.0)
+        act(pcol("nb"), P("mr", 3), scale=9.5, bias=-9.0)
+        act(c2(1, "nm"), r("DGR"), scale=-4.0, bias=P("nb"))
+
+    def short_lay(e, q="S"):
+        a, b = T2.index(ELEM[e][0]), T2.index(ELEM[e][1]) + 1
         x = r("CF2", 320 * e + 32 * a, 320 * e + 32 * b)
-        tt(x, x, r("GW2", 32 * a, 32 * b), OP.mult)
-        o = tile0("gs")
-        for s in range(4): act(r("CB", o + 512 * a + 4 * s + e, o + 512 * b, 16), x, scale=P("ms", s))
+        o = ROOM["gs"]
+        for s in range(4):
+            y = r("CB", o + 512 * a + 4 * s + e, o + 512 * b, 16)
+            if q == "S": act(y, x, scale=P("ms", s))
+            else: ts(y, x, P("ms", s), OP.mult)
 
     def setup_ends():
         ts(pcol("s3"), ps, P("mr", 3), OP.mult, 16.0, OP.add)
@@ -423,28 +421,39 @@ def rank_program(g, core, T, topo):
         ts(r("XB2"), r("X16"), 992, OP.bitwise_and)
         ts(r("OCL"), r("XA"), -16.0, OP.add)
         tc(r("OCH"), r("XB2"))
+
+    def setup_classes():
         ts(pcol("a1"), g0, P("mr", 1), OP.not_equal)
         ts(pcol("a2"), g2, P("mr", 2), OP.not_equal, 2.0, OP.mult)
+        ts(r("HD4"), r("I4"), pk, OP.is_equal)
 
-    def setup_routes():
-        act(pcol("cls"), P("a1"), bias=P("a2"))
+    def setup_stay():
+        act(pcol("m512", 4), PV("mr"), scale=512.0)
+        act(pcol("m29", 4), PV("mr"), scale=512.0 * 29)
         act(pcol("ws"), P("mr", 2), scale=2.0, bias=-1.0)
         act(pcol("wsc"), P("ws"), scale=P("n3"))
         act(pcol("wb"), pk, scale=-1.0, bias=3.0)
+
+    def setup_routes():
+        act(pcol("cls"), P("a1"), bias=P("a2"))
         act(pcol("thr"), P("mr", 3), scale=-18.0, bias=0.5)
         act(pcol("two"), P("mr", 3), bias=1.0)
         act(r("HD4"), r("HD4"), scale=-DROP - HOLD, bias=HOLD)
+        act(pcol("k4"), pk, scale=HOLD, bias=-3 * HOLD)
+        for b in range(4): act(pcol("hb%d" % b), P("k16"), scale=4.0, bias=1024.0 + b)
+
+    def setup_bits():
         act(pcol("b1"), P("mr", 1), scale=2.0, bias=P("mr", 0))
         act(pcol("bit"), P("mr", 2), scale=4.0, bias=P("b1"))
         act(pcol("bit8"), P("bit"), scale=8.0)
         act(pcol("h768"), g1, scale=2.0 * C)
-        for b in range(4): act(pcol("hb%d" % b), P("k16"), scale=4.0, bias=1024.0 + b)
 
     def setup_slots():
         act(pcol("o1"), g2, scale=2.0, bias=g0)
         act(pcol("o2"), P("o1"), scale=128.0, bias=-256.0)
         act(pcol("o3"), P("o2"), bias=float(GW))
         act(r("SLS"), r("IJF", 0, GW), bias=P("o2"))
+        for x in (r("F0", 4 * C, FS), r("SLF")): act(x, r("IJF"), scale=0.0, bias=P("o3"))
 
     def send(t):
         m = topo.engines(core, nxt)[:ENGINES]
@@ -479,6 +488,11 @@ def rank_program(g, core, T, topo):
     def moved(i, own, came):
         return [(K(own), ("QW", 128 * i))] + [(K("%s%d" % (came, k)), ("QD", 320 * i + 96 * k)) for k in range(3)]
 
+    def no_slots():
+        dma("Y", [(T.F0[:, 4 * C:FS], T.SLF[:])], rd=[r("SLF")], wr=[r("F0", 4 * C, FS)])
+
+    setup_rows()
+    quant("QX", 0, C, r("X0"))
     for t in range(R):
         pass
         mm("PA", ("QUP", 0), ("QX", 0), C)
@@ -486,69 +500,78 @@ def rank_program(g, core, T, topo):
         mm("PCC", ("QUP", 128), ("QX", 0), C)
         mm("PD", ("QUP", 256), ("QX", 0), C)
         act(r("TS"), r("PB", 0, C))
+        if t: no_slots()
         tt(r("SB1"), r("PA", 0, C), r("MX"), OP.max)
         scan(r("ST"), r("NX"), r("SB1"), OP.add, OP.min)
-        ts(r("NS", 24 - SOWN, 24), r("ST", 16 * (24 - SOWN) + 15, C, 16), -1.0, OP.mult)
+        own = 24 - SOWN[t]
+        if own < 24: ts(r("NS", own, 24), r("ST", 16 * own + 15, C, 16), -1.0, OP.mult)
         node = lambda a: r("CT", 4 * CA[a // 4] + a % 4, 4 * CA[a // 4] + 64 * a, 4)
-        for a in range(24 - SOWN, 24):
+        for a in range(own, 24):
             x = r("TM", C * (a % 2), C * (a % 2) + 16 * a)
             act(x, r("TS", 0, 16 * a), bias=col("NS", a), fn=FN.Relu)
             act(node(a), x, fn=FN.Sign, acc=col("RS", a))
         if t == 0:
+            setup_turns()
+            lay(T1A)
             setup_columns()
-            setup_rows()
-            quant("QK", 128 * TI["gone"], 128 * TI["gone"] + 128, r("CB", zb, zb + 512))
-        for j in (4, 3, 5, 2, 1, 0):
+            act(r("W0"), r("PB", 0, C), scale=P("w0"))
+            act(r("BASE"), r("PB", 0, C), scale=P("base"))
+        tiles = (4, 3, 0, 5, 2, 1)
+        for j in tiles:
             for a in range(4 * j + 3, 4 * j - 1, -1):
-                if 0 < a < 24 - SOWN:
+                if 0 < a < own:
                     ts(node(a), r("TS", 0, 16 * a), col("ST", 16 * a + 15), OP.is_gt)
-                    act(r("JK", 0, 16 * a), node(a), acc=col("RS", a))
+                    if a < VSUM: total(col("RS", a), node(a))
+                    else: act(r("JK", 0, 16 * a), node(a), acc=col("RS", a))
             if j == 0:
                 tt(r("CT", 0, 4 * C, 4), r("PA", 0, C), r("ST"), OP.is_ge)
             quant("QT", CA[j], CA[j + 1], r("CT", 4 * CA[j], 4 * CA[j + 1]))
-            if j == 3 and t:
-                quant("QIN", 0, 128, r("IN"))
-        for j in (0, 4, 3, 5, 2, 1): mm("PE", K("gone"), ("QT", CA[j]), CW[j], j == 0, j == 1)
-        scan(r("CS"), r("RST"), r("CT", 0, 4 * C, 4), OP.mult, OP.add)
-        tt(r("RC"), r("CONST"), r("RS"), OP.subtract)
-        tt(r("RC"), r("RC"), r("CS", 15, C, 16), OP.subtract)
-        act(r("W1"), r("PCC", 0, C), scale=P("w1"))
-        act(r("W2"), r("PD", 0, C), scale=P("w2"))
+            if j == 0:
+                scan(r("CS"), r("RST"), r("CT", 0, 4 * C, 4), OP.mult, OP.add)
+                tt(r("RC"), r("CONST"), r("CS", 15, C, 16), OP.add)
+                if t: quant("QIN", 0, 128, r("IN"))
+                else: quant_tiles(["gone"])
+                for i in (0, 4, 3): mm("PE", K("gone"), ("QT", CA[i]), CW[i], i == 0, False)
+            elif j in (5, 2, 1): mm("PE", K("gone"), ("QT", CA[j]), CW[j], False, j == 1)
+            if t == 0 and j == 3:
+                tc(r("OFJ"), r("LKT"))
+                tt(r("ML"), r("IJF"), r("LW"), OP.is_lt, off=r("OFJ", 0, 24))
+                act(r("W1"), r("PCC", 0, C), scale=P("w1"))
+                act(r("W2"), r("PD", 0, C), scale=P("w2"))
+                act(r("Y"), r("ML"), scale=P("ys"), bias=P("y"))
+                short_factors()
+                setup_factors()
+                zeros(r("WA"))
         if t == 0:
-            act(r("W0"), r("PB", 0, C), scale=P("w0"))
-            act(r("BASE"), r("PB", 0, C), scale=P("base"))
-            act(r("LW"), r("IJF"))
-            tc(r("OFJ"), r("LKT"))
-            tc(r("OFS"), r("LKS"))
-            tt(r("ML"), r("IJF"), r("LW"), OP.is_lt, off=r("OFJ", 0, 24))
-            act(r("Y"), r("ML"), scale=P("ys"), bias=P("y"))
-            setup_turns()
             tt(r("A0"), r("W0"), r("BASE"), OP.subtract, off=r("OFJ", 0, 24))
             tt(r("A1"), r("W1"), r("A0"), OP.subtract, off=r("OFJ", 24, 48))
             tt(r("RG"), r("W2"), r("A1"), OP.is_lt, off=r("OFJ", 48, 72))
             tt(r("RF", 0, C), r("RG"), r("Y"), OP.is_equal)
             quant("QRF", 0, 128, r("RF"))
-            quant_tiles("ld", "lc2")
-            quant_tiles("gs", "gs")
+            quant_tiles(T1A)
+            quant_tiles(["gs"])
+            tc(r("OFS"), r("LKS"))
+            for b in range(4): quant("QF", 128 * b, 128 * b + 128, r("FB", 3 - b, 515 - b))
+        halves = lambda b: act(r("F0", C * b, C * b + C), r(FBANK[b], 0, C), scale=0.5)
+        for b in range(3): mm(FBANK[b], EB(b), ("QX", 0), C)
+        for b in range(2 if t else 1): halves(b)
+        mm(FBANK[3], EB(3), ("QX", 0), C)
         pass
         scan(r("ST2"), r("HD"), r("PE", 0, C), OP.add, OP.max)
-        tt(r("PL"), r("ST2", 15, C, 16), r("RC"), OP.add)
-        ts(r("GF"), r("PL"), GW - 0.5, OP.is_lt)
+        tt(r("RC"), r("RC"), r("RS"), OP.add)
+        tt(r("GF"), r("ST2", 15, C, 16), r("RC"), OP.is_lt)
         for q in range(4):
             o = r("G", 4 * q, C, 16)
-            if q < 2: ts(o, r("GF"), P("m7", q), OP.mult, P("mr", q), OP.add)
+            if q < 2 or t == 0: ts(o, r("GF"), P("m7", q), OP.mult, P("mr", q), OP.add)
             else: act(o, r("GF"), scale=P("m7", q), bias=P("mr", q))
         quant("QG", 0, 128, r("G"))
         first = [(K("ld"), ("QRF", 0)) if t == 0 else (EB(0), ("QIN", 0)), (K("gs"), ("QG", 0))]
         sums("LA", first)
-
-        def unpack(b):
-            bk = ("PCC", "PD")[b % 2]
-            mm(bk, EB(b), ("QX", 0), C)
-            act(r("F0", C * b, C * b + C), r(bk, 0, C), scale=0.5)
+        for b in range(2 if t else 1, 4): halves(b)
 
         def in_order():
-            tc(r("PLo"), r("PL"))
+            tt(r("PL"), r("ST2", 15, C, 16), r("RC"), OP.subtract)
+            ts(r("PLo"), r("PL"), GW - 0.5, OP.add)
             scatter(r("LW"), r("PLo"), r("IJF"))
 
         def gate_list():
@@ -557,9 +580,6 @@ def rank_program(g, core, T, topo):
 
         def gates():
             for b in range(4): act(r("E", b, 4 * GW, 4), r("F0", C * b, C * b + C), scale=2.0, off=r("ELo"))
-
-        def no_slots():
-            act(r("F0", 4 * C, FS), r("IJF"), scale=0.0, bias=P("o3"))
 
         def slots():
             scatter(r("F0", 4 * C, FS), r("ELo"), r("SLS"))
@@ -572,6 +592,7 @@ def rank_program(g, core, T, topo):
             for q in range(4): act(r("G2", 4 * q, C, 16), r("GF"), scale=P("m29", q), bias=P("m512", q))
 
         def order0():
+            act(r("W1"), r("PCC", 0, C), scale=P("w1"))
             act(r("A0"), r("TS"), scale=P("w0"), off=r("OFJ", 0, 24))
 
         def order1():
@@ -579,7 +600,6 @@ def rank_program(g, core, T, topo):
 
         def order2():
             tt(r("RF", 0, C), r("W2"), r("A1"), OP.is_lt, off=r("OFJ", 48, 72))
-            quant("QRF", 0, 128, r("RF"))
 
         def weights():
             mm("PA", K("ord"), ("QRF", 0), 128)
@@ -588,47 +608,55 @@ def rank_program(g, core, T, topo):
         def layer():
             a, o = (0, 0) if t == 0 else (GW * t, 32)
             for b in range(4):
-                bk = ("PCC", "PD")[b % 2]
+                bk = ("PE", "AB")[b % 2]
                 mm(bk, ("WC", 128 * b), ("LD", a), 128)
                 act(r("H0", b, 4 * GW, 4), r(bk, o, o + GW), scale=0.015625)
             spread("HT", "H0")
 
-        un = lambda b: (lambda: unpack(b))
-        onS = [[un(0), un(1), no_slots], [un(2), un(3), lambda: spread("FT", "F0"), gates], [stay], [], [], []]
-        onV = [[in_order], [gate_list, slots], [pass_on], [lambda: quant("QG2", 0, 128, r("G2"))], [], []]
+        Qn = lambda n: (lambda: quant("Q" + n, 0, 128, r(n)))
+        early = [[in_order], [pass_on], [], [], [], []]
+        mid = [[], [], [], [], [weights], []]
+        onV = [[gate_list], [slots], [Qn("C2")], [], [], []]
+        onS = [[gates], [lambda: spread("FT", "F0")], [], [stay], [], []]
         if t:
-            onS[2].append(order0)
-            onV[3].append(order1)
-            onV[4].append(order2)
-            onS[5].append(weights)
+            onS[1].append(order0)
+            onS[2].append(lambda: act(r("W2"), r("PD", 0, C), scale=P("w2")))
+            early[2].append(order1)
+            early[3].append(order2)
+            onV[3], onV[4] = [Qn("RF")], [Qn("G2")]
+            if t == 1:
+                setup_nodes()
+                onS[4].append(setup_bits)
         else:
-            for b in range(4): quant("QF", 128 * b, 128 * b + 128, r("FB", 3 - b, 515 - b))
-            setup_factors()
-            onS[0].insert(0, setup_slots)
-            onS[1].append(setup_aways)
-            onV[2].append(lambda: quant_tiles("ad", "st"))
-            onV[2].append(lambda: ts(r("HD4"), r("I4"), pk, OP.is_equal))
-            onV[2].append(setup_ends)
-            onS[3].append(setup_routes)
-            for e in range(4): onS[1 + e].append(lambda e=e: setup_short(e))
-            onV[5].append(lambda: quant_tiles("lg", "dl2"))
-            onS[5].append(weights)
+            early[1] += [setup_aways, lambda: lay(T1B), lambda: iota(r("ALT"), [[0, C], [1, 2]], 0)]
+            onV[1], onS[1] = [], [setup_slots, setup_stay]
+            early[2] += [slots, lambda: spread("FT", "F0"), lambda: short_lay(0, "V"), setup_classes]
+            onS[2] += [lambda: short_lay(1), lambda: short_lay(2)]
+            early[3] += [lambda: quant_tiles(T1B)]
+            onS[3] += [lambda: short_lay(3)]
+            early[4] += [lambda: quant_tiles(T2[1:5]), setup_ends]
+            onV[4] = [Qn("G2")]
+            onS[4] += [setup_routes]
+            early[5] += [lambda: quant_tiles(T2[5:])]
         done = 0
+        kept = [(EB(0), ("QC2", 0))]
         for i in range(SWEEPS):
             pass
             bk, nb = ("LA", "LB")[i % 2], ("LB", "LA")[i % 2]
-            past = (first if i < 3 else [(EB(0), ("QC2", 0))]) + [x for j in range(0 if i < 3 else 2, i) for x in moved(j, "lo", "lc")]
+            past = [x for j in range(0 if i < 3 else 2, i) for x in moved(j, "lo", "lc")] + (first if i < 3 else kept)
             if i < SWEEPS - 1: sums(nb, past, True, False)
             for s in range(4): ts(r("W", s, C, 4), r(bk, 0, 96), P("mn", s), OP.max, P("mk", s), OP.min)
+            n = VSWEEP[i] if t else VFIRST[i]
+            act(r("GA", n, 1152), r("W", 0, C), off=r("OFS", n // 16, 72))
             if i == 2: act(r("C2", 0, C, 4), r(bk, 0, 96))
             quant("QW", 128 * i, 128 * i + 128, r("W"))
-            n = VSWEEP[i]
-            act(r("GA", n, 1152), r("W", 0, C), off=r("OFS", n // 16, 72))
-            tc(r("GA", 0, n), r("W", 0, C), off=r("OFS", 0, n // 16))
+            for f in early[i]: f()
+            if i == SWEEPS - 1: sums("PB", past + [(K("lg"), ("QG", 0))], True, False)
+            if n: tc(r("GA", 0, n), r("W", 0, C), off=r("OFS", 0, n // 16))
             n = 320 if t == 0 else 288
             quant("QD", 320 * i, 320 * i + n, r("GA", 0, 4 * n))
             if i < SWEEPS - 1: sums(nb, moved(i, "lo", "lc"), False, True)
-            if i == 2: quant("QC2", 0, 128, r("C2"))
+            for f in mid[i]: f()
             if t or i >= 3:
                 if done == 0: sums("AB", [(K("ad"), ("QRF", 0)) if t == 0 else (EB(1), ("QIN", 0))], True, False)
                 for j in range(done, i + 1): sums("AB", moved(j, "ao", "ac"), False, j == SWEEPS - 1)
@@ -638,8 +666,11 @@ def rank_program(g, core, T, topo):
         pass
         tt(r("VT", 0, C, 4), r("AB", 0, 96), r("WW"), OP.mult)
         quant("QVT", 0, 128, r("VT"))
-        sums("PA", [(K("lg"), ("QG2", 0)), (K("lv"), ("QVT", 0))])
         ts(r("IN", 1, C, 4), r("AB", 0, 96), P("thr"), OP.is_gt, P("two"), OP.mult)
+        sums("PA", [(K("lg"), ("QG2", 0)), (K("lv"), ("QVT", 0))])
+        sums("PB", moved(SWEEPS - 1, "lo", "lc"), False, True)
+        act(r("IN", 0, C, 4), r("PB", 0, 96))
+        layer()
         tt(r("PT", 0, C, 4), r("PA", 0, 96), r("OCL"), OP.min)
         tt(r("PT", 1, C, 4), r("PA", 0, 96), r("OCH"), OP.min)
         ts(r("PT", 2, C, 4), r("PA", 0, 96), P("cls"), OP.min)
@@ -649,7 +680,6 @@ def rank_program(g, core, T, topo):
         for A in (0, 2): mm(four[A], K("ct%d" % A), ("QPT", 0), 128)
         sums("PA", [(K("dl1"), ("QPT", 0)), (K("dl2"), ("QPT", 0))])
         for A in (1, 3): mm(four[A], K("ct%d" % A), ("QPT", 0), 128)
-        sums("PB", [(EB(0), ("QC2", 0)), (K("lg"), ("QG", 0))] + [x for j in range(2, SWEEPS) for x in moved(j, "lo", "lc")])
         for A in (2, 3, 0, 1):
             for s in range(4):
                 o, x = r("WA", FS * A + s, FS * A + C, 4), r(four[A], 0, 96)
@@ -657,38 +687,45 @@ def rank_program(g, core, T, topo):
                 else: act(o, x, scale=P("ms", s))
             if A == 0: to_list("PA", "DL")
         pass
+        fd = lambda b: act(r("FD", 2 * C * b, 2 * C * b + 2 * C, 2), r("FT", C * b), off=r("DL"))
         for j, (a, b) in enumerate((("DL", "L2"), ("L2", "L3"), ("L3", "EL"))):
             act(r("GS", VSTEP, C), r("WA"), off=r(a, VSTEP // 16, 24))
             tc(r("GS", 0, VSTEP), r("WA"), off=r(a, 0, VSTEP // 16))
             quant("QS", 0, 128, r("GS"))
             mm("PA", K("st"), ("QS", 0), 128)
-            act(r("FD", C * j, C * j + C), r("FT", C * j), off=r("DL"))
-            if j == 0:
-                act(r("IN", 0, C, 4), r("PB", 0, 96))
-                layer()
+            fd((0, 2, 1)[j])
             to_list("PA", b)
         pass
+        even = lambda n, b: r(n, 2 * C * b, 2 * C * b + 2 * C, 2)
+        odd = lambda n, b: r(n, 2 * C * b + 1, 2 * C * b + 2 * C, 2)
+        both = lambda n, b: r(n, 2 * C * b, 2 * C * b + 2 * C)
+
+        def blend(b):
+            if b in PAIRED: scan(both("Z", b), r("ALT"), both("FD", b), OP.mult, OP.add)
+            else: tt(odd("Z", b), r("FT", C * b), even("FD", b), OP.add, off=r("EL"))
+            if b >= 2: act(even("Z", b), r("HT"), off=r("HL%d" % b))
+
         act(r("SG"), r("FT", 4 * C), off=r("EL"))
-        act(r("FD", 3 * C, 4 * C), r("FT", 3 * C), off=r("DL"))
+        fd(3)
+        for b in PAIRED[::-1]: act(odd("FD", b), r("FT", C * b), off=r("EL"))
         if t == R - 1:
-            act(r("OUT", 0, C), r("NODE"), bias=P("h768"), off=r("EL"))
             quant("QIN", 0, 128, r("IN"))
             mm("PB", K("nm"), ("QIN", 0), 128)
-        for b in range(4):
-            tt(r("Z", C * b, C * b + C), r("FT", C * b), r("FD", C * b, C * b + C), OP.add, off=r("EL"))
-            if b == 0:
-                scan(r("ST2"), r("HD"), r("SG"), OP.add, OP.max)
-                for j in range(4): ts(r("HL%d" % j), r("ST2", 15, C, 16), 4.0, OP.mult, P("hb%d" % j), OP.add)
+        blend(0)
+        scan(r("ST2"), r("HD"), r("SG"), OP.add, OP.max)
+        for j in (2, 3, 0, 1): ts(r("HL%d" % j), r("ST2", 15, C, 16), 4.0, OP.mult, P("hb%d" % j), OP.add)
+        for b in (2, 3, 1): blend(b)
         if t == R - 1:
+            act(r("OUT", 0, C), r("NODE"), bias=P("h768"), off=r("EL"))
             ts(r("BN"), r("PB", 0, 96), 0.5, OP.is_gt, P("bit8"), OP.mult)
             act(r("BA"), r("IN", 1, C, 4), scale=P("bit"))
             for s in range(4):
                 act(r("ND", 4 * s, 4 * C, 16), r("BA"), scale=P("ms", s))
                 act(r("ND", 4 * s + 1, 4 * C, 16), r("BN"), scale=P("ms", s))
-        for b in range(4):
-            tt(r("X0", b, 4 * C, 4), r("HT"), r("Z", C * b, C * b + C), OP.add, off=r("HL%d" % b))
+        for b in (2, 3): scan(r("X0", b - 2, 4 * C, 2), r("ALT"), both("Z", b), OP.mult, OP.add)
+        for b in (0, 1): tt(r("X0", b, 4 * C, 4), r("HT"), odd("Z", b), OP.add, off=r("HL%d" % b))
         quant("QX", 0, C, r("X0"))
-        if t == 0: quant("QV", 0, 128, r("VV"))
+        if t == 1: quant("QV", 0, 128, r("VV"))
     pass
     mm("PA", ("QV", 0), ("QX", 0), C)
     act(r("OUT", 2 * C, 3 * C), r("PA", 0, C))

@@ -8,27 +8,28 @@ C, GW, R, SWEEPS = 384, 96, 3, 6
 JUMP = [0, 1, 4]
 
 T1A, T1B = ["ld", "lo", "lc0", "lc1", "lc2"], ["ad", "ao", "ord", "st", "ac0", "ac1", "ac2"]
-T2 = ["gs", "lg", "lv", "nm", "dl1", "ct0", "ct1", "ct2", "ct3", "dl2"]
+T2 = ["gs", "lg", "lv", "dl1", "ct0", "ct1", "ct2", "ct3", "dl2", "nm"]
 TILES = T1A + T1B + T2 + ["gone"]
 TI = {n: i for i, n in enumerate(TILES)}
 NT = len(TILES)
-ROOM = {n: 512 * i for l in (T1A, T1B + T2 + ["gone"]) for i, n in enumerate(l)}
-ELEM = [("lg", "ct3"), ("nm", "ct3"), ("ct0", "dl2"), ("dl1", "dl2")]
+ROOM = {n: i for l in (T1A, T1B + T2 + ["gone"]) for i, n in enumerate(l)}
+ELEM = [("lg", "ct3"), ("dl1", "ct3"), ("ct0", "dl2"), ("dl1", "dl2")]
 FS = 5 * C
 HOLD, DROP = 8192.0, 1048576.0
-FBANK = ["PA", "PB", "AB", "PA"]
+LINK = [0, 96, 192, 320, 448]
 VSWEEP = [0, 448, 320, 320, 512, 512]
-VFIRST = [0, 448, 192, 256, 0, 256]
+VFIRST = [0, 448, 320, 320, 320, 320]
 VSTEP = 192
 SOWN = [2, 3, 3]
-VSUM = 1
 PAIRED = [3]
 ENGINES = 8
+HOP, NEXT, LAND, FAR, SPARE, PASSES = 130, 80, 1500, 4000, 0.1, 3
 
 F32, BF, I32, U16, X4, U8 = "float32", "bfloat16", "int32", "uint16", "float8_e4m3fn_x4", "uint8"
+BYTES = {F32: 4, BF: 2, I32: 4, U16: 2, X4: 4, U8: 1}
 SCRATCH = {}
-WIDE = {"KF": "JM MD MX NX HD HD4 I4 IJF CONST SLS", "KI": "PC UL X16 XA XB2", "KB": "WT DGR GCT GCA GDT CF CF2 GW1 GW2 OCL OCH ML Y ALT",
-        "XF": "SB1 ST ST2 ST3 ST4 RS RC PL GF NS", "XB": "CS WW BA BN JK TM", "ZT": "G IN C2 G2 VT ND",
+WIDE = {"KF": "JM MD MX NX HD HD4 I4 IJF CONST SLS", "KI": "PC UL X16 XA XB2", "KB": "WT DGR GCT GCA GDT CF CF2 OCL OCH ML Y ALT",
+        "XF": "SB1 ST ST2 ST3 ST4 RS RC PL GF NS", "XB": "CS WW BA BN", "ZT": "G IN C2 G2 VT ND",
         "XU": "PLo ELo DL L2 L3 EL HL0 HL1 HL2 HL3", "KU": "ULo OFJ OFS"}
 HOME = {n: w for w in WIDE for n in WIDE[w].split()}
 PLACE, LEN = {}, {}
@@ -51,23 +52,23 @@ CA = [sum(CW[:j]) for j in range(7)]
 for _n, _w, _d in [
         ("X0", 1536, BF), ("U", 512, BF), ("VV", 512, BF), ("LKT", 72, I32), ("LKS", 72, I32), ("LK2", 96, I32),
         ("ULo", 24, U16), ("OFJ", 72, U16), ("OFS", 72, U16), ("UL", 24, I32), ("PC", 16, I32), ("X16", 96, I32), ("XA", 96, I32), ("XB2", 96, I32),
-        ("PF", 96, F32), ("WT", 512, BF), ("ZB", 512, BF), ("CB", ROOM["gone"] + 512, BF), ("FB", 516, BF), ("GOt", 512, BF),
-        ("DGR", 32, BF), ("GCT", 64, BF), ("GCA", 32, BF), ("GDT", 128, BF), ("CF", C, BF), ("CF2", 1280, BF),
+        ("PF", 96, F32), ("WT", 512, BF), ("ZB", 512, BF), ("CB", 512 * (NT - len(T1A)), BF), ("FB", 516, BF), ("GOt", 1024, BF),
+        ("DGR", 32, BF), ("GCT", 96, BF), ("GCA", 32, BF), ("GDT", 128, BF), ("CF", C, BF), ("CF2", 1280, BF),
         ("OCL", 96, BF), ("OCH", 96, BF), ("ML", C, BF), ("Y", C, BF), ("ALT", 2 * C, BF),
         ("JM", C, F32), ("MD", C, F32), ("MX", C, F32), ("NX", C, F32), ("HD", C, F32), ("HD4", 96, F32), ("I4", 96, F32), ("IJF", C, F32),
         ("CONST", 24, F32), ("SLS", 96, F32), ("RST", C, BF), ("NODE", 3 * FS + C, F32), ("SLF", C, BF),
         ("TS", C, F32), ("W0", C, F32), ("W1", C, F32), ("W2", C, F32), ("BASE", C, F32), ("A0", C, F32), ("A1", C, F32), ("RF", 512, BF), ("RG", C, BF),
         ("SB1", C, F32), ("ST", C, F32), ("ST2", C, F32), ("ST3", GW, F32), ("ST4", 96, F32), ("RS", 24, F32), ("RC", 24, F32), ("PL", 24, F32),
-        ("GF", 24, F32), ("NS", 24, F32), ("CS", C, BF), ("WW", 96, BF), ("BA", 96, BF), ("BN", 96, BF), ("JK", C, BF), ("TM", 2 * C, BF),
+        ("GF", 24, F32), ("NS", 24, F32), ("CS", C, BF), ("WW", 96, BF), ("BA", 96, BF), ("BN", 96, BF), ("JK", 4 * C, BF),
         ("PLo", 24, U16), ("ELo", 6, U16), ("DL", 24, U16), ("L2", 24, U16), ("L3", 24, U16), ("EL", 24, U16),
         ("HL0", 24, U16), ("HL1", 24, U16), ("HL2", 24, U16), ("HL3", 24, U16),
         ("CT", 4 * CA[6], BF), ("G", 512, BF), ("IN", 512, BF), ("C2", 512, BF), ("G2", 512, BF), ("VT", 512, BF), ("ND", 4 * C, BF),
-        ("W", 512, BF), ("GA", 1280, BF), ("PT", 512, BF), ("GS", 512, BF), ("WA", 3 * FS + C, BF), ("LW", C, F32), ("SG", C, BF),
+        ("GA", 4 * LINK[4], BF), ("PT", 512, BF), ("GS", 512, BF), ("WA", 3 * FS + C, BF), ("LW", C, F32), ("SG", C, BF),
         ("F0", FS, BF), ("FT", 4 * FS, BF), ("H0", 512, BF), ("HT", 2048, BF), ("FD", 8 * C, BF), ("Z", 8 * C, BF),
         ("E", 512, BF), ("OUT", 3 * C, F32)]:
     sb(_n, _w, _d)
 for _n, _w in [("QX", C), ("QU", 128), ("QUP", C), ("QV", 128), ("WC", 512), ("QK", 128 * NT), ("QF", 512), ("QT", CA[6]),
-               ("QG", 128), ("QG2", 128), ("QRF", 128), ("QW", 128 * SWEEPS), ("QD", 320 * SWEEPS), ("QC2", 128), ("QIN", 128),
+               ("QG", 128), ("QG2", 128), ("QRF", 128), ("QD", LINK[4] * SWEEPS), ("QC2", 128), ("QIN", 128),
                ("QVT", 128), ("QPT", 128), ("QS", 128), ("QE", 3 * 128), ("LD", 320), ("QND", C)]:
     mx(_n, _w)
 PS = ["PA", "PB", "PCC", "PD", "LA", "LB", "AB", "PE"]
@@ -84,83 +85,94 @@ def rank_program(g, core, T, topo):
     nxt = T.cores[(rank + 1) % len(T.cores)]
     Q = {"V": g.vector, "S": g.scalar, "T": g.tensor, "G": g, "Y": g.sync}
     SEM = {"V": "sv", "S": "ss", "T": "st", "G": "sg"}
-    cnt = {s: 0 for s in SEMAPHORES}
-    known = {q: {} for q in Q}
-    clk, wrs, rds, bank = {}, {}, {}, {}
+    ops, wrs, rds, bank = [], {}, {}, {}
 
     def overlap(a, b):
         if a[1] <= b[0] or b[1] <= a[0]: return False
         d = math.gcd(a[2], b[2])
         return not (d > 1 and (a[0] - b[0]) % d)
 
-    def await_(q, deps):
-        best = {}
-        for s, c in deps:
-            best[s] = max(best.get(s, 0), c)
-        for s, c in sorted(best.items(), key=lambda t: -t[1]):
-            if known[q].get(s, 0) >= c: continue
-            Q[q].wait_ge(T.sem[s], c)
-            known[q][s] = c
-            for s2, c2 in clk[(s, c)].items():
-                if known[q].get(s2, 0) < c2: known[q][s2] = c2
-
-    def deps_of(q, rd, wr):
-        deps = []
+    def note(ways, rd, wr, after=0, sem=None):
+        me, deps = len(ops), {}
         for n, lo, hi, st in rd:
-            if n in PS: continue
             for e in wrs.get(n, []):
-                if overlap(e[0], (lo, hi, st)): deps.append(e[1])
+                if overlap(e[0], (lo, hi, st)): deps[e[1]] = True
         for n, lo, hi, st in wr:
-            if n in PS: continue
-            for e in wrs.get(n, []):
-                if overlap(e[0], (lo, hi, st)): deps.append(e[1])
-            for e in rds.get(n, []):
-                if overlap(e[0], (lo, hi, st)): deps.append(e[1])
+            for e in wrs.get(n, []) + rds.get(n, []):
+                if overlap(e[0], (lo, hi, st)): deps[e[1]] = True
         for n in set(x[0] for x in list(rd) + list(wr) if x[0] in PS):
-            for q2, m in bank.get(n, {}).items():
-                if q2 != q: deps.append(m)
-        return deps
-
-    def record(q, m, rd, wr):
+            if n in bank: deps.setdefault(bank[n], False)
+            bank[n] = me
         for n, lo, hi, st in wr:
             if n in PS: continue
             for tab in (wrs, rds):
                 tab[n] = [e for e in tab.get(n, []) if not (e[0][0] >= lo and e[0][1] <= hi and (st == 1 or (e[0][2] == st and e[0][0] == lo)))]
-            wrs[n].append(((lo, hi, st), m, q))
+            wrs[n].append(((lo, hi, st), me))
         for n, lo, hi, st in rd:
-            if n in PS: continue
-            rds[n] = [e for e in rds.get(n, []) if not (e[2] == q and q != "D" and e[0] == (lo, hi, st))] + [((lo, hi, st), m, q)]
-        for n in set(x[0] for x in list(rd) + list(wr) if x[0] in PS):
-            b = bank.get(n, {})
-            b = {q2: m2 for q2, m2 in b.items() if q2 == q or known[q].get(m2[0], 0) < m2[1]}
-            b[q] = m
-            bank[n] = b
+            if n not in PS: rds.setdefault(n, []).append(((lo, hi, st), me))
+        op = {"ways": ways, "deps": deps, "after": after, "sem": sem}
+        ops.append(op)
 
-    def do(q, fn, rd, wr):
-        await_(q, deps_of(q, rd, wr))
-        s = SEM[q]
-        cnt[s] += 1
-        m = (s, cnt[s])
-        fn(Q[q]).then_inc(T.sem[s], 1)
-        c = dict(known[q])
-        c[s] = cnt[s]
-        clk[m] = c
-        record(q, m, rd, wr)
+    def issue():
+        n = len(ops)
+        before, behind = [list(o["deps"].items()) for o in ops], [[] for _ in ops]
+        for i in range(n):
+            for d, hard in before[i]: behind[d].append((i, hard))
 
-    dn = [0]
+        def place(key, waits, back):
+            busy, at = {q: [] for q in Q}, [None] * n
+            for i in sorted(range(n), key=lambda i: -key[i]):
+                best = None
+                for q, (fn, c) in ops[i]["ways"].items():
+                    t0 = ops[i]["after"] if back else 0.0
+                    for d, hard in waits[i]:
+                        x = ops[i if back else d]
+                        t0 = max(t0, at[d][2] + x["after"] + (HOP if at[d][0] != q or x["sem"] else NEXT if hard else 0))
+                    b = busy[q]
+                    lo, k = 0, len(b)
+                    while lo < k:
+                        m = (lo + k) // 2
+                        if b[m][1] > t0: k = m
+                        else: lo = m + 1
+                    while k < len(b) and b[k][0] < t0 + c:
+                        t0 = max(t0, b[k][1])
+                        k += 1
+                    worth = t0 + c * (1 + SPARE if q == "V" else 1)
+                    if best is None or worth < best[0]: best = (worth, q, t0, c, k)
+                _, q, t0, c, k = best
+                busy[q].insert(k, (t0, t0 + c))
+                at[i] = (q, t0, t0 + c)
+            return at
 
-    def dma(q, pairs, rd=(), wr=()):
-        s = "d%d" % dn[0]
-        dn[0] += 1
-        await_(q, deps_of("D", rd, wr))
-        for o, i in pairs:
-            Q[q].dma_start(o, i).then_inc(T.sem[s], 16)
-            cnt[s] += 16
-        m = (s, cnt[s])
-        c = dict(known[q])
-        c[s] = cnt[s]
-        clk[m] = c
-        record("D", m, rd, wr)
+        key, plan = [0.0] * n, None
+        for i in range(n - 1, -1, -1):
+            key[i] += min(c for _, c in ops[i]["ways"].values()) + ops[i]["after"]
+            for d in ops[i]["deps"]: key[d] = max(key[d], key[i] + HOP)
+        for _ in range(PASSES):
+            at = place(key, before, False)
+            end = max(x[2] + o["after"] for x, o in zip(at, ops))
+            if plan is None or end < plan[0]: plan = (end, at)
+            key = [x[2] for x in place([x[2] for x in at], behind, True)]
+        for o, x in zip(ops, plan[1]): o["q"], o["start"] = x[0], x[1]
+        cnt, known = {s: 0 for s in SEMAPHORES}, {q: {} for q in Q}
+        for o in sorted(ops, key=lambda o: o["start"]):
+            q = o["q"]
+            need = [ops[d] for d, hard in o["deps"].items() if hard or ops[d]["q"] != q]
+            for x in sorted(need, key=lambda x: -x["start"]):
+                s, c = x["mark"]
+                if known[q].get(s, 0) >= c: continue
+                Q[q].wait_ge(T.sem[s], c)
+                for s2, c2 in x["clock"].items(): known[q][s2] = max(known[q].get(s2, 0), c2)
+            call = o["ways"][q][0](Q[q])
+            if o["sem"]: s, cnt[s] = o["sem"][0], o["sem"][1]
+            else:
+                s = SEM[q]
+                cnt[s] += 1
+                call.then_inc(T.sem[s], 1)
+            o["mark"] = (s, cnt[s])
+            o["clock"] = dict({} if s.startswith("arr") else known[q], **{s: cnt[s]})
+        for s in SEMAPHORES:
+            if cnt[s]: g.wait_ge(T.sem[s], cnt[s])
 
     def r(n, lo=0, hi=None, st=1):
         w, a = PLACE[n]
@@ -173,67 +185,86 @@ def rank_program(g, core, T, topo):
     isr = lambda x: isinstance(x, tuple)
     val = lambda x: ap(x) if isr(x) else x
     size = lambda o: len(range(o[1], o[2], o[3]))
+    narrow = lambda *xs: all(BYTES[SCRATCH[x[0]][2]] == 2 for x in xs)
+    vtime = lambda n, f=1.0: max(0.83 * f * n, 53) + 40
+    stime = lambda n: max(0.83 * n, 53) + 60
+    gather = lambda n: 1.3 * n + 55
+    dn = [0]
+
+    def dma(q, pairs, rd=(), wr=(), n=None):
+        s = "d%d" % dn[0]
+        dn[0] += 1
+
+        def run(e):
+            for o, i in pairs: e.dma_start(o, i).then_inc(T.sem[s], 16)
+
+        if n is None: n = sum(size(x) * BYTES[SCRATCH[x[0]][2]] for x in (wr or rd))
+        note({q: (run, 60 * len(pairs) + (0.5 * n if q == "Y" else 0))}, rd, wr, LAND, (s, 16 * len(pairs)))
 
     def ts(o, i, s1, op0, s2=None, op1=None):
         rd = [i] + [s for s in (s1, s2) if isr(s)]
-        if op1 is None: do("V", lambda e: e.tensor_scalar(ap(o), ap(i), val(s1), None, op0), rd, [o])
-        else: do("V", lambda e: e.tensor_scalar(ap(o), ap(i), val(s1), val(s2), op0, op1), rd, [o])
+        more = () if op1 is None else (op1,)
+        note({"V": (lambda e: e.tensor_scalar(ap(o), ap(i), val(s1), val(s2), op0, *more), vtime(size(o), 0.5 if narrow(o, i) else 1))}, rd, [o])
 
     def tt(o, a, b, op, off=None):
-        if off is None: do("V", lambda e: e.tensor_tensor(ap(o), ap(a), ap(b), op), [a, b], [o])
-        else: do("V", lambda e: e.tensor_tensor(ap(o), ap(a).indirect(ap(off)), ap(b), op), [a, b, off], [o])
+        if off is None: note({"V": (lambda e: e.tensor_tensor(ap(o), ap(a), ap(b), op), vtime(size(o), 1 if a[0] in PS else 2))}, [a, b], [o])
+        else: note({"V": (lambda e: e.tensor_tensor(ap(o), ap(a).indirect(ap(off)), ap(b), op), gather(size(o)))}, [a, b, off], [o])
 
     def tc(o, a, off=None):
-        if off is None: do("V", lambda e: e.tensor_copy(ap(o), ap(a)), [a], [o])
-        else: do("V", lambda e: e.tensor_copy(ap(o), ap(a).indirect(ap(off))), [a, off], [o])
+        if off is None: note({"V": (lambda e: e.tensor_copy(ap(o), ap(a)), vtime(size(o)))}, [a], [o])
+        else: note({"V": (lambda e: e.tensor_copy(ap(o), ap(a).indirect(ap(off))), gather(size(o)))}, [a, off], [o])
 
     def scatter(win, off, a):
-        do("V", lambda e: e.tensor_copy(ap(win).indirect(ap(off)), ap(a)), [a, off], [win])
+        note({"V": (lambda e: e.tensor_copy(ap(win).indirect(ap(off)), ap(a)), 3.2 * size(a) + 50)}, [a, off], [win])
 
-    def total(o, a):
-        do("V", lambda e: e.tensor_reduce(ap(o), ap(a), AxisListType.X, OP.add), [a], [o])
-
-    def act(o, a, bias=0.0, scale=1.0, off=None, fn=COPY, acc=None):
+    def act(o, a, bias=0.0, scale=1.0, off=None, fn=COPY, acc=None, on="VS"):
         rd = [a] + [x for x in (scale, bias, off) if isr(x)]
-        if isr(bias) and fn == COPY: fn = IDENT
-        if acc is not None: do("S", lambda e: e.activation(ap(o), ap(a), fn, bias=val(bias), scale=val(scale), accum_out=ap(acc)), rd, [o, acc])
-        elif off is None: do("S", lambda e: e.activation(ap(o), ap(a), fn, bias=val(bias), scale=val(scale)), rd, [o])
-        else: do("S", lambda e: e.activation(ap(o), ap(a).indirect(ap(off)), fn, bias=val(bias), scale=val(scale)), rd, [o])
+        f = IDENT if isr(bias) and fn == COPY else fn
+        src = (lambda: ap(a)) if off is None else (lambda: ap(a).indirect(ap(off)))
+        more = lambda: {} if acc is None else {"accum_out": ap(acc)}
+        n, ways = size(o), {}
+        if "S" in on: ways["S"] = (lambda e: e.activation(ap(o), src(), f, bias=val(bias), scale=val(scale), **more()), gather(n) + 10 if off else stime(n) + 20 * (acc is not None))
+        if "V" in on and fn == COPY and acc is None:
+            ways["V"] = (lambda e: e.tensor_scalar(ap(o), src(), val(scale), val(bias), OP.mult, OP.add), gather(n) if off else vtime(n, 0.5 if narrow(o, a) else 1))
+        note(ways, rd, [o] + ([] if acc is None else [acc]))
+
+    def total(o, junk, a):
+        note({"V": (lambda e: e.tensor_reduce(ap(o), ap(a), AxisListType.X, OP.add), vtime(size(a))),
+              "S": (lambda e: e.activation(ap(junk), ap(a), COPY, accum_out=ap(o)), stime(size(a)) + 20)}, [a], [o, junk])
 
     def scan(o, a, b, op0, op1):
-        do("V", lambda e: e.tensor_tensor_scan(ap(o), ap(a), ap(b), 0.0, op0, op1), [a, b], [o])
+        note({"V": (lambda e: e.tensor_tensor_scan(ap(o), ap(a), ap(b), 0.0, op0, op1), vtime(size(o), 0.5 if narrow(o, a, b) else 1))}, [a, b], [o])
 
     def fill(o, c):
-        do("V", lambda e: e.memset(ap(o), c), [], [o])
+        note({"V": (lambda e: e.memset(ap(o), c), vtime(size(o), 0.5 if narrow(o) else 1))}, [], [o])
 
     def quant(n, a, b, src):
         q, s = r(n + "c", a, b), r(n + "s", a, b)
-        do("V", lambda e: e.quantize_mx(ap(q), ap(s), ap(src)), [src], [q, s])
+        note({"V": (lambda e: e.quantize_mx(ap(q), ap(s), ap(src)), 52 + 0.88 * (b - a))}, [src], [q, s])
 
     def pick(n, src, off):
         m, w = 16 * (off[2] - off[1]), LEN[src + "c"]
-        do("V", lambda e: e.tensor_copy(T[n + "c"][:, 0:m].bitcast(dt.uint32), T[src + "c"][:, 0:w].bitcast(dt.uint32).indirect(ap(off))), [r(src + "c"), off], [r(n + "c")])
-        do("S", lambda e: e.activation(T[n + "s"][:, 0:m], T[src + "s"][:, 0:w].indirect(ap(off)), COPY), [r(src + "s"), off], [r(n + "s")])
+        note({"V": (lambda e: e.tensor_copy(T[n + "c"][:, 0:m].bitcast(dt.uint32), T[src + "c"][:, 0:w].bitcast(dt.uint32).indirect(ap(off))), gather(m))}, [r(src + "c"), off], [r(n + "c")])
+        note({"S": (lambda e: e.activation(T[n + "s"][:, 0:m], T[src + "s"][:, 0:w].indirect(ap(off)), COPY), gather(m))}, [r(src + "s"), off], [r(n + "s")])
 
     def mm(bk, st, mv, n, start=True, stop=True):
         l, ls = r(st[0] + "c", st[1], st[1] + 128), r(st[0] + "s", st[1], st[1] + 128)
         m, ms = r(mv[0] + "c", mv[1], mv[1] + n), r(mv[0] + "s", mv[1], mv[1] + n)
         o = r(bk, 0, n)
-        do("T", lambda e: e.matmul_mx(ap(o), ap(l), ap(ls), ap(m), ap(ms), start, stop), [l, ls, m, ms], [o])
+        note({"T": (lambda e: e.matmul_mx(ap(o), ap(l), ap(ls), ap(m), ap(ms), start, stop), 0.6 * (n + 16) + 25)}, [l, ls, m, ms], [o])
 
     def sums(bk, terms, start=True, stop=True):
         for j, (st, mv) in enumerate(terms): mm(bk, st, mv, 128, start and j == 0, stop and j == len(terms) - 1)
 
     def iota(o, pat, base, cm=0):
-        fl = SCRATCH[o[0]][2] != I32
-        if fl: do("G", lambda e: e.iota(ap(o), pat, base, cm, allow_small_or_imprecise_dtypes=True), [], [o])
-        else: do("G", lambda e: e.iota(ap(o), pat, base, cm), [], [o])
+        more = {} if SCRATCH[o[0]][2] == I32 else {"allow_small_or_imprecise_dtypes": True}
+        note({"G": (lambda e: e.iota(ap(o), pat, base, cm, **more), 130 + 1.66 * size(o))}, [], [o])
 
     def const(o, c):
         iota(o, [[0, size(o)]], c)
 
     def sel(o, i, pat, op, fl, base, cm):
-        do("G", lambda e: e.affine_select(ap(o), ap(i), pat, op, fl, base, cm), [i], [o])
+        note({"G": (lambda e: e.affine_select(ap(o), ap(i), pat, op, fl, base, cm), 170 + 1.66 * size(o))}, [i], [o])
 
     def zeros(*xs):
         pairs = [(T[n][:, a:min(a + 512, hi)], T.ZB[:, 0:min(512, hi - a)]) for n, lo, hi, _ in xs for a in range(lo, hi, 512)]
@@ -242,6 +273,7 @@ def rank_program(g, core, T, topo):
     K = lambda n: ("QK", 128 * TI[n])
     EB = lambda b: ("QF", 128 * b)
     col = lambda n, j: r(n, j, j + 1)
+    room = lambda n, a=0, k=1, st=1: r("CB", 512 * ROOM[n] + a, 512 * (ROOM[n] + k), st)
     PFC = {}
 
     def pcol(name, n=1):
@@ -254,23 +286,25 @@ def rank_program(g, core, T, topo):
     CLS = lambda A: 16 * (A & 1) + 64 * (A >> 1)
     neg = lambda pat: [[-a, b] for a, b in pat]
     row = lambda j: col("MD", j)
-    cf = lambda n: r("CF", 32 * TI[n], 32 * TI[n] + 32)
-    c2 = lambda e, n, a=0, st=1: r("CF2", 320 * e + 32 * T2.index(n) + a, 320 * e + 32 * T2.index(n) + 32, st)
+    cf = lambda n, k=1: r("CF", 32 * TI[n], 32 * (TI[n] + k))
+    c2 = lambda e, n, a=0, st=1, k=1: r("CF2", 320 * e + 32 * T2.index(n) + a, 320 * e + 32 * (T2.index(n) + k), st)
 
     dma("S", [(T.U[:], T.u[:])], wr=[r("U")])
     dma("Y", [(T.X0[:], T.x[:])], wr=[r("X0")])
     dma("Y", [(T.LKT[:], T.lk[:])], wr=[r("LKT")])
     fill(r("ZB"), 0.0)
     fill(r("WT"), 1.0)
-    iota(r("PC", 0, 1), [[0, 1]], 0, 1)
-    for k in range(3):
-        iota(r("UL", 8 * k, 8 * k + 8), GRP[JUMP[k]][0], GRP[JUMP[k]][1])
-    iota(r("JM"), [[0, 24], [1, 16]], 0)
-    iota(r("I4"), [[0, 24], [1, 4]], 0)
-    iota(r("LK2"), [[4, 4], [16, 24]], 0)
-    for a in range(0, 4 * C, 512): act(r("CT", a, a + 512), r("ZB"))
     zeros(*[r("CT", 4 * CA[j] + 256 * j, 4 * CA[j + 1]) for j in range(1, 6)])
-    zeros(r("CB", 0, ROOM["ad"] + 512 * 5), r("CB", ROOM["gs"], ROOM["lg"]), r("G"), r("W", C), r("RF", C), r("GA", 1152), r("FB"))
+    zeros(r("CT", 0, 4 * C))
+    zeros(room("ld", 0, 5), room("gs"))
+    zeros(r("G"), r("RF", C), r("GA", 3 * C, 4 * LINK[3]), r("GA", 4 * LINK[3] + C))
+    zeros(r("FB", 0, 512), r("E", C))
+    fill(r("FB", 512), 0.0)
+    zeros(room("ac1", 0, 2))
+    zeros(room("lg", 0, 8))
+    zeros(r("C2"), r("G2"), r("VT"), r("IN"), r("PT", C), r("GS", C), r("H0", C))
+    for a in range(0, LEN["WA"], 2 * C): const(r("WA", a, a + 2 * C), 0)
+    zeros(room("nm"), r("ND"))
     pr = [(T.LKS[:, 0:24], T.lk[:, 0:24])]
     for h in range(8):
         a = h ^ JUMP[1]
@@ -279,181 +313,175 @@ def rank_program(g, core, T, topo):
         a = h ^ JUMP[2]
         pr.append((T.LKS[16 * h:16 * h + 64, 48:72], T.lk[16 * a:16 * a + 64, 48:72]))
     dma("Y", pr, wr=[r("LKS")])
-    zeros(r("CB", 512 * 5, ROOM["gs"]), r("CB", ROOM["lg"], ROOM["gone"]), r("C2"), r("G2"), r("E", C))
+    iota(r("LK2"), [[4, 4], [16, 24]], 0)
     dma("Y", [(T.LK2[4 * k + s:128:16, 24 * q:24 * q + 24], T.lk[4 * q + s:128:16, 24 * k:24 * k + 24]) for k in range(3) for q in range(4) for s in range(4)], wr=[r("LK2")])
-    zeros(r("VT"), r("IN"), r("PT", C), r("GS", C), r("H0", C), r("ND"))
-    dma("Y", [(T.WCc[:].bitcast(dt.uint8), T.wc[:]), (T.WCs[:], T.ws[:]), (T.VV[:], T.v[:])], wr=[r("WCc"), r("WCs"), r("VV")])
+    dma("Y", [(T.WCc[:].bitcast(dt.uint8), T.wc[:]), (T.WCs[:], T.ws[:])], wr=[r("WCc"), r("WCs")])
+    dma("Y", [(T.VV[:], T.v[:])], wr=[r("VV")])
 
-    p = col("PC", 0)
-    for j, (sh, an) in enumerate([(0, 15), (0, 3), (2, 3), (4, 1), (5, 1), (6, 1)]):
-        ts(col("PC", j + 1), p, sh, OP.arith_shift_right, an, OP.bitwise_and)
-    tc(pcol("p", 6), r("PC", 1, 7))
-    pi, ps, pk, g0, g1, g2 = [P("p", j) for j in range(6)]
-    tc(r("ULo"), r("UL"))
-    fill(r("RST"), 1.0)
-    fill(r("RST", 0, C, 16), 0.0)
-    fill(col("RS", 0), 0.0)
-    ts(r("MD"), r("JM"), pi, OP.is_equal)
-    act(r("MX"), r("MD"), scale=-2e29, bias=1e29)
-    act(r("NX"), r("MD"), scale=2e29)
-    ts(pcol("ms", 4), r("I4", 0, 4), ps, OP.is_equal)
-    ts(pcol("mr", 4), r("I4", 0, 4), pk, OP.is_equal)
-    ts(r("DGR"), r("I4", 0, 32), pk, OP.is_equal)
-    quant("QU", 0, 128, r("U"))
-    pick("QUP", "QU", r("ULo"))
-    fill(r("NX", 0, C, 16), 2e29)
-    a = ROOM["gone"]
-    sel(r("GOt"), r("WT"), [[-16, 8], [0, 64]], OP.is_ge, 0.0, 0, 1)
-    sel(r("CB", a, a + 512), r("GOt"), [[16, 8], [0, 64]], OP.is_ge, 0.0, 15, -1)
+    iota(r("PC", 0, 1), [[0, 1]], 0, 1)
+    iota(r("JM"), [[0, 24], [1, 16]], 0)
+    for k in range(3):
+        iota(r("UL", 8 * k, 8 * k + 8), GRP[JUMP[k]][0], GRP[JUMP[k]][1])
+    iota(r("I4"), [[0, 24], [1, 4]], 0)
     iota(r("IJF"), [[1, C]], 0)
     iota(r("LW"), [[1, C]], 0)
     iota(r("CONST"), [[16, 24]], 0)
+    iota(r("ALT"), [[0, C], [1, 2]], 0)
+    p = col("PC", 0)
+    for j, (sh, an) in enumerate([(0, 15), (0, 3), (2, 3), (4, 1), (5, 1), (6, 1)]):
+        ts(col("PC", j + 1), p, sh, OP.arith_shift_right, an, OP.bitwise_and)
+    tc(pcol("i"), col("PC", 1))
+    tc(pcol("p", 5), r("PC", 2, 7))
+    pi, (ps, pk, g0, g1, g2) = P("i"), [P("p", j) for j in range(5)]
+    ts(r("MD"), r("JM"), pi, OP.is_equal)
+    act(r("MX"), r("MD"), scale=-2e29, bias=1e29)
+    act(r("NX"), r("MD"), scale=2e29)
+    fill(r("NX", 0, C, 16), 2e29)
+    act(r("HD"), r("MD"), scale=-DROP - HOLD, bias=HOLD)
+    ts(r("HD4"), r("I4"), pk, OP.is_equal)
+    act(r("HD4"), r("HD4"), scale=-DROP - HOLD, bias=HOLD)
+    fill(r("RST"), 1.0)
+    fill(r("RST", 0, C, 16), 0.0)
+    fill(col("RS", 0), 0.0)
+    ts(pcol("ms", 4), r("I4", 0, 4), ps, OP.is_equal)
+    ts(pcol("mr", 4), r("I4", 0, 4), pk, OP.is_equal)
+    ts(r("DGR"), r("I4", 0, 32), pk, OP.is_equal)
+    for n, src in (("ULo", "UL"), ("OFJ", "LKT"), ("OFS", "LKS")): tc(r(n), r(src))
+    quant("QU", 0, 128, r("U"))
+    pick("QUP", "QU", r("ULo"))
+    quant("QX", 0, C, r("X0"))
+    quant("QV", 0, 128, r("VV"))
+    act(pcol("n3"), P("mr", 3), scale=-1.0, bias=1.0)
+    act(pcol("mk", 4), PV("ms"), scale=P("n3"))
+    act(pcol("mn", 4), PV("mk"), scale=-1.0)
+    act(pcol("m7", 4), PV("mr"), scale=-7.0)
+    act(pcol("m512", 4), PV("mr"), scale=512.0)
+    act(pcol("m29", 4), PV("mr"), scale=512.0 * 29)
+    act(pcol("k16"), pi, scale=HOLD, bias=-15 * HOLD)
+    act(pcol("k4"), pk, scale=HOLD, bias=-3 * HOLD)
+    act(pcol("kc"), pi, scale=1 - HOLD, bias=15 * (HOLD - 1) + GW - 0.5)
+    act(r("CONST"), r("CONST"), scale=-1.0, bias=P("kc"))
+    act(pcol("h4"), P("k16"), scale=4.0, bias=1024.0)
+    act(pcol("hb", 4), r("I4", 0, 4), bias=P("h4"))
+    act(pcol("sg1"), g0, scale=-2.0, bias=1.0)
+    act(pcol("sg2"), g2, scale=-2.0, bias=1.0)
+    act(pcol("p4"), row(4), scale=P("sg1"))
+    act(pcol("p8"), row(8), scale=P("sg2"))
+    act(pcol("ys"), row(1), scale=-2.0, bias=row(0))
+    ts(pcol("wa"), row(0), row(1), OP.subtract, row(2), OP.subtract)
+    act(pcol("w0"), row(10), scale=-1.0, bias=P("wa"))
+    ts(pcol("ya"), row(4), g0, OP.mult, row(1), OP.subtract)
+    act(pcol("yb"), row(8), scale=g2, bias=P("ya"))
+    act(pcol("y"), P("yb"), scale=-1.0, bias=1.0)
+    ts(pcol("da"), row(0), row(1), OP.add, row(4), OP.add)
+    act(pcol("dr"), P("da"), bias=row(8))
+    ts(pcol("w1"), row(6), row(2), OP.subtract, P("p4"), OP.subtract)
+    ts(pcol("w2"), row(6), row(10), OP.add, P("p8"), OP.add)
+    ts(pcol("ba"), row(0), row(1), OP.subtract, P("p4"), OP.add)
+    act(pcol("base"), P("ba"), bias=P("p8"))
+    tt(r("ML"), r("IJF"), r("LW"), OP.is_lt, off=r("OFJ", 0, 24))
+    act(r("Y"), r("ML"), scale=P("ys"), bias=P("y"))
+    ts(pcol("a1"), g0, P("mr", 1), OP.not_equal)
+    ts(pcol("a2"), g2, P("mr", 2), OP.not_equal, 2.0, OP.mult)
+    act(pcol("cls"), P("a1"), bias=P("a2"))
+    act(pcol("ws"), P("mr", 2), scale=2.0, bias=-1.0)
+    act(pcol("wsc"), P("ws"), scale=P("n3"))
+    act(pcol("wb"), pk, scale=-1.0, bias=3.0)
+    act(pcol("thr"), P("mr", 3), scale=-18.0, bias=0.5)
+    act(pcol("two"), P("mr", 3), bias=1.0)
+    act(pcol("b1"), P("mr", 1), scale=2.0, bias=P("mr", 0))
+    act(pcol("bit"), P("mr", 2), scale=4.0, bias=P("b1"))
+    act(pcol("bit8"), P("bit"), scale=8.0)
+    act(pcol("h768"), g1, scale=2.0 * C)
+    act(pcol("o1"), g2, scale=2.0, bias=g0)
+    act(pcol("o2"), P("o1"), scale=128.0, bias=-256.0)
+    act(pcol("o3"), P("o2"), bias=float(GW))
+    act(r("SLS"), r("IJF", 0, GW), bias=P("o2"))
+    act(r("SLF"), r("IJF"), scale=0.0, bias=P("o3"))
+    ts(pcol("s3"), ps, P("mr", 3), OP.mult, 16.0, OP.add)
+    for q in range(4): ts(r("X16", q, 96, 4), r("LK2", 24 * q, 24 * q + 24), P("s3"), OP.add)
+    ts(r("XA"), r("X16"), 31, OP.bitwise_and)
+    ts(r("XB2"), r("X16"), 992, OP.bitwise_and)
+    ts(r("OCL"), r("XA"), -16.0, OP.add)
+    tc(r("OCH"), r("XB2"))
+
+    turn = [0]
 
     def group_mask(o, c, src=None):
         gp, gb = GRP[c]
         n = size(o) // 32
         rep = [[0, n]] if n > 1 else []
-        x = r("GOt", 0, 32 * n)
+        turn[0] = (turn[0] + 160) % 480
+        x = r("GOt", 512 + turn[0], 512 + turn[0] + 32 * n)
         sel(x, src or o, rep + neg(gp) + [[0, 4]], OP.is_ge, 0.0, -gb, 1)
         sel(o, x, rep + gp + [[0, 4]], OP.is_ge, 0.0, gb + 15, -1)
-
-    group_mask(r("GCA"), 0, r("WT", 0, 32))
-
-    def setup_columns():
-        act(pcol("n3"), P("mr", 3), scale=-1.0, bias=1.0)
-        act(pcol("mk", 4), PV("ms"), scale=P("n3"))
-        act(pcol("mn", 4), PV("mk"), scale=-1.0)
-        act(pcol("m7", 4), PV("mr"), scale=-7.0)
-        act(pcol("k16"), pi, scale=HOLD, bias=-15 * HOLD)
-        act(pcol("kc"), pi, scale=1 - HOLD, bias=15 * (HOLD - 1) + GW - 0.5)
-        act(r("CONST"), r("CONST"), scale=-1.0, bias=P("kc"))
-        act(r("HD"), r("MD"), scale=-DROP - HOLD, bias=HOLD)
-
-    def setup_rows():
-        act(pcol("sg1"), g0, scale=-2.0, bias=1.0)
-        act(pcol("sg2"), g2, scale=-2.0, bias=1.0)
-        act(pcol("p4"), row(4), scale=P("sg1"))
-        act(pcol("p8"), row(8), scale=P("sg2"))
-        act(pcol("ys"), row(1), scale=-2.0, bias=row(0))
-        ts(pcol("wa"), row(0), row(1), OP.subtract, row(2), OP.subtract)
-        ts(pcol("w0"), P("wa"), row(10), OP.subtract)
-        ts(pcol("ya"), row(4), g0, OP.mult, row(1), OP.subtract)
-        ts(pcol("yb"), row(8), g2, OP.mult, P("ya"), OP.add)
-        ts(pcol("da"), row(0), row(1), OP.add, row(4), OP.add)
-        ts(pcol("w1"), row(6), row(2), OP.subtract, P("p4"), OP.subtract)
-        ts(pcol("w2"), row(6), row(10), OP.add, P("p8"), OP.add)
-        ts(pcol("ba"), row(0), row(1), OP.subtract, P("p4"), OP.add)
-        act(pcol("base"), P("ba"), bias=P("p8"))
-        act(pcol("y"), P("yb"), scale=-1.0, bias=1.0)
-        act(pcol("dr"), P("da"), bias=row(8))
-
-    def lay(names):
-        a, n = 32 * TI[names[0]], len(names)
-        x = r("CF", a, a + 32 * n)
-        group_mask(r("CF", a, a + 32 * (n - 2)), 0)
-        for k in (1, 2): group_mask(cf(names[k - 3]), JUMP[k])
-        for s in range(4): sel(r("CB", 5 * s, 512 * n, 16), x, [[0, 32 * n]], OP.is_ge, 0.0, 0, 0)
 
     def quant_tiles(names):
         for j in range(0, len(names), 4):
             a, n = names[j], len(names[j:j + 4])
-            quant("QK", 128 * TI[a], 128 * (TI[a] + n), r("CB", ROOM[a], ROOM[a] + 512 * n))
+            quant("QK", 128 * TI[a], 128 * (TI[a] + n), room(a, 0, n))
 
-    def setup_turns():
-        act(r("GCT", 0, 32), r("DGR"), scale=-2.0, bias=-4.0)
-        act(cf("ld"), r("GCT", 0, 32), scale=P("dr"))
-        act(cf("lo"), r("DGR"), scale=-4.0, bias=-1.0)
-        act(r("GCT", 32, 64), r("DGR"), scale=-2.0, bias=3.0)
-        for k in range(3): act(cf("lc%d" % k), r("GCT", 32, 64), scale=P("mr", k))
-        a = ROOM["gs"]
-        for s in range(4): act(r("CB", a + 4 * s, a + 512, 16), r("GCA"), scale=P("ms", s))
+    def lay(names):
+        n = len(names)
+        group_mask(cf(names[0], n - 2), 0)
+        for k in (1, 2): group_mask(cf(names[k - 3]), JUMP[k])
+        for s in range(4): sel(room(names[0], 5 * s, n, 16), cf(names[0], n), [[0, 32 * n]], OP.is_ge, 0.0, 0, 0)
+        quant_tiles(names)
 
-    def setup_aways():
-        act(cf("ad"), r("DGR"), scale=P("dr"))
-        act(cf("ao"), r("DGR"), scale=0.5)
-        act(r("GCT", 0, 32), r("DGR"), scale=-0.5)
-        act(r("GCT", 3, 32, 4), r("WT", 0, 8))
-        for k in range(3): act(cf("ac%d" % k), r("GCT", 0, 32), scale=P("mr", k))
-        a = 32 * TI["ord"]
-        for k, (x, y, op) in enumerate(((2, 10, OP.add), (6, 2, OP.subtract), (6, 10, OP.add), (0, 0, OP.subtract))):
-            ts(r("CF", a + k, a + 32, 4), r("WT", 0, 8), row(x), OP.mult, row(y), op)
-        act(pcol("sa"), P("mr", 2), scale=float(FS), bias=P("mr", 0))
-        act(cf("st"), r("WT", 0, 32), scale=P("sa"), bias=P("mr", 1))
+    def lay_short(e, a, b):
+        n = TI[b] - TI[a] + 1
+        for s in range(4): act(room(a, 4 * s + e, n, 16), c2(e, a, 0, 1, n), scale=P("ms", s))
 
-    def setup_factors():
-        sel(r("FB", 3, 515, 4), r("WT", 0, 128), [[-1, 128]], OP.is_equal, 0.0, 0, 1)
-        a = 32 * T2.index("ct0")
-        for A in range(4):
-            x = r("GDT", 32 * A, 32 * A + 32)
-            sel(x, r("WT", 0, 32), [[0, 2], [-32, 2], [0, 8]], OP.is_ge, 0.0, -CLS(A), 1)
-            sel(r("CF2", 960 + a + 32 * A, 960 + a + 32 * A + 32), x, [[0, 2], [32, 2], [0, 8]], OP.is_ge, 0.0, CLS(A) + 15, -1)
-        const(c2(0, "lg"), -1)
-        const(c2(0, "lg", 3, 4), 1)
-        for e, c in ((0, 1), (1, 1), (3, 2)): const(c2(e, "dl1"), c)
-        for e in (2, 3): const(c2(e, "dl2"), FS)
-        for e in range(3): sel(r("CF2", 320 * e + a, 320 * e + a + 128), r("CF2", 960 + a, 960 + a + 128), [[0, 32], [1, 4]], OP.is_equal, 0.0, -e, 0)
-        for e, x, y in ((0, "lg", "dl1"), (1, "nm", "dl1"), (2, "dl2", "dl2"), (3, "dl1", "dl1"), (3, "dl2", "dl2")):
-            group_mask(r("CF2", 320 * e + 32 * T2.index(x), 320 * e + 32 * T2.index(y) + 32), 0)
-
-    def setup_nodes():
-        iota(r("NODE"), [[1, LEN["NODE"]]], 0)
-        for A in range(1, 4): iota(r("NODE", FS * A, FS * A + C), [[1, C]], C * ((A & 1) + 4 * (A >> 1)))
-
-    def short_factors():
-        act(c2(0, "lv"), r("DGR"), scale=2048.0, bias=-1024.0)
-        act(c2(0, "nm"), r("DGR"), scale=-2.0)
-        act(pcol("nb"), P("mr", 3), scale=9.5, bias=-9.0)
-        act(c2(1, "nm"), r("DGR"), scale=-4.0, bias=P("nb"))
-
-    def short_lay(e, q="S"):
-        a, b = T2.index(ELEM[e][0]), T2.index(ELEM[e][1]) + 1
-        x = r("CF2", 320 * e + 32 * a, 320 * e + 32 * b)
-        o = ROOM["gs"]
-        for s in range(4):
-            y = r("CB", o + 512 * a + 4 * s + e, o + 512 * b, 16)
-            if q == "S": act(y, x, scale=P("ms", s))
-            else: ts(y, x, P("ms", s), OP.mult)
-
-    def setup_ends():
-        ts(pcol("s3"), ps, P("mr", 3), OP.mult, 16.0, OP.add)
-        for q in range(4): ts(r("X16", q, 96, 4), r("LK2", 24 * q, 24 * q + 24), P("s3"), OP.add)
-        ts(r("XA"), r("X16"), 31, OP.bitwise_and)
-        ts(r("XB2"), r("X16"), 992, OP.bitwise_and)
-        ts(r("OCL"), r("XA"), -16.0, OP.add)
-        tc(r("OCH"), r("XB2"))
-
-    def setup_classes():
-        ts(pcol("a1"), g0, P("mr", 1), OP.not_equal)
-        ts(pcol("a2"), g2, P("mr", 2), OP.not_equal, 2.0, OP.mult)
-        ts(r("HD4"), r("I4"), pk, OP.is_equal)
-
-    def setup_stay():
-        act(pcol("m512", 4), PV("mr"), scale=512.0)
-        act(pcol("m29", 4), PV("mr"), scale=512.0 * 29)
-        act(pcol("ws"), P("mr", 2), scale=2.0, bias=-1.0)
-        act(pcol("wsc"), P("ws"), scale=P("n3"))
-        act(pcol("wb"), pk, scale=-1.0, bias=3.0)
-
-    def setup_routes():
-        act(pcol("cls"), P("a1"), bias=P("a2"))
-        act(pcol("thr"), P("mr", 3), scale=-18.0, bias=0.5)
-        act(pcol("two"), P("mr", 3), bias=1.0)
-        act(r("HD4"), r("HD4"), scale=-DROP - HOLD, bias=HOLD)
-        act(pcol("k4"), pk, scale=HOLD, bias=-3 * HOLD)
-        for b in range(4): act(pcol("hb%d" % b), P("k16"), scale=4.0, bias=1024.0 + b)
-
-    def setup_bits():
-        act(pcol("b1"), P("mr", 1), scale=2.0, bias=P("mr", 0))
-        act(pcol("bit"), P("mr", 2), scale=4.0, bias=P("b1"))
-        act(pcol("bit8"), P("bit"), scale=8.0)
-        act(pcol("h768"), g1, scale=2.0 * C)
-
-    def setup_slots():
-        act(pcol("o1"), g2, scale=2.0, bias=g0)
-        act(pcol("o2"), P("o1"), scale=128.0, bias=-256.0)
-        act(pcol("o3"), P("o2"), bias=float(GW))
-        act(r("SLS"), r("IJF", 0, GW), bias=P("o2"))
-        for x in (r("F0", 4 * C, FS), r("SLF")): act(x, r("IJF"), scale=0.0, bias=P("o3"))
+    sel(r("GOt", 0, 512), r("WT"), [[-16, 8], [0, 64]], OP.is_ge, 0.0, 0, 1)
+    sel(room("gone"), r("GOt", 0, 512), [[16, 8], [0, 64]], OP.is_ge, 0.0, 15, -1)
+    quant_tiles(["gone"])
+    group_mask(c2(0, "gs"), 0, r("WT", 0, 32))
+    lay_short(0, "gs", "gs")
+    quant_tiles(["gs"])
+    act(r("GCT", 0, 32), r("DGR"), scale=-2.0, bias=-4.0)
+    act(cf("ld"), r("GCT", 0, 32), scale=P("dr"))
+    act(cf("lo"), r("DGR"), scale=-4.0, bias=-1.0)
+    act(r("GCT", 32, 64), r("DGR"), scale=-2.0, bias=3.0)
+    for k in range(3): act(cf("lc%d" % k), r("GCT", 32, 64), scale=P("mr", k))
+    lay(T1A)
+    sel(r("FB", 3, 515, 4), r("WT", 0, 128), [[-1, 128]], OP.is_equal, 0.0, 0, 1)
+    for b in range(4): quant("QF", 128 * b, 128 * b + 128, r("FB", 3 - b, 515 - b))
+    act(cf("ad"), r("DGR"), scale=P("dr"))
+    act(cf("ao"), r("DGR"), scale=0.5)
+    act(r("GCT", 64, 96), r("DGR"), scale=-0.5)
+    const(r("GCT", 67, 96, 4), 1)
+    for k in range(3): act(cf("ac%d" % k), r("GCT", 64, 96), scale=P("mr", k))
+    a = 32 * TI["ord"]
+    for k, (x, y, op) in enumerate(((2, 10, OP.add), (6, 2, OP.subtract), (6, 10, OP.add))):
+        ts(r("CF", a + k, a + 32, 4), r("WT", 0, 8), row(x), OP.mult, row(y), op)
+    const(r("CF", a + 3, a + 32, 4), 0)
+    act(pcol("sa"), P("mr", 2), scale=float(FS), bias=P("mr", 0))
+    act(cf("st"), r("WT", 0, 32), scale=P("sa"), bias=P("mr", 1))
+    lay(T1B)
+    for A in range(4):
+        x = r("GDT", 32 * A, 32 * A + 32)
+        sel(x, r("WT", 0, 32), [[0, 2], [-32, 2], [0, 8]], OP.is_ge, 0.0, -CLS(A), 1)
+        sel(c2(3, "ct%d" % A), x, [[0, 2], [32, 2], [0, 8]], OP.is_ge, 0.0, CLS(A) + 15, -1)
+    for e in range(3): sel(c2(e, "ct0", 0, 1, 4), c2(3, "ct0", 0, 1, 4), [[0, 32], [1, 4]], OP.is_equal, 0.0, -e, 0)
+    const(c2(0, "lg"), -1)
+    const(c2(0, "lg", 3, 4), 1)
+    act(c2(0, "lv"), r("DGR"), scale=2048.0, bias=-1024.0)
+    const(c2(0, "dl1"), 1)
+    group_mask(c2(0, "lg", 0, 1, 3), 0)
+    for e, n, c in ((1, "dl1", 1), (3, "dl1", 2), (2, "dl2", FS), (3, "dl2", FS)):
+        const(c2(e, n), c)
+        group_mask(c2(e, n), 0)
+    for e in range(4): lay_short(e, *ELEM[e])
+    quant_tiles(T2[1:9])
+    act(c2(0, "nm"), r("DGR"), scale=-2.0)
+    act(pcol("nb"), P("mr", 3), scale=9.5, bias=-9.0)
+    act(c2(1, "nm"), r("DGR"), scale=-4.0, bias=P("nb"))
+    for e in range(2):
+        group_mask(c2(e, "nm"), 0)
+        lay_short(e, "nm", "nm")
+    quant_tiles(["nm"])
+    for a in range(0, LEN["NODE"], 2 * C): iota(r("NODE", a, a + 2 * C), [[1, 2 * C]], 0)
+    for A in range(1, 4): iota(r("NODE", FS * A, FS * A + C), [[1, C]], C * ((A & 1) + 4 * (A >> 1)))
 
     def send(t):
         m = topo.engines(core, nxt)[:ENGINES]
@@ -461,16 +489,16 @@ def rank_program(g, core, T, topo):
         rid, pid, _ = topo.addr(nxt)
         n = 128 if t == 0 else GW
         a = 0 if t == 0 else 32 + GW * t
-        c, s = r("QEc", 128 * t, 128 * t + n), r("QEs", 128 * t, 128 * t + n)
-        await_("G", deps_of("D", [c, s], []))
         sem = T.sem["arr%d" % t]
-        g.remote_dma(T.LDc[:, a:a + n].bitcast(dt.uint8), T.QEc[:, 128 * t:128 * t + n].bitcast(dt.uint8), sem, T.sem.lcl, pid, rid, mask)
-        g.remote_dma(T.LDs[:, a:a + n], T.QEs[:, 128 * t:128 * t + n], sem, T.sem.lcl, pid, rid, mask)
-        cnt["lcl"] += 2 * len(m)
+
+        def run(e):
+            e.remote_dma(T.LDc[:, a:a + n].bitcast(dt.uint8), T.QEc[:, 128 * t:128 * t + n].bitcast(dt.uint8), sem, T.sem.lcl, pid, rid, mask)
+            e.remote_dma(T.LDs[:, a:a + n], T.QEs[:, 128 * t:128 * t + n], sem, T.sem.lcl, pid, rid, mask)
+
         pe = len(topo.engines(T.cores[(rank - 1) % len(T.cores)], core)[:ENGINES])
-        cnt["arr%d" % t] = 2 * pe
-        clk[("arr%d" % t, 2 * pe)] = {}
-        record("D", ("arr%d" % t, 2 * pe), [], [r("LDc", a, a + n), r("LDs", a, a + n)])
+        note({"G": (run, 2000)}, [r("QEc", 128 * t, 128 * t + n), r("QEs", 128 * t, 128 * t + n)],
+             [r("LDc", a, a + n), r("LDs", a, a + n)], FAR, ("arr%d" % t, 2 * pe))
+        return 2 * len(m)
 
     def spread(dst, src):
         n = LEN[src]
@@ -486,254 +514,187 @@ def rank_program(g, core, T, topo):
         ts(r(o), r("ST4", 3, 96, 4), P("k4"), OP.add)
 
     def moved(i, own, came):
-        return [(K(own), ("QW", 128 * i))] + [(K("%s%d" % (came, k)), ("QD", 320 * i + 96 * k)) for k in range(3)]
+        return [(K(n), ("QD", LINK[4] * i + LINK[k])) for k, n in enumerate([own, came + "0", came + "1", came + "2"])]
 
-    def no_slots():
-        dma("Y", [(T.F0[:, 4 * C:FS], T.SLF[:])], rd=[r("SLF")], wr=[r("F0", 4 * C, FS)])
-
-    setup_rows()
-    quant("QX", 0, C, r("X0"))
+    sent = [0]
     for t in range(R):
         pass
-        mm("PA", ("QUP", 0), ("QX", 0), C)
-        mm("PB", ("QUP", 0), ("QX", 0), C)
-        mm("PCC", ("QUP", 128), ("QX", 0), C)
-        mm("PD", ("QUP", 256), ("QX", 0), C)
-        act(r("TS"), r("PB", 0, C))
-        if t: no_slots()
+        for bk, a in (("PA", 0), ("PB", 0), ("PCC", 128), ("PD", 256)): mm(bk, ("QUP", a), ("QX", 0), C)
+        act(r("TS"), r("PB", 0, C), on="S")
+        dma("Y", [(T.F0[:, 4 * C:FS], T.SLF[:])], rd=[r("SLF")], wr=[r("F0", 4 * C, FS)])
         tt(r("SB1"), r("PA", 0, C), r("MX"), OP.max)
         scan(r("ST"), r("NX"), r("SB1"), OP.add, OP.min)
+        tt(r("CT", 0, 4 * C, 4), r("PA", 0, C), r("ST"), OP.is_ge)
         own = 24 - SOWN[t]
         if own < 24: ts(r("NS", own, 24), r("ST", 16 * own + 15, C, 16), -1.0, OP.mult)
-        node = lambda a: r("CT", 4 * CA[a // 4] + a % 4, 4 * CA[a // 4] + 64 * a, 4)
-        for a in range(own, 24):
-            x = r("TM", C * (a % 2), C * (a % 2) + 16 * a)
-            act(x, r("TS", 0, 16 * a), bias=col("NS", a), fn=FN.Relu)
-            act(node(a), x, fn=FN.Sign, acc=col("RS", a))
+        for a in range(23, 0, -1):
+            node, x = r("CT", 4 * CA[a // 4] + a % 4, 4 * CA[a // 4] + 64 * a, 4), r("JK", C * (a % 4), C * (a % 4) + 16 * a)
+            if a >= own:
+                act(x, r("TS", 0, 16 * a), bias=col("NS", a), fn=FN.Relu)
+                act(node, x, fn=FN.Sign, acc=col("RS", a))
+            else:
+                ts(node, r("TS", 0, 16 * a), col("ST", 16 * a + 15), OP.is_gt)
+                total(col("RS", a), x, node)
+        for j in (0, 4, 3, 5, 2, 1):
+            quant("QT", CA[j], CA[j + 1], r("CT", 4 * CA[j], 4 * CA[j + 1]))
+            mm("PE", K("gone"), ("QT", CA[j]), CW[j], j == 0, j == 1)
+        scan(r("CS"), r("RST"), r("CT", 0, 4 * C, 4), OP.mult, OP.add)
+        tt(r("RC"), r("CONST"), r("CS", 15, C, 16), OP.add)
+        tt(r("RC"), r("RC"), r("RS"), OP.add)
+        act(r("W1"), r("PCC", 0, C), scale=P("w1"))
+        act(r("W2"), r("PD", 0, C), scale=P("w2"))
         if t == 0:
-            setup_turns()
-            lay(T1A)
-            setup_columns()
             act(r("W0"), r("PB", 0, C), scale=P("w0"))
             act(r("BASE"), r("PB", 0, C), scale=P("base"))
-        tiles = (4, 3, 0, 5, 2, 1)
-        for j in tiles:
-            for a in range(4 * j + 3, 4 * j - 1, -1):
-                if 0 < a < own:
-                    ts(node(a), r("TS", 0, 16 * a), col("ST", 16 * a + 15), OP.is_gt)
-                    if a < VSUM: total(col("RS", a), node(a))
-                    else: act(r("JK", 0, 16 * a), node(a), acc=col("RS", a))
-            if j == 0:
-                tt(r("CT", 0, 4 * C, 4), r("PA", 0, C), r("ST"), OP.is_ge)
-            quant("QT", CA[j], CA[j + 1], r("CT", 4 * CA[j], 4 * CA[j + 1]))
-            if j == 0:
-                scan(r("CS"), r("RST"), r("CT", 0, 4 * C, 4), OP.mult, OP.add)
-                tt(r("RC"), r("CONST"), r("CS", 15, C, 16), OP.add)
-                if t: quant("QIN", 0, 128, r("IN"))
-                else: quant_tiles(["gone"])
-                for i in (0, 4, 3): mm("PE", K("gone"), ("QT", CA[i]), CW[i], i == 0, False)
-            elif j in (5, 2, 1): mm("PE", K("gone"), ("QT", CA[j]), CW[j], False, j == 1)
-            if t == 0 and j == 3:
-                tc(r("OFJ"), r("LKT"))
-                tt(r("ML"), r("IJF"), r("LW"), OP.is_lt, off=r("OFJ", 0, 24))
-                act(r("W1"), r("PCC", 0, C), scale=P("w1"))
-                act(r("W2"), r("PD", 0, C), scale=P("w2"))
-                act(r("Y"), r("ML"), scale=P("ys"), bias=P("y"))
-                short_factors()
-                setup_factors()
-                zeros(r("WA"))
-        if t == 0:
             tt(r("A0"), r("W0"), r("BASE"), OP.subtract, off=r("OFJ", 0, 24))
-            tt(r("A1"), r("W1"), r("A0"), OP.subtract, off=r("OFJ", 24, 48))
-            tt(r("RG"), r("W2"), r("A1"), OP.is_lt, off=r("OFJ", 48, 72))
-            tt(r("RF", 0, C), r("RG"), r("Y"), OP.is_equal)
-            quant("QRF", 0, 128, r("RF"))
-            quant_tiles(T1A)
-            quant_tiles(["gs"])
-            tc(r("OFS"), r("LKS"))
-            for b in range(4): quant("QF", 128 * b, 128 * b + 128, r("FB", 3 - b, 515 - b))
-        halves = lambda b: act(r("F0", C * b, C * b + C), r(FBANK[b], 0, C), scale=0.5)
-        for b in range(3): mm(FBANK[b], EB(b), ("QX", 0), C)
-        for b in range(2 if t else 1): halves(b)
-        mm(FBANK[3], EB(3), ("QX", 0), C)
-        pass
-        scan(r("ST2"), r("HD"), r("PE", 0, C), OP.add, OP.max)
-        tt(r("RC"), r("RC"), r("RS"), OP.add)
-        tt(r("GF"), r("ST2", 15, C, 16), r("RC"), OP.is_lt)
-        for q in range(4):
-            o = r("G", 4 * q, C, 16)
-            if q < 2 or t == 0: ts(o, r("GF"), P("m7", q), OP.mult, P("mr", q), OP.add)
-            else: act(o, r("GF"), scale=P("m7", q), bias=P("mr", q))
-        quant("QG", 0, 128, r("G"))
-        first = [(K("ld"), ("QRF", 0)) if t == 0 else (EB(0), ("QIN", 0)), (K("gs"), ("QG", 0))]
-        sums("LA", first)
-        for b in range(2 if t else 1, 4): halves(b)
-
-        def in_order():
-            tt(r("PL"), r("ST2", 15, C, 16), r("RC"), OP.subtract)
-            ts(r("PLo"), r("PL"), GW - 0.5, OP.add)
-            scatter(r("LW"), r("PLo"), r("IJF"))
-
-        def gate_list():
-            scan(r("ST3"), r("HD", 0, GW), r("LW", 0, GW), OP.add, OP.max)
-            ts(r("ELo"), r("ST3", 15, GW, 16), P("k16"), OP.add)
-
-        def gates():
-            for b in range(4): act(r("E", b, 4 * GW, 4), r("F0", C * b, C * b + C), scale=2.0, off=r("ELo"))
-
-        def slots():
-            scatter(r("F0", 4 * C, FS), r("ELo"), r("SLS"))
-
-        def pass_on():
-            quant("QE", 128 * t, 128 * t + 128, r("E"))
-            send(t)
-
-        def stay():
-            for q in range(4): act(r("G2", 4 * q, C, 16), r("GF"), scale=P("m29", q), bias=P("m512", q))
-
-        def order0():
-            act(r("W1"), r("PCC", 0, C), scale=P("w1"))
-            act(r("A0"), r("TS"), scale=P("w0"), off=r("OFJ", 0, 24))
+        else: act(r("A0"), r("TS"), scale=P("w0"), off=r("OFJ", 0, 24), on="S")
 
         def order1():
             tt(r("A1"), r("W1"), r("A0"), OP.subtract, off=r("OFJ", 24, 48))
 
         def order2():
-            tt(r("RF", 0, C), r("W2"), r("A1"), OP.is_lt, off=r("OFJ", 48, 72))
+            tt(r("RF" if t else "RG", 0, C), r("W2"), r("A1"), OP.is_lt, off=r("OFJ", 48, 72))
 
         def weights():
-            mm("PA", K("ord"), ("QRF", 0), 128)
-            act(r("WW"), r("PA", 0, 96), scale=P("wsc"), bias=P("wb"), fn=FN.Square)
+            if t == 0: tt(r("RF", 0, C), r("RG"), r("Y"), OP.is_equal)
+            quant("QRF", 0, 128, r("RF"))
+            mm("PD", K("ord"), ("QRF", 0), 128)
+            act(r("WW"), r("PD", 0, 96), scale=P("wsc"), bias=P("wb"), fn=FN.Square)
+
+        if t == 0:
+            for f in (order1, order2, weights): f()
+        for b in range(4):
+            bk = ("PA", "PB")[b % 2]
+            mm(bk, EB(b), ("QX", 0), C)
+            act(r("F0", C * b, C * b + C), r(bk, 0, C), scale=0.5)
+        pass
+        scan(r("ST2"), r("HD"), r("PE", 0, C), OP.add, OP.max)
+        tt(r("GF"), r("ST2", 15, C, 16), r("RC"), OP.is_lt)
+        for q in range(4): act(r("G", 4 * q, C, 16), r("GF"), scale=P("m7", q), bias=P("mr", q))
+        quant("QG", 0, 128, r("G"))
+        first = [(K("ld"), ("QRF", 0)) if t == 0 else (EB(0), ("QIN", 0)), (K("gs"), ("QG", 0))]
+        sums("LA", first)
+        for q in range(4): act(r("G2", 4 * q, C, 16), r("GF"), scale=P("m29", q), bias=P("m512", q))
+        quant("QG2", 0, 128, r("G2"))
+        tt(r("PL"), r("ST2", 15, C, 16), r("RC"), OP.subtract)
+        ts(r("PLo"), r("PL"), GW - 0.5, OP.add)
+
+        def in_order():
+            scatter(r("LW"), r("PLo"), r("IJF"))
+
+        def gates():
+            scan(r("ST3"), r("HD", 0, GW), r("LW", 0, GW), OP.add, OP.max)
+            ts(r("ELo"), r("ST3", 15, GW, 16), P("k16"), OP.add)
+            for b in range(4): act(r("E", b, 4 * GW, 4), r("F0", C * b, C * b + C), scale=2.0, off=r("ELo"), on="S")
+
+        def pass_on():
+            quant("QE", 128 * t, 128 * t + 128, r("E"))
+
+        def slots():
+            scatter(r("F0", 4 * C, FS), r("ELo"), r("SLS"))
+
+        def leave():
+            sent[0] += send(t)
+            spread("FT", "F0")
 
         def layer():
-            a, o = (0, 0) if t == 0 else (GW * t, 32)
+            a, o, last = (0 if t == 0 else GW * t), (0 if t == 0 else 32), len(ops) - 1
             for b in range(4):
-                bk = ("PE", "AB")[b % 2]
+                bk = ("PE", "PCC")[b % 2]
                 mm(bk, ("WC", 128 * b), ("LD", a), 128)
+                ops[-1]["deps"].setdefault(last, False)
                 act(r("H0", b, 4 * GW, 4), r(bk, o, o + GW), scale=0.015625)
             spread("HT", "H0")
 
-        Qn = lambda n: (lambda: quant("Q" + n, 0, 128, r(n)))
-        early = [[in_order], [pass_on], [], [], [], []]
-        mid = [[], [], [], [], [weights], []]
-        onV = [[gate_list], [slots], [Qn("C2")], [], [], []]
-        onS = [[gates], [lambda: spread("FT", "F0")], [], [stay], [], []]
-        if t:
-            onS[1].append(order0)
-            onS[2].append(lambda: act(r("W2"), r("PD", 0, C), scale=P("w2")))
-            early[2].append(order1)
-            early[3].append(order2)
-            onV[3], onV[4] = [Qn("RF")], [Qn("G2")]
-            if t == 1:
-                setup_nodes()
-                onS[4].append(setup_bits)
-        else:
-            early[1] += [setup_aways, lambda: lay(T1B), lambda: iota(r("ALT"), [[0, C], [1, 2]], 0)]
-            onV[1], onS[1] = [], [setup_slots, setup_stay]
-            early[2] += [slots, lambda: spread("FT", "F0"), lambda: short_lay(0, "V"), setup_classes]
-            onS[2] += [lambda: short_lay(1), lambda: short_lay(2)]
-            early[3] += [lambda: quant_tiles(T1B)]
-            onS[3] += [lambda: short_lay(3)]
-            early[4] += [lambda: quant_tiles(T2[1:5]), setup_ends]
-            onV[4] = [Qn("G2")]
-            onS[4] += [setup_routes]
-            early[5] += [lambda: quant_tiles(T2[5:])]
-        done = 0
+        beside = [[in_order], [pass_on, slots], [order1], [order2], [], []]
+        behind = [gates, leave, None, weights, None, layer]
+        if t == 0: beside[2], beside[3], behind[3] = [], [], None
+        sums("AB", [(K("ad"), ("QRF", 0)) if t == 0 else (EB(1), ("QIN", 0))], True, False)
         kept = [(EB(0), ("QC2", 0))]
         for i in range(SWEEPS):
             pass
             bk, nb = ("LA", "LB")[i % 2], ("LB", "LA")[i % 2]
             past = [x for j in range(0 if i < 3 else 2, i) for x in moved(j, "lo", "lc")] + (first if i < 3 else kept)
-            if i < SWEEPS - 1: sums(nb, past, True, False)
-            for s in range(4): ts(r("W", s, C, 4), r(bk, 0, 96), P("mn", s), OP.max, P("mk", s), OP.min)
+            if i == SWEEPS - 1: nb, past = "PB", past + [(K("lg"), ("QG", 0))]
+            sums(nb, past, True, False)
+            for s in range(4): ts(r("GA", s, C, 4), r(bk, 0, 96), P("mn", s), OP.max, P("mk", s), OP.min)
+            last, held = len(ops) - 1, []
+            for f in beside[i]:
+                f()
+                ops[-1]["deps"].setdefault(last, False)
+                held.append(len(ops) - 1)
+            if behind[i]: behind[i]()
+            if i == 2:
+                act(r("C2", 0, C, 4), r(bk, 0, 96))
+                quant("QC2", 0, 128, r("C2"))
             n = VSWEEP[i] if t else VFIRST[i]
-            act(r("GA", n, 1152), r("W", 0, C), off=r("OFS", n // 16, 72))
-            if i == 2: act(r("C2", 0, C, 4), r(bk, 0, 96))
-            quant("QW", 128 * i, 128 * i + 128, r("W"))
-            for f in early[i]: f()
-            if i == SWEEPS - 1: sums("PB", past + [(K("lg"), ("QG", 0))], True, False)
-            if n: tc(r("GA", 0, n), r("W", 0, C), off=r("OFS", 0, n // 16))
-            n = 320 if t == 0 else 288
-            quant("QD", 320 * i, 320 * i + n, r("GA", 0, 4 * n))
-            if i < SWEEPS - 1: sums(nb, moved(i, "lo", "lc"), False, True)
-            for f in mid[i]: f()
-            if t or i >= 3:
-                if done == 0: sums("AB", [(K("ad"), ("QRF", 0)) if t == 0 else (EB(1), ("QIN", 0))], True, False)
-                for j in range(done, i + 1): sums("AB", moved(j, "ao", "ac"), False, j == SWEEPS - 1)
-                done = i + 1
-            for f in onV[i]: f()
-            for f in onS[i]: f()
+            act(r("GA", C + n, 3 * C), r("GA", 0, C), off=r("OFS", n // 16, 48), on="S")
+            act(r("GA", 4 * LINK[3], 4 * LINK[3] + C), r("GA", 0, C), off=r("OFS", 48, 72), on="S")
+            if n: tc(r("GA", C, C + n), r("GA", 0, C), off=r("OFS", 0, n // 16))
+            n, a = 288 if t else 320, LINK[4] * i
+            quant("QD", a, a + n, r("GA", 0, 4 * n))
+            for j in held: ops[-1]["deps"].setdefault(j, False)
+            quant("QD", a + LINK[3], a + LINK[4], r("GA", 4 * LINK[3]))
+            sums(nb, moved(i, "lo", "lc"), False, True)
+            sums("AB", moved(i, "ao", "ac"), False, i == SWEEPS - 1)
         pass
         tt(r("VT", 0, C, 4), r("AB", 0, 96), r("WW"), OP.mult)
         quant("QVT", 0, 128, r("VT"))
         ts(r("IN", 1, C, 4), r("AB", 0, 96), P("thr"), OP.is_gt, P("two"), OP.mult)
         sums("PA", [(K("lg"), ("QG2", 0)), (K("lv"), ("QVT", 0))])
-        sums("PB", moved(SWEEPS - 1, "lo", "lc"), False, True)
         act(r("IN", 0, C, 4), r("PB", 0, 96))
-        layer()
+        quant("QIN", 0, 128, r("IN"))
         tt(r("PT", 0, C, 4), r("PA", 0, 96), r("OCL"), OP.min)
         tt(r("PT", 1, C, 4), r("PA", 0, 96), r("OCH"), OP.min)
         ts(r("PT", 2, C, 4), r("PA", 0, 96), P("cls"), OP.min)
         ts(r("PT", 3, C, 4), r("PA", 0, 96), -1.0, OP.mult, 0.0, OP.max)
         quant("QPT", 0, 128, r("PT"))
         four = ("LA", "LB", "PCC", "PD")
-        for A in (0, 2): mm(four[A], K("ct%d" % A), ("QPT", 0), 128)
+        for A in range(4): mm(four[A], K("ct%d" % A), ("QPT", 0), 128)
         sums("PA", [(K("dl1"), ("QPT", 0)), (K("dl2"), ("QPT", 0))])
-        for A in (1, 3): mm(four[A], K("ct%d" % A), ("QPT", 0), 128)
-        for A in (2, 3, 0, 1):
-            for s in range(4):
-                o, x = r("WA", FS * A + s, FS * A + C, 4), r(four[A], 0, 96)
-                if A < 2: ts(o, x, P("ms", s), OP.mult)
-                else: act(o, x, scale=P("ms", s))
-            if A == 0: to_list("PA", "DL")
+        to_list("PA", "DL")
+        for A in range(4):
+            for s in range(4): act(r("WA", FS * A + s, FS * A + C, 4), r(four[A], 0, 96), scale=P("ms", s), on="V" if A < 2 else "S")
+        if t == R - 1:
+            mm("PB", K("nm"), ("QIN", 0), 128)
+            ts(r("BN"), r("PB", 0, 96), 0.5, OP.is_gt, P("bit8"), OP.mult)
+            act(r("BA"), r("IN", 1, C, 4), scale=P("bit"))
+            tt(r("BA"), r("BA"), r("BN"), OP.add)
+            for s in range(4): act(r("ND", 4 * s, 4 * C, 16), r("BA"), scale=P("ms", s))
+            quant("QND", 0, C, r("ND"))
+            mm("PB", K("gone"), ("QND", 0), C)
+            act(r("OUT", C, 2 * C), r("PB", 0, C))
         pass
-        fd = lambda b: act(r("FD", 2 * C * b, 2 * C * b + 2 * C, 2), r("FT", C * b), off=r("DL"))
-        for j, (a, b) in enumerate((("DL", "L2"), ("L2", "L3"), ("L3", "EL"))):
-            act(r("GS", VSTEP, C), r("WA"), off=r(a, VSTEP // 16, 24))
+        for a, b in (("DL", "L2"), ("L2", "L3"), ("L3", "EL")):
+            act(r("GS", VSTEP, C), r("WA"), off=r(a, VSTEP // 16, 24), on="S")
             tc(r("GS", 0, VSTEP), r("WA"), off=r(a, 0, VSTEP // 16))
             quant("QS", 0, 128, r("GS"))
             mm("PA", K("st"), ("QS", 0), 128)
-            fd((0, 2, 1)[j])
             to_list("PA", b)
         pass
         even = lambda n, b: r(n, 2 * C * b, 2 * C * b + 2 * C, 2)
         odd = lambda n, b: r(n, 2 * C * b + 1, 2 * C * b + 2 * C, 2)
         both = lambda n, b: r(n, 2 * C * b, 2 * C * b + 2 * C)
-
-        def blend(b):
-            if b in PAIRED: scan(both("Z", b), r("ALT"), both("FD", b), OP.mult, OP.add)
-            else: tt(odd("Z", b), r("FT", C * b), even("FD", b), OP.add, off=r("EL"))
-            if b >= 2: act(even("Z", b), r("HT"), off=r("HL%d" % b))
-
-        act(r("SG"), r("FT", 4 * C), off=r("EL"))
-        fd(3)
-        for b in PAIRED[::-1]: act(odd("FD", b), r("FT", C * b), off=r("EL"))
-        if t == R - 1:
-            quant("QIN", 0, 128, r("IN"))
-            mm("PB", K("nm"), ("QIN", 0), 128)
-        blend(0)
+        act(r("SG"), r("FT", 4 * C), off=r("EL"), on="S")
         scan(r("ST2"), r("HD"), r("SG"), OP.add, OP.max)
-        for j in (2, 3, 0, 1): ts(r("HL%d" % j), r("ST2", 15, C, 16), 4.0, OP.mult, P("hb%d" % j), OP.add)
-        for b in (2, 3, 1): blend(b)
-        if t == R - 1:
-            act(r("OUT", 0, C), r("NODE"), bias=P("h768"), off=r("EL"))
-            ts(r("BN"), r("PB", 0, 96), 0.5, OP.is_gt, P("bit8"), OP.mult)
-            act(r("BA"), r("IN", 1, C, 4), scale=P("bit"))
-            for s in range(4):
-                act(r("ND", 4 * s, 4 * C, 16), r("BA"), scale=P("ms", s))
-                act(r("ND", 4 * s + 1, 4 * C, 16), r("BN"), scale=P("ms", s))
-        for b in (2, 3): scan(r("X0", b - 2, 4 * C, 2), r("ALT"), both("Z", b), OP.mult, OP.add)
+        for b in range(4):
+            ts(r("HL%d" % b), r("ST2", 15, C, 16), 4.0, OP.mult, P("hb", b), OP.add)
+            act(even("FD", b), r("FT", C * b), off=r("DL"), on="S")
+            if b in PAIRED:
+                act(odd("FD", b), r("FT", C * b), off=r("EL"), on="S")
+                scan(both("Z", b), r("ALT"), both("FD", b), OP.mult, OP.add)
+            else: tt(odd("Z", b), r("FT", C * b), even("FD", b), OP.add, off=r("EL"))
+        for b in (2, 3):
+            act(even("Z", b), r("HT"), off=r("HL%d" % b), on="S")
+            scan(r("X0", b - 2, 4 * C, 2), r("ALT"), both("Z", b), OP.mult, OP.add)
         for b in (0, 1): tt(r("X0", b, 4 * C, 4), r("HT"), odd("Z", b), OP.add, off=r("HL%d" % b))
         quant("QX", 0, C, r("X0"))
-        if t == 1: quant("QV", 0, 128, r("VV"))
     pass
+    act(r("OUT", 0, C), r("NODE"), bias=P("h768"), off=r("EL"), on="S")
+    dma("Y", [(T.nd[:], T.OUT[0:128:16, 0:2 * C])], rd=[r("OUT", 0, 2 * C)], n=200)
     mm("PA", ("QV", 0), ("QX", 0), C)
     act(r("OUT", 2 * C, 3 * C), r("PA", 0, C))
     dma("Y", [(T.oc[:], T.QXc[:, 0:C].bitcast(dt.uint8))] + [(T.osc[4 * k:4 * k + 4, :], T.QXs[32 * k:32 * k + 4, 0:C]) for k in range(4)], rd=[r("QXc"), r("QXs")])
     dma("Y", [(T.y[:], T.OUT[:, 2 * C:3 * C])], rd=[r("OUT", 2 * C, 3 * C)])
-    quant("QND", 0, C, r("ND"))
-    mm("PB", K("gone"), ("QND", 0), C)
-    act(r("OUT", C, 2 * C), r("PB", 0, C))
-    dma("Y", [(T.nd[:], T.OUT[0:128:16, 0:2 * C])], rd=[r("OUT", 0, 2 * C)])
-    for s in SEMAPHORES:
-        if cnt[s]: g.wait_ge(T.sem[s], cnt[s])
+    issue()
+    g.wait_ge(T.sem.lcl, sent[0])

@@ -7,30 +7,33 @@ COPY, IDENT = FN.Copy, FN.Identity
 C, GW, R, SWEEPS = 384, 96, 3, 6
 JUMP = [0, 1, 4]
 
-T1A, T1B = ["ld", "lo", "lc0", "lc1", "lc2"], ["ad", "ao", "ord", "st", "ac0", "ac1", "ac2"]
-T2 = ["gs", "lg", "lv", "dl1", "ct0", "ct1", "ct2", "ct3", "dl2", "nm"]
-TILES = T1A + T1B + T2 + ["gone"]
+T1A, T1B, T1C = ["ld", "lo", "lc0", "lc1", "lc2"], ["ad", "ao", "ord", "st", "ac0", "ac1", "ac2"], ["cw0", "cw1", "cw2", "cw3"]
+T2 = ["lg", "gr", "lv", "dl1", "ct0", "ct1", "ct2", "ct3", "dl2", "nm"]
+TILES = T1A + T1B + T1C + T2 + ["gone"]
 TI = {n: i for i, n in enumerate(TILES)}
 NT = len(TILES)
-ROOM = {n: i for l in (T1A, T1B + T2 + ["gone"]) for i, n in enumerate(l)}
-ELEM = [("lg", "ct3"), ("dl1", "ct3"), ("ct0", "dl2"), ("dl1", "dl2")]
+ROOM = {n: i for l in (T1A, T1C, T1B + T2 + ["gone"]) for i, n in enumerate(l)}
+ELEM = [("gr", "ct3"), ("dl1", "ct3"), ("ct0", "dl2"), ("dl1", "dl2")]
 FS = 5 * C
 HOLD, DROP = 8192.0, 1048576.0
 LINK = [0, 96, 192, 320, 448]
-VSWEEP = [0, 448, 320, 320, 512, 512]
-VFIRST = [0, 448, 320, 320, 320, 320]
+BESIDE = ["", "", "", "", "", ""]
+BEHIND = ["s0", "s1", "e0 a0 a1", "l0", "b0 b1", "", ""]
+VSWEEP = [448, 448, 448, 448, 448, 448]
+VFIRST = [384, 384, 384, 384, 384, 384]
+TURN = "SSSVSV"
 VSTEP = 192
-SOWN = [2, 3, 3]
-PAIRED = [3]
+SOWN = [4, 4, 4]
+PAIRED = [1, 3]
 ENGINES = 8
-HOP, NEXT, LAND, FAR, SPARE, PASSES = 130, 80, 1500, 4000, 0.1, 3
+HOP, NEXT, LAND, FAR, SPARE, PASSES = 200, 200, 1500, 4000, 0.3, 3
 
 F32, BF, I32, U16, X4, U8 = "float32", "bfloat16", "int32", "uint16", "float8_e4m3fn_x4", "uint8"
 BYTES = {F32: 4, BF: 2, I32: 4, U16: 2, X4: 4, U8: 1}
 SCRATCH = {}
 WIDE = {"KF": "JM MD MX NX HD HD4 I4 IJF CONST SLS", "KI": "PC UL X16 XA XB2", "KB": "WT DGR GCT GCA GDT CF CF2 OCL OCH ML Y ALT",
         "XF": "SB1 ST ST2 ST3 ST4 RS RC PL GF NS", "XB": "CS WW BA BN", "ZT": "G IN C2 G2 VT ND",
-        "XU": "PLo ELo DL L2 L3 EL HL0 HL1 HL2 HL3", "KU": "ULo OFJ OFS"}
+        "XU": "PLo ELo DL L2 L3 EL HL0 HL1 HL2 HL3", "KU": "ULo OFJ OFS LB1 LB16"}
 HOME = {n: w for w in WIDE for n in WIDE[w].split()}
 PLACE, LEN = {}, {}
 
@@ -52,14 +55,14 @@ CA = [sum(CW[:j]) for j in range(7)]
 for _n, _w, _d in [
         ("X0", 1536, BF), ("U", 512, BF), ("VV", 512, BF), ("LKT", 72, I32), ("LKS", 72, I32), ("LK2", 96, I32),
         ("ULo", 24, U16), ("OFJ", 72, U16), ("OFS", 72, U16), ("UL", 24, I32), ("PC", 16, I32), ("X16", 96, I32), ("XA", 96, I32), ("XB2", 96, I32),
-        ("PF", 96, F32), ("WT", 512, BF), ("ZB", 512, BF), ("CB", 512 * (NT - len(T1A)), BF), ("FB", 516, BF), ("GOt", 1024, BF),
-        ("DGR", 32, BF), ("GCT", 96, BF), ("GCA", 32, BF), ("GDT", 128, BF), ("CF", C, BF), ("CF2", 1280, BF),
+        ("PF", 96, F32), ("WT", 512, BF), ("ZB", 512, BF), ("CB", 512 * (ROOM["gone"] + 1), BF), ("FB", 516, BF), ("GOt", 1024, BF),
+        ("DGR", 32, BF), ("GCT", 96, BF), ("GCA", 32, BF), ("GDT", 128, BF), ("CF", 512, BF), ("CF2", 1280, BF),
         ("OCL", 96, BF), ("OCH", 96, BF), ("ML", C, BF), ("Y", C, BF), ("ALT", 2 * C, BF),
         ("JM", C, F32), ("MD", C, F32), ("MX", C, F32), ("NX", C, F32), ("HD", C, F32), ("HD4", 96, F32), ("I4", 96, F32), ("IJF", C, F32),
-        ("CONST", 24, F32), ("SLS", 96, F32), ("RST", C, BF), ("NODE", 3 * FS + C, F32), ("SLF", C, BF),
+        ("CONST", 96, F32), ("SLS", 96, F32), ("RST", C, BF), ("NODE", 3 * FS + C, F32), ("SLF", C, BF),
         ("TS", C, F32), ("W0", C, F32), ("W1", C, F32), ("W2", C, F32), ("BASE", C, F32), ("A0", C, F32), ("A1", C, F32), ("RF", 512, BF), ("RG", C, BF),
-        ("SB1", C, F32), ("ST", C, F32), ("ST2", C, F32), ("ST3", GW, F32), ("ST4", 96, F32), ("RS", 24, F32), ("RC", 24, F32), ("PL", 24, F32),
-        ("GF", 24, F32), ("NS", 24, F32), ("CS", C, BF), ("WW", 96, BF), ("BA", 96, BF), ("BN", 96, BF), ("JK", 4 * C, BF),
+        ("SB1", C, F32), ("ST", C, F32), ("ST2", C, F32), ("ST3", GW, F32), ("ST4", 96, F32), ("RS", 24, F32), ("RC", 96, F32), ("PL", 96, F32), ("LB1", 6, U16), ("LB16", 6, U16),
+        ("GF", 96, F32), ("NS", 24, F32), ("CS", C, BF), ("WW", 96, BF), ("BA", 96, BF), ("BN", 96, BF), ("JK", 4 * C, BF),
         ("PLo", 24, U16), ("ELo", 6, U16), ("DL", 24, U16), ("L2", 24, U16), ("L3", 24, U16), ("EL", 24, U16),
         ("HL0", 24, U16), ("HL1", 24, U16), ("HL2", 24, U16), ("HL3", 24, U16),
         ("CT", 4 * CA[6], BF), ("G", 512, BF), ("IN", 512, BF), ("C2", 512, BF), ("G2", 512, BF), ("VT", 512, BF), ("ND", 4 * C, BF),
@@ -188,7 +191,7 @@ def rank_program(g, core, T, topo):
     narrow = lambda *xs: all(BYTES[SCRATCH[x[0]][2]] == 2 for x in xs)
     vtime = lambda n, f=1.0: max(0.83 * f * n, 53) + 40
     stime = lambda n: max(0.83 * n, 53) + 60
-    gather = lambda n: 1.3 * n + 55
+    gather = lambda n: 1.6 * n + 55
     dn = [0]
 
     def dma(q, pairs, rd=(), wr=(), n=None):
@@ -296,12 +299,12 @@ def rank_program(g, core, T, topo):
     fill(r("WT"), 1.0)
     zeros(*[r("CT", 4 * CA[j] + 256 * j, 4 * CA[j + 1]) for j in range(1, 6)])
     zeros(r("CT", 0, 4 * C))
-    zeros(room("ld", 0, 5), room("gs"))
+    zeros(room("ld", 0, 5), room("lg"))
     zeros(r("G"), r("RF", C), r("GA", 3 * C, 4 * LINK[3]), r("GA", 4 * LINK[3] + C))
     zeros(r("FB", 0, 512), r("E", C))
     fill(r("FB", 512), 0.0)
     zeros(room("ac1", 0, 2))
-    zeros(room("lg", 0, 8))
+    zeros(room("gr", 0, 8))
     zeros(r("C2"), r("G2"), r("VT"), r("IN"), r("PT", C), r("GS", C), r("H0", C))
     for a in range(0, LEN["WA"], 2 * C): const(r("WA", a, a + 2 * C), 0)
     zeros(room("nm"), r("ND"))
@@ -325,7 +328,7 @@ def rank_program(g, core, T, topo):
     iota(r("I4"), [[0, 24], [1, 4]], 0)
     iota(r("IJF"), [[1, C]], 0)
     iota(r("LW"), [[1, C]], 0)
-    iota(r("CONST"), [[16, 24]], 0)
+    iota(r("CONST"), [[16, 24], [0, 4]], 0)
     iota(r("ALT"), [[0, C], [1, 2]], 0)
     p = col("PC", 0)
     for j, (sh, an) in enumerate([(0, 15), (0, 3), (2, 3), (4, 1), (5, 1), (6, 1)]):
@@ -354,13 +357,20 @@ def rank_program(g, core, T, topo):
     act(pcol("n3"), P("mr", 3), scale=-1.0, bias=1.0)
     act(pcol("mk", 4), PV("ms"), scale=P("n3"))
     act(pcol("mn", 4), PV("mk"), scale=-1.0)
-    act(pcol("m7", 4), PV("mr"), scale=-7.0)
-    act(pcol("m512", 4), PV("mr"), scale=512.0)
-    act(pcol("m29", 4), PV("mr"), scale=512.0 * 29)
+    act(pcol("m80", 4), PV("mr"), scale=80.0)
+    act(pcol("thr"), P("mr", 3), scale=-18.0, bias=0.5)
+    act(pcol("two"), P("mr", 3), bias=1.0)
     act(pcol("k16"), pi, scale=HOLD, bias=-15 * HOLD)
     act(pcol("k4"), pk, scale=HOLD, bias=-3 * HOLD)
-    act(pcol("kc"), pi, scale=1 - HOLD, bias=15 * (HOLD - 1) + GW - 0.5)
+    act(pcol("kp"), P("k4"), scale=-1.0, bias=GW - 0.5)
+    act(pcol("ks"), ps, scale=-HOLD, bias=3 * HOLD + GW - 15.5)
+    act(pcol("kc"), P("ks"), bias=pi)
     act(r("CONST"), r("CONST"), scale=-1.0, bias=P("kc"))
+    ts(r("PL"), r("I4"), pk, OP.not_equal, -1e9, OP.mult)
+    tt(r("CONST"), r("CONST"), r("PL"), OP.add)
+    act(pcol("kb"), pk, scale=16.0, bias=15.0)
+    ts(r("LB1"), r("IJF", 0, 24, 4), pk, OP.add)
+    ts(r("LB16"), r("IJF", 0, C, 64), P("kb"), OP.add)
     act(pcol("h4"), P("k16"), scale=4.0, bias=1024.0)
     act(pcol("hb", 4), r("I4", 0, 4), bias=P("h4"))
     act(pcol("sg1"), g0, scale=-2.0, bias=1.0)
@@ -387,8 +397,6 @@ def rank_program(g, core, T, topo):
     act(pcol("ws"), P("mr", 2), scale=2.0, bias=-1.0)
     act(pcol("wsc"), P("ws"), scale=P("n3"))
     act(pcol("wb"), pk, scale=-1.0, bias=3.0)
-    act(pcol("thr"), P("mr", 3), scale=-18.0, bias=0.5)
-    act(pcol("two"), P("mr", 3), bias=1.0)
     act(pcol("b1"), P("mr", 1), scale=2.0, bias=P("mr", 0))
     act(pcol("bit"), P("mr", 2), scale=4.0, bias=P("b1"))
     act(pcol("bit8"), P("bit"), scale=8.0)
@@ -423,8 +431,9 @@ def rank_program(g, core, T, topo):
 
     def lay(names):
         n = len(names)
-        group_mask(cf(names[0], n - 2), 0)
-        for k in (1, 2): group_mask(cf(names[k - 3]), JUMP[k])
+        if names != T1C:
+            group_mask(cf(names[0], n - 2), 0)
+            for k in (1, 2): group_mask(cf(names[k - 3]), JUMP[k])
         for s in range(4): sel(room(names[0], 5 * s, n, 16), cf(names[0], n), [[0, 32 * n]], OP.is_ge, 0.0, 0, 0)
         quant_tiles(names)
 
@@ -435,9 +444,11 @@ def rank_program(g, core, T, topo):
     sel(r("GOt", 0, 512), r("WT"), [[-16, 8], [0, 64]], OP.is_ge, 0.0, 0, 1)
     sel(room("gone"), r("GOt", 0, 512), [[16, 8], [0, 64]], OP.is_ge, 0.0, 15, -1)
     quant_tiles(["gone"])
-    group_mask(c2(0, "gs"), 0, r("WT", 0, 32))
-    lay_short(0, "gs", "gs")
-    quant_tiles(["gs"])
+    const(c2(0, "lg"), -7)
+    const(c2(0, "lg", 3, 4), 7)
+    group_mask(c2(0, "lg"), 0)
+    lay_short(0, "lg", "lg")
+    quant_tiles(["lg"])
     act(r("GCT", 0, 32), r("DGR"), scale=-2.0, bias=-4.0)
     act(cf("ld"), r("GCT", 0, 32), scale=P("dr"))
     act(cf("lo"), r("DGR"), scale=-4.0, bias=-1.0)
@@ -463,11 +474,15 @@ def rank_program(g, core, T, topo):
         sel(x, r("WT", 0, 32), [[0, 2], [-32, 2], [0, 8]], OP.is_ge, 0.0, -CLS(A), 1)
         sel(c2(3, "ct%d" % A), x, [[0, 2], [32, 2], [0, 8]], OP.is_ge, 0.0, CLS(A) + 15, -1)
     for e in range(3): sel(c2(e, "ct0", 0, 1, 4), c2(3, "ct0", 0, 1, 4), [[0, 32], [1, 4]], OP.is_equal, 0.0, -e, 0)
-    const(c2(0, "lg"), -1)
-    const(c2(0, "lg", 3, 4), 1)
+    for A in range(4):
+        x = r("GDT", 32 * A, 32 * A + 32)
+        sel(x, r("DGR"), [[0, 2], [-32, 2], [0, 8]], OP.is_ge, 0.0, -CLS(A), 1)
+        sel(cf("cw%d" % A), x, [[0, 2], [32, 2], [0, 8]], OP.is_ge, 0.0, CLS(A) + 15, -1)
+    lay(T1C)
+    const(c2(0, "gr"), 7)
     act(c2(0, "lv"), r("DGR"), scale=2048.0, bias=-1024.0)
     const(c2(0, "dl1"), 1)
-    group_mask(c2(0, "lg", 0, 1, 3), 0)
+    group_mask(c2(0, "gr", 0, 1, 3), 0)
     for e, n, c in ((1, "dl1", 1), (3, "dl1", 2), (2, "dl2", FS), (3, "dl2", FS)):
         const(c2(e, n), c)
         group_mask(c2(e, n), 0)
@@ -509,6 +524,9 @@ def rank_program(g, core, T, topo):
                 pairs.append((T[dst][16 * h:16 * h + 16, n * A:n * A + n], T[src][a:a + 16, 0:n]))
         dma("Y", pairs, rd=[r(src)], wr=[r(dst)])
 
+    def hold(ahead):
+        for j in ahead: ops[-1]["deps"].setdefault(j, False)
+
     def to_list(bk, o):
         scan(r("ST4"), r("HD4"), r(bk, 0, 96), OP.add, OP.max)
         ts(r(o), r("ST4", 3, 96, 4), P("k4"), OP.add)
@@ -522,8 +540,8 @@ def rank_program(g, core, T, topo):
         for bk, a in (("PA", 0), ("PB", 0), ("PCC", 128), ("PD", 256)): mm(bk, ("QUP", a), ("QX", 0), C)
         act(r("TS"), r("PB", 0, C), on="S")
         dma("Y", [(T.F0[:, 4 * C:FS], T.SLF[:])], rd=[r("SLF")], wr=[r("F0", 4 * C, FS)])
-        tt(r("SB1"), r("PA", 0, C), r("MX"), OP.max)
-        scan(r("ST"), r("NX"), r("SB1"), OP.add, OP.min)
+        for a in (C // 2, 0): tt(r("SB1", a, a + C // 2), r("PA", a, a + C // 2), r("MX", a, a + C // 2), OP.max)
+        for a in (C // 2, 0): scan(r("ST", a, a + C // 2), r("NX", a, a + C // 2), r("SB1", a, a + C // 2), OP.add, OP.min)
         tt(r("CT", 0, 4 * C, 4), r("PA", 0, C), r("ST"), OP.is_ge)
         own = 24 - SOWN[t]
         if own < 24: ts(r("NS", own, 24), r("ST", 16 * own + 15, C, 16), -1.0, OP.mult)
@@ -539,8 +557,8 @@ def rank_program(g, core, T, topo):
             quant("QT", CA[j], CA[j + 1], r("CT", 4 * CA[j], 4 * CA[j + 1]))
             mm("PE", K("gone"), ("QT", CA[j]), CW[j], j == 0, j == 1)
         scan(r("CS"), r("RST"), r("CT", 0, 4 * C, 4), OP.mult, OP.add)
-        tt(r("RC"), r("CONST"), r("CS", 15, C, 16), OP.add)
-        tt(r("RC"), r("RC"), r("RS"), OP.add)
+        tt(r("RC"), r("CS"), r("CONST"), OP.add, off=r("LB16"))
+        tt(r("GF"), r("RS"), r("RC"), OP.add, off=r("LB1"))
         act(r("W1"), r("PCC", 0, C), scale=P("w1"))
         act(r("W2"), r("PD", 0, C), scale=P("w2"))
         if t == 0:
@@ -549,11 +567,11 @@ def rank_program(g, core, T, topo):
             tt(r("A0"), r("W0"), r("BASE"), OP.subtract, off=r("OFJ", 0, 24))
         else: act(r("A0"), r("TS"), scale=P("w0"), off=r("OFJ", 0, 24), on="S")
 
-        def order1():
-            tt(r("A1"), r("W1"), r("A0"), OP.subtract, off=r("OFJ", 24, 48))
+        def order1(h):
+            tt(r("A1", 192 * h, 192 * h + 192), r("W1"), r("A0", 192 * h, 192 * h + 192), OP.subtract, off=r("OFJ", 24 + 12 * h, 36 + 12 * h))
 
-        def order2():
-            tt(r("RF" if t else "RG", 0, C), r("W2"), r("A1"), OP.is_lt, off=r("OFJ", 48, 72))
+        def order2(h):
+            tt(r("RF" if t else "RG", 192 * h, 192 * h + 192), r("W2"), r("A1", 192 * h, 192 * h + 192), OP.is_lt, off=r("OFJ", 48 + 12 * h, 60 + 12 * h))
 
         def weights():
             if t == 0: tt(r("RF", 0, C), r("RG"), r("Y"), OP.is_equal)
@@ -562,25 +580,30 @@ def rank_program(g, core, T, topo):
             act(r("WW"), r("PD", 0, 96), scale=P("wsc"), bias=P("wb"), fn=FN.Square)
 
         if t == 0:
-            for f in (order1, order2, weights): f()
+            for h in (0, 1):
+                order1(h)
+                order2(h)
+            weights()
         for b in range(4):
             bk = ("PA", "PB")[b % 2]
             mm(bk, EB(b), ("QX", 0), C)
             act(r("F0", C * b, C * b + C), r(bk, 0, C), scale=0.5)
         pass
         scan(r("ST2"), r("HD"), r("PE", 0, C), OP.add, OP.max)
-        tt(r("GF"), r("ST2", 15, C, 16), r("RC"), OP.is_lt)
-        for q in range(4): act(r("G", 4 * q, C, 16), r("GF"), scale=P("m7", q), bias=P("mr", q))
+        tt(r("G", 0, C, 4), r("ST2", 3, C, 4), r("GF"), OP.is_lt)
         quant("QG", 0, 128, r("G"))
-        first = [(K("ld"), ("QRF", 0)) if t == 0 else (EB(0), ("QIN", 0)), (K("gs"), ("QG", 0))]
+        flags = len(ops) - 1
+        first = [(K("ld"), ("QRF", 0)) if t == 0 else (EB(0), ("QIN", 0)), (K("lg"), ("QG", 0))]
         sums("LA", first)
-        for q in range(4): act(r("G2", 4 * q, C, 16), r("GF"), scale=P("m29", q), bias=P("m512", q))
+        for q in range(4): act(r("G2", 4 * q, C, 16), r("G", 4 * q, C, 16), scale=2224.0, bias=P("m80", q))
         quant("QG2", 0, 128, r("G2"))
-        tt(r("PL"), r("ST2", 15, C, 16), r("RC"), OP.subtract)
-        ts(r("PLo"), r("PL"), GW - 0.5, OP.add)
+        tt(r("PL"), r("GF"), r("ST2", 3, C, 4), OP.subtract)
+        hold([flags - 1])
+        scan(r("ST4"), r("HD4"), r("PL"), OP.add, OP.max)
+        ts(r("PLo"), r("ST4", 3, 96, 4), -1.0, OP.mult, P("kp"), OP.add)
 
-        def in_order():
-            scatter(r("LW"), r("PLo"), r("IJF"))
+        def in_order(h):
+            scatter(r("LW"), r("PLo", 12 * h, 12 * h + 12), r("IJF", 192 * h, 192 * h + 192))
 
         def gates():
             scan(r("ST3"), r("HD", 0, GW), r("LW", 0, GW), OP.add, OP.max)
@@ -595,7 +618,6 @@ def rank_program(g, core, T, topo):
 
         def leave():
             sent[0] += send(t)
-            spread("FT", "F0")
 
         def layer():
             a, o, last = (0 if t == 0 else GW * t), (0 if t == 0 else 32), len(ops) - 1
@@ -606,35 +628,48 @@ def rank_program(g, core, T, topo):
                 act(r("H0", b, 4 * GW, 4), r(bk, o, o + GW), scale=0.015625)
             spread("HT", "H0")
 
-        beside = [[in_order], [pass_on, slots], [order1], [order2], [], []]
-        behind = [gates, leave, None, weights, None, layer]
-        if t == 0: beside[2], beside[3], behind[3] = [], [], None
+        work = {"s": in_order, "a": order1, "b": order2, "e": lambda h: pass_on(), "l": lambda h: slots()}
+        then = {"s1": gates, "e0": leave, "l0": lambda: spread("FT", "F0"), "b1": weights}
+
+        def pin(names, last):
+            held = []
+            for w in names.split():
+                if t == 0 and w[0] in "ab": continue
+                work[w[0]](int(w[1]))
+                ops[-1]["deps"].setdefault(last, False)
+                held.append(len(ops) - 1)
+                if w in then: then[w]()
+            return held
+
+        held = pin(BEHIND[0], flags)
         sums("AB", [(K("ad"), ("QRF", 0)) if t == 0 else (EB(1), ("QIN", 0))], True, False)
         kept = [(EB(0), ("QC2", 0))]
         for i in range(SWEEPS):
             pass
             bk, nb = ("LA", "LB")[i % 2], ("LB", "LA")[i % 2]
             past = [x for j in range(0 if i < 3 else 2, i) for x in moved(j, "lo", "lc")] + (first if i < 3 else kept)
-            if i == SWEEPS - 1: nb, past = "PB", past + [(K("lg"), ("QG", 0))]
+            if i == SWEEPS - 1: nb, past = "PB", past + [(K("gr"), ("QG", 0))]
             sums(nb, past, True, False)
-            for s in range(4): ts(r("GA", s, C, 4), r(bk, 0, 96), P("mn", s), OP.max, P("mk", s), OP.min)
-            last, held = len(ops) - 1, []
-            for f in beside[i]:
-                f()
-                ops[-1]["deps"].setdefault(last, False)
-                held.append(len(ops) - 1)
-            if behind[i]: behind[i]()
+            even = t == 0 and i < 4
+            for s in range(4):
+                if even or TURN[i] == "S": act(r("GA", s, C, 4), r(bk, 0, 96), scale=P("mk", s), bias=P("mk", s) if even else 0.0, fn=FN.Sign)
+                else: ts(r("GA", s, C, 4), r(bk, 0, 96), P("mn", s), OP.max, P("mk", s), OP.min)
+                if "V" in ops[-1]["ways"]: hold(held)
+            ahead, held = held, pin(BESIDE[i], len(ops) - 1)
             if i == 2:
-                act(r("C2", 0, C, 4), r(bk, 0, 96))
+                act(r("C2", 0, C, 4), r(bk, 0, 96), bias=0.0 if t else 1.0)
                 quant("QC2", 0, 128, r("C2"))
             n = VSWEEP[i] if t else VFIRST[i]
             act(r("GA", C + n, 3 * C), r("GA", 0, C), off=r("OFS", n // 16, 48), on="S")
             act(r("GA", 4 * LINK[3], 4 * LINK[3] + C), r("GA", 0, C), off=r("OFS", 48, 72), on="S")
-            if n: tc(r("GA", C, C + n), r("GA", 0, C), off=r("OFS", 0, n // 16))
+            tc(r("GA", C, C + n), r("GA", 0, C), off=r("OFS", 0, n // 16))
+            hold(ahead)
             n, a = 288 if t else 320, LINK[4] * i
             quant("QD", a, a + n, r("GA", 0, 4 * n))
-            for j in held: ops[-1]["deps"].setdefault(j, False)
+            hold(held)
             quant("QD", a + LINK[3], a + LINK[4], r("GA", 4 * LINK[3]))
+            held = pin(BEHIND[i + 1], len(ops) - 1)
+            if i == SWEEPS - 1: layer()
             sums(nb, moved(i, "lo", "lc"), False, True)
             sums("AB", moved(i, "ao", "ac"), False, i == SWEEPS - 1)
         pass
@@ -650,14 +685,24 @@ def rank_program(g, core, T, topo):
         ts(r("PT", 3, C, 4), r("PA", 0, 96), -1.0, OP.mult, 0.0, OP.max)
         quant("QPT", 0, 128, r("PT"))
         four = ("LA", "LB", "PCC", "PD")
-        for A in range(4): mm(four[A], K("ct%d" % A), ("QPT", 0), 128)
+
+        def classes(n, src):
+            for A in (2, 0, 3, 1):
+                mm(four[A], K("%s%d" % (n, A)), (src, 0), 128)
+                if A != 2: ops[-1]["deps"].setdefault(len(ops) - 2, False)
+
+        classes("ct", "QPT")
         sums("PA", [(K("dl1"), ("QPT", 0)), (K("dl2"), ("QPT", 0))])
         to_list("PA", "DL")
-        for A in range(4):
-            for s in range(4): act(r("WA", FS * A + s, FS * A + C, 4), r(four[A], 0, 96), scale=P("ms", s), on="V" if A < 2 else "S")
+
+        def table():
+            for A in range(4):
+                for s in range(4): act(r("WA", FS * A + s, FS * A + C, 4), r(four[A], 0, 96), scale=P("ms", s), on="V" if A < 2 else "S")
+
+        table()
         if t == R - 1:
             mm("PB", K("nm"), ("QIN", 0), 128)
-            ts(r("BN"), r("PB", 0, 96), 0.5, OP.is_gt, P("bit8"), OP.mult)
+            ts(r("BN"), r("PB", 0, 96), -1.5, OP.is_gt, P("bit8"), OP.mult)
             act(r("BA"), r("IN", 1, C, 4), scale=P("bit"))
             tt(r("BA"), r("BA"), r("BN"), OP.add)
             for s in range(4): act(r("ND", 4 * s, 4 * C, 16), r("BA"), scale=P("ms", s))
@@ -665,12 +710,14 @@ def rank_program(g, core, T, topo):
             mm("PB", K("gone"), ("QND", 0), C)
             act(r("OUT", C, 2 * C), r("PB", 0, C))
         pass
-        for a, b in (("DL", "L2"), ("L2", "L3"), ("L3", "EL")):
+        for a, b in (("DL", "L2"), ("L2", "EL")):
             act(r("GS", VSTEP, C), r("WA"), off=r(a, VSTEP // 16, 24), on="S")
             tc(r("GS", 0, VSTEP), r("WA"), off=r(a, 0, VSTEP // 16))
             quant("QS", 0, 128, r("GS"))
+            if b == "L2": classes("cw", "QS")
             mm("PA", K("st"), ("QS", 0), 128)
             to_list("PA", b)
+            if b == "L2": table()
         pass
         even = lambda n, b: r(n, 2 * C * b, 2 * C * b + 2 * C, 2)
         odd = lambda n, b: r(n, 2 * C * b + 1, 2 * C * b + 2 * C, 2)
@@ -679,7 +726,8 @@ def rank_program(g, core, T, topo):
         scan(r("ST2"), r("HD"), r("SG"), OP.add, OP.max)
         for b in range(4):
             ts(r("HL%d" % b), r("ST2", 15, C, 16), 4.0, OP.mult, P("hb", b), OP.add)
-            act(even("FD", b), r("FT", C * b), off=r("DL"), on="S")
+            for h in (0, 1):
+                act(r("FD", 2 * C * b + C * h, 2 * C * b + C * h + C, 2), r("FT", C * b), off=r("DL", 12 * h, 12 * h + 12))
             if b in PAIRED:
                 act(odd("FD", b), r("FT", C * b), off=r("EL"), on="S")
                 scan(both("Z", b), r("ALT"), both("FD", b), OP.mult, OP.add)

@@ -6,6 +6,7 @@ OP, FN = AluOpType, ActivationFunctionType
 COPY, IDENT = FN.Copy, FN.Identity
 C, GW, R, SWEEPS = 384, 96, 3, 6
 JUMP = [0, 1, 4]
+REACH = [0, 1, 4, 5]
 
 T1A, T1B, T1C = ["ld", "lo", "lc0", "lc1", "lc2"], ["ad", "ao", "ord", "st", "ac0", "ac1", "ac2"], ["cw0", "cw1", "cw2", "cw3"]
 T2 = ["lg", "gr", "lv", "dl1", "ct0", "ct1", "ct2", "ct3", "dl2", "nm"]
@@ -14,26 +15,31 @@ TI = {n: i for i, n in enumerate(TILES)}
 NT = len(TILES)
 ROOM = {n: i for l in (T1A, T1C, T1B + T2 + ["gone"]) for i, n in enumerate(l)}
 ELEM = [("gr", "ct3"), ("dl1", "ct3"), ("ct0", "dl2"), ("dl1", "dl2")]
-FS = 5 * C
+FS = 4 * C
 HOLD, DROP = 8192.0, 1048576.0
-LINK = [0, 96, 192, 320, 448]
+LINK = [0, 128, 224, 352, 480]
 BESIDE = ["", "", "", "", "", ""]
-BEHIND = ["s0", "s1", "e0 a0 a1", "l0", "b0 b1", "", ""]
+BEHIND = ["s0", "s1", "e0", "a0 a1", "b0 b1", "", ""]
+AHEAD = [1, 3, 3]
+LAYER = 3
 VSWEEP = [448, 448, 448, 448, 448, 448]
-VFIRST = [384, 384, 384, 384, 384, 384]
-TURN = "SSSVSV"
+VFIRST = [448, 448, 448, 448, 448, 448]
+TURN = "SSSSSV"
+TORDER = (0, 3, 4, 1, 2, 5)
+BLEND = "z20 z00 f30 f10 f31 f11 p30 z21 p10 z01 h20 h30 p31 x20 p11 x30 y00 y10 h21 h31 x21 q00 x31 y01 s00 y11 s10 q01 s20"
+KEEP = [2]
 VSTEP = 192
-SOWN = [4, 4, 4]
-PAIRED = [1, 3]
+SOWN = [7, 8, 9, 10, 11, 12, 21, 22, 23]
+SFIRST = [19, 20]
 ENGINES = 8
-HOP, NEXT, LAND, FAR, SPARE, PASSES = 200, 200, 1500, 4000, 0.3, 3
+HOP, NEXT, LAND, FAR, SPARE, PASSES, PACES = 200, 200, 1500, 4000, 0.2, 8, (0.55,)
 
 F32, BF, I32, U16, X4, U8 = "float32", "bfloat16", "int32", "uint16", "float8_e4m3fn_x4", "uint8"
 BYTES = {F32: 4, BF: 2, I32: 4, U16: 2, X4: 4, U8: 1}
 SCRATCH = {}
 WIDE = {"KF": "JM MD MX NX HD HD4 I4 IJF CONST SLS", "KI": "PC UL X16 XA XB2", "KB": "WT DGR GCT GCA GDT CF CF2 OCL OCH ML Y ALT",
-        "XF": "SB1 ST ST2 ST3 ST4 RS RC PL GF NS", "XB": "CS WW BA BN", "ZT": "G IN C2 G2 VT ND",
-        "XU": "PLo ELo DL L2 L3 EL HL0 HL1 HL2 HL3", "KU": "ULo OFJ OFS LB1 LB16"}
+        "XF": "SB1 ST ST2 ST3 ST4 RS RC PL GF NS", "XB": "CS WW BA BN", "ZT": "G IN C2 G2 VT ND", "FZ": "FD Z",
+        "XU": "PLo ELo DL L2 L3 EL SLo", "KU": "ULo OFJ OFS LB1 LB16"}
 HOME = {n: w for w in WIDE for n in WIDE[w].split()}
 PLACE, LEN = {}, {}
 
@@ -50,26 +56,27 @@ def mx(name, n):
     sb(name + "s", n, U8)
 
 
-CW = [C, 128, 176, 240, 304, 368]
+CW = [C, 320, 256, 192, 128, 128]
 CA = [sum(CW[:j]) for j in range(7)]
 for _n, _w, _d in [
         ("X0", 1536, BF), ("U", 512, BF), ("VV", 512, BF), ("LKT", 72, I32), ("LKS", 72, I32), ("LK2", 96, I32),
         ("ULo", 24, U16), ("OFJ", 72, U16), ("OFS", 72, U16), ("UL", 24, I32), ("PC", 16, I32), ("X16", 96, I32), ("XA", 96, I32), ("XB2", 96, I32),
-        ("PF", 96, F32), ("WT", 512, BF), ("ZB", 512, BF), ("CB", 512 * (ROOM["gone"] + 1), BF), ("FB", 516, BF), ("GOt", 1024, BF),
+        ("PF", 128, F32), ("WT", 512, BF), ("ZB", 512, BF), ("CB", 512 * (ROOM["gone"] + 1), BF), ("FB", 2048, BF), ("GOt", 1024, BF),
         ("DGR", 32, BF), ("GCT", 96, BF), ("GCA", 32, BF), ("GDT", 128, BF), ("CF", 512, BF), ("CF2", 1280, BF),
-        ("OCL", 96, BF), ("OCH", 96, BF), ("ML", C, BF), ("Y", C, BF), ("ALT", 2 * C, BF),
+        ("OCL", 96, BF), ("OCH", 96, BF), ("ML", C, BF), ("Y", C, BF), ("ALT", C, BF), ("JS", 8 * 12 * 13, BF),
         ("JM", C, F32), ("MD", C, F32), ("MX", C, F32), ("NX", C, F32), ("HD", C, F32), ("HD4", 96, F32), ("I4", 96, F32), ("IJF", C, F32),
-        ("CONST", 96, F32), ("SLS", 96, F32), ("RST", C, BF), ("NODE", 3 * FS + C, F32), ("SLF", C, BF),
+        ("CONST", 96, F32), ("RST", C, BF), ("NODE", 3 * FS + C, F32),
         ("TS", C, F32), ("W0", C, F32), ("W1", C, F32), ("W2", C, F32), ("BASE", C, F32), ("A0", C, F32), ("A1", C, F32), ("RF", 512, BF), ("RG", C, BF),
         ("SB1", C, F32), ("ST", C, F32), ("ST2", C, F32), ("ST3", GW, F32), ("ST4", 96, F32), ("RS", 24, F32), ("RC", 96, F32), ("PL", 96, F32), ("LB1", 6, U16), ("LB16", 6, U16),
-        ("GF", 96, F32), ("NS", 24, F32), ("CS", C, BF), ("WW", 96, BF), ("BA", 96, BF), ("BN", 96, BF), ("JK", 4 * C, BF),
+        ("GF", 96, F32), ("NS", 24, F32), ("CS", C, BF), ("WW", 96, BF), ("BA", 96, BF), ("BN", 96, BF),
         ("PLo", 24, U16), ("ELo", 6, U16), ("DL", 24, U16), ("L2", 24, U16), ("L3", 24, U16), ("EL", 24, U16),
-        ("HL0", 24, U16), ("HL1", 24, U16), ("HL2", 24, U16), ("HL3", 24, U16),
+        ("SLo", 24, U16),
         ("CT", 4 * CA[6], BF), ("G", 512, BF), ("IN", 512, BF), ("C2", 512, BF), ("G2", 512, BF), ("VT", 512, BF), ("ND", 4 * C, BF),
-        ("GA", 4 * LINK[4], BF), ("PT", 512, BF), ("GS", 512, BF), ("WA", 3 * FS + C, BF), ("LW", C, F32), ("SG", C, BF),
-        ("F0", FS, BF), ("FT", 4 * FS, BF), ("H0", 512, BF), ("HT", 2048, BF), ("FD", 8 * C, BF), ("Z", 8 * C, BF),
+        ("GA", 4 * LINK[4], BF), ("PT", 512, BF), ("GS", 512, BF), ("WA", 3 * FS + C, BF), ("LW", C, F32),
+        ("FT", 4 * FS, BF), ("H0", 512, BF), ("HT", 4 * FS, BF), ("FD", 8 * C, BF), ("Z", 8 * C, BF),
         ("E", 512, BF), ("OUT", 3 * C, F32)]:
     sb(_n, _w, _d)
+PLACE["JK"], LEN["JK"] = ("FZ", 0), 16 * C
 for _n, _w in [("QX", C), ("QU", 128), ("QUP", C), ("QV", 128), ("WC", 512), ("QK", 128 * NT), ("QF", 512), ("QT", CA[6]),
                ("QG", 128), ("QG2", 128), ("QRF", 128), ("QD", LINK[4] * SWEEPS), ("QC2", 128), ("QIN", 128),
                ("QVT", 128), ("QPT", 128), ("QS", 128), ("QE", 3 * 128), ("LD", 320), ("QND", C)]:
@@ -78,7 +85,7 @@ PS = ["PA", "PB", "PCC", "PD", "LA", "LB", "AB", "PE"]
 for _n in PS:
     SCRATCH[_n] = ("psum", [128, 512], F32)
     PLACE[_n], LEN[_n] = (_n, 0), 512
-SEMAPHORES = ["sv", "ss", "st", "sg", "lcl", "arr0", "arr1", "arr2"] + ["d%d" % i for i in range(30)]
+SEMAPHORES = ["sv", "ss", "st", "sg", "lcl", "arr0", "arr1", "arr2"] + ["d%d" % i for i in range(40)]
 
 
 def rank_program(g, core, T, topo):
@@ -113,7 +120,8 @@ def rank_program(g, core, T, topo):
             wrs[n].append(((lo, hi, st), me))
         for n, lo, hi, st in rd:
             if n not in PS: rds.setdefault(n, []).append(((lo, hi, st), me))
-        op = {"ways": ways, "deps": deps, "after": after, "sem": sem}
+        both = lambda c: c if isr(c) else (c, c) if sem else (0.9 * c, 1.35 * c)
+        op = {"ways": {q: (w[0], 0.0, both(w[1])) for q, w in ways.items()}, "deps": deps, "after": after, "sem": sem}
         ops.append(op)
 
     def issue():
@@ -126,7 +134,7 @@ def rank_program(g, core, T, topo):
             busy, at = {q: [] for q in Q}, [None] * n
             for i in sorted(range(n), key=lambda i: -key[i]):
                 best = None
-                for q, (fn, c) in ops[i]["ways"].items():
+                for q, (fn, c, _) in ops[i]["ways"].items():
                     t0 = ops[i]["after"] if back else 0.0
                     for d, hard in waits[i]:
                         x = ops[i if back else d]
@@ -147,15 +155,59 @@ def rank_program(g, core, T, topo):
                 at[i] = (q, t0, t0 + c)
             return at
 
-        key, plan = [0.0] * n, None
-        for i in range(n - 1, -1, -1):
-            key[i] += min(c for _, c in ops[i]["ways"].values()) + ops[i]["after"]
-            for d in ops[i]["deps"]: key[d] = max(key[d], key[i] + HOP)
-        for _ in range(PASSES):
+        def run(late):
+            at, left, free, ready = [None] * n, [len(b) for b in before], {q: 0.0 for q in Q}, {q: {} for q in Q}
+
+            def offer(i):
+                for q in ops[i]["ways"]:
+                    ready[q][i] = max([0.0] + [at[d][2] + ops[d]["after"] + (HOP if at[d][0] != q or ops[d]["sem"] else NEXT if hard else 0) for d, hard in before[i]])
+
+            for i in range(n):
+                if not left[i]: offer(i)
+            while any(ready.values()):
+                t0, q = min((max(free[q], min(ready[q].values())), q) for q in Q if ready[q])
+                cost = lambda i, q=q: ops[i]["ways"][q][1]
+                better = lambda i: any(p != q and max(free[p], ready[p][i]) + cost(i, p) * (1 + SPARE * (p == "V")) < t0 + cost(i) * (1 + SPARE * (q == "V")) for p in ops[i]["ways"])
+                now = sorted((late[i], i) for i, x in ready[q].items() if x <= t0)
+                soon = [(x, i) for i, x in ready[q].items() if x > t0]
+                for _, i in now:
+                    if better(i): continue
+                    if not any(x < t0 + cost(i) and t0 + cost(i) - late[u] > max(0, x + cost(u) - late[i]) and late[u] < late[i] for x, u in soon): break
+                else:
+                    free[q] = min([x for x, u in soon] + [t0 + 50])
+                    continue
+                at[i] = (q, t0, t0 + cost(i))
+                free[q] = at[i][2]
+                for p in ops[i]["ways"]: del ready[p][i]
+                for j, _ in behind[i]:
+                    left[j] -= 1
+                    if not left[j]: offer(j)
+            return at
+
+        def pace(m):
+            for o in ops: o["ways"] = {q: (w[0], w[2][0] + m * (w[2][1] - w[2][0]), w[2]) for q, w in o["ways"].items()}
+
+        def length(at, m):
+            free, end = {q: 0.0 for q in Q}, [0.0] * n
+            for i in sorted(range(n), key=lambda i: at[i][1]):
+                q = at[i][0]
+                t0 = max([free[q]] + [end[d] + ops[d]["after"] + (HOP if at[d][0] != q or ops[d]["sem"] else NEXT if hard else 0) for d, hard in before[i]])
+                free[q] = end[i] = t0 + ops[i]["ways"][q][2][m]
+            return max(end)
+
+        plan = None
+        for m in PACES:
+            pace(m)
+            key = [0.0] * n
+            for i in range(n - 1, -1, -1):
+                key[i] += min(w[1] for w in ops[i]["ways"].values()) + ops[i]["after"]
+                for d in ops[i]["deps"]: key[d] = max(key[d], key[i] + HOP)
             at = place(key, before, False)
-            end = max(x[2] + o["after"] for x, o in zip(at, ops))
-            if plan is None or end < plan[0]: plan = (end, at)
-            key = [x[2] for x in place([x[2] for x in at], behind, True)]
+            for _ in range(PASSES):
+                key = [x[2] for x in place([x[2] for x in at], behind, True)]
+                at = run([max(key) - x for x in key])
+                end = length(at, 0) * length(at, 1)
+                if plan is None or end < plan[0]: plan = (end, at)
         for o, x in zip(ops, plan[1]): o["q"], o["start"] = x[0], x[1]
         cnt, known = {s: 0 for s in SEMAPHORES}, {q: {} for q in Q}
         for o in sorted(ops, key=lambda o: o["start"]):
@@ -191,7 +243,7 @@ def rank_program(g, core, T, topo):
     narrow = lambda *xs: all(BYTES[SCRATCH[x[0]][2]] == 2 for x in xs)
     vtime = lambda n, f=1.0: max(0.83 * f * n, 53) + 40
     stime = lambda n: max(0.83 * n, 53) + 60
-    gather = lambda n: 1.6 * n + 55
+    gather = lambda n, a=50: (0.9 * a + 1.17 * n, 1.35 * a + 2.24 * n)
     dn = [0]
 
     def dma(q, pairs, rd=(), wr=(), n=None):
@@ -202,7 +254,7 @@ def rank_program(g, core, T, topo):
             for o, i in pairs: e.dma_start(o, i).then_inc(T.sem[s], 16)
 
         if n is None: n = sum(size(x) * BYTES[SCRATCH[x[0]][2]] for x in (wr or rd))
-        note({q: (run, 60 * len(pairs) + (0.5 * n if q == "Y" else 0))}, rd, wr, LAND, (s, 16 * len(pairs)))
+        note({q: (run, 60 * len(pairs) + (0.6 * n if q == "Y" else 0))}, rd, wr, LAND, (s, 16 * len(pairs)))
 
     def ts(o, i, s1, op0, s2=None, op1=None):
         rd = [i] + [s for s in (s1, s2) if isr(s)]
@@ -218,7 +270,7 @@ def rank_program(g, core, T, topo):
         else: note({"V": (lambda e: e.tensor_copy(ap(o), ap(a).indirect(ap(off))), gather(size(o)))}, [a, off], [o])
 
     def scatter(win, off, a):
-        note({"V": (lambda e: e.tensor_copy(ap(win).indirect(ap(off)), ap(a)), 3.2 * size(a) + 50)}, [a, off], [win])
+        note({"V": (lambda e: e.tensor_copy(ap(win).indirect(ap(off)), ap(a)), (2.84 * size(a) + 45, 6.2 * size(a) + 68))}, [a, off], [win])
 
     def act(o, a, bias=0.0, scale=1.0, off=None, fn=COPY, acc=None, on="VS"):
         rd = [a] + [x for x in (scale, bias, off) if isr(x)]
@@ -226,7 +278,7 @@ def rank_program(g, core, T, topo):
         src = (lambda: ap(a)) if off is None else (lambda: ap(a).indirect(ap(off)))
         more = lambda: {} if acc is None else {"accum_out": ap(acc)}
         n, ways = size(o), {}
-        if "S" in on: ways["S"] = (lambda e: e.activation(ap(o), src(), f, bias=val(bias), scale=val(scale), **more()), gather(n) + 10 if off else stime(n) + 20 * (acc is not None))
+        if "S" in on: ways["S"] = (lambda e: e.activation(ap(o), src(), f, bias=val(bias), scale=val(scale), **more()), gather(n, 65) if off else stime(n) + 20 * (acc is not None))
         if "V" in on and fn == COPY and acc is None:
             ways["V"] = (lambda e: e.tensor_scalar(ap(o), src(), val(scale), val(bias), OP.mult, OP.add), gather(n) if off else vtime(n, 0.5 if narrow(o, a) else 1))
         note(ways, rd, [o] + ([] if acc is None else [acc]))
@@ -245,29 +297,30 @@ def rank_program(g, core, T, topo):
         q, s = r(n + "c", a, b), r(n + "s", a, b)
         note({"V": (lambda e: e.quantize_mx(ap(q), ap(s), ap(src)), 52 + 0.88 * (b - a))}, [src], [q, s])
 
-    def pick(n, src, off):
-        m, w = 16 * (off[2] - off[1]), LEN[src + "c"]
-        note({"V": (lambda e: e.tensor_copy(T[n + "c"][:, 0:m].bitcast(dt.uint32), T[src + "c"][:, 0:w].bitcast(dt.uint32).indirect(ap(off))), gather(m))}, [r(src + "c"), off], [r(n + "c")])
-        note({"S": (lambda e: e.activation(T[n + "s"][:, 0:m], T[src + "s"][:, 0:w].indirect(ap(off)), COPY), gather(m))}, [r(src + "s"), off], [r(n + "s")])
+    def pick(n, a, src, off):
+        m = 16 * (off[2] - off[1])
+        c, s = r(n + "c", a, a + m), r(n + "s", a, a + m)
+        note({"V": (lambda e: e.tensor_copy(ap(c).bitcast(dt.uint32), T[src + "c"][:].bitcast(dt.uint32).indirect(ap(off))), gather(m))}, [r(src + "c"), off], [c])
+        note({"S": (lambda e: e.activation(ap(s), T[src + "s"][:].indirect(ap(off)), COPY), gather(m))}, [r(src + "s"), off], [s])
 
     def mm(bk, st, mv, n, start=True, stop=True):
         l, ls = r(st[0] + "c", st[1], st[1] + 128), r(st[0] + "s", st[1], st[1] + 128)
         m, ms = r(mv[0] + "c", mv[1], mv[1] + n), r(mv[0] + "s", mv[1], mv[1] + n)
         o = r(bk, 0, n)
-        note({"T": (lambda e: e.matmul_mx(ap(o), ap(l), ap(ls), ap(m), ap(ms), start, stop), 0.6 * (n + 16) + 25)}, [l, ls, m, ms], [o])
+        note({"T": (lambda e: e.matmul_mx(ap(o), ap(l), ap(ls), ap(m), ap(ms), start, stop), 0.68 * (n + 16) + 30)}, [l, ls, m, ms], [o])
 
     def sums(bk, terms, start=True, stop=True):
         for j, (st, mv) in enumerate(terms): mm(bk, st, mv, 128, start and j == 0, stop and j == len(terms) - 1)
 
     def iota(o, pat, base, cm=0):
         more = {} if SCRATCH[o[0]][2] == I32 else {"allow_small_or_imprecise_dtypes": True}
-        note({"G": (lambda e: e.iota(ap(o), pat, base, cm, **more), 130 + 1.66 * size(o))}, [], [o])
+        note({"G": (lambda e: e.iota(ap(o), pat, base, cm, **more), 170 + 2.1 * size(o))}, [], [o])
 
     def const(o, c):
         iota(o, [[0, size(o)]], c)
 
     def sel(o, i, pat, op, fl, base, cm):
-        note({"G": (lambda e: e.affine_select(ap(o), ap(i), pat, op, fl, base, cm), 170 + 1.66 * size(o))}, [i], [o])
+        note({"G": (lambda e: e.affine_select(ap(o), ap(i), pat, op, fl, base, cm), 220 + 2.1 * size(o))}, [i], [o])
 
     def zeros(*xs):
         pairs = [(T[n][:, a:min(a + 512, hi)], T.ZB[:, 0:min(512, hi - a)]) for n, lo, hi, _ in xs for a in range(lo, hi, 512)]
@@ -286,28 +339,27 @@ def rank_program(g, core, T, topo):
     P = lambda name, j=0: col("PF", PFC[name][0] + j)
     PV = lambda name: r("PF", PFC[name][0], PFC[name][0] + PFC[name][1])
     GRP = {0: ([[16, 8]], 0), 1: ([[32, 4], [-16, 2]], 16), 4: ([[-64, 2], [16, 4]], 64)}
-    CLS = lambda A: 16 * (A & 1) + 64 * (A >> 1)
     neg = lambda pat: [[-a, b] for a, b in pat]
     row = lambda j: col("MD", j)
     cf = lambda n, k=1: r("CF", 32 * TI[n], 32 * (TI[n] + k))
     c2 = lambda e, n, a=0, st=1, k=1: r("CF2", 320 * e + 32 * T2.index(n) + a, 320 * e + 32 * (T2.index(n) + k), st)
 
     dma("S", [(T.U[:], T.u[:])], wr=[r("U")])
-    dma("Y", [(T.X0[:], T.x[:])], wr=[r("X0")])
+    for a in (0, 2 * C): dma("Y", [(T.X0[:, a:a + 2 * C], T.x[:, a:a + 2 * C])], wr=[r("X0", a, a + 2 * C)])
     dma("Y", [(T.LKT[:], T.lk[:])], wr=[r("LKT")])
     fill(r("ZB"), 0.0)
     fill(r("WT"), 1.0)
-    zeros(*[r("CT", 4 * CA[j] + 256 * j, 4 * CA[j + 1]) for j in range(1, 6)])
-    zeros(r("CT", 0, 4 * C))
+    zeros(*[r("CT", 4 * CA[j] + 64 * (21 - 4 * j), 4 * CA[j + 1]) for j in range(6)])
     zeros(room("ld", 0, 5), room("lg"))
-    zeros(r("G"), r("RF", C), r("GA", 3 * C, 4 * LINK[3]), r("GA", 4 * LINK[3] + C))
-    zeros(r("FB", 0, 512), r("E", C))
-    fill(r("FB", 512), 0.0)
+    zeros(r("G"), r("RF", C), *[r("GA", 4 * LINK[k] - 128, 4 * LINK[k]) for k in (1, 3, 4)])
+    zeros(r("FB"), r("E", C))
+    zeros(r("PT", C), r("GS", C))
     zeros(room("ac1", 0, 2))
     zeros(room("gr", 0, 8))
-    zeros(r("C2"), r("G2"), r("VT"), r("IN"), r("PT", C), r("GS", C), r("H0", C))
-    for a in range(0, LEN["WA"], 2 * C): const(r("WA", a, a + 2 * C), 0)
-    zeros(room("nm"), r("ND"))
+    zeros(r("C2"), r("G2"), r("VT"), r("H0"))
+    for a in range(C, LEN["WA"] - C, C):
+        if a % FS: const(r("WA", a, a + C), 0)
+    for x in (room("nm"), r("ND", 0, 512), r("ND", 512, 1024), r("ND", 1024), r("IN")): const(x, 0)
     pr = [(T.LKS[:, 0:24], T.lk[:, 0:24])]
     for h in range(8):
         a = h ^ JUMP[1]
@@ -327,12 +379,12 @@ def rank_program(g, core, T, topo):
         iota(r("UL", 8 * k, 8 * k + 8), GRP[JUMP[k]][0], GRP[JUMP[k]][1])
     iota(r("I4"), [[0, 24], [1, 4]], 0)
     iota(r("IJF"), [[1, C]], 0)
-    iota(r("LW"), [[1, C]], 0)
     iota(r("CONST"), [[16, 24], [0, 4]], 0)
-    iota(r("ALT"), [[0, C], [1, 2]], 0)
+    iota(r("ALT"), [[0, C // 2], [1, 2]], 0)
     p = col("PC", 0)
     for j, (sh, an) in enumerate([(0, 15), (0, 3), (2, 3), (4, 1), (5, 1), (6, 1)]):
         ts(col("PC", j + 1), p, sh, OP.arith_shift_right, an, OP.bitwise_and)
+    tc(pcol("p0"), p)
     tc(pcol("i"), col("PC", 1))
     tc(pcol("p", 5), r("PC", 2, 7))
     pi, (ps, pk, g0, g1, g2) = P("i"), [P("p", j) for j in range(5)]
@@ -351,8 +403,8 @@ def rank_program(g, core, T, topo):
     ts(r("DGR"), r("I4", 0, 32), pk, OP.is_equal)
     for n, src in (("ULo", "UL"), ("OFJ", "LKT"), ("OFS", "LKS")): tc(r(n), r(src))
     quant("QU", 0, 128, r("U"))
-    pick("QUP", "QU", r("ULo"))
-    quant("QX", 0, C, r("X0"))
+    for a, b in ((0, 8), (8, 24)): pick("QUP", 16 * a, "QU", r("ULo", a, b))
+    for a in (0, C // 2): quant("QX", a, a + C // 2, r("X0", 4 * a, 4 * a + 2 * C))
     quant("QV", 0, 128, r("VV"))
     act(pcol("n3"), P("mr", 3), scale=-1.0, bias=1.0)
     act(pcol("mk", 4), PV("ms"), scale=P("n3"))
@@ -371,8 +423,6 @@ def rank_program(g, core, T, topo):
     act(pcol("kb"), pk, scale=16.0, bias=15.0)
     ts(r("LB1"), r("IJF", 0, 24, 4), pk, OP.add)
     ts(r("LB16"), r("IJF", 0, C, 64), P("kb"), OP.add)
-    act(pcol("h4"), P("k16"), scale=4.0, bias=1024.0)
-    act(pcol("hb", 4), r("I4", 0, 4), bias=P("h4"))
     act(pcol("sg1"), g0, scale=-2.0, bias=1.0)
     act(pcol("sg2"), g2, scale=-2.0, bias=1.0)
     act(pcol("p4"), row(4), scale=P("sg1"))
@@ -389,23 +439,25 @@ def rank_program(g, core, T, topo):
     ts(pcol("w2"), row(6), row(10), OP.add, P("p8"), OP.add)
     ts(pcol("ba"), row(0), row(1), OP.subtract, P("p4"), OP.add)
     act(pcol("base"), P("ba"), bias=P("p8"))
+    iota(r("LW"), [[1, C]], 0)
     tt(r("ML"), r("IJF"), r("LW"), OP.is_lt, off=r("OFJ", 0, 24))
     act(r("Y"), r("ML"), scale=P("ys"), bias=P("y"))
-    ts(pcol("a1"), g0, P("mr", 1), OP.not_equal)
-    ts(pcol("a2"), g2, P("mr", 2), OP.not_equal, 2.0, OP.mult)
-    act(pcol("cls"), P("a1"), bias=P("a2"))
+    act(pcol("r23"), P("mr", 2), bias=P("mr", 3))
+    for A, x in ((1, P("mr", 2)), (2, P("mr", 3)), (3, P("r23"))):
+        act(pcol("tb%d" % A, 4), PV("ms"), scale=x)
+        act(pcol("sg%d_" % A), x, scale=-2.0, bias=1.0)
+        act(pcol("ta%d" % A, 4), PV("ms"), scale=P("sg%d_" % A))
     act(pcol("ws"), P("mr", 2), scale=2.0, bias=-1.0)
     act(pcol("wsc"), P("ws"), scale=P("n3"))
     act(pcol("wb"), pk, scale=-1.0, bias=3.0)
     act(pcol("b1"), P("mr", 1), scale=2.0, bias=P("mr", 0))
     act(pcol("bit"), P("mr", 2), scale=4.0, bias=P("b1"))
     act(pcol("bit8"), P("bit"), scale=8.0)
-    act(pcol("h768"), g1, scale=2.0 * C)
-    act(pcol("o1"), g2, scale=2.0, bias=g0)
-    act(pcol("o2"), P("o1"), scale=128.0, bias=-256.0)
-    act(pcol("o3"), P("o2"), bias=float(GW))
-    act(r("SLS"), r("IJF", 0, GW), bias=P("o2"))
-    act(r("SLF"), r("IJF"), scale=0.0, bias=P("o3"))
+    ts(pcol("n0"), pi, -1.0, OP.mult, P("p0"), OP.add)
+    act(pcol("nd0"), P("n0"), scale=C / 16.0)
+    act(pcol("nd1"), P("sg1"), scale=float(C), bias=P("nd0"))
+    act(pcol("nd2"), P("sg2"), scale=4.0 * C, bias=P("nd0"))
+    act(pcol("nd3"), P("sg2"), scale=4.0 * C, bias=P("nd1"))
     ts(pcol("s3"), ps, P("mr", 3), OP.mult, 16.0, OP.add)
     for q in range(4): ts(r("X16", q, 96, 4), r("LK2", 24 * q, 24 * q + 24), P("s3"), OP.add)
     ts(r("XA"), r("X16"), 31, OP.bitwise_and)
@@ -434,7 +486,7 @@ def rank_program(g, core, T, topo):
         if names != T1C:
             group_mask(cf(names[0], n - 2), 0)
             for k in (1, 2): group_mask(cf(names[k - 3]), JUMP[k])
-        for s in range(4): sel(room(names[0], 5 * s, n, 16), cf(names[0], n), [[0, 32 * n]], OP.is_ge, 0.0, 0, 0)
+        for s in range(4): act(room(names[0], 5 * s, n, 16), cf(names[0], n))
         quant_tiles(names)
 
     def lay_short(e, a, b):
@@ -455,8 +507,8 @@ def rank_program(g, core, T, topo):
     act(r("GCT", 32, 64), r("DGR"), scale=-2.0, bias=3.0)
     for k in range(3): act(cf("lc%d" % k), r("GCT", 32, 64), scale=P("mr", k))
     lay(T1A)
-    sel(r("FB", 3, 515, 4), r("WT", 0, 128), [[-1, 128]], OP.is_equal, 0.0, 0, 1)
-    for b in range(4): quant("QF", 128 * b, 128 * b + 128, r("FB", 3 - b, 515 - b))
+    for b in range(4): sel(r("FB", 513 * b, 512 * b + 512, 4), r("WT", 0, 128), [[-1, 128]], OP.is_equal, 0.0, 0, 1)
+    quant("QF", 0, 512, r("FB"))
     act(cf("ad"), r("DGR"), scale=P("dr"))
     act(cf("ao"), r("DGR"), scale=0.5)
     act(r("GCT", 64, 96), r("DGR"), scale=-0.5)
@@ -466,26 +518,36 @@ def rank_program(g, core, T, topo):
     for k, (x, y, op) in enumerate(((2, 10, OP.add), (6, 2, OP.subtract), (6, 10, OP.add))):
         ts(r("CF", a + k, a + 32, 4), r("WT", 0, 8), row(x), OP.mult, row(y), op)
     const(r("CF", a + 3, a + 32, 4), 0)
-    act(pcol("sa"), P("mr", 2), scale=float(FS), bias=P("mr", 0))
-    act(cf("st"), r("WT", 0, 32), scale=P("sa"), bias=P("mr", 1))
+    act(pcol("sa"), P("mr", 2), scale=FS - 1.0, bias=1.0)
+    act(pcol("sb"), P("mr", 3), scale=2.0 * FS - 1, bias=P("sa"))
+    act(cf("st"), r("WT", 0, 32), scale=P("sb"))
     lay(T1B)
+    def class_mask(o, A, src):
+        if A < 3: return group_mask(o, REACH[A], src)
+        for a, b in ((0, 80), (16, 16)):
+            x = r("GDT", 32 + a, 48 + a)
+            sel(x, (src[0], src[1] + a, src[1] + a + 16, 1), [[-32, 2], [16, 2], [0, 4]], OP.is_ge, 0.0, -b, 1)
+            sel((o[0], o[1] + a, o[1] + a + 16, 1), x, [[32, 2], [-16, 2], [0, 4]], OP.is_ge, 0.0, b + 15, -1)
+
+    ts(r("GDT", 0, 32), r("I4", 0, 32), 1.5, OP.is_lt)
+    for k in (1, 2): act(r("GDT", 1 + k, 32, 4), r("WT", 0, 8), scale=P("mr", k))
     for A in range(4):
-        x = r("GDT", 32 * A, 32 * A + 32)
-        sel(x, r("WT", 0, 32), [[0, 2], [-32, 2], [0, 8]], OP.is_ge, 0.0, -CLS(A), 1)
-        sel(c2(3, "ct%d" % A), x, [[0, 2], [32, 2], [0, 8]], OP.is_ge, 0.0, CLS(A) + 15, -1)
-    for e in range(3): sel(c2(e, "ct0", 0, 1, 4), c2(3, "ct0", 0, 1, 4), [[0, 32], [1, 4]], OP.is_equal, 0.0, -e, 0)
-    for A in range(4):
-        x = r("GDT", 32 * A, 32 * A + 32)
-        sel(x, r("DGR"), [[0, 2], [-32, 2], [0, 8]], OP.is_ge, 0.0, -CLS(A), 1)
-        sel(cf("cw%d" % A), x, [[0, 2], [32, 2], [0, 8]], OP.is_ge, 0.0, CLS(A) + 15, -1)
+        class_mask(c2(3, "ct%d" % A), A, r("GDT", 0, 32))
+        class_mask(cf("cw%d" % A), A, r("DGR"))
+    for e in range(3):
+        sel(c2(e, "ct0", 0, 1, 4), c2(3, "ct0", 0, 1, 4), [[0, 32], [1, 4]], OP.is_equal if e < 2 else OP.is_ge, 0.0, -e, 0)
     lay(T1C)
     const(c2(0, "gr"), 7)
     act(c2(0, "lv"), r("DGR"), scale=2048.0, bias=-1024.0)
     const(c2(0, "dl1"), 1)
     group_mask(c2(0, "gr", 0, 1, 3), 0)
-    for e, n, c in ((1, "dl1", 1), (3, "dl1", 2), (2, "dl2", FS), (3, "dl2", FS)):
-        const(c2(e, n), c)
-        group_mask(c2(e, n), 0)
+    for e, c in ((1, 1), (3, 2)):
+        const(c2(e, "dl1"), c)
+        group_mask(c2(e, "dl1"), 0)
+    act(pcol("d1"), P("mr", 1), scale=float(FS))
+    act(pcol("d2"), P("mr", 2), scale=2.0 * FS, bias=P("d1"))
+    act(r("GDT", 64, 96), r("WT", 0, 32), scale=P("d2"))
+    for e in (2, 3): group_mask(c2(e, "dl2"), 0, r("GDT", 64, 96))
     for e in range(4): lay_short(e, *ELEM[e])
     quant_tiles(T2[1:9])
     act(c2(0, "nm"), r("DGR"), scale=-2.0)
@@ -495,34 +557,35 @@ def rank_program(g, core, T, topo):
         group_mask(c2(e, "nm"), 0)
         lay_short(e, "nm", "nm")
     quant_tiles(["nm"])
-    for a in range(0, LEN["NODE"], 2 * C): iota(r("NODE", a, a + 2 * C), [[1, 2 * C]], 0)
-    for A in range(1, 4): iota(r("NODE", FS * A, FS * A + C), [[1, C]], C * ((A & 1) + 4 * (A >> 1)))
+    for a in range(0, LEN["NODE"], C):
+        if a % FS: const(r("NODE", a, a + C), 0)
+        else: act(r("NODE", a, a + C), r("IJF"), bias=P("nd%d" % (a // FS)))
 
     def send(t):
         m = topo.engines(core, nxt)[:ENGINES]
-        mask = sum(1 << e for e in m)
         rid, pid, _ = topo.addr(nxt)
         n = 128 if t == 0 else GW
         a = 0 if t == 0 else 32 + GW * t
         sem = T.sem["arr%d" % t]
 
+        o, mask = 128 * t, sum(1 << x for x in m)
+
         def run(e):
-            e.remote_dma(T.LDc[:, a:a + n].bitcast(dt.uint8), T.QEc[:, 128 * t:128 * t + n].bitcast(dt.uint8), sem, T.sem.lcl, pid, rid, mask)
-            e.remote_dma(T.LDs[:, a:a + n], T.QEs[:, 128 * t:128 * t + n], sem, T.sem.lcl, pid, rid, mask)
+            e.remote_dma(T.LDc[:, a:a + n].bitcast(dt.uint8), T.QEc[:, o:o + n].bitcast(dt.uint8), sem, T.sem.lcl, pid, rid, mask)
+            e.remote_dma(T.LDs[:, a:a + n], T.QEs[:, o:o + n], sem, T.sem.lcl, pid, rid, mask)
 
         pe = len(topo.engines(T.cores[(rank - 1) % len(T.cores)], core)[:ENGINES])
-        note({"G": (run, 2000)}, [r("QEc", 128 * t, 128 * t + n), r("QEs", 128 * t, 128 * t + n)],
-             [r("LDc", a, a + n), r("LDs", a, a + n)], FAR, ("arr%d" % t, 2 * pe))
+        note({"G": (run, 2000)}, [r("QEc", o, o + n), r("QEs", o, o + n)], [r("LDc", a, a + n), r("LDs", a, a + n)], FAR, ("arr%d" % t, 2 * pe))
         return 2 * len(m)
 
-    def spread(dst, src):
-        n = LEN[src]
+    def spread(n, lo=1, hi=4):
         pairs = []
-        for A in range(4):
-            for h in range(8):
-                a = CLS(A) + 16 * (h & 2)
-                pairs.append((T[dst][16 * h:16 * h + 16, n * A:n * A + n], T[src][a:a + 16, 0:n]))
-        dma("Y", pairs, rd=[r(src)], wr=[r(dst)])
+        for A in range(lo, hi):
+            k = 4 if REACH[A] == 4 else 1
+            for h in range(0, 8, k):
+                a = 16 * (h ^ REACH[A])
+                pairs.append((T[n][16 * h:16 * (h + k), FS * A:FS * A + FS], T[n][a:a + 16 * k, 0:FS]))
+        if pairs: dma("Y", pairs, rd=[r(n, 0, FS)], wr=[r(n, FS * lo, FS * hi)])
 
     def hold(ahead):
         for j in ahead: ops[-1]["deps"].setdefault(j, False)
@@ -534,36 +597,43 @@ def rank_program(g, core, T, topo):
     def moved(i, own, came):
         return [(K(n), ("QD", LINK[4] * i + LINK[k])) for k, n in enumerate([own, came + "0", came + "1", came + "2"])]
 
-    sent = [0]
+    sent, H, VB, SB = [0], C // 2, ("PA", "AB"), ("PB", "LB")
+    half = lambda n, h: r(n, H * h, H * h + H)
+
+    def scores(j, h):
+        if j == 0:
+            for bk in (VB[h], SB[h]): mm(bk, ("QUP", 0), ("QX", H * h), H)
+            act(half("TS", h), r(SB[h], 0, H), on="S")
+            tt(half("SB1", h), r(VB[h], 0, H), half("MX", h), OP.max)
+        if j == 1: scan(half("ST", h), half("NX", h), half("SB1", h), OP.add, OP.min)
+        if j == 2: ts(r("NS", 12 * h, 12 * h + 12), r("ST", H * h + 15, H * h + H, 16), -1.0, OP.mult)
+
     for t in range(R):
         pass
-        for bk, a in (("PA", 0), ("PB", 0), ("PCC", 128), ("PD", 256)): mm(bk, ("QUP", a), ("QX", 0), C)
-        act(r("TS"), r("PB", 0, C), on="S")
-        dma("Y", [(T.F0[:, 4 * C:FS], T.SLF[:])], rd=[r("SLF")], wr=[r("F0", 4 * C, FS)])
-        for a in (C // 2, 0): tt(r("SB1", a, a + C // 2), r("PA", a, a + C // 2), r("MX", a, a + C // 2), OP.max)
-        for a in (C // 2, 0): scan(r("ST", a, a + C // 2), r("NX", a, a + C // 2), r("SB1", a, a + C // 2), OP.add, OP.min)
-        tt(r("CT", 0, 4 * C, 4), r("PA", 0, C), r("ST"), OP.is_ge)
-        own = 24 - SOWN[t]
-        if own < 24: ts(r("NS", own, 24), r("ST", 16 * own + 15, C, 16), -1.0, OP.mult)
+        for h in range(1 if t else 0, 2):
+            for j in range(3): scores(j, h)
+        for bk, a in (("PCC", 128), ("PD", 256)): mm(bk, ("QUP", a), ("QX", 0), C)
+        for h in (0, 1): tt(r("CT", 4 * H * h, 4 * H * h + 4 * H, 4), r(VB[h], 0, H), half("ST", h), OP.is_ge)
         for a in range(23, 0, -1):
-            node, x = r("CT", 4 * CA[a // 4] + a % 4, 4 * CA[a // 4] + 64 * a, 4), r("JK", C * (a % 4), C * (a % 4) + 16 * a)
-            if a >= own:
+            j, e = divmod(24 - a, 4)
+            node, x = r("CT", 4 * CA[j] + e, 4 * CA[j] + 64 * a, 4), r("JK" if a > 12 else "JS", 8 * a * (a - 1), 8 * a * (a + 1))
+            if a in SOWN or t == 0 and a in SFIRST:
                 act(x, r("TS", 0, 16 * a), bias=col("NS", a), fn=FN.Relu)
                 act(node, x, fn=FN.Sign, acc=col("RS", a))
             else:
                 ts(node, r("TS", 0, 16 * a), col("ST", 16 * a + 15), OP.is_gt)
                 total(col("RS", a), x, node)
-        for j in (0, 4, 3, 5, 2, 1):
+        for j in TORDER:
             quant("QT", CA[j], CA[j + 1], r("CT", 4 * CA[j], 4 * CA[j + 1]))
-            mm("PE", K("gone"), ("QT", CA[j]), CW[j], j == 0, j == 1)
+            mm("PE", K("gone"), ("QT", CA[j]), CW[j], j == TORDER[0], j == TORDER[-1])
         scan(r("CS"), r("RST"), r("CT", 0, 4 * C, 4), OP.mult, OP.add)
         tt(r("RC"), r("CS"), r("CONST"), OP.add, off=r("LB16"))
         tt(r("GF"), r("RS"), r("RC"), OP.add, off=r("LB1"))
         act(r("W1"), r("PCC", 0, C), scale=P("w1"))
         act(r("W2"), r("PD", 0, C), scale=P("w2"))
         if t == 0:
-            act(r("W0"), r("PB", 0, C), scale=P("w0"))
-            act(r("BASE"), r("PB", 0, C), scale=P("base"))
+            act(r("W0"), r("TS"), scale=P("w0"))
+            act(r("BASE"), r("TS"), scale=P("base"))
             tt(r("A0"), r("W0"), r("BASE"), OP.subtract, off=r("OFJ", 0, 24))
         else: act(r("A0"), r("TS"), scale=P("w0"), off=r("OFJ", 0, 24), on="S")
 
@@ -587,7 +657,7 @@ def rank_program(g, core, T, topo):
         for b in range(4):
             bk = ("PA", "PB")[b % 2]
             mm(bk, EB(b), ("QX", 0), C)
-            act(r("F0", C * b, C * b + C), r(bk, 0, C), scale=0.5)
+            act(r("FT", C * b, C * b + C), r(bk, 0, C), scale=0.5)
         pass
         scan(r("ST2"), r("HD"), r("PE", 0, C), OP.add, OP.max)
         tt(r("G", 0, C, 4), r("ST2", 3, C, 4), r("GF"), OP.is_lt)
@@ -601,6 +671,8 @@ def rank_program(g, core, T, topo):
         hold([flags - 1])
         scan(r("ST4"), r("HD4"), r("PL"), OP.add, OP.max)
         ts(r("PLo"), r("ST4", 3, 96, 4), -1.0, OP.mult, P("kp"), OP.add)
+        ts(r("SLo"), r("PLo"), float(GW), OP.min)
+        spread("FT", 1, AHEAD[t])
 
         def in_order(h):
             scatter(r("LW"), r("PLo", 12 * h, 12 * h + 12), r("IJF", 192 * h, 192 * h + 192))
@@ -608,16 +680,15 @@ def rank_program(g, core, T, topo):
         def gates():
             scan(r("ST3"), r("HD", 0, GW), r("LW", 0, GW), OP.add, OP.max)
             ts(r("ELo"), r("ST3", 15, GW, 16), P("k16"), OP.add)
-            for b in range(4): act(r("E", b, 4 * GW, 4), r("F0", C * b, C * b + C), scale=2.0, off=r("ELo"), on="S")
+            for b in range(4): act(r("E", b, 4 * GW, 4), r("FT", C * b, C * b + C), scale=2.0, off=r("ELo"), on="S")
 
         def pass_on():
             quant("QE", 128 * t, 128 * t + 128, r("E"))
 
-        def slots():
-            scatter(r("F0", 4 * C, FS), r("ELo"), r("SLS"))
-
         def leave():
             sent[0] += send(t)
+            spread("FT", AHEAD[t], 4)
+            hold([len(ops) - 2])
 
         def layer():
             a, o, last = (0 if t == 0 else GW * t), (0 if t == 0 else 32), len(ops) - 1
@@ -625,11 +696,13 @@ def rank_program(g, core, T, topo):
                 bk = ("PE", "PCC")[b % 2]
                 mm(bk, ("WC", 128 * b), ("LD", a), 128)
                 ops[-1]["deps"].setdefault(last, False)
-                act(r("H0", b, 4 * GW, 4), r(bk, o, o + GW), scale=0.015625)
-            spread("HT", "H0")
+                act(r("H0", 128 * b, 128 * b + GW), r(bk, o, o + GW), scale=0.015625)
+                for h in (0, 1):
+                    act(r("HT", C * b + H * h, C * b + H * h + H), r("H0", 128 * b, 128 * b + 128), off=r("SLo", 12 * h, 12 * h + 12))
+            spread("HT")
 
-        work = {"s": in_order, "a": order1, "b": order2, "e": lambda h: pass_on(), "l": lambda h: slots()}
-        then = {"s1": gates, "e0": leave, "l0": lambda: spread("FT", "F0"), "b1": weights}
+        work = {"s": in_order, "a": order1, "b": order2, "e": lambda h: pass_on()}
+        then = {"s1": gates, "e0": leave, "b1": weights}
 
         def pin(names, last):
             held = []
@@ -643,46 +716,50 @@ def rank_program(g, core, T, topo):
 
         held = pin(BEHIND[0], flags)
         sums("AB", [(K("ad"), ("QRF", 0)) if t == 0 else (EB(1), ("QIN", 0))], True, False)
-        kept = [(EB(0), ("QC2", 0))]
         for i in range(SWEEPS):
             pass
             bk, nb = ("LA", "LB")[i % 2], ("LB", "LA")[i % 2]
-            past = [x for j in range(0 if i < 3 else 2, i) for x in moved(j, "lo", "lc")] + (first if i < 3 else kept)
+            c = max([-1] + [j for j in KEEP if j <= i])
+            past = [x for j in range(max(c, 0), i) for x in moved(j, "lo", "lc")] + (first if c < 0 else [])
             if i == SWEEPS - 1: nb, past = "PB", past + [(K("gr"), ("QG", 0))]
             sums(nb, past, True, False)
-            even = t == 0 and i < 4
+            even = t == 0 and i <= KEEP[0]
             for s in range(4):
                 if even or TURN[i] == "S": act(r("GA", s, C, 4), r(bk, 0, 96), scale=P("mk", s), bias=P("mk", s) if even else 0.0, fn=FN.Sign)
                 else: ts(r("GA", s, C, 4), r(bk, 0, 96), P("mn", s), OP.max, P("mk", s), OP.min)
                 if "V" in ops[-1]["ways"]: hold(held)
             ahead, held = held, pin(BESIDE[i], len(ops) - 1)
-            if i == 2:
-                act(r("C2", 0, C, 4), r(bk, 0, 96), bias=0.0 if t else 1.0)
+            if i == c:
+                act(r("C2", 0, C, 4), r(bk, 0, 96), bias=1.0 if even else 0.0)
                 quant("QC2", 0, 128, r("C2"))
+            if c >= 0: mm(nb, EB(0), ("QC2", 0), 128, not past, False)
             n = VSWEEP[i] if t else VFIRST[i]
-            act(r("GA", C + n, 3 * C), r("GA", 0, C), off=r("OFS", n // 16, 48), on="S")
+            o, a = 4 * LINK[1], LINK[4] * i
+            act(r("GA", o + n, o + 2 * C), r("GA", 0, C), off=r("OFS", n // 16, 48), on="S")
             act(r("GA", 4 * LINK[3], 4 * LINK[3] + C), r("GA", 0, C), off=r("OFS", 48, 72), on="S")
-            tc(r("GA", C, C + n), r("GA", 0, C), off=r("OFS", 0, n // 16))
+            tc(r("GA", o, o + n), r("GA", 0, C), off=r("OFS", 0, n // 16))
             hold(ahead)
-            n, a = 288 if t else 320, LINK[4] * i
-            quant("QD", a, a + n, r("GA", 0, 4 * n))
+            quant("QD", a, a + LINK[1], r("GA", 0, o))
+            hold([len(ops) - 2])
+            n = 192 if t else 224
+            quant("QD", a + LINK[1], a + LINK[1] + n, r("GA", o, o + 4 * n))
             hold(held)
             quant("QD", a + LINK[3], a + LINK[4], r("GA", 4 * LINK[3]))
             held = pin(BEHIND[i + 1], len(ops) - 1)
-            if i == SWEEPS - 1: layer()
+            if i == LAYER: layer()
             sums(nb, moved(i, "lo", "lc"), False, True)
             sums("AB", moved(i, "ao", "ac"), False, i == SWEEPS - 1)
         pass
         tt(r("VT", 0, C, 4), r("AB", 0, 96), r("WW"), OP.mult)
         quant("QVT", 0, 128, r("VT"))
         ts(r("IN", 1, C, 4), r("AB", 0, 96), P("thr"), OP.is_gt, P("two"), OP.mult)
-        sums("PA", [(K("lg"), ("QG2", 0)), (K("lv"), ("QVT", 0))])
+        for bk in ("PA", "PE"): sums(bk, [(K("lg"), ("QG2", 0)), (K("lv"), ("QVT", 0))])
         act(r("IN", 0, C, 4), r("PB", 0, 96))
         quant("QIN", 0, 128, r("IN"))
         tt(r("PT", 0, C, 4), r("PA", 0, 96), r("OCL"), OP.min)
         tt(r("PT", 1, C, 4), r("PA", 0, 96), r("OCH"), OP.min)
-        ts(r("PT", 2, C, 4), r("PA", 0, 96), P("cls"), OP.min)
-        ts(r("PT", 3, C, 4), r("PA", 0, 96), -1.0, OP.mult, 0.0, OP.max)
+        ts(r("PT", 2, C, 4), r("PA", 0, 96), 1.0, OP.min)
+        act(r("PT", 3, C, 4), r("PE", 0, 96), scale=-1.0, fn=FN.Relu)
         quant("QPT", 0, 128, r("PT"))
         four = ("LA", "LB", "PCC", "PD")
 
@@ -697,7 +774,9 @@ def rank_program(g, core, T, topo):
 
         def table():
             for A in range(4):
-                for s in range(4): act(r("WA", FS * A + s, FS * A + C, 4), r(four[A], 0, 96), scale=P("ms", s), on="V" if A < 2 else "S")
+                for s in range(4):
+                    act(r("WA", FS * A + s, FS * A + C, 4), r(four[A], 0, 96), scale=P("ta%d" % A if A else "ms", s),
+                        bias=P("tb%d" % A, s) if A else 0.0, on="V" if A < 2 else "S")
 
         table()
         if t == R - 1:
@@ -707,6 +786,7 @@ def rank_program(g, core, T, topo):
             tt(r("BA"), r("BA"), r("BN"), OP.add)
             for s in range(4): act(r("ND", 4 * s, 4 * C, 16), r("BA"), scale=P("ms", s))
             quant("QND", 0, C, r("ND"))
+            bits = len(ops) - 1
             mm("PB", K("gone"), ("QND", 0), C)
             act(r("OUT", C, 2 * C), r("PB", 0, C))
         pass
@@ -718,31 +798,37 @@ def rank_program(g, core, T, topo):
             mm("PA", K("st"), ("QS", 0), 128)
             to_list("PA", b)
             if b == "L2": table()
+            elif t == R - 1: hold([bits])
         pass
-        even = lambda n, b: r(n, 2 * C * b, 2 * C * b + 2 * C, 2)
-        odd = lambda n, b: r(n, 2 * C * b + 1, 2 * C * b + 2 * C, 2)
-        both = lambda n, b: r(n, 2 * C * b, 2 * C * b + 2 * C)
-        act(r("SG"), r("FT", 4 * C), off=r("EL"), on="S")
-        scan(r("ST2"), r("HD"), r("SG"), OP.add, OP.max)
-        for b in range(4):
-            ts(r("HL%d" % b), r("ST2", 15, C, 16), 4.0, OP.mult, P("hb", b), OP.add)
-            for h in (0, 1):
-                act(r("FD", 2 * C * b + C * h, 2 * C * b + C * h + C, 2), r("FT", C * b), off=r("DL", 12 * h, 12 * h + 12))
-            if b in PAIRED:
-                act(odd("FD", b), r("FT", C * b), off=r("EL"), on="S")
-                scan(both("Z", b), r("ALT"), both("FD", b), OP.mult, OP.add)
-            else: tt(odd("Z", b), r("FT", C * b), even("FD", b), OP.add, off=r("EL"))
-        for b in (2, 3):
-            act(even("Z", b), r("HT"), off=r("HL%d" % b), on="S")
-            scan(r("X0", b - 2, 4 * C, 2), r("ALT"), both("Z", b), OP.mult, OP.add)
-        for b in (0, 1): tt(r("X0", b, 4 * C, 4), r("HT"), odd("Z", b), OP.add, off=r("HL%d" % b))
-        quant("QX", 0, C, r("X0"))
+        part = lambda n, b, h, a, st: r(n, 2 * C * b + C * h + a, 2 * C * b + C * h + C, st)
+        for h in (0, 1):
+            for b in (2, 0, 3, 1): act(part("FD", b, h, 0, 2), r("FT", C * b), off=r("DL", 12 * h, 12 * h + 12))
+        done = {}
+        for w in BLEND.split():
+            b, h = int(w[1]), int(w[2])
+            e, x = r("EL", 12 * h, 12 * h + 12), lambda a, st: r("X0", 4 * H * h + a, 4 * H * h + 4 * H, st)
+            if w[0] == "z": tt(part("Z", b, h, 1, 2), r("FT", C * b), part("FD", b, h, 0, 2), OP.add, off=e)
+            if w[0] == "f": act(part("FD", b, h, 1, 2), r("FT", C * b), off=e, on="S")
+            if w[0] == "p": scan(part("Z", b, h, 0, 1), r("ALT", 0, C), part("FD", b, h, 0, 1), OP.mult, OP.add)
+            if w[0] == "h": act(part("Z", b, h, 0, 2), r("HT", C * b), off=e, on="S")
+            if w[0] == "x": scan(x(b - 2, 2), r("ALT", 0, C), part("Z", b, h, 0, 1), OP.mult, OP.add)
+            if w[0] == "y": tt(x(b, 4), r("HT", C * b), part("Z", b, h, 1, 2), OP.add, off=e)
+            if w[0] == "q": quant("QX", H * h, H * h + H, x(0, 1))
+            if w[0] == "s":
+                if t == R - 1: continue
+                scores(b, h)
+            q = w[0] in "fh"
+            if q in done: hold([done[q]])
+            done[q] = len(ops) - 1
     pass
-    act(r("OUT", 0, C), r("NODE"), bias=P("h768"), off=r("EL"), on="S")
+    act(r("OUT", 0, C), r("NODE"), off=r("EL"), on="S")
     dma("Y", [(T.nd[:], T.OUT[0:128:16, 0:2 * C])], rd=[r("OUT", 0, 2 * C)], n=200)
-    mm("PA", ("QV", 0), ("QX", 0), C)
-    act(r("OUT", 2 * C, 3 * C), r("PA", 0, C))
-    dma("Y", [(T.oc[:], T.QXc[:, 0:C].bitcast(dt.uint8))] + [(T.osc[4 * k:4 * k + 4, :], T.QXs[32 * k:32 * k + 4, 0:C]) for k in range(4)], rd=[r("QXc"), r("QXs")])
-    dma("Y", [(T.y[:], T.OUT[:, 2 * C:3 * C])], rd=[r("OUT", 2 * C, 3 * C)])
+    for h in (0, 1):
+        a, y = H * h, r("OUT", 2 * C + H * h, 2 * C + H * h + H)
+        mm(VB[h], ("QV", 0), ("QX", a), H)
+        act(y, r(VB[h], 0, H))
+        dma("Y", [(T.oc[:, 4 * a:4 * a + 4 * H], T.QXc[:, a:a + H].bitcast(dt.uint8))], rd=[r("QXc", a, a + H)])
+        dma("Y", [(T.y[:, a:a + H], ap(y))], rd=[y])
+    dma("S", [(T.osc[4 * k:4 * k + 4, :], T.QXs[32 * k:32 * k + 4, 0:C]) for k in range(4)], rd=[r("QXs")])
     issue()
     g.wait_ge(T.sem.lcl, sent[0])

import math
from concourse.bass import DstId, RemoteDMATransfer
from concourse.mybir import dt, AluOpType, AxisListType, ActivationFunctionType

OP, FN = AluOpType, ActivationFunctionType
COPY, IDENT = FN.Copy, FN.Identity
C, GW, R, SWEEPS = 384, 96, 3, 6
JUMP = [0, 1, 4]
REACH = [0, 1, 4, 5]

T1A, T1B, T1C = ["ld", "lo", "lc0", "lc1", "lc2"], ["ad", "ao", "ord", "st", "ac0", "ac1", "ac2"], ["cw0", "cw1", "cw2", "cw3"]
T2 = ["lg", "gr", "lv", "dl1", "ct0", "ct1", "ct2", "ct3", "dl2", "nm"]
TILES = T1A + T1B + T1C + T2 + ["gone"]
TI = {n: i for i, n in enumerate(TILES)}
NT = len(TILES)
ROOM = {n: i for l in (T1A, T1C, T1B + T2 + ["gone"]) for i, n in enumerate(l)}
ELEM = [("gr", "ct3"), ("dl1", "ct3"), ("ct0", "dl2"), ("dl1", "dl2")]
FS = 4 * C
HOLD, DROP = 8192.0, 1048576.0
LINK = [0, 128, 224, 352, 480]
BESIDE = ["", "", "", "", "", ""]
BEHIND = ["s0", "s1", "e0", "a0 a1", "b0 b1", "", ""]
AHEAD = [1, 3, 3]
LAYER = 3
VSWEEP = [448, 448, 448, 448, 448, 448]
VFIRST = [448, 448, 448, 448, 448, 448]
TURN = "SSSSSV"
TORDER = (0, 3, 4, 1, 2, 5)
BLEND = "z20 z00 f30 f10 f31 f11 p30 z21 p10 z01 h20 h30 p31 x20 p11 x30 y00 y10 h21 h31 x21 q00 x31 y01 s00 y11 s10 q01 s20"
KEEP = [2]
VSTEP = 192
SOWN = [7, 8, 9, 10, 11, 12, 21, 22, 23]
SFIRST = [19, 20]
ENGINES = 8
HOP, NEXT, LAND, FAR, SPARE, PASSES, PACES = 200, 200, 1500, 4000, 0.2, 8, (0.55,)

F32, BF, I32, U16, X4, U8 = "float32", "bfloat16", "int32", "uint16", "float8_e4m3fn_x4", "uint8"
BYTES = {F32: 4, BF: 2, I32: 4, U16: 2, X4: 4, U8: 1}
SCRATCH = {}
WIDE = {"KF": "JM MD MX NX HD HD4 I4 IJF CONST SLS", "KI": "PC UL X16 XA XB2", "KB": "WT DGR GCT GCA GDT CF CF2 OCL OCH ML Y ALT",
        "XF": "SB1 ST ST2 ST3 ST4 RS RC PL GF NS", "XB": "CS WW BA BN", "ZT": "G IN C2 G2 VT ND", "FZ": "FD Z",
        "XU": "PLo ELo DL L2 L3 EL SLo", "KU": "ULo OFJ OFS LB1 LB16"}
HOME = {n: w for w in WIDE for n in WIDE[w].split()}
PLACE, LEN = {}, {}


def sb(name, n, d):
    w = HOME.get(name, name)
    a = SCRATCH[w][1][1] if w in SCRATCH else 0
    PLACE[name], LEN[name] = (w, a), n
    SCRATCH[w] = ("sbuf", [128, a + (n if w == name else (n + 15) // 16 * 16)], d)


def mx(name, n):
    sb(name + "c", n, X4)
    sb(name + "s", n, U8)


CW = [C, 320, 256, 192, 128, 128]
CA = [sum(CW[:j]) for j in range(7)]
for _n, _w, _d in [
        ("X0", 1536, BF), ("U", 512, BF), ("VV", 512, BF), ("LKT", 72, I32), ("LKS", 72, I32), ("LK2", 96, I32),
        ("ULo", 24, U16), ("OFJ", 72, U16), ("OFS", 72, U16), ("UL", 24, I32), ("PC", 16, I32), ("X16", 96, I32), ("XA", 96, I32), ("XB2", 96, I32),
        ("PF", 128, F32), ("WT", 512, BF), ("ZB", 512, BF), ("CB", 512 * (ROOM["gone"] + 1), BF), ("FB", 2048, BF), ("GOt", 1024, BF),
        ("DGR", 32, BF), ("GCT", 96, BF), ("GCA", 32, BF), ("GDT", 128, BF), ("CF", 512, BF), ("CF2", 1280, BF),
        ("OCL", 96, BF), ("OCH", 96, BF), ("ML", C, BF), ("Y", C, BF), ("ALT", C, BF), ("JS", 8 * 12 * 13, BF),
        ("JM", C, F32), ("MD", C, F32), ("MX", C, F32), ("NX", C, F32), ("HD", C, F32), ("HD4", 96, F32), ("I4", 96, F32), ("IJF", C, F32),
        ("CONST", 96, F32), ("RST", C, BF), ("NODE", 3 * FS + C, F32),
        ("TS", C, F32), ("W0", C, F32), ("W1", C, F32), ("W2", C, F32), ("BASE", C, F32), ("A0", C, F32), ("A1", C, F32), ("RF", 512, BF), ("RG", C, BF),
        ("SB1", C, F32), ("ST", C, F32), ("ST2", C, F32), ("ST3", GW, F32), ("ST4", 96, F32), ("RS", 24, F32), ("RC", 96, F32), ("PL", 96, F32), ("LB1", 6, U16), ("LB16", 6, U16),
        ("GF", 96, F32), ("NS", 24, F32), ("CS", C, BF), ("WW", 96, BF), ("BA", 96, BF), ("BN", 96, BF),
        ("PLo", 24, U16), ("ELo", 6, U16), ("DL", 24, U16), ("L2", 24, U16), ("L3", 24, U16), ("EL", 24, U16),
        ("SLo", 24, U16),
        ("CT", 4 * CA[6], BF), ("G", 512, BF), ("IN", 512, BF), ("C2", 512, BF), ("G2", 512, BF), ("VT", 512, BF), ("ND", 4 * C, BF),
        ("GA", 4 * LINK[4], BF), ("PT", 512, BF), ("GS", 512, BF), ("WA", 3 * FS + C, BF), ("LW", C, F32),
        ("FT", 4 * FS, BF), ("H0", 512, BF), ("HT", 4 * FS, BF), ("FD", 8 * C, BF), ("Z", 8 * C, BF),
        ("E", 512, BF), ("OUT", 3 * C, F32)]:
    sb(_n, _w, _d)
PLACE["JK"], LEN["JK"] = ("FZ", 0), 16 * C
for _n, _w in [("QX", C), ("QU", 128), ("QUP", C), ("QV", 128), ("WC", 512), ("QK", 128 * NT), ("QF", 512), ("QT", CA[6]),
               ("QG", 128), ("QG2", 128), ("QRF", 128), ("QD", LINK[4] * SWEEPS), ("QC2", 128), ("QIN", 128),
               ("QVT", 128), ("QPT", 128), ("QS", 128), ("QE", 3 * 128), ("LD", 320), ("QND", C)]:
    mx(_n, _w)
PS = ["PA", "PB", "PCC", "PD", "LA", "LB", "AB", "PE"]
for _n in PS:
    SCRATCH[_n] = ("psum", [128, 512], F32)
    PLACE[_n], LEN[_n] = (_n, 0), 512
SEMAPHORES = ["sv", "ss", "st", "sg", "lcl", "arr0", "arr1", "arr2"] + ["d%d" % i for i in range(40)]


def rank_program(g, core, T, topo):
    rank = T.rank_of(core)
    if rank is None:
        return
    nxt = T.cores[(rank + 1) % len(T.cores)]
    Q = {"V": g.vector, "S": g.scalar, "T": g.tensor, "G": g, "Y": g.sync}
    SEM = {"V": "sv", "S": "ss", "T": "st", "G": "sg"}
    ops, wrs, rds, bank = [], {}, {}, {}

    def overlap(a, b):
        if a[1] <= b[0] or b[1] <= a[0]: return False
        d = math.gcd(a[2], b[2])
        return not (d > 1 and (a[0] - b[0]) % d)

    def note(ways, rd, wr, after=0, sem=None):
        me, deps = len(ops), {}
        for n, lo, hi, st in rd:
            for e in wrs.get(n, []):
                if overlap(e[0], (lo, hi, st)): deps[e[1]] = True
        for n, lo, hi, st in wr:
            for e in wrs.get(n, []) + rds.get(n, []):
                if overlap(e[0], (lo, hi, st)): deps[e[1]] = True
        for n in set(x[0] for x in list(rd) + list(wr) if x[0] in PS):
            if n in bank: deps.setdefault(bank[n], False)
            bank[n] = me
        for n, lo, hi, st in wr:
            if n in PS: continue
            for tab in (wrs, rds):
                tab[n] = [e for e in tab.get(n, []) if not (e[0][0] >= lo and e[0][1] <= hi and (st == 1 or (e[0][2] == st and e[0][0] == lo)))]
            wrs[n].append(((lo, hi, st), me))
        for n, lo, hi, st in rd:
            if n not in PS: rds.setdefault(n, []).append(((lo, hi, st), me))
        both = lambda c: c if isr(c) else (c, c) if sem else (0.9 * c, 1.35 * c)
        op = {"ways": {q: (w[0], 0.0, both(w[1])) for q, w in ways.items()}, "deps": deps, "after": after, "sem": sem}
        ops.append(op)

    def issue():
        n = len(ops)
        before, behind = [list(o["deps"].items()) for o in ops], [[] for _ in ops]
        for i in range(n):
            for d, hard in before[i]: behind[d].append((i, hard))

        def place(key, waits, back):
            busy, at = {q: [] for q in Q}, [None] * n
            for i in sorted(range(n), key=lambda i: -key[i]):
                best = None
                for q, (fn, c, _) in ops[i]["ways"].items():
                    t0 = ops[i]["after"] if back else 0.0
                    for d, hard in waits[i]:
                        x = ops[i if back else d]
                        t0 = max(t0, at[d][2] + x["after"] + (HOP if at[d][0] != q or x["sem"] else NEXT if hard else 0))
                    b = busy[q]
                    lo, k = 0, len(b)
                    while lo < k:
                        m = (lo + k) // 2
                        if b[m][1] > t0: k = m
                        else: lo = m + 1
                    while k < len(b) and b[k][0] < t0 + c:
                        t0 = max(t0, b[k][1])
                        k += 1
                    worth = t0 + c * (1 + SPARE if q == "V" else 1)
                    if best is None or worth < best[0]: best = (worth, q, t0, c, k)
                _, q, t0, c, k = best
                busy[q].insert(k, (t0, t0 + c))
                at[i] = (q, t0, t0 + c)
            return at

        def run(late):
            at, left, free, ready = [None] * n, [len(b) for b in before], {q: 0.0 for q in Q}, {q: {} for q in Q}

            def offer(i):
                for q in ops[i]["ways"]:
                    ready[q][i] = max([0.0] + [at[d][2] + ops[d]["after"] + (HOP if at[d][0] != q or ops[d]["sem"] else NEXT if hard else 0) for d, hard in before[i]])

            for i in range(n):
                if not left[i]: offer(i)
            while any(ready.values()):
                t0, q = min((max(free[q], min(ready[q].values())), q) for q in Q if ready[q])
                cost = lambda i, q=q: ops[i]["ways"][q][1]
                better = lambda i: any(p != q and max(free[p], ready[p][i]) + cost(i, p) * (1 + SPARE * (p == "V")) < t0 + cost(i) * (1 + SPARE * (q == "V")) for p in ops[i]["ways"])
                now = sorted((late[i], i) for i, x in ready[q].items() if x <= t0)
                soon = [(x, i) for i, x in ready[q].items() if x > t0]
                for _, i in now:
                    if better(i): continue
                    if not any(x < t0 + cost(i) and t0 + cost(i) - late[u] > max(0, x + cost(u) - late[i]) and late[u] < late[i] for x, u in soon): break
                else:
                    free[q] = min([x for x, u in soon] + [t0 + 50])
                    continue
                at[i] = (q, t0, t0 + cost(i))
                free[q] = at[i][2]
                for p in ops[i]["ways"]: del ready[p][i]
                for j, _ in behind[i]:
                    left[j] -= 1
                    if not left[j]: offer(j)
            return at

        def pace(m):
            for o in ops: o["ways"] = {q: (w[0], w[2][0] + m * (w[2][1] - w[2][0]), w[2]) for q, w in o["ways"].items()}

        def length(at, m):
            free, end = {q: 0.0 for q in Q}, [0.0] * n
            for i in sorted(range(n), key=lambda i: at[i][1]):
                q = at[i][0]
                t0 = max([free[q]] + [end[d] + ops[d]["after"] + (HOP if at[d][0] != q or ops[d]["sem"] else NEXT if hard else 0) for d, hard in before[i]])
                free[q] = end[i] = t0 + ops[i]["ways"][q][2][m]
            return max(end)

        plan = None
        for m in PACES:
            pace(m)
            key = [0.0] * n
            for i in range(n - 1, -1, -1):
                key[i] += min(w[1] for w in ops[i]["ways"].values()) + ops[i]["after"]
                for d in ops[i]["deps"]: key[d] = max(key[d], key[i] + HOP)
            at = place(key, before, False)
            for _ in range(PASSES):
                key = [x[2] for x in place([x[2] for x in at], behind, True)]
                at = run([max(key) - x for x in key])
                end = length(at, 0) * length(at, 1)
                if plan is None or end < plan[0]: plan = (end, at)
        for o, x in zip(ops, plan[1]): o["q"], o["start"] = x[0], x[1]
        cnt, known = {s: 0 for s in SEMAPHORES}, {q: {} for q in Q}
        for o in sorted(ops, key=lambda o: o["start"]):
            q = o["q"]
            need = [ops[d] for d, hard in o["deps"].items() if hard or ops[d]["q"] != q]
            for x in sorted(need, key=lambda x: -x["start"]):
                s, c = x["mark"]
                if known[q].get(s, 0) >= c: continue
                Q[q].wait_ge(T.sem[s], c)
                for s2, c2 in x["clock"].items(): known[q][s2] = max(known[q].get(s2, 0), c2)
            call = o["ways"][q][0](Q[q])
            if o["sem"]: s, cnt[s] = o["sem"][0], o["sem"][1]
            else:
                s = SEM[q]
                cnt[s] += 1
                call.then_inc(T.sem[s], 1)
            o["mark"] = (s, cnt[s])
            o["clock"] = dict({} if s.startswith("arr") else known[q], **{s: cnt[s]})
        for s in SEMAPHORES:
            if cnt[s]: g.wait_ge(T.sem[s], cnt[s])

    def r(n, lo=0, hi=None, st=1):
        w, a = PLACE[n]
        return (w, a + lo, a + (LEN[n] if hi is None else hi), st)

    def ap(x):
        n, lo, hi, st = x
        return T[n][:, lo:hi] if st == 1 else T[n][:, lo:hi:st]

    isr = lambda x: isinstance(x, tuple)
    val = lambda x: ap(x) if isr(x) else x
    size = lambda o: len(range(o[1], o[2], o[3]))
    narrow = lambda *xs: all(BYTES[SCRATCH[x[0]][2]] == 2 for x in xs)
    vtime = lambda n, f=1.0: max(0.83 * f * n, 53) + 40
    stime = lambda n: max(0.83 * n, 53) + 60
    gather = lambda n, a=50: (0.9 * a + 1.17 * n, 1.35 * a + 2.24 * n)
    dn = [0]

    def dma(q, pairs, rd=(), wr=(), n=None):
        s = "d%d" % dn[0]
        dn[0] += 1

        def run(e):
            for o, i in pairs: e.dma_start(o, i).then_inc(T.sem[s], 16)

        if n is None: n = sum(size(x) * BYTES[SCRATCH[x[0]][2]] for x in (wr or rd))
        note({q: (run, 60 * len(pairs) + (0.6 * n if q == "Y" else 0))}, rd, wr, LAND, (s, 16 * len(pairs)))

    def ts(o, i, s1, op0, s2=None, op1=None):
        rd = [i] + [s for s in (s1, s2) if isr(s)]
        more = () if op1 is None else (op1,)
        note({"V": (lambda e: e.tensor_scalar(ap(o), ap(i), val(s1), val(s2), op0, *more), vtime(size(o), 0.5 if narrow(o, i) else 1))}, rd, [o])

    def tt(o, a, b, op, off=None):
        if off is None: note({"V": (lambda e: e.tensor_tensor(ap(o), ap(a), ap(b), op), vtime(size(o), 1 if a[0] in PS else 2))}, [a, b], [o])
        else: note({"V": (lambda e: e.tensor_tensor(ap(o), ap(a).indirect(ap(off)), ap(b), op), gather(size(o)))}, [a, b, off], [o])

    def tc(o, a, off=None):
        if off is None: note({"V": (lambda e: e.tensor_copy(ap(o), ap(a)), vtime(size(o)))}, [a], [o])
        else: note({"V": (lambda e: e.tensor_copy(ap(o), ap(a).indirect(ap(off))), gather(size(o)))}, [a, off], [o])

    def scatter(win, off, a):
        note({"V": (lambda e: e.tensor_copy(ap(win).indirect(ap(off)), ap(a)), (2.84 * size(a) + 45, 6.2 * size(a) + 68))}, [a, off], [win])

    def act(o, a, bias=0.0, scale=1.0, off=None, fn=COPY, acc=None, on="VS"):
        rd = [a] + [x for x in (scale, bias, off) if isr(x)]
        f = IDENT if isr(bias) and fn == COPY else fn
        src = (lambda: ap(a)) if off is None else (lambda: ap(a).indirect(ap(off)))
        more = lambda: {} if acc is None else {"accum_out": ap(acc)}
        n, ways = size(o), {}
        if "S" in on: ways["S"] = (lambda e: e.activation(ap(o), src(), f, bias=val(bias), scale=val(scale), **more()), gather(n, 65) if off else stime(n) + 20 * (acc is not None))
        if "V" in on and fn == COPY and acc is None:
            ways["V"] = (lambda e: e.tensor_scalar(ap(o), src(), val(scale), val(bias), OP.mult, OP.add), gather(n) if off else vtime(n, 0.5 if narrow(o, a) else 1))
        note(ways, rd, [o] + ([] if acc is None else [acc]))

    def total(o, junk, a):
        note({"V": (lambda e: e.tensor_reduce(ap(o), ap(a), AxisListType.X, OP.add), vtime(size(a))),
              "S": (lambda e: e.activation(ap(junk), ap(a), COPY, accum_out=ap(o)), stime(size(a)) + 20)}, [a], [o, junk])

    def scan(o, a, b, op0, op1):
        note({"V": (lambda e: e.tensor_tensor_scan(ap(o), ap(a), ap(b), 0.0, op0, op1), vtime(size(o), 0.5 if narrow(o, a, b) else 1))}, [a, b], [o])

    def fill(o, c):
        note({"V": (lambda e: e.memset(ap(o), c), vtime(size(o), 0.5 if narrow(o) else 1))}, [], [o])

    def quant(n, a, b, src):
        q, s = r(n + "c", a, b), r(n + "s", a, b)
        note({"V": (lambda e: e.quantize_mx(ap(q), ap(s), ap(src)), 52 + 0.88 * (b - a))}, [src], [q, s])

    def pick(n, a, src, off):
        m = 16 * (off[2] - off[1])
        c, s = r(n + "c", a, a + m), r(n + "s", a, a + m)
        note({"V": (lambda e: e.tensor_copy(ap(c).bitcast(dt.uint32), T[src + "c"][:].bitcast(dt.uint32).indirect(ap(off))), gather(m))}, [r(src + "c"), off], [c])
        note({"S": (lambda e: e.activation(ap(s), T[src + "s"][:].indirect(ap(off)), COPY), gather(m))}, [r(src + "s"), off], [s])

    def mm(bk, st, mv, n, start=True, stop=True):
        l, ls = r(st[0] + "c", st[1], st[1] + 128), r(st[0] + "s", st[1], st[1] + 128)
        m, ms = r(mv[0] + "c", mv[1], mv[1] + n), r(mv[0] + "s", mv[1], mv[1] + n)
        o = r(bk, 0, n)
        note({"T": (lambda e: e.matmul_mx(ap(o), ap(l), ap(ls), ap(m), ap(ms), start, stop), 0.68 * (n + 16) + 30)}, [l, ls, m, ms], [o])

    def sums(bk, terms, start=True, stop=True):
        for j, (st, mv) in enumerate(terms): mm(bk, st, mv, 128, start and j == 0, stop and j == len(terms) - 1)

    def iota(o, pat, base, cm=0):
        more = {} if SCRATCH[o[0]][2] == I32 else {"allow_small_or_imprecise_dtypes": True}
        note({"G": (lambda e: e.iota(ap(o), pat, base, cm, **more), 170 + 2.1 * size(o))}, [], [o])

    def const(o, c):
        iota(o, [[0, size(o)]], c)

    def sel(o, i, pat, op, fl, base, cm):
        note({"G": (lambda e: e.affine_select(ap(o), ap(i), pat, op, fl, base, cm), 220 + 2.1 * size(o))}, [i], [o])

    def zeros(*xs):
        pairs = [(T[n][:, a:min(a + 512, hi)], T.ZB[:, 0:min(512, hi - a)]) for n, lo, hi, _ in xs for a in range(lo, hi, 512)]
        dma("Y", pairs, rd=[r("ZB")], wr=xs)

    K = lambda n: ("QK", 128 * TI[n])
    EB = lambda b: ("QF", 128 * b)
    col = lambda n, j: r(n, j, j + 1)
    room = lambda n, a=0, k=1, st=1: r("CB", 512 * ROOM[n] + a, 512 * (ROOM[n] + k), st)
    PFC = {}

    def pcol(name, n=1):
        PFC[name] = sum(x[1] for x in PFC.values()), n
        return r("PF", PFC[name][0], PFC[name][0] + n)

    P = lambda name, j=0: col("PF", PFC[name][0] + j)
    PV = lambda name: r("PF", PFC[name][0], PFC[name][0] + PFC[name][1])
    GRP = {0: ([[16, 8]], 0), 1: ([[32, 4], [-16, 2]], 16), 4: ([[-64, 2], [16, 4]], 64)}
    neg = lambda pat: [[-a, b] for a, b in pat]
    row = lambda j: col("MD", j)
    cf = lambda n, k=1: r("CF", 32 * TI[n], 32 * (TI[n] + k))
    c2 = lambda e, n, a=0, st=1, k=1: r("CF2", 320 * e + 32 * T2.index(n) + a, 320 * e + 32 * (T2.index(n) + k), st)

    dma("S", [(T.U[:], T.u[:])], wr=[r("U")])
    for a in (0, 2 * C): dma("Y", [(T.X0[:, a:a + 2 * C], T.x[:, a:a + 2 * C])], wr=[r("X0", a, a + 2 * C)])
    dma("Y", [(T.LKT[:], T.lk[:])], wr=[r("LKT")])
    fill(r("ZB"), 0.0)
    fill(r("WT"), 1.0)
    zeros(*[r("CT", 4 * CA[j] + 64 * (21 - 4 * j), 4 * CA[j + 1]) for j in range(6)])
    zeros(room("ld", 0, 5), room("lg"))
    zeros(r("G"), r("RF", C), *[r("GA", 4 * LINK[k] - 128, 4 * LINK[k]) for k in (1, 3, 4)])
    zeros(r("FB"), r("E", C))
    zeros(r("PT", C), r("GS", C))
    zeros(room("ac1", 0, 2))
    zeros(room("gr", 0, 8))
    zeros(r("C2"), r("G2"), r("VT"), r("H0"))
    for a in range(C, LEN["WA"] - C, C):
        if a % FS: const(r("WA", a, a + C), 0)
    for x in (room("nm"), r("ND", 0, 512), r("ND", 512, 1024), r("ND", 1024), r("IN")): const(x, 0)
    pr = [(T.LKS[:, 0:24], T.lk[:, 0:24])]
    for h in range(8):
        a = h ^ JUMP[1]
        pr.append((T.LKS[16 * h:16 * h + 16, 24:48], T.lk[16 * a:16 * a + 16, 24:48]))
    for h in range(0, 8, 4):
        a = h ^ JUMP[2]
        pr.append((T.LKS[16 * h:16 * h + 64, 48:72], T.lk[16 * a:16 * a + 64, 48:72]))
    dma("Y", pr, wr=[r("LKS")])
    iota(r("LK2"), [[4, 4], [16, 24]], 0)
    dma("Y", [(T.LK2[4 * k + s:128:16, 24 * q:24 * q + 24], T.lk[4 * q + s:128:16, 24 * k:24 * k + 24]) for k in range(3) for q in range(4) for s in range(4)], wr=[r("LK2")])
    dma("Y", [(T.WCc[:].bitcast(dt.uint8), T.wc[:]), (T.WCs[:], T.ws[:])], wr=[r("WCc"), r("WCs")])
    dma("Y", [(T.VV[:], T.v[:])], wr=[r("VV")])

    iota(r("PC", 0, 1), [[0, 1]], 0, 1)
    iota(r("JM"), [[0, 24], [1, 16]], 0)
    for k in range(3):
        iota(r("UL", 8 * k, 8 * k + 8), GRP[JUMP[k]][0], GRP[JUMP[k]][1])
    iota(r("I4"), [[0, 24], [1, 4]], 0)
    iota(r("IJF"), [[1, C]], 0)
    iota(r("CONST"), [[16, 24], [0, 4]], 0)
    iota(r("ALT"), [[0, C // 2], [1, 2]], 0)
    p = col("PC", 0)
    for j, (sh, an) in enumerate([(0, 15), (0, 3), (2, 3), (4, 1), (5, 1), (6, 1)]):
        ts(col("PC", j + 1), p, sh, OP.arith_shift_right, an, OP.bitwise_and)
    tc(pcol("p0"), p)
    tc(pcol("i"), col("PC", 1))
    tc(pcol("p", 5), r("PC", 2, 7))
    pi, (ps, pk, g0, g1, g2) = P("i"), [P("p", j) for j in range(5)]
    ts(r("MD"), r("JM"), pi, OP.is_equal)
    act(r("MX"), r("MD"), scale=-2e29, bias=1e29)
    act(r("NX"), r("MD"), scale=2e29)
    fill(r("NX", 0, C, 16), 2e29)
    act(r("HD"), r("MD"), scale=-DROP - HOLD, bias=HOLD)
    ts(r("HD4"), r("I4"), pk, OP.is_equal)
    act(r("HD4"), r("HD4"), scale=-DROP - HOLD, bias=HOLD)
    fill(r("RST"), 1.0)
    fill(r("RST", 0, C, 16), 0.0)
    fill(col("RS", 0), 0.0)
    ts(pcol("ms", 4), r("I4", 0, 4), ps, OP.is_equal)
    ts(pcol("mr", 4), r("I4", 0, 4), pk, OP.is_equal)
    ts(r("DGR"), r("I4", 0, 32), pk, OP.is_equal)
    for n, src in (("ULo", "UL"), ("OFJ", "LKT"), ("OFS", "LKS")): tc(r(n), r(src))
    quant("QU", 0, 128, r("U"))
    for a, b in ((0, 8), (8, 24)): pick("QUP", 16 * a, "QU", r("ULo", a, b))
    for a in (0, C // 2): quant("QX", a, a + C // 2, r("X0", 4 * a, 4 * a + 2 * C))
    quant("QV", 0, 128, r("VV"))
    act(pcol("n3"), P("mr", 3), scale=-1.0, bias=1.0)
    act(pcol("mk", 4), PV("ms"), scale=P("n3"))
    act(pcol("mn", 4), PV("mk"), scale=-1.0)
    act(pcol("m80", 4), PV("mr"), scale=80.0)
    act(pcol("thr"), P("mr", 3), scale=-18.0, bias=0.5)
    act(pcol("two"), P("mr", 3), bias=1.0)
    act(pcol("k16"), pi, scale=HOLD, bias=-15 * HOLD)
    act(pcol("k4"), pk, scale=HOLD, bias=-3 * HOLD)
    act(pcol("kp"), P("k4"), scale=-1.0, bias=GW - 0.5)
    act(pcol("ks"), ps, scale=-HOLD, bias=3 * HOLD + GW - 15.5)
    act(pcol("kc"), P("ks"), bias=pi)
    act(r("CONST"), r("CONST"), scale=-1.0, bias=P("kc"))
    ts(r("PL"), r("I4"), pk, OP.not_equal, -1e9, OP.mult)
    tt(r("CONST"), r("CONST"), r("PL"), OP.add)
    act(pcol("kb"), pk, scale=16.0, bias=15.0)
    ts(r("LB1"), r("IJF", 0, 24, 4), pk, OP.add)
    ts(r("LB16"), r("IJF", 0, C, 64), P("kb"), OP.add)
    act(pcol("sg1"), g0, scale=-2.0, bias=1.0)
    act(pcol("sg2"), g2, scale=-2.0, bias=1.0)
    act(pcol("p4"), row(4), scale=P("sg1"))
    act(pcol("p8"), row(8), scale=P("sg2"))
    act(pcol("ys"), row(1), scale=-2.0, bias=row(0))
    ts(pcol("wa"), row(0), row(1), OP.subtract, row(2), OP.subtract)
    act(pcol("w0"), row(10), scale=-1.0, bias=P("wa"))
    ts(pcol("ya"), row(4), g0, OP.mult, row(1), OP.subtract)
    act(pcol("yb"), row(8), scale=g2, bias=P("ya"))
    act(pcol("y"), P("yb"), scale=-1.0, bias=1.0)
    ts(pcol("da"), row(0), row(1), OP.add, row(4), OP.add)
    act(pcol("dr"), P("da"), bias=row(8))
    ts(pcol("w1"), row(6), row(2), OP.subtract, P("p4"), OP.subtract)
    ts(pcol("w2"), row(6), row(10), OP.add, P("p8"), OP.add)
    ts(pcol("ba"), row(0), row(1), OP.subtract, P("p4"), OP.add)
    act(pcol("base"), P("ba"), bias=P("p8"))
    iota(r("LW"), [[1, C]], 0)
    tt(r("ML"), r("IJF"), r("LW"), OP.is_lt, off=r("OFJ", 0, 24))
    act(r("Y"), r("ML"), scale=P("ys"), bias=P("y"))
    act(pcol("r23"), P("mr", 2), bias=P("mr", 3))
    for A, x in ((1, P("mr", 2)), (2, P("mr", 3)), (3, P("r23"))):
        act(pcol("tb%d" % A, 4), PV("ms"), scale=x)
        act(pcol("sg%d_" % A), x, scale=-2.0, bias=1.0)
        act(pcol("ta%d" % A, 4), PV("ms"), scale=P("sg%d_" % A))
    act(pcol("ws"), P("mr", 2), scale=2.0, bias=-1.0)
    act(pcol("wsc"), P("ws"), scale=P("n3"))
    act(pcol("wb"), pk, scale=-1.0, bias=3.0)
    act(pcol("b1"), P("mr", 1), scale=2.0, bias=P("mr", 0))
    act(pcol("bit"), P("mr", 2), scale=4.0, bias=P("b1"))
    act(pcol("bit8"), P("bit"), scale=8.0)
    ts(pcol("n0"), pi, -1.0, OP.mult, P("p0"), OP.add)
    act(pcol("nd0"), P("n0"), scale=C / 16.0)
    act(pcol("nd1"), P("sg1"), scale=float(C), bias=P("nd0"))
    act(pcol("nd2"), P("sg2"), scale=4.0 * C, bias=P("nd0"))
    act(pcol("nd3"), P("sg2"), scale=4.0 * C, bias=P("nd1"))
    ts(pcol("s3"), ps, P("mr", 3), OP.mult, 16.0, OP.add)
    for q in range(4): ts(r("X16", q, 96, 4), r("LK2", 24 * q, 24 * q + 24), P("s3"), OP.add)
    ts(r("XA"), r("X16"), 31, OP.bitwise_and)
    ts(r("XB2"), r("X16"), 992, OP.bitwise_and)
    ts(r("OCL"), r("XA"), -16.0, OP.add)
    tc(r("OCH"), r("XB2"))

    turn = [0]

    def group_mask(o, c, src=None):
        gp, gb = GRP[c]
        n = size(o) // 32
        rep = [[0, n]] if n > 1 else []
        turn[0] = (turn[0] + 160) % 480
        x = r("GOt", 512 + turn[0], 512 + turn[0] + 32 * n)
        sel(x, src or o, rep + neg(gp) + [[0, 4]], OP.is_ge, 0.0, -gb, 1)
        sel(o, x, rep + gp + [[0, 4]], OP.is_ge, 0.0, gb + 15, -1)

    def quant_tiles(names):
        for j in range(0, len(names), 4):
            a, n = names[j], len(names[j:j + 4])
            quant("QK", 128 * TI[a], 128 * (TI[a] + n), room(a, 0, n))

    def lay(names):
        n = len(names)
        if names != T1C:
            group_mask(cf(names[0], n - 2), 0)
            for k in (1, 2): group_mask(cf(names[k - 3]), JUMP[k])
        for s in range(4): act(room(names[0], 5 * s, n, 16), cf(names[0], n))
        quant_tiles(names)

    def lay_short(e, a, b):
        n = TI[b] - TI[a] + 1
        for s in range(4): act(room(a, 4 * s + e, n, 16), c2(e, a, 0, 1, n), scale=P("ms", s))

    sel(r("GOt", 0, 512), r("WT"), [[-16, 8], [0, 64]], OP.is_ge, 0.0, 0, 1)
    sel(room("gone"), r("GOt", 0, 512), [[16, 8], [0, 64]], OP.is_ge, 0.0, 15, -1)
    quant_tiles(["gone"])
    const(c2(0, "lg"), -7)
    const(c2(0, "lg", 3, 4), 7)
    group_mask(c2(0, "lg"), 0)
    lay_short(0, "lg", "lg")
    quant_tiles(["lg"])
    act(r("GCT", 0, 32), r("DGR"), scale=-2.0, bias=-4.0)
    act(cf("ld"), r("GCT", 0, 32), scale=P("dr"))
    act(cf("lo"), r("DGR"), scale=-4.0, bias=-1.0)
    act(r("GCT", 32, 64), r("DGR"), scale=-2.0, bias=3.0)
    for k in range(3): act(cf("lc%d" % k), r("GCT", 32, 64), scale=P("mr", k))
    lay(T1A)
    for b in range(4): sel(r("FB", 513 * b, 512 * b + 512, 4), r("WT", 0, 128), [[-1, 128]], OP.is_equal, 0.0, 0, 1)
    quant("QF", 0, 512, r("FB"))
    act(cf("ad"), r("DGR"), scale=P("dr"))
    act(cf("ao"), r("DGR"), scale=0.5)
    act(r("GCT", 64, 96), r("DGR"), scale=-0.5)
    const(r("GCT", 67, 96, 4), 1)
    for k in range(3): act(cf("ac%d" % k), r("GCT", 64, 96), scale=P("mr", k))
    a = 32 * TI["ord"]
    for k, (x, y, op) in enumerate(((2, 10, OP.add), (6, 2, OP.subtract), (6, 10, OP.add))):
        ts(r("CF", a + k, a + 32, 4), r("WT", 0, 8), row(x), OP.mult, row(y), op)
    const(r("CF", a + 3, a + 32, 4), 0)
    act(pcol("sa"), P("mr", 2), scale=FS - 1.0, bias=1.0)
    act(pcol("sb"), P("mr", 3), scale=2.0 * FS - 1, bias=P("sa"))
    act(cf("st"), r("WT", 0, 32), scale=P("sb"))
    lay(T1B)
    def class_mask(o, A, src):
        if A < 3: return group_mask(o, REACH[A], src)
        for a, b in ((0, 80), (16, 16)):
            x = r("GDT", 32 + a, 48 + a)
            sel(x, (src[0], src[1] + a, src[1] + a + 16, 1), [[-32, 2], [16, 2], [0, 4]], OP.is_ge, 0.0, -b, 1)
            sel((o[0], o[1] + a, o[1] + a + 16, 1), x, [[32, 2], [-16, 2], [0, 4]], OP.is_ge, 0.0, b + 15, -1)

    ts(r("GDT", 0, 32), r("I4", 0, 32), 1.5, OP.is_lt)
    for k in (1, 2): act(r("GDT", 1 + k, 32, 4), r("WT", 0, 8), scale=P("mr", k))
    for A in range(4):
        class_mask(c2(3, "ct%d" % A), A, r("GDT", 0, 32))
        class_mask(cf("cw%d" % A), A, r("DGR"))
    for e in range(3):
        sel(c2(e, "ct0", 0, 1, 4), c2(3, "ct0", 0, 1, 4), [[0, 32], [1, 4]], OP.is_equal if e < 2 else OP.is_ge, 0.0, -e, 0)
    lay(T1C)
    const(c2(0, "gr"), 7)
    act(c2(0, "lv"), r("DGR"), scale=2048.0, bias=-1024.0)
    const(c2(0, "dl1"), 1)
    group_mask(c2(0, "gr", 0, 1, 3), 0)
    for e, c in ((1, 1), (3, 2)):
        const(c2(e, "dl1"), c)
        group_mask(c2(e, "dl1"), 0)
    act(pcol("d1"), P("mr", 1), scale=float(FS))
    act(pcol("d2"), P("mr", 2), scale=2.0 * FS, bias=P("d1"))
    act(r("GDT", 64, 96), r("WT", 0, 32), scale=P("d2"))
    for e in (2, 3): group_mask(c2(e, "dl2"), 0, r("GDT", 64, 96))
    for e in range(4): lay_short(e, *ELEM[e])
    quant_tiles(T2[1:9])
    act(c2(0, "nm"), r("DGR"), scale=-2.0)
    act(pcol("nb"), P("mr", 3), scale=9.5, bias=-9.0)
    act(c2(1, "nm"), r("DGR"), scale=-4.0, bias=P("nb"))
    for e in range(2):
        group_mask(c2(e, "nm"), 0)
        lay_short(e, "nm", "nm")
    quant_tiles(["nm"])
    for a in range(0, LEN["NODE"], C):
        if a % FS: const(r("NODE", a, a + C), 0)
        else: act(r("NODE", a, a + C), r("IJF"), bias=P("nd%d" % (a // FS)))

    def send(t):
        m = topo.engines(core, nxt)[:ENGINES]
        rid, pid, _ = topo.addr(nxt)
        n = 128 if t == 0 else GW
        a = 0 if t == 0 else 32 + GW * t
        sem = T.sem["arr%d" % t]

        o, mask = 128 * t, sum(1 << x for x in m)

        def run(e):
            e.remote_dma(T.LDc[:, a:a + n].bitcast(dt.uint8), T.QEc[:, o:o + n].bitcast(dt.uint8), sem, T.sem.lcl, pid, rid, mask)
            e.remote_dma(T.LDs[:, a:a + n], T.QEs[:, o:o + n], sem, T.sem.lcl, pid, rid, mask)

        pe = len(topo.engines(T.cores[(rank - 1) % len(T.cores)], core)[:ENGINES])
        note({"G": (run, 2000)}, [r("QEc", o, o + n), r("QEs", o, o + n)], [r("LDc", a, a + n), r("LDs", a, a + n)], FAR, ("arr%d" % t, 2 * pe))
        return 2 * len(m)

    def spread(n, lo=1, hi=4):
        pairs = []
        for A in range(lo, hi):
            k = 4 if REACH[A] == 4 else 1
            for h in range(0, 8, k):
                a = 16 * (h ^ REACH[A])
                pairs.append((T[n][16 * h:16 * (h + k), FS * A:FS * A + FS], T[n][a:a + 16 * k, 0:FS]))
        if pairs: dma("Y", pairs, rd=[r(n, 0, FS)], wr=[r(n, FS * lo, FS * hi)])

    def hold(ahead):
        for j in ahead: ops[-1]["deps"].setdefault(j, False)

    def to_list(bk, o):
        scan(r("ST4"), r("HD4"), r(bk, 0, 96), OP.add, OP.max)
        ts(r(o), r("ST4", 3, 96, 4), P("k4"), OP.add)

    def moved(i, own, came):
        return [(K(n), ("QD", LINK[4] * i + LINK[k])) for k, n in enumerate([own, came + "0", came + "1", came + "2"])]

    sent, H, VB, SB = [0], C // 2, ("PA", "AB"), ("PB", "LB")
    half = lambda n, h: r(n, H * h, H * h + H)

    def scores(j, h):
        if j == 0:
            for bk in (VB[h], SB[h]): mm(bk, ("QUP", 0), ("QX", H * h), H)
            act(half("TS", h), r(SB[h], 0, H), on="S")
            tt(half("SB1", h), r(VB[h], 0, H), half("MX", h), OP.max)
        if j == 1: scan(half("ST", h), half("NX", h), half("SB1", h), OP.add, OP.min)
        if j == 2: ts(r("NS", 12 * h, 12 * h + 12), r("ST", H * h + 15, H * h + H, 16), -1.0, OP.mult)

    for t in range(R):
        pass
        for h in range(1 if t else 0, 2):
            for j in range(3): scores(j, h)
        for bk, a in (("PCC", 128), ("PD", 256)): mm(bk, ("QUP", a), ("QX", 0), C)
        for h in (0, 1): tt(r("CT", 4 * H * h, 4 * H * h + 4 * H, 4), r(VB[h], 0, H), half("ST", h), OP.is_ge)
        for a in range(23, 0, -1):
            j, e = divmod(24 - a, 4)
            node, x = r("CT", 4 * CA[j] + e, 4 * CA[j] + 64 * a, 4), r("JK" if a > 12 else "JS", 8 * a * (a - 1), 8 * a * (a + 1))
            if a in SOWN or t == 0 and a in SFIRST:
                act(x, r("TS", 0, 16 * a), bias=col("NS", a), fn=FN.Relu)
                act(node, x, fn=FN.Sign, acc=col("RS", a))
            else:
                ts(node, r("TS", 0, 16 * a), col("ST", 16 * a + 15), OP.is_gt)
                total(col("RS", a), x, node)
        for j in TORDER:
            quant("QT", CA[j], CA[j + 1], r("CT", 4 * CA[j], 4 * CA[j + 1]))
            mm("PE", K("gone"), ("QT", CA[j]), CW[j], j == TORDER[0], j == TORDER[-1])
        scan(r("CS"), r("RST"), r("CT", 0, 4 * C, 4), OP.mult, OP.add)
        tt(r("RC"), r("CS"), r("CONST"), OP.add, off=r("LB16"))
        tt(r("GF"), r("RS"), r("RC"), OP.add, off=r("LB1"))
        act(r("W1"), r("PCC", 0, C), scale=P("w1"))
        act(r("W2"), r("PD", 0, C), scale=P("w2"))
        if t == 0:
            act(r("W0"), r("TS"), scale=P("w0"))
            act(r("BASE"), r("TS"), scale=P("base"))
            tt(r("A0"), r("W0"), r("BASE"), OP.subtract, off=r("OFJ", 0, 24))
        else: act(r("A0"), r("TS"), scale=P("w0"), off=r("OFJ", 0, 24), on="S")

        def order1(h):
            tt(r("A1", 192 * h, 192 * h + 192), r("W1"), r("A0", 192 * h, 192 * h + 192), OP.subtract, off=r("OFJ", 24 + 12 * h, 36 + 12 * h))

        def order2(h):
            tt(r("RF" if t else "RG", 192 * h, 192 * h + 192), r("W2"), r("A1", 192 * h, 192 * h + 192), OP.is_lt, off=r("OFJ", 48 + 12 * h, 60 + 12 * h))

        def weights():
            if t == 0: tt(r("RF", 0, C), r("RG"), r("Y"), OP.is_equal)
            quant("QRF", 0, 128, r("RF"))
            mm("PD", K("ord"), ("QRF", 0), 128)
            act(r("WW"), r("PD", 0, 96), scale=P("wsc"), bias=P("wb"), fn=FN.Square)

        if t == 0:
            for h in (0, 1):
                order1(h)
                order2(h)
            weights()
        for b in range(4):
            bk = ("PA", "PB")[b % 2]
            mm(bk, EB(b), ("QX", 0), C)
            act(r("FT", C * b, C * b + C), r(bk, 0, C), scale=0.5)
        pass
        scan(r("ST2"), r("HD"), r("PE", 0, C), OP.add, OP.max)
        tt(r("G", 0, C, 4), r("ST2", 3, C, 4), r("GF"), OP.is_lt)
        quant("QG", 0, 128, r("G"))
        flags = len(ops) - 1
        first = [(K("ld"), ("QRF", 0)) if t == 0 else (EB(0), ("QIN", 0)), (K("lg"), ("QG", 0))]
        sums("LA", first)
        for q in range(4): act(r("G2", 4 * q, C, 16), r("G", 4 * q, C, 16), scale=2224.0, bias=P("m80", q))
        quant("QG2", 0, 128, r("G2"))
        tt(r("PL"), r("GF"), r("ST2", 3, C, 4), OP.subtract)
        hold([flags - 1])
        scan(r("ST4"), r("HD4"), r("PL"), OP.add, OP.max)
        ts(r("PLo"), r("ST4", 3, 96, 4), -1.0, OP.mult, P("kp"), OP.add)
        ts(r("SLo"), r("PLo"), float(GW), OP.min)
        spread("FT", 1, AHEAD[t])

        def in_order(h):
            scatter(r("LW"), r("PLo", 12 * h, 12 * h + 12), r("IJF", 192 * h, 192 * h + 192))

        def gates():
            scan(r("ST3"), r("HD", 0, GW), r("LW", 0, GW), OP.add, OP.max)
            ts(r("ELo"), r("ST3", 15, GW, 16), P("k16"), OP.add)
            for b in range(4): act(r("E", b, 4 * GW, 4), r("FT", C * b, C * b + C), scale=2.0, off=r("ELo"), on="S")

        def pass_on():
            quant("QE", 128 * t, 128 * t + 128, r("E"))

        def leave():
            sent[0] += send(t)
            spread("FT", AHEAD[t], 4)
            hold([len(ops) - 2])

        def layer():
            a, o, last = (0 if t == 0 else GW * t), (0 if t == 0 else 32), len(ops) - 1
            for b in range(4):
                bk = ("PE", "PCC")[b % 2]
                mm(bk, ("WC", 128 * b), ("LD", a), 128)
                ops[-1]["deps"].setdefault(last, False)
                act(r("H0", 128 * b, 128 * b + GW), r(bk, o, o + GW), scale=0.015625)
                for h in (0, 1):
                    act(r("HT", C * b + H * h, C * b + H * h + H), r("H0", 128 * b, 128 * b + 128), off=r("SLo", 12 * h, 12 * h + 12))
            spread("HT")

        work = {"s": in_order, "a": order1, "b": order2, "e": lambda h: pass_on()}
        then = {"s1": gates, "e0": leave, "b1": weights}

        def pin(names, last):
            held = []
            for w in names.split():
                if t == 0 and w[0] in "ab": continue
                work[w[0]](int(w[1]))
                ops[-1]["deps"].setdefault(last, False)
                held.append(len(ops) - 1)
                if w in then: then[w]()
            return held

        held = pin(BEHIND[0], flags)
        sums("AB", [(K("ad"), ("QRF", 0)) if t == 0 else (EB(1), ("QIN", 0))], True, False)
        for i in range(SWEEPS):
            pass
            bk, nb = ("LA", "LB")[i % 2], ("LB", "LA")[i % 2]
            c = max([-1] + [j for j in KEEP if j <= i])
            past = [x for j in range(max(c, 0), i) for x in moved(j, "lo", "lc")] + (first if c < 0 else [])
            if i == SWEEPS - 1: nb, past = "PB", past + [(K("gr"), ("QG", 0))]
            sums(nb, past, True, False)
            even = t == 0 and i <= KEEP[0]
            for s in range(4):
                if even or TURN[i] == "S": act(r("GA", s, C, 4), r(bk, 0, 96), scale=P("mk", s), bias=P("mk", s) if even else 0.0, fn=FN.Sign)
                else: ts(r("GA", s, C, 4), r(bk, 0, 96), P("mn", s), OP.max, P("mk", s), OP.min)
                if "V" in ops[-1]["ways"]: hold(held)
            ahead, held = held, pin(BESIDE[i], len(ops) - 1)
            if i == c:
                act(r("C2", 0, C, 4), r(bk, 0, 96), bias=1.0 if even else 0.0)
                quant("QC2", 0, 128, r("C2"))
            if c >= 0: mm(nb, EB(0), ("QC2", 0), 128, not past, False)
            n = VSWEEP[i] if t else VFIRST[i]
            o, a = 4 * LINK[1], LINK[4] * i
            act(r("GA", o + n, o + 2 * C), r("GA", 0, C), off=r("OFS", n // 16, 48), on="S")
            act(r("GA", 4 * LINK[3], 4 * LINK[3] + C), r("GA", 0, C), off=r("OFS", 48, 72), on="S")
            tc(r("GA", o, o + n), r("GA", 0, C), off=r("OFS", 0, n // 16))
            hold(ahead)
            quant("QD", a, a + LINK[1], r("GA", 0, o))
            hold([len(ops) - 2])
            n = 192 if t else 224
            quant("QD", a + LINK[1], a + LINK[1] + n, r("GA", o, o + 4 * n))
            hold(held)
            quant("QD", a + LINK[3], a + LINK[4], r("GA", 4 * LINK[3]))
            held = pin(BEHIND[i + 1], len(ops) - 1)
            if i == LAYER: layer()
            sums(nb, moved(i, "lo", "lc"), False, True)
            sums("AB", moved(i, "ao", "ac"), False, i == SWEEPS - 1)
        pass
        tt(r("VT", 0, C, 4), r("AB", 0, 96), r("WW"), OP.mult)
        quant("QVT", 0, 128, r("VT"))
        ts(r("IN", 1, C, 4), r("AB", 0, 96), P("thr"), OP.is_gt, P("two"), OP.mult)
        for bk in ("PA", "PE"): sums(bk, [(K("lg"), ("QG2", 0)), (K("lv"), ("QVT", 0))])
        act(r("IN", 0, C, 4), r("PB", 0, 96))
        quant("QIN", 0, 128, r("IN"))
        tt(r("PT", 0, C, 4), r("PA", 0, 96), r("OCL"), OP.min)
        tt(r("PT", 1, C, 4), r("PA", 0, 96), r("OCH"), OP.min)
        ts(r("PT", 2, C, 4), r("PA", 0, 96), 1.0, OP.min)
        act(r("PT", 3, C, 4), r("PE", 0, 96), scale=-1.0, fn=FN.Relu)
        quant("QPT", 0, 128, r("PT"))
        four = ("LA", "LB", "PCC", "PD")

        def classes(n, src):
            for A in (2, 0, 3, 1):
                mm(four[A], K("%s%d" % (n, A)), (src, 0), 128)
                if A != 2: ops[-1]["deps"].setdefault(len(ops) - 2, False)

        classes("ct", "QPT")
        sums("PA", [(K("dl1"), ("QPT", 0)), (K("dl2"), ("QPT", 0))])
        to_list("PA", "DL")

        def table():
            for A in range(4):
                for s in range(4):
                    act(r("WA", FS * A + s, FS * A + C, 4), r(four[A], 0, 96), scale=P("ta%d" % A if A else "ms", s),
                        bias=P("tb%d" % A, s) if A else 0.0, on="V" if A < 2 else "S")

        table()
        if t == R - 1:
            mm("PB", K("nm"), ("QIN", 0), 128)
            ts(r("BN"), r("PB", 0, 96), -1.5, OP.is_gt, P("bit8"), OP.mult)
            act(r("BA"), r("IN", 1, C, 4), scale=P("bit"))
            tt(r("BA"), r("BA"), r("BN"), OP.add)
            for s in range(4): act(r("ND", 4 * s, 4 * C, 16), r("BA"), scale=P("ms", s))
            quant("QND", 0, C, r("ND"))
            bits = len(ops) - 1
            mm("PB", K("gone"), ("QND", 0), C)
            act(r("OUT", C, 2 * C), r("PB", 0, C))
        pass
        for a, b in (("DL", "L2"), ("L2", "EL")):
            act(r("GS", VSTEP, C), r("WA"), off=r(a, VSTEP // 16, 24), on="S")
            tc(r("GS", 0, VSTEP), r("WA"), off=r(a, 0, VSTEP // 16))
            quant("QS", 0, 128, r("GS"))
            if b == "L2": classes("cw", "QS")
            mm("PA", K("st"), ("QS", 0), 128)
            to_list("PA", b)
            if b == "L2": table()
            elif t == R - 1: hold([bits])
        pass
        part = lambda n, b, h, a, st: r(n, 2 * C * b + C * h + a, 2 * C * b + C * h + C, st)
        for h in (0, 1):
            for b in (2, 0, 3, 1): act(part("FD", b, h, 0, 2), r("FT", C * b), off=r("DL", 12 * h, 12 * h + 12))
        done = {}
        for w in BLEND.split():
            b, h = int(w[1]), int(w[2])
            e, x = r("EL", 12 * h, 12 * h + 12), lambda a, st: r("X0", 4 * H * h + a, 4 * H * h + 4 * H, st)
            if w[0] == "z": tt(part("Z", b, h, 1, 2), r("FT", C * b), part("FD", b, h, 0, 2), OP.add, off=e)
            if w[0] == "f": act(part("FD", b, h, 1, 2), r("FT", C * b), off=e, on="S")
            if w[0] == "p": scan(part("Z", b, h, 0, 1), r("ALT", 0, C), part("FD", b, h, 0, 1), OP.mult, OP.add)
            if w[0] == "h": act(part("Z", b, h, 0, 2), r("HT", C * b), off=e, on="S")
            if w[0] == "x": scan(x(b - 2, 2), r("ALT", 0, C), part("Z", b, h, 0, 1), OP.mult, OP.add)
            if w[0] == "y": tt(x(b, 4), r("HT", C * b), part("Z", b, h, 1, 2), OP.add, off=e)
            if w[0] == "q": quant("QX", H * h, H * h + H, x(0, 1))
            if w[0] == "s":
                if t == R - 1: continue
                scores(b, h)
            q = w[0] in "fh"
            if q in done: hold([done[q]])
            done[q] = len(ops) - 1
    pass
    act(r("OUT", 0, C), r("NODE"), off=r("EL"), on="S")
    dma("Y", [(T.nd[:], T.OUT[0:128:16, 0:2 * C])], rd=[r("OUT", 0, 2 * C)], n=200)
    for h in (0, 1):
        a, y = H * h, r("OUT", 2 * C + H * h, 2 * C + H * h + H)
        mm(VB[h], ("QV", 0), ("QX", a), H)
        act(y, r(VB[h], 0, H))
        dma("Y", [(T.oc[:, 4 * a:4 * a + 4 * H], T.QXc[:, a:a + H].bitcast(dt.uint8))], rd=[r("QXc", a, a + H)])
        dma("Y", [(T.y[:, a:a + H], ap(y))], rd=[y])
    dma("S", [(T.osc[4 * k:4 * k + 4, :], T.QXs[32 * k:32 * k + 4, 0:C]) for k in range(4)], rd=[r("QXs")])
    issue()
    g.wait_ge(T.sem.lcl, sent[0])
